import numpy as np, ml_dtypes
CORES = [16,17,18,19,32,33,34,35]
N = 8
import mx_ref
BF = ml_dtypes.bfloat16
def gcols(t, e):
    v = np.concatenate([t.reshape(8, 16, -1, 4), np.zeros((8, 16, 1, 4), BF)], axis=2)
    return np.ascontiguousarray(np.stack([v[g][:, e[g]] for g in range(8)])).reshape(128, -1)
def tile(rs):
    return np.stack(rs, axis=2).reshape(128, -1).astype(BF)
def pick(q, e):
    c = np.concatenate([q[0].reshape(128, -1, 4), np.zeros((128, 1, 4), np.uint8)], axis=1); s = np.concatenate([q[1], np.ones((16, 1), np.uint8)], axis=1)
    return (np.ascontiguousarray(c[:, e].reshape(128, -1)), np.ascontiguousarray(s[:, e]))
def join(*qs):
    return (np.concatenate([q[0] for q in qs], axis=1), np.concatenate([q[1] for q in qs], axis=1))
def put(q, e, v):
    c, s = q[0].reshape(128, -1, 4).copy(), q[1].copy(); c[:, e] = v[0].reshape(128, -1, 4); s[:, e] = v[1]
    return (c.reshape(128, -1), s)
def pk(c, s):
    return (np.ascontiguousarray(c), mx_ref.live(s))
def emit(q):
    return q[0], q[1]
def packed(v, rng):
    q = [mx_ref.quantize(np.ascontiguousarray(v[r])) for r in range(N)]
    return np.stack([a for a, b in q]), np.stack([mx_ref.plane(b, rng) for a, b in q])
def values_of_codes():
    e, c = np.zeros((128, 128, 4), np.float32), np.zeros((128, 2, 4), np.uint8)
    e[np.arange(128), np.arange(128), 0] = 1
    c[:127, :, 0] = np.arange(256).reshape(2, 128).T[:127]
    return mx_ref.matmul(mx_ref.quantize(e.reshape(128, 512).astype(BF)), (c.reshape(128, 8), np.full((16, 2), 127, np.uint8))).T.reshape(-1).astype(np.float64)
CODE_VALUE, SCALE_VALUE = values_of_codes(), 2.0 ** (np.arange(256) - 127.0)
def decode(q):
    return (CODE_VALUE[q[0]].reshape(16, 8, -1, 4) * SCALE_VALUE[q[1]][:, None, :, None] + 0.0).reshape(128, -1).astype(np.float32)
def f(rng, *shape):
    return mx_ref.flush((rng.standard_normal(shape, dtype=np.float32) * np.exp2(rng.integers(-2, 3, shape[:-1] + (1,)))).astype(BF))
def wide(rng, *shape, cols=0):
    v = rng.standard_normal(shape, dtype=np.float32) * np.exp2(rng.integers(-12, 13, shape)).astype(np.float32)
    if cols: v *= np.repeat(np.exp2(rng.integers(-cols, cols + 1, shape[:-2] + (1, shape[-1] // 4))) * (rng.random(shape[:-2] + (1, shape[-1] // 4)) > 0.0625), 4, axis=-1).astype(np.float32)
    return mx_ref.flush(v.astype(BF))
C, B, K, R = 256, 16, 96, 3
def numbers_of(rng):
    return {"x": np.array(f(rng, N, 128, 4 * C)), "u": np.array(f(rng, N, 128, 512)), "v": np.array(f(rng, N, 128, 512))}
def layers(rng):
    return np.array(f(rng, N, 128, 2048)).reshape(N, 8, 16, 4, 8, 16, 4)
def weights(rng, w):
    c, p = packed(np.ascontiguousarray(w).reshape(N, 128, 2048), rng)
    return {"wc": c, "ws": p}
def lone(u, k, k2=0.0):
    a = u.reshape(N, 128, 128, 4)
    a[:, :, ::16] = 0
    for h in range(0, 128, 16):
        a[:, h, h, 0] = np.asarray(k, np.float32).astype(BF)
        a[:, h + 1, h, 0] = np.asarray(k2, np.float32).astype(BF)
    return a.reshape(N, 128, 512)
def setup_inputs(rng):
    return {**numbers_of(rng), **weights(rng, layers(rng))}
def setup_inputs_ties(rng):
    d = numbers_of(rng)
    m = C // B
    k = (rng.permutation(m) % 5)[:, None]
    one = 1 << rng.integers(0, 8, (N // 2, 2, m, B))
    two = one | (1 << rng.integers(0, 8, one.shape))
    w = np.where(k == 0, one * rng.integers(0, 2, one.shape), np.where(k == 3, two, 0))
    each = 1 << (np.arange(B) % 8)
    w[:, 0] += np.where(k == 2, each, 0)
    w[:, 1] += np.where(k == 4, each, 0)
    w = (w ^ rng.integers(0, 256, 4)[rng.integers(0, 4, (N // 2, 1, m, 1))]).reshape(N, 1, C)
    x = np.zeros((N, 8, 16, C, 4), np.float32)
    x[:, :, 0, :, 0] = ((w >> np.arange(8)[:, None]) & 1) * 2.0 - 1.0
    z = (N, 8, 8, C, 4)
    x[:, :, 8:] = (1.0 + (2 * rng.integers(0, 64, z) + 1) * 2.0 ** -7) * np.exp2(-rng.integers(2, 9, z)) * (rng.integers(0, 2, z) * 2.0 - 1.0)
    x[:, :, 8, :, 0] = 126.0 * (rng.integers(0, 2, (N, 8, C)) * 2.0 - 1.0)
    a = layers(rng)
    a[:, :, :, :, :, :8] = 0
    a[:, :, :, :, rng.permutation(8)[:4]] = 0
    return {"x": x.reshape(N, 128, 4 * C).astype(BF), "u": lone(d["u"], 1.0), "v": d["v"], **weights(rng, a)}
def setup_inputs_near(rng):
    d = numbers_of(rng)
    x = d["x"].reshape(N, 8, 16, C, 4)
    o = np.repeat(rng.permutation(N // 2) % 2, 2)
    small = (o == 0)[:, None, None]
    s = np.where(small, rng.choice([1.125, 2.0, -40.0, -40.0], (N, 8, C)) * 2.0 ** -30, rng.integers(-1, 2, (N, 8, C)))
    less = np.where(small, -1.25 * 2.0 ** -30, np.zeros((N, 8, C)))
    for r in range(N):
        for g in rng.permutation(8)[:4]:
            c = rng.integers(C)
            s[r, g, c] = 2.0 ** 29
            less[r, g, c] = 2.0 ** 29
    x[:, :, :8] = 0
    x[:, :, 0, :, 0] = s.astype(np.float32).astype(BF)
    x[:, :, 1, :, 0] = less.astype(np.float32).astype(BF)
    w = layers(rng)
    w[:, :, :8] = 0
    w[:, :, :, :, :, :8] = 0
    return {"x": x.reshape(N, 128, 4 * C), "u": lone(d["u"], np.where(o == 0, 1.125 * 2.0 ** -30, 1.0), np.where(o == 0, 2.0 ** -30, 1.0)), "v": d["v"], **weights(rng, w)}
def setup_inputs_late(rng):
    d = numbers_of(rng)
    x = d["x"].reshape(N, 8, 16, C, 4)
    p = rng.permutation(N // 2)
    c = rng.choice([-1.0, 1.0]) * (1.0 - 2.0 * (p // 2 % 2))
    s = np.stack([c, np.where(p % 2 == 0, c, -c)], axis=1).reshape(N)
    x[:, :, 0] = s.astype(np.float32).astype(BF)[:, None, None, None]
    z = (N, 8, C, 4)
    a = (1.0 + (2 * rng.integers(0, 64, z) + 1) * 2.0 ** -7) * np.exp2(-rng.integers(13, 15, z))
    a[:, 0, :, 0] = 1.96875
    x[:, 7, 8:] = (a * (rng.integers(0, 2, z) * 2.0 - 1.0)).astype(np.float32).astype(BF)
    x[:, 6, 8:] = 0
    w = layers(rng)
    w[:, :, :, :, 6:, 8:] = 0
    for i in range(8, 16):
        for b in range(4): w[:, 7, i, b, 6, i, b] = 32
    w[:, 7, 8, 0, 6, 8, 0] = 0
    return {"x": x.reshape(N, 128, 4 * C), "u": lone(d["u"], 1.0), "v": d["v"], **weights(rng, w)}
def setup_inputs_ends(rng):
    d = numbers_of(rng)
    x = np.zeros((N, 8, 16, C, 4), np.float32)
    u = d["u"].reshape(N, 8, 16, 128, 4)
    u[:, :, :, ::16] = 0
    w = np.zeros((N, 128, 4, 128, 4), np.float32)
    i = np.arange(128)
    o = rng.permutation(N // 2) % 2
    for p in range(N // 2):
        e = slice(2 * p, 2 * p + 2)
        k = 2.0 ** 30 if o[p] == 0 else 2.0 ** -30
        for g in range(8): u[e, g, :, 16 * g] = k
        if o[p] == 0:
            c = rng.choice([-1.0, 1.0], (C // B, 1)) * np.ones((1, 8))
            h = np.argsort(rng.random(c.shape), axis=1)[:, :2]
            np.put_along_axis(c, h, -c[:, :2], axis=1)
            m = rng.permutation(C // B)[:2]
            c[m[0]], c[m[1]] = 1.0, -1.0
            s = 0.75 + 0.25 * rng.random((2, 8, 16, C, 4))
            for a in m: s[:, :, :, B * a:B * a + B] = 1.0
            x[e] = 2.0 ** 30 * s * np.repeat(c.T, B, axis=1)[:, None, :, None]
            for g in rng.permutation(8)[:4]: u[e, :, :, 16 * g] = k
            d["v"][e] = (2.0 ** 30 * rng.choice([-1.0, 1.0], (2, 128, 512))).astype(np.float32).astype(BF)
            for b in range(4): w[e, i, b, i, b] = -1
        else:
            x[e] = 2.0 ** -30
            for g in range(8): x[2 * p + 1, g][:, np.arange(C) % B % 8 == g] = -7.0 * 2.0 ** -30
    d["v"] = (np.where(d["v"] < 0, -1.0, 1.0) * np.where(rng.permutation(N) % 2, 2.0 ** -30, 2.0 ** 30)[:, None, None]).astype(np.float32).astype(BF)
    return {"x": x.reshape(N, 128, 4 * C).astype(BF), "u": u.reshape(N, 128, 512), "v": d["v"], **weights(rng, w.astype(BF))}
def setup_inputs_spread(rng):
    d = setup_inputs(rng)
    d["x"] = wide(rng, N, 128, 4 * C, cols=6)
    return d
def check_inputs(d):
    b = []
    for k in ("x", "u", "v"):
        a = np.abs(d[k].astype(np.float32))
        if not (np.isfinite(a).all() and ((a == 0) | (a >= 2.0 ** -30) & (a <= 2.0 ** 30)).all()): b.append("a value of " + k)
    none, least, most = [emit(mx_ref.quantize(np.full((128, 16), k, np.float32).astype(BF)))[1][0, 0] for k in (0.0, 2.0 ** -30, 2.0 ** 30)]
    for r in range(N):
        if ((d["wc"][r] == 0x7F) | (d["wc"][r] == 0xFF)).any(): b.append("wc: a code that is no number")
        s = mx_ref.live(d["ws"][r])
        if ((s != none) & ((s < least) | (s > most))).any(): b.append("ws: a scale out of range")
    return b
def reference(x, u, v, wc, ws):
    qu = [mx_ref.quantize(u[r]) for r in range(N)]
    lay = [pk(wc[r], ws[r]) for r in range(N)]
    now = [x[r] for r in range(N)]
    mate = np.arange(N) ^ 1
    after = (np.arange(C)[:, None] + np.arange(1, C)) % C
    for t in range(R):
        q = [mx_ref.quantize(now[r]) for r in range(N)]
        own = [decode(q[r]).astype(BF) for r in range(N)]
        word = np.stack([np.packbits(mx_ref.matmul(qu[r], q[r])[::16] > 0, axis=0, bitorder="little")[0] for r in range(N)])
        theirs = word[:, :, None] ^ np.repeat(word[mate].reshape(N, -1, B), B, axis=1)
        ours = word[:, :, None] ^ word[:, after]
        care = np.full((N, C), 255, np.uint8)
        a, kept = np.zeros((N, 8, C), np.int64), np.zeros((N, 8, C), np.int64)
        for k in range(8):
            g = (3 * t + k) % 8
            bit = np.uint8(1 << g)
            keep = np.any((theirs & care[:, :, None]) == bit, axis=2)
            hit = (ours & care[:, :, None]) == bit
            first = after[np.arange(C), np.argmax(hit, axis=2)]
            a[:, g] = np.where(~keep & np.any(hit, axis=2), first, np.arange(C))
            kept[:, g] = keep
            care = np.where(keep, care, care & np.uint8(255 - (1 << g)))
        l = np.argsort(kept, axis=2, kind="stable")[:, :, :K]
        z = [((own[r].astype(np.float32) + gcols(own[r], a[r]).astype(np.float32)) * np.float32(0.5)).astype(BF) for r in range(N)]
        sent = [mx_ref.quantize(gcols(z[r], l[r])) for r in range(N)]
        now = []
        for r in range(N):
            came = sent[mate[r]]
            held = decode(came)
            made = tile([mx_ref.matmul(pick(lay[r], np.arange(128 * b, 128 * b + 128)), came) * np.float32(0.03125) + held[:, b::4] for b in range(4)]).reshape(8, 16, K, 4)
            new = z[r].reshape(8, 16, C, 4).copy()
            for g in range(8): new[g][:, l[r, g]] = made[g]
            now.append(new.reshape(128, 4 * C))
    y, al = np.zeros((N, 128, C), np.float32), np.zeros((N, 8, C + K), np.float32)
    oc, osc = np.zeros((N, 128, 4 * C), np.uint8), np.zeros((N, 16, C), np.uint8)
    for r in range(N):
        q = mx_ref.quantize(now[r])
        y[r] = mx_ref.matmul(mx_ref.quantize(v[r]), q)
        al[r] = np.concatenate([a[r], l[r]], axis=1)
        oc[r], osc[r] = emit(q)
    return {"y": y, "al": al, "oc": oc, "osc": osc}

@@ -1,0 +1,560 @@
+from concourse.bass import IndirectOffsetOnAxis
+from concourse.mybir import dt, AluOpType, AxisListType, ActivationFunctionType
+
+F32, BF, I32, U16, F8, U8 = "float32", "bfloat16", "int32", "uint16", "float8_e4m3fn_x4", "uint8"
+SCRATCH = {}
+for _n, _w, _d in [
+        ("X0", 1024, BF), ("UT", 512, BF), ("VT", 512, BF), ("WQ", 512, F8), ("WS", 512, U8),
+        ("UQ", 128, F8), ("US", 128, U8), ("VQ", 128, F8), ("VS", 128, U8), ("URQ", 384, F8), ("URS", 384, U8),
+        ("HT", 256, F32), ("ELT", 2048, BF), ("ELQ", 512, F8), ("ELS", 512, U8),
+        ("CMT", 1024, BF), ("CMQ", 256, F8), ("CMS", 256, U8), ("COT", 1024, BF), ("COQ", 256, F8), ("COS", 256, U8),
+        ("HMT", 1024, BF), ("HMQ", 256, F8), ("HMS", 256, U8), ("MTT", 1024, BF), ("MTQ", 256, F8), ("MTS", 256, U8),
+        ("ICOL", 512, F32), ("VB", 256, BF), ("I8", 128, BF), ("I16", 128, BF), ("JP", 256, BF), ("TH", 128, F32),
+        ("IP", 10, I32), ("SC", 16, F32), ("UI", 24, I32), ("UL", 24, U16), ("PLF", 16, F32), ("PL", 16, U16),
+        ("ILF", 64, F32), ("IL", 32, U16), ("NI", 48, I32), ("NS", 16, F32),
+        ("EQT", 518, BF), ("TB", 1548, BF), ("TK", 16, F32), ("H25", 256, BF), ("H50", 16, F32), ("H10", 96, F32),
+        ("H8", 16, F32), ("NEG", 256, F32), ("JL", 32, F32), ("MK", 192, F32),
+        ("XQ", 256, F8), ("XS", 256, U8), ("XT", 1024, BF), ("BT", 768, BF), ("BQ", 192, F8), ("BS", 192, U8),
+        ("W8", 32, F32), ("PB", 32, F32), ("IX", 2, I32), ("SG", 48, F32), ("RS", 1548, BF),
+        ("OT", 1024, BF), ("OQ", 256, F8), ("OS", 256, U8), ("DS", 1024, F32), ("DT", 1024, BF), ("DQ", 256, F8), ("DP", 256, U8),
+        ("HI", 192, BF), ("E", 256, BF), ("XH", 256, F32), ("GS", 64, F32), ("TM", 32, F32),
+        ("RP", 16, F32), ("KK", 96, F32), ("AL", 24, F32), ("INC", 512, F32), ("O", 512, F32), ("XO", 4096, F32),
+        ("YI", 64, I32), ("YT", 64, I32), ("AI", 48, I32),
+        ("LF", 192, F32), ("DL", 64, F32), ("AF", 64, F32), ("WC", 160, F32), ("AU", 16, U16), ("PU", 16, U16), ("LU", 8, U16), ("SU", 16, U16),
+        ("LR", 256, F32), ("LM", 96, F32), ("HP", 2048, BF), ("XW", 1408, BF), ("ET", 512, BF), ("YO", 256, F32)]:
+    SCRATCH[_n] = ("sbuf", [128, _w], _d)
+for _t in range(3):
+    SCRATCH["MS%d" % _t] = ("sbuf", [128, 64], BF)
+    SCRATCH["WL%d" % _t] = ("sbuf", [128, 64], BF)
+    SCRATCH["LB%d" % _t] = ("sbuf", [128, 16], I32)
+    SCRATCH["AC%d" % _t] = ("sbuf", [128, 128], F8)
+    SCRATCH["AS%d" % _t] = ("sbuf", [128, 128], U8)
+    if _t == 0:
+        SCRATCH["EQ"] = ("sbuf", [128, 128], F8)
+        SCRATCH["ES"] = ("sbuf", [128, 128], U8)
+for _b in range(8):
+    SCRATCH["B%d" % _b] = ("psum", [128, 512], F32)
+SCRATCH["tab"] = ("dram", [256, 774], BF)
+SEMAPHORES = ["cV", "cA", "cP", "cG", "dx", "du", "dv", "dw", "dtab", "dfill", "dout"]
+for _t in range(3):
+    SEMAPHORES += ["wa%d" % _t, "ca%d" % _t, "lw%d" % _t, "lc%d" % _t, "dl%d" % _t, "di%d" % _t]
+
+
+def rank_program(g, core, T, topo):
+    rank = T.rank_of(core)
+    if rank is None:
+        return
+    mate = T.cores[rank + 1 if rank % 2 == 0 else rank - 1]
+    A, AF = AluOpType, ActivationFunctionType
+    X = AxisListType.X
+    Q = {"V": g.vector, "A": g.scalar, "P": g.tensor, "G": g, "Y": g.sync}
+    own = {"V": "cV", "A": "cA", "P": "cP", "G": "cG", "Y": None}
+    tot, lastw, readers, epoch, known = {}, {}, {}, {}, {e: {} for e in Q}
+
+    def need(e, toks):
+        for s, v in sorted(toks):
+            n = tot[s] if v is None else v
+            if known[e].get(s, 0) < n:
+                Q[e].wait_ge(T.sem[s], n)
+                known[e][s] = n
+
+    def deps(e, r, w, add, compute):
+        toks = {}
+
+        def put(tk, war=False):
+            s, v = tk
+            if war and compute and s == own[e]:
+                return
+            n = tot[s] if v is None else v
+            toks[s] = max(toks.get(s, 0), n)
+        for k in r:
+            for tk in lastw.get(k, []):
+                put(tk)
+            if k[0] == "B" and k[1:].isdigit():
+                for tk in readers.get(k, []):
+                    put(tk, True)
+        for k in w:
+            for tk in lastw.get(k, []):
+                put(tk)
+            for tk in readers.get(k, []):
+                put(tk, True)
+        for k in add:
+            if readers.get(k):
+                epoch[k] = lastw.get(k, []) + readers[k]
+                lastw[k], readers[k] = [], []
+            for tk in epoch.get(k, []):
+                put(tk)
+        need(e, list(toks.items()))
+
+    def note(tk, r, w, add):
+        for k in r:
+            readers.setdefault(k, []).append(tk)
+        for k in w:
+            lastw[k], readers[k], epoch[k] = [tk], [], [tk]
+        for k in add:
+            lastw.setdefault(k, []).append(tk)
+
+    def op(e, f, r, w=(), add=()):
+        r, w, add = r.split(), (w.split() if w else []), (add.split() if add else [])
+        deps(e, r, w, add, True)
+        s = own[e]
+        f().then_inc(T.sem[s], 1)
+        tot[s] = tot.get(s, 0) + 1
+        note((s, tot[s]), r, w, add)
+
+    def dma(e, out, in_, s, r, w="", add=""):
+        r, w, add = r.split(), w.split(), add.split()
+        deps(e, r, w, add, False)
+        Q[e].dma_start(out, in_).then_inc(T.sem[s], 16)
+        tot[s] = tot.get(s, 0) + 16
+        note((s, None), r, w, add)
+
+    eng = topo.engines(core, mate)
+    ne = 1
+    while ne * 2 <= len(eng):
+        ne *= 2
+    msk = 0
+    for _e in eng[:ne]:
+        msk |= 1 << _e
+    rid, pid = topo.addr(mate)[:2]
+
+    def remote(out, in_, rs, ls, r, w):
+        deps("G", r.split(), [], [], False)
+        g.remote_dma(out_ap=out, in_ap=in_, remote_sem=T.sem[rs], local_sem=T.sem[ls], pid=pid, routing_id=rid, dma_engine_mask=msk)
+        tot[ls] = tot.get(ls, 0) + ne
+        tot[rs] = tot.get(rs, 0) + ne
+        note((ls, None), r.split(), [], [])
+        for k in w.split():
+            lastw.setdefault(k, []).append((rs, None))
+
+    v, ac, pe = g.vector, g.scalar, g.tensor
+
+    def ts(out, in0, s1, s2, o0, o1, r, w="", add=""):
+        if o1 is None:
+            op("V", lambda: v.tensor_scalar(out, in0, s1, None, o0), r, w, add)
+        else:
+            op("V", lambda: v.tensor_scalar(out, in0, s1, s2, o0, o1), r, w, add)
+
+    def tt(out, a, b, o, r, w="", add=""):
+        op("V", lambda: v.tensor_tensor(out, a, b, o), r, w, add)
+
+    def cp(out, a, r, w="", add=""):
+        op("V", lambda: v.tensor_copy(out, a), r, w, add)
+
+    def scan(out, d0, d1, ini, o0, o1, r, w="", add=""):
+        op("V", lambda: v.tensor_tensor_scan(out, d0, d1, ini, o0, o1), r, w, add)
+
+    def fill(ap, c, w="", add=""):
+        op("V", lambda: v.memset(ap, c), "", w, add)
+
+    def quant(c, s, t, r, w):
+        op("V", lambda: v.quantize_mx(c, s, t), r, w)
+
+    def act(out, in_, r, w="", add="", scale=1.0):
+        if scale == 1.0:
+            op("A", lambda: ac.activation(out, in_, AF.Copy), r, w, add)
+        else:
+            op("A", lambda: ac.activation(out, in_, AF.Copy, scale=scale), r, w, add)
+
+    def mm(out, l, ls, rr, rs, a, z, r, w="", add=""):
+        op("P", lambda: pe.matmul_mx(out, l, ls, rr, rs, a, z), r, w, add)
+
+    def iota(out, pat, base, ch, w, flag=True):
+        if flag:
+            op("G", lambda: g.iota(out, pat, base, ch, allow_small_or_imprecise_dtypes=True), "", w)
+        else:
+            op("G", lambda: g.iota(out, pat, base, ch), "", w)
+
+    dma("Y", T.X0[:], T.x[:], "dx", "", "X0")
+    dma("A", T.UT[:], T.u[:], "du", "", "UT")
+    dma("Y", T.WQ[:].bitcast(dt.uint8), T.wc[:], "dw", "", "WQ")
+    dma("Y", T.WS[:], T.ws[:], "dw", "", "WS")
+    dma("A", T.VT[:], T.v[:], "dv", "", "VT")
+
+    iota(T.IP[:, 0:1], [[0, 1]], 0, 1, "ip0", False)
+    iota(T.UI[:], [[3, 3], [0, 8]], 0, 1, "UI", False)
+    iota(T.ICOL[:], [[1, 512]], 0, 0, "ICOL")
+    iota(T.SC[:, 0:1], [[0, 1]], 0, 1, "s0")
+    iota(T.SC[:, 4:5], [[0, 1]], 128, 1, "s4")
+    iota(T.SC[:, 5:7], [[-128, 2]], 255, -1, "s5 s6")
+    iota(T.I8[:], [[1, 16], [0, 8]], 0, 0, "I8")
+    iota(T.I16[:], [[0, 8], [1, 16]], 0, 0, "I16")
+    iota(T.JP[:, 0:128], [[4, 4], [1, 2], [16, 16]], 0, 0, "JP0")
+    iota(T.JP[:, 128:256], [[4, 4], [1, 2], [16, 16]], 2, 0, "JP1")
+    iota(T.VB[:], [[1, 256]], 0, 0, "VB")
+    iota(T.PLF[:], [[-2, 2], [-4, 4], [-1, 2]], 255, 0, "PLF")
+    iota(T.JL[:, 16:32], [[16, 16]], 0, 0, "JLF")
+    iota(T.NEG[:], [[0, 256]], -1, 0, "NEG")
+
+    DEAD = 262144.0
+
+    def flat(nm, width, c):
+        for a in range(0, width, 512):
+            b = min(width, a + 512)
+            o, i = T[nm][:, a:b], T.ICOL[:, 0:b - a]
+            if c == 0.0:
+                op("A", lambda: ac.activation(o, i, AF.Copy, scale=0.0), "ICOL", "", nm)
+            else:
+                op("A", lambda: ac.activation(o, i, AF.Identity, bias=c, scale=0.0), "ICOL", "", nm)
+        epoch[nm] = list(lastw[nm])
+
+    for k in range(8):
+        fill(T.TK[:, k::8], 0.05 * 0.25 ** k, "", "TK")
+    for nm, c, n in (("H50", 0.5, 8), ("H25", 0.25, 8), ("H8", 1.0, 8), ("H10", 1.0, 16)):
+        fill(T[nm][:], c, nm)
+    for st, n in ((1, 2), (2, 4), (4, 8), (8, 16)):
+        fill(T.ILF[:, st:32:n], {1: 1.0, 2: 2.0, 4: 3.0, 8: 4.0}[st], "", "ILF")
+    fill(T.ILF[:, 0:1], 13.0, "", "ILF")
+    fill(T.ILF[:, 16:17], 6.0, "", "ILF")
+    fill(T.YT[:], 0, "YT")
+    for nm in ("AL", "DL", "AF", "BT", "OT"):
+        fill(T[nm][:], 0.0, nm)
+    fill(T.ET[:, 384:512], 0.0, "ET4")
+    for nm, n in (("H50", 8), ("H25", 8), ("H8", 8), ("H10", 16)):
+        fill(T[nm][:, 0::n], 0.0, nm)
+    flat("CMT", 1024, 0.0)
+    flat("COT", 1024, 0.0)
+    IP, SC = T.IP, T.SC
+    for c, m in ((1, 15), (4, 1), (5, 3), (6, 7)):
+        ts(IP[:, c:c + 1], IP[:, 0:1], m, None, A.bitwise_and, None, "ip0", "ip%d" % c)
+    for c, m in ((2, 4),):
+        ts(IP[:, c:c + 1], IP[:, 0:1], m, None, A.arith_shift_right, None, "ip0", "ip%d" % c)
+
+    def sc(c):
+        return SC[:, c:c + 1]
+    for c, i, m, a in ((1, 1, 1.0, 0.0), (2, 2, 1.0, 0.0), (3, 2, 1.0, 8.0), (10, 1, 16.0, 0.0)):
+        ts(sc(c), IP[:, i:i + 1], m, a, A.mult, A.add, "ip%d" % i, "s%d" % c)
+    ts(T.UI[:], T.UI[:], 7, None, A.bitwise_and, None, "UI", "UI")
+    ts(T.UL[:], T.UI[:], 16, None, A.mult, None, "UI", "UL")
+    quant(T.UQ[:], T.US[:], T.UT[:], "UT", "UQ US")
+    cp(T.URQ[:].bitcast(dt.uint32), T.UQ[:].bitcast(dt.uint32).indirect(T.UL[:]), "UQ UL", "URQ")
+    op("A", lambda: ac.activation(T.URS[:], T.US[:].indirect(T.UL[:]), AF.Copy), "US UL", "URS")
+    so = [0]
+    for k in range(8):
+        so.append(so[-1] + 1 + (256 >> k))
+
+    def ones(nm, o, n, c):
+        op("A", lambda: ac.activation(T[nm][:, o:o + n], T.ICOL[:, 0:n], AF.Identity, bias=c, scale=0.0), "ICOL", "", nm)
+    flat("EQT", 518, 0.0)
+    for k in range(8):
+        ones("EQT", so[k], 1, DEAD)
+    ones("EQT", so[7] + 2, 1, DEAD)
+    epoch["EQT"] = list(lastw["EQT"])
+    for o, n, c in ((129, 127, 0.0), (256, 512, 0.0), (768, 6, 0.0), (775, 127, 0.0), (1030, 512, 0.0), (1542, 6, 0.0), (128, 1, -256.0), (774, 1, -256.0)):
+        ones("TB", o, n, c)
+    epoch["TB"] = list(lastw["TB"])
+    for k in range(8):
+        ones("TB", 1030 + so[k] + (1 if k == 7 else 0), 1, DEAD)
+    epoch["tb1"] = epoch["tb0"] = list(lastw["TB"])
+    flat("HMT", 1024, 0.0)
+    ts(T.TH[:], T.I8[:], sc(1), 1e29, A.not_equal, A.mult, "I8 s1", "TH")
+    for h in range(2):
+        for b in range(2):
+            ts(T.CMT[:, 512 * h + b:512 * h + 512:4], T.I16[:], sc(2 + b), float(1 + h), A.is_equal, A.mult, "I16 s%d" % (2 + b), "", "CMT")
+    for s in range(2):
+        for b in range(2):
+            ts(T.COT[:, 512 * s + 2 + b:512 * s + 512:4], T.JP[:, 128 * s:128 * s + 128], sc(0 if b == 0 else 4), None, A.is_equal, None,
+               "JP%d s0 s4" % s, "", "COT")
+    quant(T.CMQ[:], T.CMS[:], T.CMT[:], "CMT", "CMQ CMS")
+    quant(T.COQ[:], T.COS[:], T.COT[:], "COT", "COQ COS")
+    fill(T.H50[:], 0.5, "H50")
+    fill(T.H50[:, 0::8], 0.0, "H50")
+
+    def setup_b(n):
+        if n < 2:
+            ts(T.HMT[:, n::4], T.VB[:], sc(5 + n), 256.0, A.is_equal, A.mult, "VB s%d" % (5 + n), "", "HMT")
+        elif n < 6:
+            ts(T.MTT[:, n - 2::4], T.VB[:], sc(0 if n < 4 else 4), None, A.is_equal, None, "VB s0 s4", "", "MTT")
+        elif n == 6:
+            ts(T.PL[:], T.PLF[:], sc(10), None, A.subtract, None, "PLF s10", "PL")
+        else:
+            quant(T.HMQ[:], T.HMS[:], T.HMT[:], "HMT", "HMQ HMS")
+            quant(T.MTQ[:], T.MTS[:], T.MTT[:], "MTT", "MTQ MTS")
+
+    def setup_c():
+        for k in range(7):
+            ts(T.NI[:, k:k + 1], IP[:, 0:1], k, None, A.arith_shift_right, None, "ip0", "", "NI")
+        a = T.TB[:, 0:128]
+        ts(a, T.VB[:, 0:128], sc(0), DEAD, A.is_equal, A.mult, "VB s0", "ta0")
+        ts(T.NI[:, 16:23], T.NI[:, 0:7], 1, None, A.bitwise_and, None, "NI", "NB")
+        setup_b(6)
+        ts(T.NI[:, 32:39], T.NI[:, 16:23], -2, 1, A.mult, A.add, "NB", "NC")
+        setup_b(5)
+        tt(T.NS[:, 0:7], T.NI[:, 0:7], T.NI[:, 32:39], A.add, "NI NC", "NS")
+        setup_b(2)
+        for k in range(7):
+            o, n = so[k] + 1, 128 >> k
+            ts(T.EQT[:, o:o + n], T.VB[:, 0:n], T.NS[:, k:k + 1], DEAD, A.is_equal, A.mult, "VB NS", "", "EQT")
+        for k in range(8):
+            o, n = so[k], (128 >> k) + 1
+            tt(T.TB[:, 256 + o:256 + o + n], T.EQT[:, o:o + n], T.EQT[:, o + 1:o + n + 1], A.subtract, "EQT TB", "", "tb0")
+        for k in range(7):
+            o, n = 256 + so[k], 128 >> k
+            i1, o1, i2, o2 = T.TB[:, o + 1:o + n], T.TB[:, 774 + o + n + 1:774 + o + 2 * n], T.TB[:, o:o + 1], T.TB[:, 774 + o + n:774 + o + n + 1]
+            if n > 1:
+                act(o1, i1, "tb0 TB", "", "tb1")
+            op("A", lambda: ac.activation(o2, i2, AF.Identity, bias=-DEAD, scale=1.0), "tb0 TB", "", "tb1")
+        for k in range(7):
+            o, n = so[k] + 1, 128 >> k
+            b = T.TB[:, 0:128:1 << k]
+            tt(b, b, T.EQT[:, o:o + n], A.add, "EQT ta0", "ta0")
+            if k != 2 and k < 5:
+                setup_b(k)
+        ts(a, a, -256.0 / DEAD, None, A.mult, None, "ta0", "ta0")
+        act(T.TB[:, 902:1030], a, "ta0", "ta1")
+        for h in range(2):
+            dma("Y", T.tab[128 * h:128 * h + 128, :], T.TB[:, 774 * h:774 * h + 774], "dtab", "ta%d tb%d TB" % (h, h), "", "tab")
+
+    def setup_e():
+        for b in range(4):
+            ts(T.ELT[:, 512 * b + b:512 * b + 512:4], T.VB[:, 0:128], sc(0), 32.0, A.is_equal, A.mult, "VB s0", "", "ELT")
+        quant(T.ELQ[:], T.ELS[:], T.ELT[:], "ELT", "ELQ ELS")
+
+    def setup_f():
+        ts(T.JL[:, 0:16], T.JL[:, 16:32], sc(1), None, A.add, None, "JLF s1", "JL")
+        ts(T.MK[:, 96:192], T.I16[:, 0:96], sc(1), 8000.0, A.not_equal, A.mult, "I16 s1", "mk0")
+        tt(T.MK[:, 1:96], T.MK[:, 97:192], T.MK[:, 96:191], A.subtract, "mk0", "MK")
+        ts(T.MK[:, 16:96:16], T.MK[:, 16:96:16], 3000.0, None, A.subtract, None, "MK", "MK")
+        cp(T.MK[:, 0:1], T.MK[:, 96:97], "mk0 MK", "MK")
+        quant(T.VQ[:], T.VS[:], T.VT[:], "VT", "VQ VS")
+
+    def setup_d():
+        for i in range(3):
+            ts(sc(12 + i), IP[:, 4 + i:5 + i], 0.0, None, A.is_equal, None, "ip%d" % (4 + i), "r%d" % (1 + i))
+        tt(sc(8), sc(12), sc(13), A.add, "r1 r2", "s8")
+        tt(sc(8), sc(8), sc(14), A.add, "s8 r3", "s8")
+        ts(sc(9), IP[:, 1:2], 0.0, None, A.is_equal, None, "ip1", "s9")
+        ts(T.ILF[:, 32:64], T.ILF[:, 0:32], sc(9), sc(8), A.mult, A.add, "ILF s9 s8", "ILG")
+        cp(T.IL[:, 0:16], T.ILF[:, 32:48], "ILG", "IL0")
+        ts(T.IL[:, 16:32], T.ILF[:, 48:64], 8.0, None, A.add, None, "ILG", "IL1")
+
+    def B(b):
+        return T["B%d" % b]
+
+    DB = (2, 5, 6, 7)
+    for t in range(3):
+        last = t == 2
+        src, key = (T.X0, "X0") if t == 0 else (T.XT, "XT")
+        for h in range(2):
+            quant(T.XQ[:, 128 * h:128 * h + 128], T.XS[:, 128 * h:128 * h + 128], src[:, 512 * h:512 * h + 512], key, "XQ%d" % h)
+        if t == 0:
+            for i in range(3):
+                dma("Y", T["AC%d" % i][:, 96:128].bitcast(dt.uint8), T.XQ[:, 0:32].bitcast(dt.uint8), "dfill", "XQ0", "", "AC%d" % i)
+                dma("Y", T["AS%d" % i][:, 96:128], T.XS[:, 0:32], "dfill", "XQ0", "", "AS%d" % i)
+        for s in range(2):
+            mm(B(s)[:, 0:128], T.XQ[:, 128 * s:128 * s + 128], T.XS[:, 128 * s:128 * s + 128], T.URQ[:, 128 * t:128 * t + 128], T.URS[:, 128 * t:128 * t + 128],
+               True, True, "XQ%d URQ URS" % s, "B%d" % s)
+        for s in range(2):
+            tt(T.BT[:, s:512:4], B(s)[:, 0:128], T.TH[:], A.is_gt, "B%d TH" % s, "", "BT")
+            ts(T.BT[:, 2 + s:512:4], B(s)[:, 0:128], 0.0, None, A.is_gt, None, "B%d" % s, "", "BT")
+        for s in range(2):
+            ts(T.W8[:, 8 * s:8 * s + 8], B(s)[:, 0:8], 0.0, 128.0, A.is_gt, A.mult, "B%d" % s, "", "W8")
+        quant(T.BQ[:], T.BS[:], T.BT[:], "BT", "BQ BS")
+        mm(B(2)[:, 0:128], T.CMQ[:, 0:128], T.CMS[:, 0:128], T.BQ[:, 0:128], T.BS[:, 0:128], True, False, "CMQ CMS BQ BS", "B2")
+        mm(B(2)[:, 0:128], T.CMQ[:, 128:256], T.CMS[:, 128:256], T.BQ[:, 64:192], T.BS[:, 64:192], False, True, "CMQ CMS BQ BS", "", "B2")
+        for s in range(2):
+            mm(B(3 + s)[:, 0:128], T.COQ[:, 128 * s:128 * s + 128], T.COS[:, 128 * s:128 * s + 128], T.BQ[:, 0:128], T.BS[:, 0:128], True, True,
+               "COQ COS BQ BS", "B%d" % (3 + s))
+        act(T["MS%d" % t][:], B(2)[:, 0:64], "B2", "MS%d" % t)
+        remote(T["WL%d" % t][:], T["MS%d" % t][:], "wa%d" % t, "lw%d" % t, "MS%d" % t, "WL%d" % t)
+        def places():
+            for s in range(2):
+                ts(T.PB[:, 8 * s:8 * s + 8], B(3 + s)[:, 0:8], 128.0, None, A.mult, None, "B%d" % (3 + s), "", "PB")
+            scan(T.PB[:, 16:32], T.H50[:], T.PB[:, 0:16], 0.0, A.mult, A.add, "H50 PB", "PW")
+            cp(T.IX[:], T.PB[:, 23::8], "PW", "IX")
+            for i, (a, b) in enumerate(((-128.0, 8192.0), (-256.0, 16384.0), (64.0, 0.0))):
+                op("A", lambda: ac.activation(T.SG[:, 16 * i:16 * i + 16], T.PB[:, 0:16], AF.Identity, bias=b, scale=a), "PB", "", "SG")
+        if t == 0:
+            setup_c()
+        scan(T.W8[:, 16:32], T.H50[:], T.W8[:, 0:16], 0.0, A.mult, A.add, "H50 W8", "WW")
+        if t == 0:
+            setup_b(7)
+        for s in range(2):
+            ts(T.OT[:, s::4], T.VB[:], T.W8[:, 8 * s + 23:8 * s + 24], None, A.is_equal, None, "VB WW", "", "OT")
+        quant(T.OQ[:], T.OS[:], T.OT[:], "OT", "OQ OS")
+        for h in range(2):
+            mm(B(5 + h)[:, 0:256], T.OQ[:, 128 * h:128 * h + 128], T.OS[:, 128 * h:128 * h + 128], T.HMQ[:], T.HMS[:], True, True, "OQ OS HMQ HMS", "B%d" % (5 + h))
+        places()
+        if t == 0:
+            setup_d()
+        for h in range(2):
+            scan(T.DS[:, 512 * h:512 * h + 256], T.NEG[:], B(5 + h)[:, 0:256], 0.0, A.add, A.max, "NEG B%d" % (5 + h), "DR%d" % h)
+        for h in range(2):
+            scan(T.DS[:, 512 * h + 256:512 * h + 512], T.NEG[:], B(5 + h)[:, 0:256], T.DS[:, 512 * h + 255:512 * h + 256], A.add, A.max,
+                 "NEG DR%d B%d" % (h, 5 + h), "DS%d" % h)
+        D0, D1 = [T.DS[:, 512 * h + 256:512 * h + 512].indirect(T.PL[:]) for h in range(2)]
+        op("A", lambda: ac.activation(T.HT[:], D0, AF.Identity, bias=201326592.0), "DS0 PL", "HT")
+        op("A", lambda: ac.activation(T.DT[:, 0::4], T.HT[:], AF.Identity, bias=-201326592.0), "HT", "dt0")
+        ts(T.DT[:, 2::4], D1, 201326592.0, 201326592.0, A.add, A.subtract, "DS1 PL", "dt2")
+        tt(T.DT[:, 3::4], D1, T.DT[:, 2::4], A.subtract, "DS1 PL dt2", "dt3")
+        tt(T.DT[:, 1::4], D0, T.DT[:, 0::4], A.subtract, "DS0 PL dt0", "dt1")
+        WL = T["WL%d" % t]
+        HI, HI2, LO, GS = T.HI[:, 0:64], T.HI[:, 64:128], T.HI[:, 128:192], T.GS[:, 0:32]
+        ts(HI2, WL[:], 2.0, 2.0, A.is_ge, A.mult, "WL%d" % t, "HI2")
+        ts(HI, WL[:], 2.0, None, A.is_ge, None, "WL%d" % t, "HI")
+        quant(T.DQ[:], T.DP[:], T.DT[:], "dt0 dt1 dt2 dt3", "DQ DP")
+        for s in range(2):
+            mm(B(s)[:, 0:256], T.DQ[:, 128 * s:128 * s + 128], T.DP[:, 128 * s:128 * s + 128], T.MTQ[:], T.MTS[:], True, True, "DQ DP MTQ MTS", "B%d" % s)
+        deps("G", ["IX", "tab"], ["RS"], [], False)
+        for s in range(2):
+            g.indirect_dma_start(T.RS[:, 774 * s:774 * s + 774], None, T.tab[:], IndirectOffsetOnAxis(ap=T.IX[:, s:s + 1], axis=0),
+                                 bounds_check=255).then_inc(T.sem["di%d" % t], 16)
+        tot["di%d" % t] = 32
+        note(("di%d" % t, None), ["IX", "tab"], ["RS"], [])
+        def halves():
+            for b in range(4):
+                kb = "B%d" % DB[b]
+                mm(B(DB[b])[:, 0:256], T.ELQ[:, 128 * b:128 * b + 128], T.ELS[:, 128 * b:128 * b + 128], T.XQ[:], T.XS[:], True, True, "ELQ ELS XQ0 XQ1", kb)
+                for a in range(2):
+                    act(T.HP[:, 1024 * a + 256 * b:1024 * a + 256 * b + 256], B(DB[b])[:, 0:256], kb, "", "HP", scale=0.015625)
+        if t == 0:
+            flat("ELT", 2048, 0.0)
+        else:
+            halves()
+        tt(LO, WL[:], HI2, A.subtract, "WL%d HI2" % t, "LO")
+        for s in range(2):
+            tt(T.E[:, 128 * s + 64:128 * s + 128], B(3 + s)[:, 64:128], HI, A.not_equal, "B%d HI" % (3 + s), "", "E")
+        for s in range(2):
+            tt(T.E[:, 128 * s:128 * s + 64], B(3 + s)[:, 0:64], LO, A.not_equal, "B%d LO" % (3 + s), "", "E")
+        scan(T.XH[:], T.H25[:], T.E[:], 0.0, A.mult, A.add, "H25 E", "XH")
+        GA = T.GS[:, 32:64]
+        ts(GA, T.XH[:, 7::8], -163840.0, 5.0, A.mult, A.add, "XH", "GA")
+        op("V", lambda: v.reciprocal(GS, GA), "GA", "GS")
+        lastw["gs0"] = lastw["gs1"] = lastw["GS"]
+        for k in range(8):
+            for s in range(2):
+                c = 8 * s + k
+                op("V", lambda: v.tensor_reduce(T.RP[:, c:c + 1], T.GS[:, 16 * s:16 * s + 16], X, A.min, negate=True), "gs%d" % s, "rp%d" % c)
+            if k == 7:
+                break
+            for s in range(2):
+                c = 8 * s + k
+                ts(T.TM[:, 16 * s:16 * s + 16], T.E[:, 128 * s + k:128 * s + 128:8], T.RP[:, c:c + 1], 0.062 * 0.25 ** k, A.min, A.subtract,
+                   "E rp%d" % c, "tm%d" % s)
+            for s in range(2):
+                a = T.GS[:, 16 * s:16 * s + 16]
+                tt(a, a, T.TM[:, 16 * s:16 * s + 16], A.max, "gs%d tm%d" % (s, s), "gs%d" % s)
+        K = T.KK[:, 0:16]
+        tt(K, T.RP[:], T.TK[:], A.is_gt, "TK " + " ".join("rp%d" % c for c in range(16)), "K")
+        tt(T.KK[:, 16:32], K, T.SG[:, 0:16], A.mult, "K SG", "KA")
+        tt(T.KK[:, 32:48], K, T.SG[:, 16:32], A.mult, "K SG", "KB")
+        tt(T.KK[:, 48:64], K, T.SG[:, 32:48], A.mult, "K SG", "KC")
+        scan(T.KK[:, 80:96], T.H8[:], T.KK[:, 16:32], 0.0, A.mult, A.add, "H8 KA", "CU")
+        for s in range(2):
+            op("V", lambda: v.tensor_reduce(T.AL[:, 16 + s:17 + s], T.KK[:, 48 + 8 * s:56 + 8 * s], X, A.add), "KC AL", "al%d" % s)
+        tt(T.AL[:, 0:16], T.KK[:, 32:48], T.KK[:, 80:96], A.subtract, "KB CU AL", "al2")
+        if t == 0:
+            setup_e()
+            halves()
+        for s in range(2):
+            tt(T.INC[:, 256 * s:256 * s + 256], T.AL[:].indirect(T.IL[:, 16 * s:16 * s + 16]), T.RS[:, 774 * s:774 * s + 256], A.add,
+               "al0 al1 al2 RS IL0 IL1", "INC%d" % s)
+        for s in range(2):
+            scan(T.O[:, 256 * s:256 * s + 256], T.INC[:, 256 * s:256 * s + 256], B(s)[:, 0:256], 0.0, A.add, A.max, "INC%d B%d" % (s, s), "O%d" % s)
+        for s in range(2):
+            for k in range(8):
+                n, e, o = 256 >> k, 256 * (8 * s + k + 1), 774 * s + 256 + so[k]
+                scan(T.XO[:, e - n:e], T.RS[:, o:o + n], T.O[:, 256 * s + (1 << k) - 1:256 * s + 256:1 << k], -65536.0, A.add, A.max, "RS O%d" % s, "", "XO")
+        act(T.KK[:, 64:80], K, "K", "K2", scale=16384.0)
+        ts(T.YI[:, 0:16], T.XO[:, 255::256], -1.0, 4096.0, A.mult, A.add, "XO", "Y0")
+        ts(T.YI[:, 16:32], T.YI[:, 0:16], 8191, None, A.bitwise_and, None, "Y0", "Y1")
+        g0 = 3 * t % 8
+        for s in range(2):
+            for a, b, c in ((0, 8 - g0, g0), (8 - g0, 8, 0)):
+                if a < b:
+                    tt(T.YT[:, 16 * s + c:16 * s + c + b - a], T.YI[:, 16 + 8 * s + a:16 + 8 * s + b], T.KK[:, 64 + 8 * s + a:64 + 8 * s + b], A.add, "Y1 K2", "", "YT")
+        op("V", lambda: v.transpose(T.YT[:, 32:64], T.YT[:, 0:32]), "YT", "TR")
+        LB, lb = T["LB%d" % t], "LB%d" % t
+        for q in range(8):
+            dma("Y" if q % 2 == 0 else "A", LB[16 * q:16 * q + 16, :], T.YT[q::16, 32:64], "dl%d" % t, "TR", "", lb)
+        if t == 0:
+            setup_f()
+        L = T.LF
+        ts(T.DL[:, 0:16], LB[:], 16384.0, None, A.is_lt, None, lb + " DL", "dl")
+        ts(T.AI[:, 16:32], LB[:], 8191, None, A.bitwise_and, None, lb, "ai0")
+        op("V", lambda: v.transpose(T.DL[:, 32:64], T.DL[:, 0:32]), "dl", "dt")
+        ts(T.AI[:, 32:48], T.AI[:, 16:32], 4096, None, A.min, None, "ai0", "ai1")
+        scan(T.WC[:, 0:32], T.H10[:, 0:32], T.DL[:, 32:64], 0.0, A.mult, A.add, "H10 dt", "w0")
+        tt(T.AI[:, 16:32], T.AI[:, 32:48], T.JL[:, 0:16], A.add, "ai1 JL", "ai0")
+
+        def mean(b):
+            b, h = divmod(b, 2)
+            o = 256 * b + 128 * h
+            tt(T.XW[:, o + 96 * b:o + 96 * b + 128], T.HP[:, 256 * b:256 * b + 256].indirect(T.AU[:, 8 * h:8 * h + 8]),
+               T.HP[:, 1024 + o:1152 + o], A.add, "HP AU", "", "XZ%d" % b)
+        for i in range(2):
+            ts(T.WC[:, 32 + 16 * i:48 + 16 * i], T.WC[:, 0:16], 0.0, T.WC[:, 16 * i + 15:16 * i + 16], A.mult, A.add, "w0", "w%d" % (1 + i))
+        ts(T.AI[:, 0:16], T.AI[:, 16:32], 255, None, A.bitwise_and, None, "ai0", "ai")
+        op("V", lambda: v.transpose(T.WC[:, 64:128], T.WC[:, 0:64]), "w0 w1 w2", "wt")
+        cp(T.AU[:], T.AI[:, 0:16], "ai", "AU")
+        act(L[:, 16:32], T.DL[:, 0:16], "dl", "l1", scale=-1024.0)
+        JL = T.JL[:, 0:16]
+        tt(L[:, 32:48], L[:, 16:32], JL, A.add, "l1 JL", "l2")
+        Wi, Cn, Bi = T.WC[:, 64:80], T.WC[:, 96:112], T.WC[:, 128:144]
+        scan(Bi, T.NEG[:, 0:16], Cn, 0.0, A.max, A.add, "wt NEG", "bi")
+        tt(L[:, 48:64], Wi, Cn, A.subtract, "wt", "l3")
+        mean(0)
+        tt(L[:, 64:80], L[:, 48:64], Bi, A.add, "l3 bi", "l4")
+        mean(1)
+        ts(L[:, 80:96], L[:, 64:80], 1.0, T.WC[:, 143:144], A.subtract, A.subtract, "l4 bi", "l5")
+        tt(L[:, 96:112], L[:, 32:48], L[:, 64:80], A.subtract, "l2 l4", "l6")
+        mean(2)
+        tt(L[:, 112:128], L[:, 80:96], L[:, 96:112], A.max, "l5 l6", "l7")
+        mean(3)
+        ts(T.PU[:], L[:, 112:128], T.WC[:, 143:144], None, A.add, None, "l7 bi", "PU")
+        mean(4)
+        mean(5)
+        op("V", lambda: v.tensor_copy(T.LR[:].indirect(T.PU[:]), T.ICOL[:, 0:256]), "PU ICOL", "LR")
+        ts(L[:, 128:144], L[:, 112:128], T.WC[:, 143:144], None, A.add, None, "l7 bi", "pos")
+        ts(L[:, 144:160], L[:, 128:144], 96.0, None, A.is_lt, None, "pos", "m0")
+        tt(L[:, 160:176], L[:, 128:144], JL, A.subtract, "pos JL", "m1")
+        scan(T.LM[:], T.MK[:, 0:96], T.LR[:, 0:96], 0.0, A.add, A.max, "MK LR", "ln")
+        ts(L[:, 176:192], L[:, 160:176], 256.0, None, A.add, None, "m1", "m2")
+        mean(6)
+        mean(7)
+        ts(T.LU[:, 0:6], T.LM[:, 15::16], T.MK[:, 111:112], None, A.subtract, None, "ln MK", "LU")
+        tt(L[:, 160:176], L[:, 176:192], L[:, 144:160], A.mult, "m2 m0", "m3")
+        for b in range(4):
+            o, i = T.ET[:, b:384:4], T.XW[:, 352 * b:352 * b + 256].indirect(T.LU[:, 0:6])
+            if b in (0, 2):
+                op("A", lambda: ac.activation(o, i, AF.Copy), "XZ%d LU" % b, "", "ET")
+            else:
+                op("V", lambda: v.tensor_copy(o, i), "XZ%d LU" % b, "", "ET")
+        quant(T.EQ[:], T.ES[:], T.ET[:], "ET ET4", "EQ ES")
+        remote(T["AC%d" % t][:, 0:96].bitcast(dt.uint8), T.EQ[:, 0:96].bitcast(dt.uint8), "ca%d" % t, "lc%d" % t, "EQ", "AC%d" % t)
+        remote(T["AS%d" % t][:, 0:96], T.ES[:, 0:96], "ca%d" % t, "lc%d" % t, "ES", "AS%d" % t)
+        tt(L[:, 176:192], L[:, 160:176], JL, A.add, "m3 JL", "m2")
+        cp(T.SU[:], L[:, 176:192], "m2", "SU")
+        if last:
+            cp(T.AF[:, 0:16], T.AI[:, 0:16], "ai AF", "af")
+            op("V", lambda: v.transpose(T.AF[:, 32:64], T.AF[:, 0:32]), "af", "at")
+            for q in range(8):
+                p = 32 * (q // 2)
+                dma("Y", T.al[q:q + 1, 0:256], T.AF[p:p + 16, 32 + 16 * (q % 2):48 + 16 * (q % 2)], "dout", "at")
+            dma("Y", T.al[:, 256:352], T.LR[0::16, 0:96], "dout", "LR")
+        AC, AS = T["AC%d" % t], T["AS%d" % t]
+        for b in range(4):
+            kb = "B%d" % DB[b]
+            mm(B(DB[b])[:, 0:128], T.WQ[:, 128 * b:128 * b + 128], T.WS[:, 128 * b:128 * b + 128], AC[:], AS[:], True, False, "WQ WS AC%d AS%d" % (t, t), kb)
+            mm(B(DB[b])[:, 0:128], T.ELQ[:, 128 * b:128 * b + 128], T.ELS[:, 128 * b:128 * b + 128], AC[:], AS[:], False, True, "ELQ ELS AC%d AS%d" % (t, t), "", kb)
+        for b in range(4):
+            kb, o, i = "B%d" % DB[b], T.XW[:, 352 * b + 256:352 * b + 352], B(DB[b])[:, 0:96]
+            act(o, i, kb, "XT%d" % b, scale=0.03125)
+        for b in range(4):
+            o, i = T.XT[:, b::4], T.XW[:, 352 * b:352 * b + 352].indirect(T.SU[:])
+            if b == 3:
+                o1, o2 = T.XT[:, 3:512:4], T.XT[:, 515::4]
+                i1, i2 = [T.XW[:, 1056:1408].indirect(T.SU[:, 8 * h:8 * h + 8]) for h in range(2)]
+                op("A", lambda: ac.activation(o1, i1, AF.Copy), "XZ3 XT3 SU", "", "XT")
+                op("V", lambda: v.tensor_copy(o2, i2), "XZ3 XT3 SU", "", "XT")
+            else:
+                op("V", lambda: v.tensor_copy(o, i), "XZ%d XT%d SU" % (b, b), "", "XT")
+    quant(T.XQ[:], T.XS[:], T.XT[:], "XT", "XQ0 XQ1")
+    dma("Y", T.oc[:], T.XQ[:].bitcast(dt.uint8), "dout", "XQ0 XQ1")
+    for k in range(4):
+        dma("A", T.osc[4 * k:4 * k + 4, :], T.XS[32 * k:32 * k + 4, :], "dout", "XQ0 XQ1")
+    mm(B(3)[:, 0:256], T.VQ[:], T.VS[:], T.XQ[:], T.XS[:], True, True, "VQ VS XQ0 XQ1", "B3")
+    cp(T.YO[:], B(3)[:, 0:256], "B3", "YO")
+    dma("Y", T.y[:], T.YO[:], "dout", "YO")
+    for s in sorted(tot):
+        need("G", [(s, tot[s])])

@@ -1,43 +1,42 @@
-from concourse.bass import IndirectOffsetOnAxis
-from concourse.mybir import dt, AluOpType, AxisListType, ActivationFunctionType
+from concourse.mybir import dt, AluOpType, ActivationFunctionType
 
 F32, BF, I32, U16, F8, U8 = "float32", "bfloat16", "int32", "uint16", "float8_e4m3fn_x4", "uint8"
 SCRATCH = {}
 for _n, _w, _d in [
         ("X0", 1024, BF), ("UT", 512, BF), ("VT", 512, BF), ("WQ", 512, F8), ("WS", 512, U8),
         ("UQ", 128, F8), ("US", 128, U8), ("VQ", 128, F8), ("VS", 128, U8), ("URQ", 384, F8), ("URS", 384, U8),
-        ("HT", 256, F32), ("ELT", 2048, BF), ("ELQ", 512, F8), ("ELS", 512, U8),
-        ("CMT", 1024, BF), ("CMQ", 256, F8), ("CMS", 256, U8), ("COT", 1024, BF), ("COQ", 256, F8), ("COS", 256, U8),
-        ("HMT", 1024, BF), ("HMQ", 256, F8), ("HMS", 256, U8), ("MTT", 1024, BF), ("MTQ", 256, F8), ("MTS", 256, U8),
-        ("ICOL", 512, F32), ("VB", 256, BF), ("I8", 128, BF), ("I16", 128, BF), ("JP", 256, BF), ("TH", 128, F32),
-        ("IP", 10, I32), ("SC", 16, F32), ("UI", 24, I32), ("UL", 24, U16), ("PLF", 16, F32), ("PL", 16, U16),
-        ("ILF", 64, F32), ("IL", 32, U16), ("NI", 48, I32), ("NS", 16, F32),
-        ("EQT", 518, BF), ("TB", 1548, BF), ("TK", 16, F32), ("H25", 256, BF), ("H50", 16, F32), ("H10", 96, F32),
-        ("H8", 16, F32), ("NEG", 256, F32), ("JL", 32, F32), ("MK", 192, F32),
-        ("XQ", 256, F8), ("XS", 256, U8), ("XT", 1024, BF), ("BT", 768, BF), ("BQ", 192, F8), ("BS", 192, U8),
-        ("W8", 32, F32), ("PB", 32, F32), ("IX", 2, I32), ("SG", 48, F32), ("RS", 1548, BF),
-        ("OT", 1024, BF), ("OQ", 256, F8), ("OS", 256, U8), ("DS", 1024, F32), ("DT", 1024, BF), ("DQ", 256, F8), ("DP", 256, U8),
-        ("HI", 192, BF), ("E", 256, BF), ("XH", 256, F32), ("GS", 64, F32), ("TM", 32, F32),
-        ("RP", 16, F32), ("KK", 96, F32), ("AL", 24, F32), ("INC", 512, F32), ("O", 512, F32), ("XO", 4096, F32),
-        ("YI", 64, I32), ("YT", 64, I32), ("AI", 48, I32),
-        ("LF", 192, F32), ("DL", 64, F32), ("AF", 64, F32), ("WC", 160, F32), ("AU", 16, U16), ("PU", 16, U16), ("LU", 8, U16), ("SU", 16, U16),
-        ("LR", 256, F32), ("LM", 96, F32), ("HP", 2048, BF), ("XW", 1408, BF), ("ET", 512, BF), ("YO", 256, F32)]:
+        ("ELT", 2048, BF), ("ELQ", 512, F8), ("ELS", 512, U8), ("CT", 1024, BF), ("CQ", 256, F8), ("CS", 256, U8),
+        ("HMT", 1024, BF), ("HMQ", 256, F8), ("HMS", 256, U8), ("MTT", 2048, BF), ("MTQ", 512, F8), ("MTS", 512, U8),
+        ("ICOL", 256, F32), ("VB", 256, BF), ("I8", 128, BF), ("I16", 256, BF), ("JP", 128, BF), ("TH", 128, F32),
+        ("IP", 16, I32), ("SC", 24, F32), ("UI", 24, I32), ("UL", 24, U16), ("PLF", 16, F32), ("PL", 16, U16),
+        ("RW", 32, F32), ("FR", 136, F32), ("FS", 128, F32), ("LS", 80, U16), ("KC", 768, BF),
+        ("CB", 64, F32), ("CE", 128, F32), ("RST", 128, F32), ("TK", 16, F32), ("H4", 144, F32), ("HS", 96, F32),
+        ("NEG", 256, BF), ("JL", 48, F32), ("MK", 224, F32),
+        ("XQ", 256, F8), ("XS", 256, U8), ("XT", 1024, BF), ("BT", 608, BF), ("BQ", 152, F8), ("BS", 152, U8),
+        ("W4", 144, F32), ("W2", 16, F32), ("WN", 40, F32), ("SG", 96, F32),
+        ("OT", 1024, BF), ("OQ", 256, F8), ("OS", 256, U8), ("HB", 512, BF), ("DS", 1024, BF), ("DG", 512, BF), ("DH", 512, BF),
+        ("DT", 1024, BF), ("DQ", 256, F8), ("DP", 256, U8), ("MH", 512, BF), ("HH", 512, F32), ("H16", 34, F32),
+        ("BD", 128, F32), ("EM", 256, F32), ("YY", 128, I32), ("EK", 224, I32), ("HL", 64, F32), ("RR", 256, F32),
+        ("KK", 24, F32), ("UU", 96, F32), ("AL", 40, F32), ("INC", 512, F32), ("IN2", 64, F32), ("O", 512, F32), ("O2", 64, F32),
+        ("PK", 256, F32), ("YT", 96, F32), ("AI", 32, I32), ("LF", 160, F32), ("DL", 128, F32), ("WC", 96, F32), ("AF", 64, F32),
+        ("AU", 16, U16), ("PU", 16, U16), ("LU", 8, U16), ("SU", 16, U16), ("LR", 256, F32), ("LM", 96, F32),
+        ("FW", 1024, BF), ("GW", 1024, BF), ("XW", 1408, BF), ("ET", 512, BF), ("EQ", 128, F8), ("ES", 128, U8), ("YO", 256, F32)]:
     SCRATCH[_n] = ("sbuf", [128, _w], _d)
 for _t in range(3):
-    SCRATCH["MS%d" % _t] = ("sbuf", [128, 64], BF)
-    SCRATCH["WL%d" % _t] = ("sbuf", [128, 64], BF)
-    SCRATCH["LB%d" % _t] = ("sbuf", [128, 16], I32)
+    SCRATCH["MS%d" % _t] = ("sbuf", [128, 16], F32)
+    SCRATCH["WL%d" % _t] = ("sbuf", [128, 16], F32)
+    SCRATCH["LB%d" % _t] = ("sbuf", [128, 16], F32)
     SCRATCH["AC%d" % _t] = ("sbuf", [128, 128], F8)
     SCRATCH["AS%d" % _t] = ("sbuf", [128, 128], U8)
-    if _t == 0:
-        SCRATCH["EQ"] = ("sbuf", [128, 128], F8)
-        SCRATCH["ES"] = ("sbuf", [128, 128], U8)
 for _b in range(8):
     SCRATCH["B%d" % _b] = ("psum", [128, 512], F32)
-SCRATCH["tab"] = ("dram", [256, 774], BF)
-SEMAPHORES = ["cV", "cA", "cP", "cG", "dx", "du", "dv", "dw", "dtab", "dfill", "dout"]
+SEMAPHORES = ["cV", "cA", "cP", "cG", "dx", "du", "dv", "dw", "dfill", "dout"]
 for _t in range(3):
-    SEMAPHORES += ["wa%d" % _t, "ca%d" % _t, "lw%d" % _t, "lc%d" % _t, "dl%d" % _t, "di%d" % _t]
+    SEMAPHORES += ["wa%d" % _t, "ca%d" % _t, "lw%d" % _t, "lc%d" % _t, "dl%d" % _t]
+
+RAISE = 2.0 ** -6
+UNIT = 2.0 ** -17
+TOP = 0x15555
 
 
 def rank_program(g, core, T, topo):
@@ -46,7 +45,6 @@ def rank_program(g, core, T, topo):
         return
     mate = T.cores[rank + 1 if rank % 2 == 0 else rank - 1]
     A, AF = AluOpType, ActivationFunctionType
-    X = AxisListType.X
     Q = {"V": g.vector, "A": g.scalar, "P": g.tensor, "G": g, "Y": g.sync}
     own = {"V": "cV", "A": "cA", "P": "cP", "G": "cG", "Y": None}
     tot, lastw, readers, epoch, known = {}, {}, {}, {}, {e: {} for e in Q}
@@ -68,7 +66,7 @@ def rank_program(g, core, T, topo):
             n = tot[s] if v is None else v
             toks[s] = max(toks.get(s, 0), n)
         for k in r:
-            for tk in lastw.get(k, []):
+            for tk in lastw[k]:
                 put(tk)
             if k[0] == "B" and k[1:].isdigit():
                 for tk in readers.get(k, []):
@@ -80,22 +78,22 @@ def rank_program(g, core, T, topo):
                 put(tk, True)
         for k in add:
             if readers.get(k):
-                epoch[k] = lastw.get(k, []) + readers[k]
+                epoch[k] = [(tk, False) for tk in lastw.get(k, [])] + [(tk, True) for tk in readers[k]]
                 lastw[k], readers[k] = [], []
-            for tk in epoch.get(k, []):
-                put(tk)
+            for tk, war in epoch.get(k, []):
+                put(tk, war or e == "P")
         need(e, list(toks.items()))
 
     def note(tk, r, w, add):
         for k in r:
             readers.setdefault(k, []).append(tk)
         for k in w:
-            lastw[k], readers[k], epoch[k] = [tk], [], [tk]
+            lastw[k], readers[k], epoch[k] = [tk], [], [(tk, False)]
         for k in add:
             lastw.setdefault(k, []).append(tk)
 
-    def op(e, f, r, w=(), add=()):
-        r, w, add = r.split(), (w.split() if w else []), (add.split() if add else [])
+    def op(e, f, r, w="", add=""):
+        r, w, add = r.split(), w.split(), add.split()
         deps(e, r, w, add, True)
         s = own[e]
         f().then_inc(T.sem[s], 1)
@@ -144,17 +142,25 @@ def rank_program(g, core, T, topo):
     def scan(out, d0, d1, ini, o0, o1, r, w="", add=""):
         op("V", lambda: v.tensor_tensor_scan(out, d0, d1, ini, o0, o1), r, w, add)
 
+    def turn(out, a, r, w):
+        op("V", lambda: v.transpose(out, a), r, w)
+
     def fill(ap, c, w="", add=""):
         op("V", lambda: v.memset(ap, c), "", w, add)
 
     def quant(c, s, t, r, w):
         op("V", lambda: v.quantize_mx(c, s, t), r, w)
 
-    def act(out, in_, r, w="", add="", scale=1.0):
-        if scale == 1.0:
+    def act(out, in_, r, w="", add="", scale=1.0, bias=None):
+        if bias is not None:
+            op("A", lambda: ac.activation(out, in_, AF.Identity, bias=bias, scale=scale), r, w, add)
+        elif scale == 1.0:
             op("A", lambda: ac.activation(out, in_, AF.Copy), r, w, add)
         else:
             op("A", lambda: ac.activation(out, in_, AF.Copy, scale=scale), r, w, add)
+
+    def row(out, n, a, b, w="", add=""):
+        act(out, T.ICOL[:, 0:n], "ICOL", w, add, scale=float(a), bias=float(b))
 
     def mm(out, l, ls, rr, rs, a, z, r, w="", add=""):
         op("P", lambda: pe.matmul_mx(out, l, ls, rr, rs, a, z), r, w, add)
@@ -165,173 +171,166 @@ def rank_program(g, core, T, topo):
         else:
             op("G", lambda: g.iota(out, pat, base, ch), "", w)
 
-    dma("Y", T.X0[:], T.x[:], "dx", "", "X0")
-    dma("A", T.UT[:], T.u[:], "du", "", "UT")
-    dma("Y", T.WQ[:].bitcast(dt.uint8), T.wc[:], "dw", "", "WQ")
-    dma("Y", T.WS[:], T.ws[:], "dw", "", "WS")
-    dma("A", T.VT[:], T.v[:], "dv", "", "VT")
-
-    iota(T.IP[:, 0:1], [[0, 1]], 0, 1, "ip0", False)
-    iota(T.UI[:], [[3, 3], [0, 8]], 0, 1, "UI", False)
-    iota(T.ICOL[:], [[1, 512]], 0, 0, "ICOL")
-    iota(T.SC[:, 0:1], [[0, 1]], 0, 1, "s0")
-    iota(T.SC[:, 4:5], [[0, 1]], 128, 1, "s4")
-    iota(T.SC[:, 5:7], [[-128, 2]], 255, -1, "s5 s6")
-    iota(T.I8[:], [[1, 16], [0, 8]], 0, 0, "I8")
-    iota(T.I16[:], [[0, 8], [1, 16]], 0, 0, "I16")
-    iota(T.JP[:, 0:128], [[4, 4], [1, 2], [16, 16]], 0, 0, "JP0")
-    iota(T.JP[:, 128:256], [[4, 4], [1, 2], [16, 16]], 2, 0, "JP1")
-    iota(T.VB[:], [[1, 256]], 0, 0, "VB")
-    iota(T.PLF[:], [[-2, 2], [-4, 4], [-1, 2]], 255, 0, "PLF")
-    iota(T.JL[:, 16:32], [[16, 16]], 0, 0, "JLF")
-    iota(T.NEG[:], [[0, 256]], -1, 0, "NEG")
-
-    DEAD = 262144.0
-
-    def flat(nm, width, c):
-        for a in range(0, width, 512):
-            b = min(width, a + 512)
-            o, i = T[nm][:, a:b], T.ICOL[:, 0:b - a]
-            if c == 0.0:
-                op("A", lambda: ac.activation(o, i, AF.Copy, scale=0.0), "ICOL", "", nm)
-            else:
-                op("A", lambda: ac.activation(o, i, AF.Identity, bias=c, scale=0.0), "ICOL", "", nm)
-        epoch[nm] = list(lastw[nm])
-
-    for k in range(8):
-        fill(T.TK[:, k::8], 0.05 * 0.25 ** k, "", "TK")
-    for nm, c, n in (("H50", 0.5, 8), ("H25", 0.25, 8), ("H8", 1.0, 8), ("H10", 1.0, 16)):
-        fill(T[nm][:], c, nm)
-    for st, n in ((1, 2), (2, 4), (4, 8), (8, 16)):
-        fill(T.ILF[:, st:32:n], {1: 1.0, 2: 2.0, 4: 3.0, 8: 4.0}[st], "", "ILF")
-    fill(T.ILF[:, 0:1], 13.0, "", "ILF")
-    fill(T.ILF[:, 16:17], 6.0, "", "ILF")
-    fill(T.YT[:], 0, "YT")
-    for nm in ("AL", "DL", "AF", "BT", "OT"):
-        fill(T[nm][:], 0.0, nm)
-    fill(T.ET[:, 384:512], 0.0, "ET4")
-    for nm, n in (("H50", 8), ("H25", 8), ("H8", 8), ("H10", 16)):
-        fill(T[nm][:, 0::n], 0.0, nm)
-    flat("CMT", 1024, 0.0)
-    flat("COT", 1024, 0.0)
-    IP, SC = T.IP, T.SC
-    for c, m in ((1, 15), (4, 1), (5, 3), (6, 7)):
-        ts(IP[:, c:c + 1], IP[:, 0:1], m, None, A.bitwise_and, None, "ip0", "ip%d" % c)
-    for c, m in ((2, 4),):
-        ts(IP[:, c:c + 1], IP[:, 0:1], m, None, A.arith_shift_right, None, "ip0", "ip%d" % c)
-
-    def sc(c):
-        return SC[:, c:c + 1]
-    for c, i, m, a in ((1, 1, 1.0, 0.0), (2, 2, 1.0, 0.0), (3, 2, 1.0, 8.0), (10, 1, 16.0, 0.0)):
-        ts(sc(c), IP[:, i:i + 1], m, a, A.mult, A.add, "ip%d" % i, "s%d" % c)
-    ts(T.UI[:], T.UI[:], 7, None, A.bitwise_and, None, "UI", "UI")
-    ts(T.UL[:], T.UI[:], 16, None, A.mult, None, "UI", "UL")
-    quant(T.UQ[:], T.US[:], T.UT[:], "UT", "UQ US")
-    cp(T.URQ[:].bitcast(dt.uint32), T.UQ[:].bitcast(dt.uint32).indirect(T.UL[:]), "UQ UL", "URQ")
-    op("A", lambda: ac.activation(T.URS[:], T.US[:].indirect(T.UL[:]), AF.Copy), "US UL", "URS")
-    so = [0]
-    for k in range(8):
-        so.append(so[-1] + 1 + (256 >> k))
-
-    def ones(nm, o, n, c):
-        op("A", lambda: ac.activation(T[nm][:, o:o + n], T.ICOL[:, 0:n], AF.Identity, bias=c, scale=0.0), "ICOL", "", nm)
-    flat("EQT", 518, 0.0)
-    for k in range(8):
-        ones("EQT", so[k], 1, DEAD)
-    ones("EQT", so[7] + 2, 1, DEAD)
-    epoch["EQT"] = list(lastw["EQT"])
-    for o, n, c in ((129, 127, 0.0), (256, 512, 0.0), (768, 6, 0.0), (775, 127, 0.0), (1030, 512, 0.0), (1542, 6, 0.0), (128, 1, -256.0), (774, 1, -256.0)):
-        ones("TB", o, n, c)
-    epoch["TB"] = list(lastw["TB"])
-    for k in range(8):
-        ones("TB", 1030 + so[k] + (1 if k == 7 else 0), 1, DEAD)
-    epoch["tb1"] = epoch["tb0"] = list(lastw["TB"])
-    flat("HMT", 1024, 0.0)
-    ts(T.TH[:], T.I8[:], sc(1), 1e29, A.not_equal, A.mult, "I8 s1", "TH")
-    for h in range(2):
-        for b in range(2):
-            ts(T.CMT[:, 512 * h + b:512 * h + 512:4], T.I16[:], sc(2 + b), float(1 + h), A.is_equal, A.mult, "I16 s%d" % (2 + b), "", "CMT")
-    for s in range(2):
-        for b in range(2):
-            ts(T.COT[:, 512 * s + 2 + b:512 * s + 512:4], T.JP[:, 128 * s:128 * s + 128], sc(0 if b == 0 else 4), None, A.is_equal, None,
-               "JP%d s0 s4" % s, "", "COT")
-    quant(T.CMQ[:], T.CMS[:], T.CMT[:], "CMT", "CMQ CMS")
-    quant(T.COQ[:], T.COS[:], T.COT[:], "COT", "COQ COS")
-    fill(T.H50[:], 0.5, "H50")
-    fill(T.H50[:, 0::8], 0.0, "H50")
-
-    def setup_b(n):
-        if n < 2:
-            ts(T.HMT[:, n::4], T.VB[:], sc(5 + n), 256.0, A.is_equal, A.mult, "VB s%d" % (5 + n), "", "HMT")
-        elif n < 6:
-            ts(T.MTT[:, n - 2::4], T.VB[:], sc(0 if n < 4 else 4), None, A.is_equal, None, "VB s0 s4", "", "MTT")
-        elif n == 6:
-            ts(T.PL[:], T.PLF[:], sc(10), None, A.subtract, None, "PLF s10", "PL")
-        else:
-            quant(T.HMQ[:], T.HMS[:], T.HMT[:], "HMT", "HMQ HMS")
-            quant(T.MTQ[:], T.MTS[:], T.MTT[:], "MTT", "MTQ MTS")
-
-    def setup_c():
-        for k in range(7):
-            ts(T.NI[:, k:k + 1], IP[:, 0:1], k, None, A.arith_shift_right, None, "ip0", "", "NI")
-        a = T.TB[:, 0:128]
-        ts(a, T.VB[:, 0:128], sc(0), DEAD, A.is_equal, A.mult, "VB s0", "ta0")
-        ts(T.NI[:, 16:23], T.NI[:, 0:7], 1, None, A.bitwise_and, None, "NI", "NB")
-        setup_b(6)
-        ts(T.NI[:, 32:39], T.NI[:, 16:23], -2, 1, A.mult, A.add, "NB", "NC")
-        setup_b(5)
-        tt(T.NS[:, 0:7], T.NI[:, 0:7], T.NI[:, 32:39], A.add, "NI NC", "NS")
-        setup_b(2)
-        for k in range(7):
-            o, n = so[k] + 1, 128 >> k
-            ts(T.EQT[:, o:o + n], T.VB[:, 0:n], T.NS[:, k:k + 1], DEAD, A.is_equal, A.mult, "VB NS", "", "EQT")
-        for k in range(8):
-            o, n = so[k], (128 >> k) + 1
-            tt(T.TB[:, 256 + o:256 + o + n], T.EQT[:, o:o + n], T.EQT[:, o + 1:o + n + 1], A.subtract, "EQT TB", "", "tb0")
-        for k in range(7):
-            o, n = 256 + so[k], 128 >> k
-            i1, o1, i2, o2 = T.TB[:, o + 1:o + n], T.TB[:, 774 + o + n + 1:774 + o + 2 * n], T.TB[:, o:o + 1], T.TB[:, 774 + o + n:774 + o + n + 1]
-            if n > 1:
-                act(o1, i1, "tb0 TB", "", "tb1")
-            op("A", lambda: ac.activation(o2, i2, AF.Identity, bias=-DEAD, scale=1.0), "tb0 TB", "", "tb1")
-        for k in range(7):
-            o, n = so[k] + 1, 128 >> k
-            b = T.TB[:, 0:128:1 << k]
-            tt(b, b, T.EQT[:, o:o + n], A.add, "EQT ta0", "ta0")
-            if k != 2 and k < 5:
-                setup_b(k)
-        ts(a, a, -256.0 / DEAD, None, A.mult, None, "ta0", "ta0")
-        act(T.TB[:, 902:1030], a, "ta0", "ta1")
-        for h in range(2):
-            dma("Y", T.tab[128 * h:128 * h + 128, :], T.TB[:, 774 * h:774 * h + 774], "dtab", "ta%d tb%d TB" % (h, h), "", "tab")
-
-    def setup_e():
-        for b in range(4):
-            ts(T.ELT[:, 512 * b + b:512 * b + 512:4], T.VB[:, 0:128], sc(0), 32.0, A.is_equal, A.mult, "VB s0", "", "ELT")
-        quant(T.ELQ[:], T.ELS[:], T.ELT[:], "ELT", "ELQ ELS")
-
-    def setup_f():
-        ts(T.JL[:, 0:16], T.JL[:, 16:32], sc(1), None, A.add, None, "JLF s1", "JL")
-        ts(T.MK[:, 96:192], T.I16[:, 0:96], sc(1), 8000.0, A.not_equal, A.mult, "I16 s1", "mk0")
-        tt(T.MK[:, 1:96], T.MK[:, 97:192], T.MK[:, 96:191], A.subtract, "mk0", "MK")
-        ts(T.MK[:, 16:96:16], T.MK[:, 16:96:16], 3000.0, None, A.subtract, None, "MK", "MK")
-        cp(T.MK[:, 0:1], T.MK[:, 96:97], "mk0 MK", "MK")
-        quant(T.VQ[:], T.VS[:], T.VT[:], "VT", "VQ VS")
-
-    def setup_d():
-        for i in range(3):
-            ts(sc(12 + i), IP[:, 4 + i:5 + i], 0.0, None, A.is_equal, None, "ip%d" % (4 + i), "r%d" % (1 + i))
-        tt(sc(8), sc(12), sc(13), A.add, "r1 r2", "s8")
-        tt(sc(8), sc(8), sc(14), A.add, "s8 r3", "s8")
-        ts(sc(9), IP[:, 1:2], 0.0, None, A.is_equal, None, "ip1", "s9")
-        ts(T.ILF[:, 32:64], T.ILF[:, 0:32], sc(9), sc(8), A.mult, A.add, "ILF s9 s8", "ILG")
-        cp(T.IL[:, 0:16], T.ILF[:, 32:48], "ILG", "IL0")
-        ts(T.IL[:, 16:32], T.ILF[:, 48:64], 8.0, None, A.add, None, "ILG", "IL1")
+    def where0(out, in_, pat, base, r, add):
+        op("G", lambda: g.affine_select(out, in_, pat, A.is_equal, 0.0, base, 1), r, "", add)
 
     def B(b):
         return T["B%d" % b]
 
-    DB = (2, 5, 6, 7)
+    IP, SC, LS = T.IP, T.SC, T.LS
+
+    def sc(c):
+        return SC[:, c:c + 1]
+    KL, BL, BI, AI2, EI, PI = LS[:, 0:4], LS[:, 4:6], LS[:, 6:10], LS[:, 10:14], LS[:, 14:22], LS[:, 22:30]
+    H1, H2, HN, HC = T.HS[:, 0:32], T.HS[:, 32:48], T.HS[:, 48:64], T.HS[:, 64:96]
+
+    dma("A", T.UT[:], T.u[:], "du", "", "UT")
+    dma("Y", T.X0[:], T.x[:], "dx", "", "X0")
+    dma("Y", T.WQ[:].bitcast(dt.uint8), T.wc[:], "dw", "", "WQ")
+    dma("Y", T.WS[:], T.ws[:], "dw", "", "WS")
+    dma("Y", T.VT[:], T.v[:], "dv", "", "VT")
+
+    iota(IP[:, 0:1], [[0, 1]], 0, 1, "ip0", False)
+    iota(T.UI[:], [[3, 3], [0, 8]], 7 + 128, -1, "UI", False)
+    iota(T.I16[:], [[0, 16], [1, 16]], 0, 0, "I16")
+    iota(SC[:, 4:8], [[-2, 2], [128, 2]], 0, 1, "s4")
+    iota(T.JP[:], [[4, 4], [1, 2], [16, 16]], 0, 0, "JP")
+    iota(T.I8[:], [[1, 16], [0, 8]], 0, 0, "I8")
+    iota(T.ICOL[:], [[1, 256]], 0, 0, "ICOL")
+    fill(T.CT[:], 0.0, "CT")
+    fill(T.BT[:], 0.0, "BT")
+    fill(T.H4[:], 4.0, "H4")
+    ts(IP[:, 1:2], IP[:, 0:1], 15, None, A.bitwise_and, None, "ip0", "ip1")
+    ts(IP[:, 2:3], IP[:, 0:1], 4, None, A.arith_shift_right, None, "ip0", "ip2")
+    ts(T.UI[:], T.UI[:], 7, None, A.bitwise_and, None, "UI", "UI")
+    fill(T.H4[:, 0::8], 0.0, "H4")
+    for c, i, a in ((1, 1, 0.0), (2, 2, 0.0), (3, 2, 8.0)):
+        ts(sc(c), IP[:, i:i + 1], a, None, A.add, None, "ip%d" % i, "s%d" % c)
+    ts(T.UL[:], T.UI[:], 16, None, A.mult, None, "UI", "UL")
+    fill(T.OT[:], 0.0, "OT")
+    for s in range(2):
+        ts(T.CT[:, s:512:4], T.I16[:, 0:128], sc(2 + s), None, A.is_equal, None, "I16 s%d" % (2 + s), "", "CT")
+    for s in range(2):
+        for h in range(2):
+            ts(T.CT[:, 512 * s + 2 + h:512 * s + 512:4], T.JP[:], sc(4 + 2 * s + h), None, A.is_equal, None, "JP s4", "", "CT")
+    quant(T.UQ[:], T.US[:], T.UT[:], "UT", "UQ US")
+    ts(T.TH[:], T.I8[:], sc(1), 1e29, A.not_equal, A.mult, "I8 s1", "TH")
+    cp(T.URQ[:, 0:128].bitcast(dt.uint32), T.UQ[:].bitcast(dt.uint32).indirect(T.UL[:, 0:8]), "UQ UL", "URQ0")
+    act(T.URS[:, 0:128], T.US[:].indirect(T.UL[:, 0:8]), "US UL", "URS0")
+    act(T.HMT[:], T.CT[:], "CT", "HMT", scale=0.0)
+    iota(T.VB[:], [[1, 256]], 0, 0, "VB")
+
+    def rows():
+        row(T.HS[:, 32:64], 32, 0, 2, "HS2")
+        row(T.HS[:, 32:48:8], 2, 0, 0, "HS2")
+        row(T.HS[:, 48:64:4], 4, 0, 0, "HS2")
+        row(T.NEG[:], 256, 0, -1, "NEG")
+        for o, n in ((1, 2), (2, 4), (4, 8)):
+            act(T.CB[:, o::n], T.I16[:, o:64:n], "I16", "", "CB", scale=1.0 / n, bias=-o / n)
+        act(T.CB[:, 0::8], T.I16[:, 0:64:8], "I16", "", "CB", scale=-0.125, bias=1.0)
+        for o, n in ((0, 16), (16, 8), (24, 4), (28, 2)):
+            row(T.CE[:, o:o + n:2], n // 2, 2, 1, "", "CE0")
+            row(T.CE[:, o + 1:o + n:2], n // 2, 2, 0, "", "CE0")
+        row(T.CE[:, 30:32], 2, 0, -1, "", "CE0")
+        for o, n, z in ((17, 2, 0), (18, 4, 1), (20, 8, 2), (24, 16, 3), (16, 16, 4)):
+            row(T.FR[:, o:32:n], 16 // n, 0, z, "", "FR")
+        for o, n, z in ((0, 8, 1), (8, 4, 2), (12, 2, 3), (14, 2, 3)):
+            row(T.FR[:, 48 + o:48 + o + n], n, 1 << z, (1 << z) - 1, "", "FR")
+            if o < 14:
+                row(T.FR[:, 32 + o:32 + o + max(n, 4)], max(n, 4), 0, z, "", "FR")
+        for k in range(8):
+            row(T.FR[:, 112 + k::8], 3, 0, 64 * (k // 4) + 31 - (16 >> k % 4), "", "EB")
+        act(T.CE[:, 32:64], T.CE[:, 0:32], "CE0", "CE1")
+        for i in range(3):
+            o = -3 * i % 8
+            act(T.FR[:, 64 + 16 * i:80 + 16 * i], T.FR[:, 112 + o:128 + o], "EB", "", "FR")
+        act(T.CE[:, 64:128], T.CE[:, 0:64], "CE0 CE1", "CE")
+
+    def rows_b():
+        row(T.HS[:, 0:32], 32, 0, 1, "H1")
+        row(T.HS[:, 64:96], 32, 0, 1, "HC")
+        row(T.RST[:], 128, 0, 1, "RST")
+        for k in range(8):
+            row(T.TK[:, 2 * k:2 * k + 2], 2, 0, TOP - 2 * 4 ** k, "", "TK")
+        row(T.HS[:, 0:32:16], 2, 0, 0, "H1")
+        row(T.HS[:, 64:96:16], 2, 0, 0, "HC")
+        row(T.HS[:, 76:96:16], 2, 0, 0, "", "HC")
+        for o in (0, 16, 24, 28, 30):
+            row(T.RST[:, o::32], 4, 0, 0, "", "RST")
+        row(T.AL[:, 34:40], 6, 0, 0, "al0")
+        row(T.WN[:, 32:40], 8, 0, 0, "wn0")
+
+    def number_rows():
+        iota(T.PLF[:], [[-2, 2], [-4, 4], [-1, 2]], 255, 0, "PLF")
+        iota(T.FR[:, 0:16], [[8, 2], [0, 2], [2, 4]], 0, 0, "FR0")
+        for c, pat, base in ((0, [[0, 2], [1, 2]], 0), (4, [[0, 2], [16, 2]], 14), (8, [[-4, 2], [8, 2]], 20), (12, [[12, 2], [16, 2]], 0),
+                             (16, [[-10, 2], [-15, 2]], 28), (20, [[16, 4]], 0)):
+            iota(T.RW[:, c:c + 4], pat, base, 0, "rw%d" % c)
+        iota(IP[:, 8:11], [[-3, 3]], 24, 1, "ip8", False)
+        iota(T.JL[:, 16:32], [[16, 16]], 0, 0, "JLF")
+
+    def falling_order():
+        ts(IP[:, 3:4], IP[:, 0:1], 5, None, A.arith_shift_right, None, "ip0", "ip3")
+        ts(IP[:, 4:5], IP[:, 2:3], 1, None, A.bitwise_and, None, "ip2", "ip4")
+        ts(sc(8), IP[:, 1:2], -16.0, 255.0, A.mult, A.add, "ip1", "s8")
+        ts(sc(16), IP[:, 1:2], 16.0, None, A.mult, None, "ip1", "s16")
+        ts(sc(9), IP[:, 3:4], -4.0, sc(8), A.mult, A.add, "ip3 s8", "s9")
+        fill(T.KC[:, 0:256], UNIT, "KC0")
+        ts(sc(10), IP[:, 4:5], -1.0, sc(9), A.mult, A.add, "ip4 s9", "s10")
+        fill(T.KC[:, 256:768], 32.0, "KC1")
+        ts(sc(11), sc(10), -2.0, None, A.add, None, "s10", "s11")
+        for s in range(2):
+            ts(T.HMT[:, s::4], T.VB[:], sc(10 + s), 256.0, A.is_equal, A.mult, "VB s%d" % (10 + s), "", "HMT")
+        quant(T.HMQ[:], T.HMS[:], T.HMT[:], "HMT", "HMQ HMS")
+
+    def word_order():
+        for h in range(2):
+            where0(T.MTT[:, 2 * h:1024:4], T.KC[:, 0:256], [[-1, 256]], 128 * h, "KC0", "mt%d" % h)
+            where0(T.MTT[:, 1024 + 2 * h::4], T.KC[:, 0:256], [[-1, 16], [-16, 16]], 128 * h, "KC0", "mt%d" % h)
+        for b in range(4):
+            where0(T.ELT[:, 512 * b:512 * b + 512], T.KC[:, 256:768], [[-1, 128], [128, 4]], -128 * b, "KC1", "ELT")
+
+    def lists():
+        ts(T.MK[:, 112:224], T.I16[:, 0:112], sc(1), 8000.0, A.not_equal, A.mult, "I16 s1", "mk0")
+        ts(T.PL[:], T.PLF[:], sc(16), None, A.subtract, None, "PLF s16", "PL")
+        tt(T.MK[:, 1:112], T.MK[:, 113:224], T.MK[:, 112:223], A.subtract, "mk0", "MK")
+        cp(T.MK[:, 0:1], T.MK[:, 112:113], "mk0", "mk1")
+        ts(T.MK[:, 16:112:16], T.MK[:, 16:112:16], 3000.0, None, A.subtract, None, "MK", "MK")
+        ts(IP[:, 12:15], IP[:, 8:11], 7, None, A.bitwise_and, None, "ip8", "ip12")
+        scan(T.FS[:, 0:112], T.MK[:, 0:112], T.FR[:, 0:112], 0.0, A.add, A.max, "MK mk1 FR FR0", "fs0")
+        for s in range(2):
+            ts(LS[:, 30 + s:36:2], IP[:, 12:15], 2.0, float(s), A.mult, A.add, "ip12", "", "LS")
+        ts(T.FS[:, 112:119], T.FS[:, 15:112:16], T.MK[:, 127:128], None, A.subtract, None, "fs0 mk0", "FS")
+        ts(sc(12), IP[:, 1:2], 0.0, None, A.is_equal, None, "ip1", "s12")
+        k2, tz, z1, p1 = [T.FS[:, 112 + i:113 + i] for i in range(4)]
+        ts(sc(13), tz, 2.0, None, A.is_le, None, "FS", "s13")
+        ts(T.RW[:, 24:28], T.RW[:, 16:20], sc(12), tz, A.mult, A.add, "rw16 s12 FS", "rw24")
+        ts(T.RW[:, 28:32], T.RW[:, 8:12], tz, 30.0, A.subtract, A.subtract, "rw8 FS", "rw28")
+        ts(LS[:, 14:22:2], T.RW[:, 8:12], 3.0, None, A.add, None, "rw8", "", "LS")
+        ts(LS[:, 15:22:2], T.RW[:, 8:12], z1, 3.0, A.subtract, A.add, "rw8 FS", "", "LS")
+        ts(BI, T.RW[:, 28:32], sc(13), 32.0, A.mult, A.add, "rw28 s13", "", "LS")
+        ts(BL, T.RW[:, 4:6], k2, 0.5, A.subtract, A.mult, "rw4 FS", "", "LS")
+        tt(T.RW[:, 24:28], T.RW[:, 24:28], T.RW[:, 12:16], A.add, "rw24 rw12", "rw24")
+        ts(KL, T.RW[:, 0:4], k2, None, A.add, None, "rw0 FS", "", "LS")
+        ts(LS[:, 22:30:2], T.RW[:, 20:24], sc(1), None, A.add, None, "rw20 s1", "", "LS")
+        ts(LS[:, 23:30:2], T.RW[:, 20:24], p1, None, A.add, None, "rw20 FS", "", "LS")
+        cp(AI2, T.RW[:, 24:28], "rw24", "", "LS")
+        for s in range(2):
+            ts(LS[:, 36 + s:42:2], T.FS[:, 116:119], 32.0 * s, None, A.add, None, "FS", "", "LS")
+            ts(LS[:, 48 + 16 * s:64 + 16 * s], T.PLF[:], 0.0, T.RW[:, 24 + s:25 + s], A.mult, A.add, "PLF rw24", "", "LS")
+
+    def late():
+        ts(T.JL[:, 0:16], T.JL[:, 16:32], sc(1), None, A.add, None, "JLF s1", "JL")
+        ts(T.JL[:, 32:48], T.JL[:, 16:32], sc(1), 131072.0, A.add, A.add, "JLF s1", "JB")
+        fill(T.DL[:, 0:64], 0.0, "dl pm")
+        ts(sc(14), sc(12), -1.0, None, A.mult, None, "s12", "s14")
+        fill(T.ET[:, 384:512], 0.0, "ET4")
+        cp(T.DL[:, 0:1], sc(14), "s14 pm", "pm")
+        fill(T.AF[:], 0.0, "AF")
+
+    quant(T.CQ[:], T.CS[:], T.CT[:], "CT", "CQ CS")
+    rows()
+    DB = (4, 5, 6, 7)
     for t in range(3):
         last = t == 2
         src, key = (T.X0, "X0") if t == 0 else (T.XT, "XT")
@@ -341,193 +340,202 @@ def rank_program(g, core, T, topo):
             for i in range(3):
                 dma("Y", T["AC%d" % i][:, 96:128].bitcast(dt.uint8), T.XQ[:, 0:32].bitcast(dt.uint8), "dfill", "XQ0", "", "AC%d" % i)
                 dma("Y", T["AS%d" % i][:, 96:128], T.XS[:, 0:32], "dfill", "XQ0", "", "AS%d" % i)
+        ur = "URQ%d URS%d" % (min(t, 1), min(t, 1))
         for s in range(2):
             mm(B(s)[:, 0:128], T.XQ[:, 128 * s:128 * s + 128], T.XS[:, 128 * s:128 * s + 128], T.URQ[:, 128 * t:128 * t + 128], T.URS[:, 128 * t:128 * t + 128],
-               True, True, "XQ%d URQ URS" % s, "B%d" % s)
+               True, True, "XQ%d %s" % (s, ur), "B%d" % s)
+        if t == 0:
+            falling_order()
         for s in range(2):
-            tt(T.BT[:, s:512:4], B(s)[:, 0:128], T.TH[:], A.is_gt, "B%d TH" % s, "", "BT")
-            ts(T.BT[:, 2 + s:512:4], B(s)[:, 0:128], 0.0, None, A.is_gt, None, "B%d" % s, "", "BT")
-        for s in range(2):
-            ts(T.W8[:, 8 * s:8 * s + 8], B(s)[:, 0:8], 0.0, 128.0, A.is_gt, A.mult, "B%d" % s, "", "W8")
+            tt(T.BT[:, 32 + s:544:4], B(s)[:, 0:128], T.TH[:], A.is_gt, "B%d TH" % s, "", "BT")
+            ts(T.BT[:, 546 + s:576:4], B(s)[:, 0:8], 0.0, None, A.is_gt, None, "B%d" % s, "", "BT")
         quant(T.BQ[:], T.BS[:], T.BT[:], "BT", "BQ BS")
-        mm(B(2)[:, 0:128], T.CMQ[:, 0:128], T.CMS[:, 0:128], T.BQ[:, 0:128], T.BS[:, 0:128], True, False, "CMQ CMS BQ BS", "B2")
-        mm(B(2)[:, 0:128], T.CMQ[:, 128:256], T.CMS[:, 128:256], T.BQ[:, 64:192], T.BS[:, 64:192], False, True, "CMQ CMS BQ BS", "", "B2")
-        for s in range(2):
-            mm(B(3 + s)[:, 0:128], T.COQ[:, 128 * s:128 * s + 128], T.COS[:, 128 * s:128 * s + 128], T.BQ[:, 0:128], T.BS[:, 0:128], True, True,
-               "COQ COS BQ BS", "B%d" % (3 + s))
-        act(T["MS%d" % t][:], B(2)[:, 0:64], "B2", "MS%d" % t)
+        mm(B(2)[:, 0:144], T.CQ[:, 0:128], T.CS[:, 0:128], T.BQ[:, 8:152], T.BS[:, 8:152], True, False, "CQ CS BQ BS", "B2")
+        mm(B(2)[:, 0:144], T.CQ[:, 128:256], T.CS[:, 128:256], T.BQ[:, 0:144], T.BS[:, 0:144], False, True, "CQ CS BQ BS", "", "B2")
+        scan(T.W4[:], T.H4[:], B(2)[:, 0:144], 0.0, A.mult, A.add, "H4 B2", "W4")
+        scan(T.W2[:], H2, B(2)[:, 128:144], 0.0, A.mult, A.add, "HS2 B2", "W2")
+        cp(T["MS%d" % t][:], T.W4[:, 7:128:8], "W4", "MS%d" % t)
         remote(T["WL%d" % t][:], T["MS%d" % t][:], "wa%d" % t, "lw%d" % t, "MS%d" % t, "WL%d" % t)
-        def places():
-            for s in range(2):
-                ts(T.PB[:, 8 * s:8 * s + 8], B(3 + s)[:, 0:8], 128.0, None, A.mult, None, "B%d" % (3 + s), "", "PB")
-            scan(T.PB[:, 16:32], T.H50[:], T.PB[:, 0:16], 0.0, A.mult, A.add, "H50 PB", "PW")
-            cp(T.IX[:], T.PB[:, 23::8], "PW", "IX")
-            for i, (a, b) in enumerate(((-128.0, 8192.0), (-256.0, 16384.0), (64.0, 0.0))):
-                op("A", lambda: ac.activation(T.SG[:, 16 * i:16 * i + 16], T.PB[:, 0:16], AF.Identity, bias=b, scale=a), "PB", "", "SG")
-        if t == 0:
-            setup_c()
-        scan(T.W8[:, 16:32], T.H50[:], T.W8[:, 0:16], 0.0, A.mult, A.add, "H50 W8", "WW")
-        if t == 0:
-            setup_b(7)
+        scan(T.WN[:, 16:32], HN, B(2)[:, 128:144], 0.0, A.mult, A.add, "HS2 B2", "P4")
         for s in range(2):
-            ts(T.OT[:, s::4], T.VB[:], T.W8[:, 8 * s + 23:8 * s + 24], None, A.is_equal, None, "VB WW", "", "OT")
+            ts(T.OT[:, s::4], T.VB[:], T.W2[:, 8 * s + 7:8 * s + 8], None, A.is_equal, None, "VB W2", "", "OT")
+        act(T.WN[:, 0:16], B(2)[:, 128:144], "B2", "bits")
         quant(T.OQ[:], T.OS[:], T.OT[:], "OT", "OQ OS")
         for h in range(2):
-            mm(B(5 + h)[:, 0:256], T.OQ[:, 128 * h:128 * h + 128], T.OS[:, 128 * h:128 * h + 128], T.HMQ[:], T.HMS[:], True, True, "OQ OS HMQ HMS", "B%d" % (5 + h))
-        places()
-        if t == 0:
-            setup_d()
-        for h in range(2):
-            scan(T.DS[:, 512 * h:512 * h + 256], T.NEG[:], B(5 + h)[:, 0:256], 0.0, A.add, A.max, "NEG B%d" % (5 + h), "DR%d" % h)
-        for h in range(2):
-            scan(T.DS[:, 512 * h + 256:512 * h + 512], T.NEG[:], B(5 + h)[:, 0:256], T.DS[:, 512 * h + 255:512 * h + 256], A.add, A.max,
-                 "NEG DR%d B%d" % (h, 5 + h), "DS%d" % h)
-        D0, D1 = [T.DS[:, 512 * h + 256:512 * h + 512].indirect(T.PL[:]) for h in range(2)]
-        op("A", lambda: ac.activation(T.HT[:], D0, AF.Identity, bias=201326592.0), "DS0 PL", "HT")
-        op("A", lambda: ac.activation(T.DT[:, 0::4], T.HT[:], AF.Identity, bias=-201326592.0), "HT", "dt0")
-        ts(T.DT[:, 2::4], D1, 201326592.0, 201326592.0, A.add, A.subtract, "DS1 PL", "dt2")
-        tt(T.DT[:, 3::4], D1, T.DT[:, 2::4], A.subtract, "DS1 PL dt2", "dt3")
-        tt(T.DT[:, 1::4], D0, T.DT[:, 0::4], A.subtract, "DS0 PL dt0", "dt1")
-        WL = T["WL%d" % t]
-        HI, HI2, LO, GS = T.HI[:, 0:64], T.HI[:, 64:128], T.HI[:, 128:192], T.GS[:, 0:32]
-        ts(HI2, WL[:], 2.0, 2.0, A.is_ge, A.mult, "WL%d" % t, "HI2")
-        ts(HI, WL[:], 2.0, None, A.is_ge, None, "WL%d" % t, "HI")
-        quant(T.DQ[:], T.DP[:], T.DT[:], "dt0 dt1 dt2 dt3", "DQ DP")
-        for s in range(2):
-            mm(B(s)[:, 0:256], T.DQ[:, 128 * s:128 * s + 128], T.DP[:, 128 * s:128 * s + 128], T.MTQ[:], T.MTS[:], True, True, "DQ DP MTQ MTS", "B%d" % s)
-        deps("G", ["IX", "tab"], ["RS"], [], False)
-        for s in range(2):
-            g.indirect_dma_start(T.RS[:, 774 * s:774 * s + 774], None, T.tab[:], IndirectOffsetOnAxis(ap=T.IX[:, s:s + 1], axis=0),
-                                 bounds_check=255).then_inc(T.sem["di%d" % t], 16)
-        tot["di%d" % t] = 32
-        note(("di%d" % t, None), ["IX", "tab"], ["RS"], [])
-        def halves():
+            mm(B(h)[:, 0:256], T.OQ[:, 128 * h:128 * h + 128], T.OS[:, 128 * h:128 * h + 128], T.HMQ[:], T.HMS[:], True, True, "OQ OS HMQ HMS", "B%d" % h)
+            act(T.HB[:, 256 * h:256 * h + 256], B(h)[:, 0:256], "B%d" % h, "HB%d" % h)
+
+        def unpack():
             for b in range(4):
-                kb = "B%d" % DB[b]
-                mm(B(DB[b])[:, 0:256], T.ELQ[:, 128 * b:128 * b + 128], T.ELS[:, 128 * b:128 * b + 128], T.XQ[:], T.XS[:], True, True, "ELQ ELS XQ0 XQ1", kb)
-                for a in range(2):
-                    act(T.HP[:, 1024 * a + 256 * b:1024 * a + 256 * b + 256], B(DB[b])[:, 0:256], kb, "", "HP", scale=0.015625)
+                mm(B(DB[b])[:, 0:256], T.ELQ[:, 128 * b:128 * b + 128], T.ELS[:, 128 * b:128 * b + 128], T.XQ[:], T.XS[:], True, True,
+                   "ELQ ELS XQ0 XQ1", "B%d" % DB[b])
+
+        def window():
+            for b in range(4):
+                act(T.FW[:, 256 * b:256 * b + 256], B(DB[b])[:, 0:256], "B%d" % DB[b], "FW%d" % b)
         if t == 0:
-            flat("ELT", 2048, 0.0)
+            number_rows()
+            rows_b()
+            word_order()
+            lists()
         else:
-            halves()
-        tt(LO, WL[:], HI2, A.subtract, "WL%d HI2" % t, "LO")
+            unpack()
         for s in range(2):
-            tt(T.E[:, 128 * s + 64:128 * s + 128], B(3 + s)[:, 64:128], HI, A.not_equal, "B%d HI" % (3 + s), "", "E")
-        for s in range(2):
-            tt(T.E[:, 128 * s:128 * s + 64], B(3 + s)[:, 0:64], LO, A.not_equal, "B%d LO" % (3 + s), "", "E")
-        scan(T.XH[:], T.H25[:], T.E[:], 0.0, A.mult, A.add, "H25 E", "XH")
-        GA = T.GS[:, 32:64]
-        ts(GA, T.XH[:, 7::8], -163840.0, 5.0, A.mult, A.add, "XH", "GA")
-        op("V", lambda: v.reciprocal(GS, GA), "GA", "GS")
-        lastw["gs0"] = lastw["gs1"] = lastw["GS"]
-        for k in range(8):
+            ts(T.MH[:, 256 * s:256 * s + 256], T.I16[:], T.WN[:, 19 + 8 * s:20 + 8 * s], 1.0 - RAISE, A.is_gt, A.subtract, "I16 P4", "MH%d" % s)
+        for h in range(2):
+            scan(T.DS[:, 512 * h:512 * h + 256], T.NEG[:], T.HB[:, 256 * h:256 * h + 256], 0.0, A.add, A.max, "NEG HB%d" % h, "DR%d" % h)
+        for h in range(2):
+            scan(T.DS[:, 512 * h + 256:512 * h + 512], T.NEG[:], T.HB[:, 256 * h:256 * h + 256], T.DS[:, 512 * h + 255:512 * h + 256], A.add, A.max,
+                 "NEG DR%d HB%d" % (h, h), "DS%d" % h)
+            act(T.DG[:, 256 * h:256 * h + 256], T.DS[:, 512 * h + 256:512 * h + 512].indirect(T.PL[:]), "DS%d PL" % h, "DG%d" % h)
+            act(T.DH[:, 256 * h:256 * h + 256], T.DG[:, 256 * h:256 * h + 256], "DG%d" % h, "DH%d" % h, bias=2055.5)
+        tt(T.BD[:, 0:64], T.WN[:].indirect(BI), T.CB[:], A.is_equal, "P4 bits wn0 LS CB", "bd0")
+        tt(T.EM[:, 0:128], T.WN[:].indirect(EI), T.CE[:], A.is_equal, "P4 bits wn0 LS CE0 CE1 CE", "em0")
+
+        def signs():
+            act(T.SG[:, 64:96], T.WN[:].indirect(BL), "P4 bits wn0 LS", "sg")
+            act(T.H16[:, 32:34], T.WN[:, 19:32:8], "P4", "HO", scale=RAISE, bias=-15 * RAISE)
+            for a, b, m, c in ((0, 4, -2, 1), (4, 12, 1, 0), (12, 20, -2, 1), (20, 28, 1, 0), (28, 32, -2, 1)):
+                act(T.SG[:, a:b], T.SG[:, 64 + a:64 + b], "sg", "", "SG", scale=m * RAISE, bias=c * RAISE)
+            act(T.SG[:, 32:64], T.SG[:, 64:96], "sg", "", "SG", scale=-4 * RAISE, bias=2 * RAISE)
+            act(T.BD[:, 64:128], T.BD[:, 0:64], "bd0", "BD", scale=-256 * UNIT)
+            act(T.EM[:, 128:256], T.EM[:, 0:128], "em0", "EM", scale=1 / UNIT)
+        signs()
+        if t == 0:
+            for h in range(2):
+                act(T.MTT[:, 2 * h + 1::4], T.MTT[:, 2 * h::4], "mt%d" % h, "mu%d" % h)
+        else:
+            window()
+
+        def high(h):
+            ts(T.DT[:, 2 * h::4], T.DH[:, 256 * h:256 * h + 256], 2048.0, None, A.subtract, None, "DH%d" % h, "dh%d" % h)
+
+        def low(h):
+            scan(T.DT[:, 2 * h + 1::4], T.DG[:, 256 * h:256 * h + 256], T.DT[:, 2 * h::4], 0.0, A.max, A.subtract, "DG%d dh%d" % (h, h), "dw%d" % h)
+
+        def table():
+            quant(T.DQ[:], T.DP[:], T.DT[:], "dh0 dw0 dh1 dw1", "DQ DP")
+            if t == 0:
+                quant(T.MTQ[:], T.MTS[:], T.MTT[:], "mt0 mt1 mu0 mu1", "MTQ MTS")
             for s in range(2):
-                c = 8 * s + k
-                op("V", lambda: v.tensor_reduce(T.RP[:, c:c + 1], T.GS[:, 16 * s:16 * s + 16], X, A.min, negate=True), "gs%d" % s, "rp%d" % c)
+                mm(B(s)[:], T.DQ[:, 128 * s:128 * s + 128], T.DP[:, 128 * s:128 * s + 128], T.MTQ[:], T.MTS[:], True, True, "DQ DP MTQ MTS", "B%d" % s)
+
+        def block(s):
+            scan(T.HH[:, 256 * s:256 * s + 256], T.MH[:, 256 * s:256 * s + 256], B(s)[:, 256:512], 0.0, A.add, A.max, "MH%d B%d" % (s, s), "HH%d" % s)
+            act(T.H16[:, 16 * s:16 * s + 16], T.HH[:, 256 * s + 15:256 * s + 256:16], "HH%d HO" % s, "H16%d" % s, bias=T.H16[:, 32 + s:33 + s])
+
+        def same(k):
+            ts(T.EK[:, 32 * k:32 * k + 32], T.YY[:, 0:32], 4 ** k, None, A.bitwise_and, None, "YY", "ek%d" % k)
+        WL, H, NK = T["WL%d" % t], T.HL[:, 0:32], T.HL[:, 32:64]
+        for s in range(2):
+            ts(T.YY[:, 16 * s:16 * s + 16], WL[:], T.W4[:, 135 + 8 * s:136 + 8 * s], float(TOP), A.subtract, A.add, "WL%d W4" % t, "", "YY")
+        ts(T.YY[:, 32:64], T.YY[:, 0:32], TOP, None, A.bitwise_and, None, "YY", "y1")
+        same(0)
+        ts(NK, T.YY[:, 32:64], float(TOP), 2.0 * TOP, A.not_equal, A.mult, "y1", "nk0 nk1")
+        same(1)
+        tt(H, T.YY[:, 32:64], NK, A.min, "y1 nk0 nk1", "H")
+        same(2)
+        between = {(0, 0): lambda: high(0), (0, 2): lambda: low(0), (1, 0): lambda: same(3), (1, 2): lambda: high(1), (2, 0): lambda: same(4),
+                   (2, 2): lambda: low(1), (3, 0): lambda: same(5), (3, 2): table, (4, 0): lambda: same(6),
+                   (5, 2): lambda: block(0), (6, 2): lambda: block(1)}
+        for k in range(8):
+            scan(T.RR[:, 32 * k:32 * k + 32], H1, H, 0.0, A.mult, A.max, "H1 H", "rr%d" % k)
+            if (k, 0) in between:
+                between[k, 0]()
             if k == 7:
                 break
             for s in range(2):
-                c = 8 * s + k
-                ts(T.TM[:, 16 * s:16 * s + 16], T.E[:, 128 * s + k:128 * s + 128:8], T.RP[:, c:c + 1], 0.062 * 0.25 ** k, A.min, A.subtract,
-                   "E rp%d" % c, "tm%d" % s)
-            for s in range(2):
-                a = T.GS[:, 16 * s:16 * s + 16]
-                tt(a, a, T.TM[:, 16 * s:16 * s + 16], A.max, "gs%d tm%d" % (s, s), "gs%d" % s)
+                ts(T.HL[:, 32 + 16 * s:48 + 16 * s], T.EK[:, 32 * k + 16 * s:32 * k + 16 * s + 16], T.RR[:, 32 * k + 16 * s + 15:32 * k + 16 * s + 16],
+                   1.5 * 4 ** k - TOP, A.subtract, A.is_ge, "ek%d rr%d" % (k, k), "nk%d" % s)
+            tt(H, H, NK, A.mult, "H nk0 nk1", "H")
+            if (k, 2) in between:
+                between[k, 2]()
         K = T.KK[:, 0:16]
-        tt(K, T.RP[:], T.TK[:], A.is_gt, "TK " + " ".join("rp%d" % c for c in range(16)), "K")
-        tt(T.KK[:, 16:32], K, T.SG[:, 0:16], A.mult, "K SG", "KA")
-        tt(T.KK[:, 32:48], K, T.SG[:, 16:32], A.mult, "K SG", "KB")
-        tt(T.KK[:, 48:64], K, T.SG[:, 32:48], A.mult, "K SG", "KC")
-        scan(T.KK[:, 80:96], T.H8[:], T.KK[:, 16:32], 0.0, A.mult, A.add, "H8 KA", "CU")
-        for s in range(2):
-            op("V", lambda: v.tensor_reduce(T.AL[:, 16 + s:17 + s], T.KK[:, 48 + 8 * s:56 + 8 * s], X, A.add), "KC AL", "al%d" % s)
-        tt(T.AL[:, 0:16], T.KK[:, 32:48], T.KK[:, 80:96], A.subtract, "KB CU AL", "al2")
+        tt(K, T.RR[:, 15::16], T.TK[:], A.is_gt, "TK " + " ".join("rr%d" % k for k in range(8)), "K")
         if t == 0:
-            setup_e()
-            halves()
+            quant(T.ELQ[:], T.ELS[:], T.ELT[:], "ELT", "ELQ ELS")
+            unpack()
+        tt(T.UU[:, 0:64], K.indirect(KL), T.SG[:, 0:64], A.mult, "K LS SG", "UU")
+        ts(T.YT[:, 64:96], K.indirect(LS[:, 30 + 2 * t:32 + 2 * t]), -1048832.0, 1048576.0, A.mult, A.add, "K LS", "KM")
+        scan(T.UU[:, 64:96], HC, T.UU[:, 0:32], 0.0, A.mult, A.add, "HC UU", "CU")
+        tt(T.AL[:, 0:32], T.UU[:, 32:64], T.UU[:, 64:96], A.subtract, "UU CU", "al1")
+        ts(T.AL[:, 32:34], T.UU[:, 67:96:16], -1.0, -256 * UNIT, A.mult, A.add, "CU", "al2")
+        al = "al0 al1 al2 LS"
+        act(T.INC[:, 256:512], T.AL[:].indirect(LS[:, 64:80]), al, "INC1")
+        cp(T.INC[:, 0:256], T.AL[:].indirect(LS[:, 48:64]), al, "INC0")
+        tt(T.IN2[:], T.AL[:].indirect(AI2), T.BD[:, 64:128], A.add, al + " BD", "IN2")
+        if t == 0:
+            window()
         for s in range(2):
-            tt(T.INC[:, 256 * s:256 * s + 256], T.AL[:].indirect(T.IL[:, 16 * s:16 * s + 16]), T.RS[:, 774 * s:774 * s + 256], A.add,
-               "al0 al1 al2 RS IL0 IL1", "INC%d" % s)
+            scan(T.O[:, 256 * s:256 * s + 256], T.INC[:, 256 * s:256 * s + 256], B(s)[:, 0:256], T.UU[:, 71 + 16 * s:72 + 16 * s], A.add, A.max,
+                 "INC%d B%d CU" % (s, s), "O%d" % s)
         for s in range(2):
-            scan(T.O[:, 256 * s:256 * s + 256], T.INC[:, 256 * s:256 * s + 256], B(s)[:, 0:256], 0.0, A.add, A.max, "INC%d B%d" % (s, s), "O%d" % s)
+            scan(T.O2[:, 16 * s:16 * s + 16], T.IN2[:, 16 * s:16 * s + 16], T.H16[:, 16 * s:16 * s + 16], T.UU[:, 71 + 16 * s:72 + 16 * s], A.add, A.max,
+                 "IN2 H16%d CU" % s, "", "O2")
         for s in range(2):
-            for k in range(8):
-                n, e, o = 256 >> k, 256 * (8 * s + k + 1), 774 * s + 256 + so[k]
-                scan(T.XO[:, e - n:e], T.RS[:, o:o + n], T.O[:, 256 * s + (1 << k) - 1:256 * s + 256:1 << k], -65536.0, A.add, A.max, "RS O%d" % s, "", "XO")
-        act(T.KK[:, 64:80], K, "K", "K2", scale=16384.0)
-        ts(T.YI[:, 0:16], T.XO[:, 255::256], -1.0, 4096.0, A.mult, A.add, "XO", "Y0")
-        ts(T.YI[:, 16:32], T.YI[:, 0:16], 8191, None, A.bitwise_and, None, "Y0", "Y1")
-        g0 = 3 * t % 8
-        for s in range(2):
-            for a, b, c in ((0, 8 - g0, g0), (8 - g0, 8, 0)):
-                if a < b:
-                    tt(T.YT[:, 16 * s + c:16 * s + c + b - a], T.YI[:, 16 + 8 * s + a:16 + 8 * s + b], T.KK[:, 64 + 8 * s + a:64 + 8 * s + b], A.add, "Y1 K2", "", "YT")
-        op("V", lambda: v.transpose(T.YT[:, 32:64], T.YT[:, 0:32]), "YT", "TR")
+            scan(T.O2[:, 32 + 16 * s:48 + 16 * s], T.IN2[:, 32 + 16 * s:48 + 16 * s], T.O[:, 256 * s + 15:256 * s + 256:16], T.UU[:, 75 + 16 * s:76 + 16 * s],
+                 A.add, A.max, "IN2 O%d CU" % s, "", "O2")
+        tt(T.PK[:, 0:128], T.O2[:].indirect(PI), T.EM[:, 128:256], A.mult, "O2 LS EM", "PK")
+        scan(T.PK[:, 128:256], T.RST[:], T.PK[:, 0:128], 0.0, A.mult, A.add, "RST PK", "PS")
+        tt(T.YT[:, 0:32], T.PK[:, 128:256].indirect(LS[:, 36 + 2 * t:38 + 2 * t]), T.YT[:, 64:96], A.min, "PS LS KM", "YT")
+        turn(T.YT[:, 32:64], T.YT[:, 0:32], "YT", "TR")
         LB, lb = T["LB%d" % t], "LB%d" % t
         for q in range(8):
             dma("Y" if q % 2 == 0 else "A", LB[16 * q:16 * q + 16, :], T.YT[q::16, 32:64], "dl%d" % t, "TR", "", lb)
         if t == 0:
-            setup_f()
-        L = T.LF
-        ts(T.DL[:, 0:16], LB[:], 16384.0, None, A.is_lt, None, lb + " DL", "dl")
-        ts(T.AI[:, 16:32], LB[:], 8191, None, A.bitwise_and, None, lb, "ai0")
-        op("V", lambda: v.transpose(T.DL[:, 32:64], T.DL[:, 0:32]), "dl", "dt")
-        ts(T.AI[:, 32:48], T.AI[:, 16:32], 4096, None, A.min, None, "ai0", "ai1")
-        scan(T.WC[:, 0:32], T.H10[:, 0:32], T.DL[:, 32:64], 0.0, A.mult, A.add, "H10 dt", "w0")
-        tt(T.AI[:, 16:32], T.AI[:, 32:48], T.JL[:, 0:16], A.add, "ai1 JL", "ai0")
+            late()
+            cp(T.URQ[:, 128:384].bitcast(dt.uint32), T.UQ[:].bitcast(dt.uint32).indirect(T.UL[:, 8:24]), "UQ UL", "URQ1")
+            act(T.URS[:, 128:384], T.US[:].indirect(T.UL[:, 8:24]), "US UL", "URS1")
+        if t == 1:
+            quant(T.VQ[:], T.VS[:], T.VT[:], "VT", "VQ VS")
+        L, JL, D = T.LF, T.JL[:, 0:16], T.DL[:, 32:48]
 
         def mean(b):
-            b, h = divmod(b, 2)
-            o = 256 * b + 128 * h
-            tt(T.XW[:, o + 96 * b:o + 96 * b + 128], T.HP[:, 256 * b:256 * b + 256].indirect(T.AU[:, 8 * h:8 * h + 8]),
-               T.HP[:, 1024 + o:1152 + o], A.add, "HP AU", "", "XZ%d" % b)
-        for i in range(2):
-            ts(T.WC[:, 32 + 16 * i:48 + 16 * i], T.WC[:, 0:16], 0.0, T.WC[:, 16 * i + 15:16 * i + 16], A.mult, A.add, "w0", "w%d" % (1 + i))
+            tt(T.XW[:, 352 * b:352 * b + 256], T.GW[:, 256 * b:256 * b + 256], B(DB[b])[:, 0:256], A.add, "GW%d B%d" % (b, DB[b]), "XZ%d" % b)
+        ts(D, LB[:], 0.0, None, A.is_ge, None, lb, "dl")
+        tt(T.AI[:, 16:32], T.JL[:, 32:48], LB[:], A.subtract, lb + " JB", "ai0")
+        scan(T.DL[:, 1:17], T.NEG[:, 0:16], D, sc(14), A.max, A.add, "dl NEG s14", "pm")
         ts(T.AI[:, 0:16], T.AI[:, 16:32], 255, None, A.bitwise_and, None, "ai0", "ai")
-        op("V", lambda: v.transpose(T.WC[:, 64:128], T.WC[:, 0:64]), "w0 w1 w2", "wt")
+        turn(T.DL[:, 64:128], T.DL[:, 0:64], "dl pm", "dt")
         cp(T.AU[:], T.AI[:, 0:16], "ai", "AU")
-        act(L[:, 16:32], T.DL[:, 0:16], "dl", "l1", scale=-1024.0)
-        JL = T.JL[:, 0:16]
-        tt(L[:, 32:48], L[:, 16:32], JL, A.add, "l1 JL", "l2")
-        Wi, Cn, Bi = T.WC[:, 64:80], T.WC[:, 96:112], T.WC[:, 128:144]
-        scan(Bi, T.NEG[:, 0:16], Cn, 0.0, A.max, A.add, "wt NEG", "bi")
-        tt(L[:, 48:64], Wi, Cn, A.subtract, "wt", "l3")
-        mean(0)
-        tt(L[:, 64:80], L[:, 48:64], Bi, A.add, "l3 bi", "l4")
-        mean(1)
-        ts(L[:, 80:96], L[:, 64:80], 1.0, T.WC[:, 143:144], A.subtract, A.subtract, "l4 bi", "l5")
-        tt(L[:, 96:112], L[:, 32:48], L[:, 64:80], A.subtract, "l2 l4", "l6")
-        mean(2)
-        tt(L[:, 112:128], L[:, 80:96], L[:, 96:112], A.max, "l5 l6", "l7")
-        mean(3)
-        ts(T.PU[:], L[:, 112:128], T.WC[:, 143:144], None, A.add, None, "l7 bi", "PU")
-        mean(4)
-        mean(5)
-        op("V", lambda: v.tensor_copy(T.LR[:].indirect(T.PU[:]), T.ICOL[:, 0:256]), "PU ICOL", "LR")
-        ts(L[:, 128:144], L[:, 112:128], T.WC[:, 143:144], None, A.add, None, "l7 bi", "pos")
-        ts(L[:, 144:160], L[:, 128:144], 96.0, None, A.is_lt, None, "pos", "m0")
-        tt(L[:, 160:176], L[:, 128:144], JL, A.subtract, "pos JL", "m1")
-        scan(T.LM[:], T.MK[:, 0:96], T.LR[:, 0:96], 0.0, A.add, A.max, "MK LR", "ln")
-        ts(L[:, 176:192], L[:, 160:176], 256.0, None, A.add, None, "m1", "m2")
-        mean(6)
-        mean(7)
-        ts(T.LU[:, 0:6], T.LM[:, 15::16], T.MK[:, 111:112], None, A.subtract, None, "ln MK", "LU")
-        tt(L[:, 160:176], L[:, 176:192], L[:, 144:160], A.mult, "m2 m0", "m3")
         for b in range(4):
+            act(T.GW[:, 256 * b:256 * b + 256], T.FW[:, 256 * b:256 * b + 256].indirect(T.AU[:]), "FW%d AU" % b, "GW%d" % b)
+        scan(T.WC[:, 0:32], H1, T.DL[:, 64:96], 0.0, A.mult, A.add, "H1 dt", "sa")
+        ts(L[:, 0:16], D, -1024.0, None, A.mult, None, "dl", "l1")
+        for i in range(2):
+            scan(T.WC[:, 32 + 16 * i:48 + 16 * i], T.NEG[:, 0:16], T.DL[:, 96 + 16 * i:112 + 16 * i], T.WC[:, 16 * i + 15:16 * i + 16],
+                 A.max, A.add, "NEG dt sa", "", "cb")
+        tt(L[:, 16:32], L[:, 0:16], JL, A.add, "l1 JL", "l2")
+        turn(T.WC[:, 64:96], T.WC[:, 32:64], "cb", "ct")
+        C, DN = T.WC[:, 64:80], T.WC[:, 80:81]
+        ts(L[:, 32:48], C, DN, None, A.subtract, None, "ct", "l5")
+        tt(L[:, 48:64], L[:, 16:32], C, A.subtract, "l2 ct", "l6")
+        tt(L[:, 64:80], L[:, 32:48], L[:, 48:64], A.max, "l5 l6", "l7")
+        mean(0)
+        ts(T.PU[:], L[:, 64:80], DN, None, A.add, None, "l7 ct", "PU")
+        ts(L[:, 80:96], L[:, 64:80], DN, 256.0, A.add, A.add, "l7 ct", "pos")
+        op("V", lambda: v.tensor_copy(T.LR[:].indirect(T.PU[:]), T.ICOL[:]), "PU ICOL", "LR")
+        mean(1)
+        scan(T.LM[:], T.MK[:, 0:96], T.LR[:, 0:96], 0.0, A.add, A.max, "MK mk1 LR", "ln")
+        mean(2)
+        ts(T.LU[:, 0:6], T.LM[:, 15::16], T.MK[:, 127:128], None, A.subtract, None, "ln mk0", "LU")
+        mean(3)
+        for b in (0, 2, 1, 3):
             o, i = T.ET[:, b:384:4], T.XW[:, 352 * b:352 * b + 256].indirect(T.LU[:, 0:6])
-            if b in (0, 2):
-                op("A", lambda: ac.activation(o, i, AF.Copy), "XZ%d LU" % b, "", "ET")
+            if b < 2:
+                act(o, i, "XZ%d LU" % b, "", "ET", scale=2.0 ** -6)
             else:
-                op("V", lambda: v.tensor_copy(o, i), "XZ%d LU" % b, "", "ET")
+                ts(o, i, 2.0 ** -6, None, A.mult, None, "XZ%d LU" % b, "", "ET")
         quant(T.EQ[:], T.ES[:], T.ET[:], "ET ET4", "EQ ES")
         remote(T["AC%d" % t][:, 0:96].bitcast(dt.uint8), T.EQ[:, 0:96].bitcast(dt.uint8), "ca%d" % t, "lc%d" % t, "EQ", "AC%d" % t)
         remote(T["AS%d" % t][:, 0:96], T.ES[:, 0:96], "ca%d" % t, "lc%d" % t, "ES", "AS%d" % t)
-        tt(L[:, 176:192], L[:, 160:176], JL, A.add, "m3 JL", "m2")
-        cp(T.SU[:], L[:, 176:192], "m2", "SU")
+        ts(L[:, 96:112], L[:, 80:96], 352.0, 4096.0, A.is_lt, A.mult, "pos", "m0")
+        tt(L[:, 112:128], L[:, 96:112], L[:, 80:96], A.min, "m0 pos", "m1")
+        tt(L[:, 128:144], L[:, 112:128], JL, A.max, "m1 JL", "m2")
+        cp(T.SU[:], L[:, 128:144], "m2", "SU")
         if last:
             cp(T.AF[:, 0:16], T.AI[:, 0:16], "ai AF", "af")
-            op("V", lambda: v.transpose(T.AF[:, 32:64], T.AF[:, 0:32]), "af", "at")
+            turn(T.AF[:, 32:64], T.AF[:, 0:32], "af", "at")
             for q in range(8):
                 p = 32 * (q // 2)
                 dma("Y", T.al[q:q + 1, 0:256], T.AF[p:p + 16, 32 + 16 * (q % 2):48 + 16 * (q % 2)], "dout", "at")
@@ -539,16 +547,13 @@ def rank_program(g, core, T, topo):
             mm(B(DB[b])[:, 0:128], T.ELQ[:, 128 * b:128 * b + 128], T.ELS[:, 128 * b:128 * b + 128], AC[:], AS[:], False, True, "ELQ ELS AC%d AS%d" % (t, t), "", kb)
         for b in range(4):
             kb, o, i = "B%d" % DB[b], T.XW[:, 352 * b + 256:352 * b + 352], B(DB[b])[:, 0:96]
-            act(o, i, kb, "XT%d" % b, scale=0.03125)
-        for b in range(4):
-            o, i = T.XT[:, b::4], T.XW[:, 352 * b:352 * b + 352].indirect(T.SU[:])
-            if b == 3:
-                o1, o2 = T.XT[:, 3:512:4], T.XT[:, 515::4]
-                i1, i2 = [T.XW[:, 1056:1408].indirect(T.SU[:, 8 * h:8 * h + 8]) for h in range(2)]
-                op("A", lambda: ac.activation(o1, i1, AF.Copy), "XZ3 XT3 SU", "", "XT")
-                op("V", lambda: v.tensor_copy(o2, i2), "XZ3 XT3 SU", "", "XT")
+            o2, i2 = T.XT[:, b::4], T.XW[:, 352 * b:352 * b + 352].indirect(T.SU[:])
+            if b % 2 == 0:
+                act(o, i, kb, "XT%d" % b, scale=2.0)
+                act(o2, i2, "XZ%d XT%d SU" % (b, b), "", "XT", scale=2.0 ** -6)
             else:
-                op("V", lambda: v.tensor_copy(o, i), "XZ%d XT%d SU" % (b, b), "", "XT")
+                ts(o, i, 2.0, None, A.mult, None, kb, "XT%d" % b)
+                ts(o2, i2, 2.0 ** -6, None, A.mult, None, "XZ%d XT%d SU" % (b, b), "", "XT")
     quant(T.XQ[:], T.XS[:], T.XT[:], "XT", "XQ0 XQ1")
     dma("Y", T.oc[:], T.XQ[:].bitcast(dt.uint8), "dout", "XQ0 XQ1")
     for k in range(4):

@@ -4,35 +4,35 @@ F32, BF, I32, U16, F8, U8 = "float32", "bfloat16", "int32", "uint16", "float8_e4
 SCRATCH = {}
 for _n, _w, _d in [
         ("X0", 1024, BF), ("UT", 512, BF), ("VT", 512, BF), ("WQ", 512, F8), ("WS", 512, U8),
-        ("UQ", 128, F8), ("US", 128, U8), ("VQ", 128, F8), ("VS", 128, U8), ("URQ", 384, F8), ("URS", 384, U8),
-        ("ELT", 2048, BF), ("ELQ", 512, F8), ("ELS", 512, U8), ("CT", 1024, BF), ("CQ", 256, F8), ("CS", 256, U8),
+        ("UQ", 128, F8), ("US", 128, U8), ("VQ", 128, F8), ("VS", 128, U8), ("URQ", 432, F8), ("URS", 432, U8),
+        ("ELT", 2048, BF), ("ELQ", 512, F8), ("ELS", 512, U8), ("CT", 1536, BF), ("CQ", 384, F8), ("CS", 384, U8),
         ("HMT", 1024, BF), ("HMQ", 256, F8), ("HMS", 256, U8), ("MTT", 2048, BF), ("MTQ", 512, F8), ("MTS", 512, U8),
-        ("ICOL", 256, F32), ("VB", 256, BF), ("I8", 128, BF), ("I16", 256, BF), ("JP", 128, BF), ("TH", 128, F32),
-        ("IP", 16, I32), ("SC", 24, F32), ("UI", 24, I32), ("UL", 24, U16), ("PLF", 16, F32), ("PL", 16, U16),
-        ("RW", 32, F32), ("FR", 136, F32), ("FS", 128, F32), ("LS", 80, U16), ("KC", 768, BF),
-        ("CB", 64, F32), ("CE", 128, F32), ("RST", 128, F32), ("TK", 16, F32), ("H4", 144, F32), ("HS", 96, F32),
-        ("NEG", 256, BF), ("JL", 48, F32), ("MK", 224, F32),
+        ("ICOL", 256, F32), ("VB", 256, BF), ("I8", 144, BF), ("I16", 256, BF), ("JP", 128, BF), ("TH", 144, F32),
+        ("IP", 16, I32), ("SC", 24, F32), ("UI", 30, I32), ("UL", 30, U16), ("PLF", 16, F32), ("PL", 16, U16),
+        ("RW", 32, F32), ("FR", 152, F32), ("FS", 136, F32), ("LS", 80, U16), ("KC", 768, BF),
+        ("CB", 64, F32), ("CE", 128, F32), ("RST", 64, F32), ("TK", 16, F32), ("H4", 128, F32), ("HS", 96, F32),
+        ("NEG", 256, BF), ("JL", 48, F32), ("MK", 256, F32),
         ("XQ", 256, F8), ("XS", 256, U8), ("XT", 1024, BF), ("BT", 608, BF), ("BQ", 152, F8), ("BS", 152, U8),
-        ("W4", 144, F32), ("W2", 16, F32), ("WN", 40, F32), ("SG", 96, F32),
+        ("W4", 128, F32), ("W2", 32, F32), ("WN", 72, F32), ("SG", 64, F32),
         ("OT", 1024, BF), ("OQ", 256, F8), ("OS", 256, U8), ("HB", 512, BF), ("DS", 1024, BF), ("DG", 512, BF), ("DH", 512, BF),
         ("DT", 1024, BF), ("DQ", 256, F8), ("DP", 256, U8), ("MH", 512, BF), ("HH", 512, F32), ("H16", 34, F32),
-        ("BD", 128, F32), ("EM", 256, F32), ("YY", 128, I32), ("EK", 224, I32), ("HL", 64, F32), ("RR", 256, F32),
-        ("KK", 24, F32), ("UU", 96, F32), ("AL", 40, F32), ("INC", 512, F32), ("IN2", 64, F32), ("O", 512, F32), ("O2", 64, F32),
-        ("PK", 256, F32), ("YT", 96, F32), ("AI", 32, I32), ("LF", 160, F32), ("DL", 128, F32), ("WC", 96, F32), ("AF", 64, F32),
+        ("BD", 128, F32), ("EM", 256, F32), ("YY", 64, I32), ("EK", 224, I32), ("HL", 64, F32), ("RR", 256, F32),
+        ("KK", 32, F32), ("UU", 80, F32), ("AL", 64, F32), ("INC", 512, F32), ("IN2", 64, F32), ("O", 512, F32), ("O2", 64, F32),
+        ("PK", 256, F32), ("YT", 128, F32), ("AI", 32, I32), ("LF", 160, F32), ("DL", 128, F32), ("WC", 96, F32), ("AF", 64, F32),
         ("AU", 16, U16), ("PU", 16, U16), ("LU", 8, U16), ("SU", 16, U16), ("LR", 256, F32), ("LM", 96, F32),
         ("FW", 1024, BF), ("GW", 1024, BF), ("XW", 1408, BF), ("ET", 512, BF), ("EQ", 128, F8), ("ES", 128, U8), ("YO", 256, F32)]:
     SCRATCH[_n] = ("sbuf", [128, _w], _d)
 for _t in range(3):
     SCRATCH["MS%d" % _t] = ("sbuf", [128, 16], F32)
     SCRATCH["WL%d" % _t] = ("sbuf", [128, 16], F32)
-    SCRATCH["LB%d" % _t] = ("sbuf", [128, 16], F32)
+    SCRATCH["LB%d" % _t] = ("sbuf", [128, 32], F32)
     SCRATCH["AC%d" % _t] = ("sbuf", [128, 128], F8)
     SCRATCH["AS%d" % _t] = ("sbuf", [128, 128], U8)
 for _b in range(8):
     SCRATCH["B%d" % _b] = ("psum", [128, 512], F32)
 SEMAPHORES = ["cV", "cA", "cP", "cG", "dx", "du", "dv", "dw", "dfill", "dout"]
 for _t in range(3):
-    SEMAPHORES += ["wa%d" % _t, "ca%d" % _t, "lw%d" % _t, "lc%d" % _t, "dl%d" % _t]
+    SEMAPHORES += ["wa%d" % _t, "ca%d" % _t, "lw%d" % _t, "lc%d" % _t, "dl%d" % _t, "dk%d" % _t]
 
 RAISE = 2.0 ** -6
 UNIT = 2.0 ** -17
@@ -174,6 +174,18 @@ def rank_program(g, core, T, topo):
     def where0(out, in_, pat, base, r, add):
         op("G", lambda: g.affine_select(out, in_, pat, A.is_equal, 0.0, base, 1), r, "", add)
 
+    def weave(chain, fillers):
+        fillers = list(fillers)
+        for c in chain:
+            c()
+            if fillers:
+                f = fillers.pop(0)
+                if f:
+                    f()
+        for f in fillers:
+            if f:
+                f()
+
     def B(b):
         return T["B%d" % b]
 
@@ -181,8 +193,8 @@ def rank_program(g, core, T, topo):
 
     def sc(c):
         return SC[:, c:c + 1]
-    KL, BL, BI, AI2, EI, PI = LS[:, 0:4], LS[:, 4:6], LS[:, 6:10], LS[:, 10:14], LS[:, 14:22], LS[:, 22:30]
-    H1, H2, HN, HC = T.HS[:, 0:32], T.HS[:, 32:48], T.HS[:, 48:64], T.HS[:, 64:96]
+    KL, BL, BI, AI2, EI, PI = LS[:, 0:4], LS[:, 26:30], LS[:, 6:10], LS[:, 10:14], LS[:, 14:22], LS[:, 22:26]
+    H1, H2, HN = T.HS[:, 0:32], T.HS[:, 32:48], T.HS[:, 48:64]
 
     dma("A", T.UT[:], T.u[:], "du", "", "UT")
     dma("Y", T.X0[:], T.x[:], "dx", "", "X0")
@@ -191,40 +203,64 @@ def rank_program(g, core, T, topo):
     dma("Y", T.VT[:], T.v[:], "dv", "", "VT")
 
     iota(IP[:, 0:1], [[0, 1]], 0, 1, "ip0", False)
-    iota(T.UI[:], [[3, 3], [0, 8]], 7 + 128, -1, "UI", False)
+    iota(T.UI[:], [[3, 3], [0, 10]], 7 + 128, -1, "UI", False)
     iota(T.I16[:], [[0, 16], [1, 16]], 0, 0, "I16")
+    iota(T.I8[:], [[1, 18], [0, 8]], 0, 0, "I8")
     iota(SC[:, 4:8], [[-2, 2], [128, 2]], 0, 1, "s4")
     iota(T.JP[:], [[4, 4], [1, 2], [16, 16]], 0, 0, "JP")
-    iota(T.I8[:], [[1, 16], [0, 8]], 0, 0, "I8")
     iota(T.ICOL[:], [[1, 256]], 0, 0, "ICOL")
     fill(T.CT[:], 0.0, "CT")
     fill(T.BT[:], 0.0, "BT")
-    fill(T.H4[:], 4.0, "H4")
     ts(IP[:, 1:2], IP[:, 0:1], 15, None, A.bitwise_and, None, "ip0", "ip1")
     ts(IP[:, 2:3], IP[:, 0:1], 4, None, A.arith_shift_right, None, "ip0", "ip2")
     ts(T.UI[:], T.UI[:], 7, None, A.bitwise_and, None, "UI", "UI")
-    fill(T.H4[:, 0::8], 0.0, "H4")
+    fill(T.H4[:], 4.0, "H4")
     for c, i, a in ((1, 1, 0.0), (2, 2, 0.0), (3, 2, 8.0)):
         ts(sc(c), IP[:, i:i + 1], a, None, A.add, None, "ip%d" % i, "s%d" % c)
     ts(T.UL[:], T.UI[:], 16, None, A.mult, None, "UI", "UL")
-    fill(T.OT[:], 0.0, "OT")
+    fill(T.H4[:, 0::8], 0.0, "H4")
+    ts(IP[:, 3:4], IP[:, 0:1], 5, None, A.arith_shift_right, None, "ip0", "ip3")
+    ts(IP[:, 4:5], IP[:, 2:3], 1, None, A.bitwise_and, None, "ip2", "ip4")
+    ts(sc(8), IP[:, 1:2], -16.0, 255.0, A.mult, A.add, "ip1", "s8")
     for s in range(2):
         ts(T.CT[:, s:512:4], T.I16[:, 0:128], sc(2 + s), None, A.is_equal, None, "I16 s%d" % (2 + s), "", "CT")
+    ts(sc(9), IP[:, 3:4], -4.0, sc(8), A.mult, A.add, "ip3 s8", "s9")
+    ts(T.TH[:], T.I8[:], sc(1), 1e29, A.not_equal, A.mult, "I8 s1", "TH")
+    ts(sc(10), IP[:, 4:5], -1.0, sc(9), A.mult, A.add, "ip4 s9", "s10")
     for s in range(2):
         for h in range(2):
-            ts(T.CT[:, 512 * s + 2 + h:512 * s + 512:4], T.JP[:], sc(4 + 2 * s + h), None, A.is_equal, None, "JP s4", "", "CT")
+            ts(T.CT[:, 512 * s + 512 + h:512 * s + 1024:4], T.JP[:], sc(4 + 2 * s + h), None, A.is_equal, None, "JP s4", "", "CT")
+    fill(T.TH[:, 136:144], 0.0, "TH")
+    for a in range(0, 1024, 256):
+        act(T.HMT[:, a:a + 256], T.I16[:], "I16", "", "HMT", scale=0.0)
+    epoch["HMT"] = [(tk, False) for tk in lastw["HMT"]]
     quant(T.UQ[:], T.US[:], T.UT[:], "UT", "UQ US")
-    ts(T.TH[:], T.I8[:], sc(1), 1e29, A.not_equal, A.mult, "I8 s1", "TH")
-    cp(T.URQ[:, 0:128].bitcast(dt.uint32), T.UQ[:].bitcast(dt.uint32).indirect(T.UL[:, 0:8]), "UQ UL", "URQ0")
-    act(T.URS[:, 0:128], T.US[:].indirect(T.UL[:, 0:8]), "US UL", "URS0")
-    act(T.HMT[:], T.CT[:], "CT", "HMT", scale=0.0)
-    iota(T.VB[:], [[1, 256]], 0, 0, "VB")
+    ts(sc(11), sc(10), -2.0, None, A.add, None, "s10", "s11")
+
+    def steps(i):
+        cp(T.URQ[:, 144 * i:144 * i + 144].bitcast(dt.uint32), T.UQ[:].bitcast(dt.uint32).indirect(T.UL[:, 10 * i:10 * i + 9]), "UQ UL", "URQ%d" % i)
+        act(T.URS[:, 144 * i:144 * i + 144], T.US[:].indirect(T.UL[:, 10 * i:10 * i + 9]), "US UL", "URS%d" % i)
+    steps(0)
 
     def rows():
         row(T.HS[:, 32:64], 32, 0, 2, "HS2")
-        row(T.HS[:, 32:48:8], 2, 0, 0, "HS2")
-        row(T.HS[:, 48:64:4], 4, 0, 0, "HS2")
         row(T.NEG[:], 256, 0, -1, "NEG")
+        row(T.HS[:, 32:48:8], 2, 0, 0, "HS2")
+        row(T.HS[:, 48:64:4], 4, 0, 0, "", "HS2")
+        for o, n, z in ((17, 2, 0), (18, 4, 1), (20, 8, 2), (24, 16, 3), (16, 16, 4)):
+            row(T.FR[:, o:32:n], 16 // n, 0, z, "", "FR")
+        for o, n, z in ((0, 8, 1), (8, 4, 2), (12, 2, 3), (14, 2, 3)):
+            row(T.FR[:, 48 + o:48 + o + n], n, 1 << z, (1 << z) - 1, "", "FR")
+            if o < 14:
+                row(T.FR[:, 32 + o:32 + o + max(n, 4)], max(n, 4), 0, z, "", "FR")
+        row(T.HS[:, 0:32], 32, 0, 1, "H1")
+        for i in range(3):
+            o = -3 * i % 8
+            act(T.FR[:, 64 + 16 * i:80 + 16 * i], T.FR[:, 128 + o:144 + o], "EB", "", "FR")
+        row(T.HS[:, 0:32:16], 2, 0, 0, "H1")
+        row(T.WN[:, 32:40], 8, 0, 0, "wn0")
+
+    def rows_b():
         for o, n in ((1, 2), (2, 4), (4, 8)):
             act(T.CB[:, o::n], T.I16[:, o:64:n], "I16", "", "CB", scale=1.0 / n, bias=-o / n)
         act(T.CB[:, 0::8], T.I16[:, 0:64:8], "I16", "", "CB", scale=-0.125, bias=1.0)
@@ -232,138 +268,130 @@ def rank_program(g, core, T, topo):
             row(T.CE[:, o:o + n:2], n // 2, 2, 1, "", "CE0")
             row(T.CE[:, o + 1:o + n:2], n // 2, 2, 0, "", "CE0")
         row(T.CE[:, 30:32], 2, 0, -1, "", "CE0")
-        for o, n, z in ((17, 2, 0), (18, 4, 1), (20, 8, 2), (24, 16, 3), (16, 16, 4)):
-            row(T.FR[:, o:32:n], 16 // n, 0, z, "", "FR")
-        for o, n, z in ((0, 8, 1), (8, 4, 2), (12, 2, 3), (14, 2, 3)):
-            row(T.FR[:, 48 + o:48 + o + n], n, 1 << z, (1 << z) - 1, "", "FR")
-            if o < 14:
-                row(T.FR[:, 32 + o:32 + o + max(n, 4)], max(n, 4), 0, z, "", "FR")
-        for k in range(8):
-            row(T.FR[:, 112 + k::8], 3, 0, 64 * (k // 4) + 31 - (16 >> k % 4), "", "EB")
-        act(T.CE[:, 32:64], T.CE[:, 0:32], "CE0", "CE1")
-        for i in range(3):
-            o = -3 * i % 8
-            act(T.FR[:, 64 + 16 * i:80 + 16 * i], T.FR[:, 112 + o:128 + o], "EB", "", "FR")
-        act(T.CE[:, 64:128], T.CE[:, 0:64], "CE0 CE1", "CE")
 
-    def rows_b():
-        row(T.HS[:, 0:32], 32, 0, 1, "H1")
+    def rows_c():
+        act(T.CE[:, 32:64], T.CE[:, 0:32], "CE0", "CE1")
         row(T.HS[:, 64:96], 32, 0, 1, "HC")
-        row(T.RST[:], 128, 0, 1, "RST")
-        for k in range(8):
-            row(T.TK[:, 2 * k:2 * k + 2], 2, 0, TOP - 2 * 4 ** k, "", "TK")
-        row(T.HS[:, 0:32:16], 2, 0, 0, "H1")
-        row(T.HS[:, 64:96:16], 2, 0, 0, "HC")
-        row(T.HS[:, 76:96:16], 2, 0, 0, "", "HC")
+        act(T.CE[:, 64:128], T.CE[:, 0:64], "CE0 CE1", "CE")
+        row(T.RST[:], 64, 0, 1, "RST")
+        row(T.HS[:, 64:80:8], 2, 0, 0, "", "HC")
+        row(T.HS[:, 80:96:4], 4, 0, 0, "", "HC")
         for o in (0, 16, 24, 28, 30):
-            row(T.RST[:, o::32], 4, 0, 0, "", "RST")
-        row(T.AL[:, 34:40], 6, 0, 0, "al0")
-        row(T.WN[:, 32:40], 8, 0, 0, "wn0")
+            row(T.RST[:, o::32], 2, 0, 0, "", "RST")
+        row(T.AL[:, 16:32], 16, 0, 0, "al2")
+        row(T.KK[:, 0:16], 16, 0, 0, "K0 K1")
 
     def number_rows():
+        for z in range(4):
+            op("G", lambda: g.iota(T.FR[:, 128 + z::4], [[0, 3], [64, 2]], 31 - (16 >> z), 0, allow_small_or_imprecise_dtypes=True), "", "", "EB")
         iota(T.PLF[:], [[-2, 2], [-4, 4], [-1, 2]], 255, 0, "PLF")
-        iota(T.FR[:, 0:16], [[8, 2], [0, 2], [2, 4]], 0, 0, "FR0")
-        for c, pat, base in ((0, [[0, 2], [1, 2]], 0), (4, [[0, 2], [16, 2]], 14), (8, [[-4, 2], [8, 2]], 20), (12, [[12, 2], [16, 2]], 0),
-                             (16, [[-10, 2], [-15, 2]], 28), (20, [[16, 4]], 0)):
+        iota(T.FR[:, 0:16], [[1, 2], [0, 2], [2, 4]], 0, 0, "FR0")
+        iota(T.FR[:, 112:128], [[8, 2], [-40, 2], [-1, 4]], 47, 0, "FR7")
+        for c, pat, base in ((0, [[8, 2], [0, 2]], 0), (4, [[-4, 2], [16, 2]], 0), (8, [[-4, 2], [8, 2]], 20), (12, [[0, 2], [8, 2]], 0),
+                             (16, [[7, 2], [0, 2]], 12), (20, [[16, 4]], 0)):
             iota(T.RW[:, c:c + 4], pat, base, 0, "rw%d" % c)
         iota(IP[:, 8:11], [[-3, 3]], 24, 1, "ip8", False)
         iota(T.JL[:, 16:32], [[16, 16]], 0, 0, "JLF")
 
     def falling_order():
-        ts(IP[:, 3:4], IP[:, 0:1], 5, None, A.arith_shift_right, None, "ip0", "ip3")
-        ts(IP[:, 4:5], IP[:, 2:3], 1, None, A.bitwise_and, None, "ip2", "ip4")
-        ts(sc(8), IP[:, 1:2], -16.0, 255.0, A.mult, A.add, "ip1", "s8")
-        ts(sc(16), IP[:, 1:2], 16.0, None, A.mult, None, "ip1", "s16")
-        ts(sc(9), IP[:, 3:4], -4.0, sc(8), A.mult, A.add, "ip3 s8", "s9")
-        fill(T.KC[:, 0:256], UNIT, "KC0")
-        ts(sc(10), IP[:, 4:5], -1.0, sc(9), A.mult, A.add, "ip4 s9", "s10")
-        fill(T.KC[:, 256:768], 32.0, "KC1")
-        ts(sc(11), sc(10), -2.0, None, A.add, None, "s10", "s11")
         for s in range(2):
             ts(T.HMT[:, s::4], T.VB[:], sc(10 + s), 256.0, A.is_equal, A.mult, "VB s%d" % (10 + s), "", "HMT")
         quant(T.HMQ[:], T.HMS[:], T.HMT[:], "HMT", "HMQ HMS")
 
     def word_order():
-        for h in range(2):
-            where0(T.MTT[:, 2 * h:1024:4], T.KC[:, 0:256], [[-1, 256]], 128 * h, "KC0", "mt%d" % h)
-            where0(T.MTT[:, 1024 + 2 * h::4], T.KC[:, 0:256], [[-1, 16], [-16, 16]], 128 * h, "KC0", "mt%d" % h)
+        for i in range(4):
+            where0(T.MTT[:, i:1024:4], T.KC[:, 0:256], [[-1, 256]], 128 * (i // 2), "KC0", "MT0")
+        for i in range(4):
+            where0(T.MTT[:, 1024 + i::4], T.KC[:, 0:256], [[-1, 16], [-16, 16]], 128 * (i // 2), "KC0", "MT1")
         for b in range(4):
             where0(T.ELT[:, 512 * b:512 * b + 512], T.KC[:, 256:768], [[-1, 128], [128, 4]], -128 * b, "KC1", "ELT")
 
     def lists():
-        ts(T.MK[:, 112:224], T.I16[:, 0:112], sc(1), 8000.0, A.not_equal, A.mult, "I16 s1", "mk0")
+        ts(T.MK[:, 128:256], T.I16[:, 0:128], sc(1), 8000.0, A.not_equal, A.mult, "I16 s1", "mk0")
+        ts(sc(16), IP[:, 1:2], 16.0, None, A.mult, None, "ip1", "s16")
+        tt(T.MK[:, 1:128], T.MK[:, 129:256], T.MK[:, 128:255], A.subtract, "mk0", "MK")
+        cp(T.MK[:, 0:1], T.MK[:, 128:129], "mk0", "mk1")
+        ts(T.MK[:, 16:128:16], T.MK[:, 16:128:16], 3000.0, None, A.subtract, None, "MK", "MK")
         ts(T.PL[:], T.PLF[:], sc(16), None, A.subtract, None, "PLF s16", "PL")
-        tt(T.MK[:, 1:112], T.MK[:, 113:224], T.MK[:, 112:223], A.subtract, "mk0", "MK")
-        cp(T.MK[:, 0:1], T.MK[:, 112:113], "mk0", "mk1")
-        ts(T.MK[:, 16:112:16], T.MK[:, 16:112:16], 3000.0, None, A.subtract, None, "MK", "MK")
         ts(IP[:, 12:15], IP[:, 8:11], 7, None, A.bitwise_and, None, "ip8", "ip12")
-        scan(T.FS[:, 0:112], T.MK[:, 0:112], T.FR[:, 0:112], 0.0, A.add, A.max, "MK mk1 FR FR0", "fs0")
+        scan(T.FS[:, 0:128], T.MK[:, 0:128], T.FR[:, 0:128], 0.0, A.add, A.max, "MK mk1 FR FR0 FR7", "fs0")
         for s in range(2):
             ts(LS[:, 30 + s:36:2], IP[:, 12:15], 2.0, float(s), A.mult, A.add, "ip12", "", "LS")
-        ts(T.FS[:, 112:119], T.FS[:, 15:112:16], T.MK[:, 127:128], None, A.subtract, None, "fs0 mk0", "FS")
+        ts(T.FS[:, 128:136], T.FS[:, 15:128:16], T.MK[:, 143:144], None, A.subtract, None, "fs0 mk0", "FS")
         ts(sc(12), IP[:, 1:2], 0.0, None, A.is_equal, None, "ip1", "s12")
-        k2, tz, z1, p1 = [T.FS[:, 112 + i:113 + i] for i in range(4)]
+        scan(T.RR[:, 0:8], T.H4[:, 1:65:8], T.NEG[:, 0:8], 0.25, A.mult, A.max, "H4 NEG", "rr0")
+        for s in range(2):
+            ts(T.TK[:, s::2], T.RR[:, 0:8], -2.0, float(TOP), A.mult, A.add, "rr0", "", "TK")
+
+    def lists_b():
+        ks, tz, z1, p1, bs = [T.FS[:, 128 + i:129 + i] for i in (0, 1, 2, 3, 7)]
+        ts(LS[:, 14:22:2], T.RW[:, 8:12], 3.0, None, A.add, None, "rw8", "", "LS")
         ts(sc(13), tz, 2.0, None, A.is_le, None, "FS", "s13")
         ts(T.RW[:, 24:28], T.RW[:, 16:20], sc(12), tz, A.mult, A.add, "rw16 s12 FS", "rw24")
         ts(T.RW[:, 28:32], T.RW[:, 8:12], tz, 30.0, A.subtract, A.subtract, "rw8 FS", "rw28")
-        ts(LS[:, 14:22:2], T.RW[:, 8:12], 3.0, None, A.add, None, "rw8", "", "LS")
         ts(LS[:, 15:22:2], T.RW[:, 8:12], z1, 3.0, A.subtract, A.add, "rw8 FS", "", "LS")
-        ts(BI, T.RW[:, 28:32], sc(13), 32.0, A.mult, A.add, "rw28 s13", "", "LS")
-        ts(BL, T.RW[:, 4:6], k2, 0.5, A.subtract, A.mult, "rw4 FS", "", "LS")
+        ts(BL, T.RW[:, 4:8], bs, None, A.add, None, "rw4 FS", "", "LS")
         tt(T.RW[:, 24:28], T.RW[:, 24:28], T.RW[:, 12:16], A.add, "rw24 rw12", "rw24")
-        ts(KL, T.RW[:, 0:4], k2, None, A.add, None, "rw0 FS", "", "LS")
-        ts(LS[:, 22:30:2], T.RW[:, 20:24], sc(1), None, A.add, None, "rw20 s1", "", "LS")
-        ts(LS[:, 23:30:2], T.RW[:, 20:24], p1, None, A.add, None, "rw20 FS", "", "LS")
+        ts(BI, T.RW[:, 28:32], sc(13), 32.0, A.mult, A.add, "rw28 s13", "", "LS")
+        ts(KL, T.RW[:, 0:4], ks, None, A.add, None, "rw0 FS", "", "LS")
+        ts(LS[:, 22:26:2], T.RW[:, 20:22], sc(1), None, A.add, None, "rw20 s1", "", "LS")
+        ts(LS[:, 23:26:2], T.RW[:, 20:22], p1, None, A.add, None, "rw20 FS", "", "LS")
         cp(AI2, T.RW[:, 24:28], "rw24", "", "LS")
         for s in range(2):
-            ts(LS[:, 36 + s:42:2], T.FS[:, 116:119], 32.0 * s, None, A.add, None, "FS", "", "LS")
+            ts(LS[:, 36 + s:42:2], T.FS[:, 132:135], 32.0 * s, None, A.add, None, "FS", "", "LS")
             ts(LS[:, 48 + 16 * s:64 + 16 * s], T.PLF[:], 0.0, T.RW[:, 24 + s:25 + s], A.mult, A.add, "PLF rw24", "", "LS")
 
     def late():
-        ts(T.JL[:, 0:16], T.JL[:, 16:32], sc(1), None, A.add, None, "JLF s1", "JL")
-        ts(T.JL[:, 32:48], T.JL[:, 16:32], sc(1), 131072.0, A.add, A.add, "JLF s1", "JB")
         fill(T.DL[:, 0:64], 0.0, "dl pm")
         ts(sc(14), sc(12), -1.0, None, A.mult, None, "s12", "s14")
-        fill(T.ET[:, 384:512], 0.0, "ET4")
+        ts(T.JL[:, 0:16], T.JL[:, 16:32], sc(1), None, A.add, None, "JLF s1", "JL")
+        ts(T.JL[:, 32:48], T.JL[:, 16:32], sc(1), 131072.0, A.add, A.add, "JLF s1", "JB")
         cp(T.DL[:, 0:1], sc(14), "s14 pm", "pm")
-        fill(T.AF[:], 0.0, "AF")
+        fill(T.ET[:, 384:512], 0.0, "ET4")
 
     quant(T.CQ[:], T.CS[:], T.CT[:], "CT", "CQ CS")
+    number_rows()
+    iota(T.VB[:], [[1, 256]], 0, 0, "VB")
     rows()
     DB = (4, 5, 6, 7)
     for t in range(3):
         last = t == 2
-        src, key = (T.X0, "X0") if t == 0 else (T.XT, "XT")
+        src = T.X0 if t == 0 else T.XT
         for h in range(2):
-            quant(T.XQ[:, 128 * h:128 * h + 128], T.XS[:, 128 * h:128 * h + 128], src[:, 512 * h:512 * h + 512], key, "XQ%d" % h)
+            quant(T.XQ[:, 128 * h:128 * h + 128], T.XS[:, 128 * h:128 * h + 128], src[:, 512 * h:512 * h + 512], "X0" if t == 0 else "XT X3%d" % h, "XQ%d" % h)
         if t == 0:
             for i in range(3):
                 dma("Y", T["AC%d" % i][:, 96:128].bitcast(dt.uint8), T.XQ[:, 0:32].bitcast(dt.uint8), "dfill", "XQ0", "", "AC%d" % i)
                 dma("Y", T["AS%d" % i][:, 96:128], T.XS[:, 0:32], "dfill", "XQ0", "", "AS%d" % i)
-        ur = "URQ%d URS%d" % (min(t, 1), min(t, 1))
         for s in range(2):
-            mm(B(s)[:, 0:128], T.XQ[:, 128 * s:128 * s + 128], T.XS[:, 128 * s:128 * s + 128], T.URQ[:, 128 * t:128 * t + 128], T.URS[:, 128 * t:128 * t + 128],
-               True, True, "XQ%d %s" % (s, ur), "B%d" % s)
+            mm(B(s)[:, 0:144], T.XQ[:, 128 * s:128 * s + 128], T.XS[:, 128 * s:128 * s + 128], T.URQ[:, 144 * t:144 * t + 144], T.URS[:, 144 * t:144 * t + 144],
+               True, True, "XQ%d URQ%d URS%d" % (s, t, t), "B%d" % s)
         if t == 0:
-            falling_order()
+            fill(T.KC[:, 0:256], UNIT, "KC0")
+            fill(T.KC[:, 256:768], 32.0, "KC1")
         for s in range(2):
-            tt(T.BT[:, 32 + s:544:4], B(s)[:, 0:128], T.TH[:], A.is_gt, "B%d TH" % s, "", "BT")
-            ts(T.BT[:, 546 + s:576:4], B(s)[:, 0:8], 0.0, None, A.is_gt, None, "B%d" % s, "", "BT")
+            tt(T.BT[:, s:576:4], B(s)[:, 0:144], T.TH[:], A.is_gt, "B%d TH" % s, "", "BT")
         quant(T.BQ[:], T.BS[:], T.BT[:], "BT", "BQ BS")
-        mm(B(2)[:, 0:144], T.CQ[:, 0:128], T.CS[:, 0:128], T.BQ[:, 8:152], T.BS[:, 8:152], True, False, "CQ CS BQ BS", "B2")
-        mm(B(2)[:, 0:144], T.CQ[:, 128:256], T.CS[:, 128:256], T.BQ[:, 0:144], T.BS[:, 0:144], False, True, "CQ CS BQ BS", "", "B2")
-        scan(T.W4[:], T.H4[:], B(2)[:, 0:144], 0.0, A.mult, A.add, "H4 B2", "W4")
-        scan(T.W2[:], H2, B(2)[:, 128:144], 0.0, A.mult, A.add, "HS2 B2", "W2")
-        cp(T["MS%d" % t][:], T.W4[:, 7:128:8], "W4", "MS%d" % t)
+        mm(B(2)[:, 0:128], T.CQ[:, 0:128], T.CS[:, 0:128], T.BQ[:, 0:128], T.BS[:, 0:128], True, True, "CQ CS BQ BS", "B2")
+        mm(B(3)[:, 0:128], T.CQ[:, 128:256], T.CS[:, 128:256], T.BQ[:, 24:152], T.BS[:, 24:152], True, False, "CQ CS BQ BS", "B3")
+        mm(B(3)[:, 0:128], T.CQ[:, 256:384], T.CS[:, 256:384], T.BQ[:, 16:144], T.BS[:, 16:144], False, True, "CQ CS BQ BS", "", "B3")
+        if t == 0:
+            fill(T.OT[:], 0.0, "OT")
+        scan(T.W4[:], T.H4[:], B(2)[:, 0:128], 0.0, A.mult, A.add, "H4 B2", "W4")
+        cp(T["MS%d" % t][:], T.W4[:, 7::8], "W4", "MS%d" % t)
         remote(T["WL%d" % t][:], T["MS%d" % t][:], "wa%d" % t, "lw%d" % t, "MS%d" % t, "WL%d" % t)
-        scan(T.WN[:, 16:32], HN, B(2)[:, 128:144], 0.0, A.mult, A.add, "HS2 B2", "P4")
+        bits = B(3)[:, 112:128]
+        scan(T.W2[:, 0:16], H2, bits, 0.0, A.mult, A.add, "HS2 B3", "W2")
+        scan(T.WN[:, 16:32], HN, bits, 0.0, A.mult, A.add, "HS2 B3", "P4")
         for s in range(2):
             ts(T.OT[:, s::4], T.VB[:], T.W2[:, 8 * s + 7:8 * s + 8], None, A.is_equal, None, "VB W2", "", "OT")
-        act(T.WN[:, 0:16], B(2)[:, 128:144], "B2", "bits")
+        scan(T.W2[:, 16:32], T.H4[:, 0:16], bits, 0.0, A.mult, A.add, "H4 B3", "W3")
+        act(T.WN[:, 0:16], bits, "B3", "bits")
         quant(T.OQ[:], T.OS[:], T.OT[:], "OT", "OQ OS")
+        if t == 0:
+            falling_order()
         for h in range(2):
             mm(B(h)[:, 0:256], T.OQ[:, 128 * h:128 * h + 128], T.OS[:, 128 * h:128 * h + 128], T.HMQ[:], T.HMS[:], True, True, "OQ OS HMQ HMS", "B%d" % h)
-            act(T.HB[:, 256 * h:256 * h + 256], B(h)[:, 0:256], "B%d" % h, "HB%d" % h)
 
         def unpack():
             for b in range(4):
@@ -373,39 +401,42 @@ def rank_program(g, core, T, topo):
         def window():
             for b in range(4):
                 act(T.FW[:, 256 * b:256 * b + 256], B(DB[b])[:, 0:256], "B%d" % DB[b], "FW%d" % b)
+
+        def signs():
+            act(T.SG[:], T.WN[:].indirect(BL), "P4 bits pm1 pm2 wn0 LS", "SG", scale=RAISE)
+            act(T.H16[:, 32:34], T.WN[:, 19:32:8], "P4", "HO", scale=RAISE, bias=-15 * RAISE)
+
+        def holds():
+            for s in range(2):
+                ts(T.MH[:, 256 * s:256 * s + 256], T.I16[:], T.WN[:, 19 + 8 * s:20 + 8 * s], 1.0 - RAISE, A.is_gt, A.subtract, "I16 P4", "MH%d" % s)
+
+        def marks():
+            tt(T.BD[:, 0:64], T.WN[:, 0:40].indirect(BI), T.CB[:], A.is_equal, "P4 bits wn0 LS CB", "bd0")
+            tt(T.EM[:, 0:128], T.WN[:, 0:40].indirect(EI), T.CE[:], A.is_equal, "P4 bits wn0 LS CE0 CE1 CE", "em0")
+        for i in (1, 2):
+            act(T.WN[:, 24 + 16 * i:40 + 16 * i], T.WN[:, 0:16], "bits", "pm%d" % i, scale=-2.0 * i, bias=1.0 * i)
         if t == 0:
-            number_rows()
-            rows_b()
             word_order()
-            lists()
+            rows_b()
         else:
             unpack()
-        for s in range(2):
-            ts(T.MH[:, 256 * s:256 * s + 256], T.I16[:], T.WN[:, 19 + 8 * s:20 + 8 * s], 1.0 - RAISE, A.is_gt, A.subtract, "I16 P4", "MH%d" % s)
         for h in range(2):
+            act(T.HB[:, 256 * h:256 * h + 256], B(h)[:, 0:256], "B%d" % h, "HB%d" % h)
+        if t == 0:
+            rows_c()
+            lists()
+        else:
+            holds()
+            marks()
+
+        def turn1(h):
             scan(T.DS[:, 512 * h:512 * h + 256], T.NEG[:], T.HB[:, 256 * h:256 * h + 256], 0.0, A.add, A.max, "NEG HB%d" % h, "DR%d" % h)
-        for h in range(2):
+
+        def turn2(h):
             scan(T.DS[:, 512 * h + 256:512 * h + 512], T.NEG[:], T.HB[:, 256 * h:256 * h + 256], T.DS[:, 512 * h + 255:512 * h + 256], A.add, A.max,
                  "NEG DR%d HB%d" % (h, h), "DS%d" % h)
             act(T.DG[:, 256 * h:256 * h + 256], T.DS[:, 512 * h + 256:512 * h + 512].indirect(T.PL[:]), "DS%d PL" % h, "DG%d" % h)
             act(T.DH[:, 256 * h:256 * h + 256], T.DG[:, 256 * h:256 * h + 256], "DG%d" % h, "DH%d" % h, bias=2055.5)
-        tt(T.BD[:, 0:64], T.WN[:].indirect(BI), T.CB[:], A.is_equal, "P4 bits wn0 LS CB", "bd0")
-        tt(T.EM[:, 0:128], T.WN[:].indirect(EI), T.CE[:], A.is_equal, "P4 bits wn0 LS CE0 CE1 CE", "em0")
-
-        def signs():
-            act(T.SG[:, 64:96], T.WN[:].indirect(BL), "P4 bits wn0 LS", "sg")
-            act(T.H16[:, 32:34], T.WN[:, 19:32:8], "P4", "HO", scale=RAISE, bias=-15 * RAISE)
-            for a, b, m, c in ((0, 4, -2, 1), (4, 12, 1, 0), (12, 20, -2, 1), (20, 28, 1, 0), (28, 32, -2, 1)):
-                act(T.SG[:, a:b], T.SG[:, 64 + a:64 + b], "sg", "", "SG", scale=m * RAISE, bias=c * RAISE)
-            act(T.SG[:, 32:64], T.SG[:, 64:96], "sg", "", "SG", scale=-4 * RAISE, bias=2 * RAISE)
-            act(T.BD[:, 64:128], T.BD[:, 0:64], "bd0", "BD", scale=-256 * UNIT)
-            act(T.EM[:, 128:256], T.EM[:, 0:128], "em0", "EM", scale=1 / UNIT)
-        signs()
-        if t == 0:
-            for h in range(2):
-                act(T.MTT[:, 2 * h + 1::4], T.MTT[:, 2 * h::4], "mt%d" % h, "mu%d" % h)
-        else:
-            window()
 
         def high(h):
             ts(T.DT[:, 2 * h::4], T.DH[:, 256 * h:256 * h + 256], 2048.0, None, A.subtract, None, "DH%d" % h, "dh%d" % h)
@@ -415,122 +446,185 @@ def rank_program(g, core, T, topo):
 
         def table():
             quant(T.DQ[:], T.DP[:], T.DT[:], "dh0 dw0 dh1 dw1", "DQ DP")
+            for b in range(4):
+                s, o = b % 2, 256 * (b // 2)
+                if t == 0 and b == 2:
+                    order(1)
+                mm(B(b)[:, 0:256], T.DQ[:, 128 * s:128 * s + 128], T.DP[:, 128 * s:128 * s + 128], T.MTQ[:, o:o + 256], T.MTS[:, o:o + 256], True, True,
+                   "DQ DP MQ%d" % (b // 2), "B%d" % b)
+
+        def order(i):
             if t == 0:
-                quant(T.MTQ[:], T.MTS[:], T.MTT[:], "mt0 mt1 mu0 mu1", "MTQ MTS")
-            for s in range(2):
-                mm(B(s)[:], T.DQ[:, 128 * s:128 * s + 128], T.DP[:, 128 * s:128 * s + 128], T.MTQ[:], T.MTS[:], True, True, "DQ DP MTQ MTS", "B%d" % s)
+                quant(T.MTQ[:, 256 * i:256 * i + 256], T.MTS[:, 256 * i:256 * i + 256], T.MTT[:, 1024 * i:1024 * i + 1024], "MT%d" % i, "MQ%d" % i)
 
         def block(s):
-            scan(T.HH[:, 256 * s:256 * s + 256], T.MH[:, 256 * s:256 * s + 256], B(s)[:, 256:512], 0.0, A.add, A.max, "MH%d B%d" % (s, s), "HH%d" % s)
+            scan(T.HH[:, 256 * s:256 * s + 256], T.MH[:, 256 * s:256 * s + 256], B(2 + s)[:, 0:256], 0.0, A.add, A.max, "MH%d B%d" % (s, 2 + s), "HH%d" % s)
             act(T.H16[:, 16 * s:16 * s + 16], T.HH[:, 256 * s + 15:256 * s + 256:16], "HH%d HO" % s, "H16%d" % s, bias=T.H16[:, 32 + s:33 + s])
+
+        WL, H, NK = T["WL%d" % t], T.HL[:, 0:32], T.HL[:, 32:64]
 
         def same(k):
             ts(T.EK[:, 32 * k:32 * k + 32], T.YY[:, 0:32], 4 ** k, None, A.bitwise_and, None, "YY", "ek%d" % k)
-        WL, H, NK = T["WL%d" % t], T.HL[:, 0:32], T.HL[:, 32:64]
-        for s in range(2):
-            ts(T.YY[:, 16 * s:16 * s + 16], WL[:], T.W4[:, 135 + 8 * s:136 + 8 * s], float(TOP), A.subtract, A.add, "WL%d W4" % t, "", "YY")
-        ts(T.YY[:, 32:64], T.YY[:, 0:32], TOP, None, A.bitwise_and, None, "YY", "y1")
-        same(0)
-        ts(NK, T.YY[:, 32:64], float(TOP), 2.0 * TOP, A.not_equal, A.mult, "y1", "nk0 nk1")
-        same(1)
-        tt(H, T.YY[:, 32:64], NK, A.min, "y1 nk0 nk1", "H")
-        same(2)
-        between = {(0, 0): lambda: high(0), (0, 2): lambda: low(0), (1, 0): lambda: same(3), (1, 2): lambda: high(1), (2, 0): lambda: same(4),
-                   (2, 2): lambda: low(1), (3, 0): lambda: same(5), (3, 2): table, (4, 0): lambda: same(6),
-                   (5, 2): lambda: block(0), (6, 2): lambda: block(1)}
-        for k in range(8):
+
+        def sums():
+            for s in range(2):
+                ts(T.YY[:, 16 * s:16 * s + 16], WL[:], T.W2[:, 23 + 8 * s:24 + 8 * s], float(TOP), A.subtract, A.add, "WL%d W3" % t, "", "YY")
+
+        def best(k):
             scan(T.RR[:, 32 * k:32 * k + 32], H1, H, 0.0, A.mult, A.max, "H1 H", "rr%d" % k)
-            if (k, 0) in between:
-                between[k, 0]()
-            if k == 7:
-                break
+
+        def live(k):
             for s in range(2):
                 ts(T.HL[:, 32 + 16 * s:48 + 16 * s], T.EK[:, 32 * k + 16 * s:32 * k + 16 * s + 16], T.RR[:, 32 * k + 16 * s + 15:32 * k + 16 * s + 16],
                    1.5 * 4 ** k - TOP, A.subtract, A.is_ge, "ek%d rr%d" % (k, k), "nk%d" % s)
-            tt(H, H, NK, A.mult, "H nk0 nk1", "H")
-            if (k, 2) in between:
-                between[k, 2]()
+        chain = [sums,
+                 lambda: ts(T.YY[:, 32:64], T.YY[:, 0:32], TOP, None, A.bitwise_and, None, "YY", "y1"),
+                 lambda: ts(NK, T.YY[:, 32:64], float(TOP), 2.0 * TOP, A.not_equal, A.mult, "y1", "nk0 nk1"),
+                 lambda: tt(H, T.YY[:, 32:64], NK, A.min, "y1 nk0 nk1", "H")]
+        for k in range(8):
+            chain.append(lambda k=k: best(k))
+            if k < 7:
+                chain += [lambda k=k: live(k), lambda: tt(H, H, NK, A.mult, "H nk0 nk1", "H")]
+
         K = T.KK[:, 0:16]
-        tt(K, T.RR[:, 15::16], T.TK[:], A.is_gt, "TK " + " ".join("rr%d" % k for k in range(8)), "K")
+
+        def kept(i):
+            a, b, o = ((0, 4, 0), (4, 7, 0), (0, 8, 16))[i]
+            tt(T.KK[:, o + 2 * a:o + 2 * b], T.RR[:, 32 * a + 15:32 * b:16], T.TK[:, 2 * a:2 * b], A.is_gt, "TK " + " ".join("rr%d" % k for k in range(a, b)), "K%d" % i)
+
+        def raised(n):
+            tt(T.UU[:, 32 * n:32 * n + 32], K.indirect(LS[:, 2 * n:2 * n + 2]), T.SG[:, 32 * n:32 * n + 32], A.mult, "K0 K1 LS SG", "UU%d" % n)
+        CU = (T.UU[:, 64:80], T.AL[:, 48:64])
+
+        def summed(n):
+            scan(CU[n], T.HS[:, 64 + 16 * n:80 + 16 * n], T.UU[:, 32 * n:32 * n + 16], 0.0, A.mult, A.add, "HC UU%d" % n, "CU%d" % n)
+
+        def strides(n):
+            tt(T.AL[:, 32 * n:32 * n + 16], T.UU[:, 32 * n + 16:32 * n + 32], CU[n], A.subtract, "UU%d CU%d" % (n, n), "al%d" % n)
+            if n == 0:
+                ts(T.AL[:, 16:32:8], T.UU[:, 67:80:8], -1.0, -256 * UNIT, A.mult, A.add, "CU0", "al2")
+                for s in range(2):
+                    act(T.INC[:, 256 * s:256 * s + 256], T.AL[:, 0:32].indirect(LS[:, 48 + 16 * s:64 + 16 * s]), "al0 al2 LS", "INC%d" % s)
+
+        def borders(n):
+            tt(T.IN2[:, 32 * n:32 * n + 32], T.AL[:, 32 * n:32 * n + 32].indirect(LS[:, 10 + 2 * n:12 + 2 * n]), T.BD[:, 64 + 32 * n:96 + 32 * n], A.add,
+               ("al0 al2", "al1 CU1")[n] + " LS BD", "IN2%d" % n)
+
+        def start(s):
+            return T.UU[:, 71 + 8 * s:72 + 8 * s]
+
+        def blocks(s):
+            scan(T.O[:, 256 * s:256 * s + 256], T.INC[:, 256 * s:256 * s + 256], B(s)[:, 0:256], start(s), A.add, A.max, "INC%d B%d CU0" % (s, s), "O%d" % s)
+
+        def runs(n):
+            for s in range(2):
+                o, d = 32 * n + 16 * s, (T.H16[:, 16 * s:16 * s + 16], T.O[:, 256 * s + 15:256 * s + 256:16])[n]
+                scan(T.O2[:, o:o + 16], T.IN2[:, o:o + 16], d, start(s), A.add, A.max, "IN2%d CU0 %s%d" % (n, ("H16", "O")[n], s), "", "O2%d" % n)
+
+        def ends(n):
+            tt(T.PK[:, 64 * n:64 * n + 64], T.O2[:, 32 * n:32 * n + 32].indirect(PI), T.EM[:, 128 + 64 * n:192 + 64 * n], A.mult, "O2%d LS EM" % n, "PK%d" % n)
+
+        def picked(n):
+            scan(T.PK[:, 128 + 64 * n:192 + 64 * n], T.RST[:], T.PK[:, 64 * n:64 * n + 64], 0.0, A.mult, A.add, "RST PK%d" % n, "PS%d" % n)
+
+        def scaled():
+            signs()
+            act(T.BD[:, 64:128], T.BD[:, 0:64], "bd0", "BD", scale=-256 * UNIT)
+            act(T.EM[:, 128:256], T.EM[:, 0:128], "em0", "EM", scale=1 / UNIT)
+        LB, lb, lk = T["LB%d" % t], "LB%d" % t, "LK%d" % t
+
+        def flags():
+            turn(T.YT[:, 96:128], T.YT[:, 64:96], "KM", "TK2")
+            for q in range(8):
+                dma("Y" if q % 2 == 0 else "A", LB[16 * q:16 * q + 16, 16:32], T.YT[q::16, 96:128], "dk%d" % t, "TK2", "", lk)
+
+        def P(f, *a):
+            return lambda: f(*a)
+        for f in (turn1, turn2):
+            for h in range(2):
+                f(h)
+        if t == 0:
+            lists_b()
+            marks()
+            holds()
+        scaled()
+        weave(chain, [None, P(same, 0), P(same, 1), P(same, 2), None, P(order, 0), P(same, 3),
+                      P(high, 0), P(low, 0), P(same, 4), P(high, 1), P(low, 1), P(same, 5), table,
+                      P(kept, 0), P(raised, 0), P(summed, 0), P(strides, 0), P(same, 6), P(borders, 0), P(block, 0), P(block, 1),
+                      P(blocks, 0), P(kept, 1), P(blocks, 1)])
         if t == 0:
             quant(T.ELQ[:], T.ELS[:], T.ELT[:], "ELT", "ELQ ELS")
             unpack()
-        tt(T.UU[:, 0:64], K.indirect(KL), T.SG[:, 0:64], A.mult, "K LS SG", "UU")
-        ts(T.YT[:, 64:96], K.indirect(LS[:, 30 + 2 * t:32 + 2 * t]), -1048832.0, 1048576.0, A.mult, A.add, "K LS", "KM")
-        scan(T.UU[:, 64:96], HC, T.UU[:, 0:32], 0.0, A.mult, A.add, "HC UU", "CU")
-        tt(T.AL[:, 0:32], T.UU[:, 32:64], T.UU[:, 64:96], A.subtract, "UU CU", "al1")
-        ts(T.AL[:, 32:34], T.UU[:, 67:96:16], -1.0, -256 * UNIT, A.mult, A.add, "CU", "al2")
-        al = "al0 al1 al2 LS"
-        act(T.INC[:, 256:512], T.AL[:].indirect(LS[:, 64:80]), al, "INC1")
-        cp(T.INC[:, 0:256], T.AL[:].indirect(LS[:, 48:64]), al, "INC0")
-        tt(T.IN2[:], T.AL[:].indirect(AI2), T.BD[:, 64:128], A.add, al + " BD", "IN2")
-        if t == 0:
-            window()
-        for s in range(2):
-            scan(T.O[:, 256 * s:256 * s + 256], T.INC[:, 256 * s:256 * s + 256], B(s)[:, 0:256], T.UU[:, 71 + 16 * s:72 + 16 * s], A.add, A.max,
-                 "INC%d B%d CU" % (s, s), "O%d" % s)
-        for s in range(2):
-            scan(T.O2[:, 16 * s:16 * s + 16], T.IN2[:, 16 * s:16 * s + 16], T.H16[:, 16 * s:16 * s + 16], T.UU[:, 71 + 16 * s:72 + 16 * s], A.add, A.max,
-                 "IN2 H16%d CU" % s, "", "O2")
-        for s in range(2):
-            scan(T.O2[:, 32 + 16 * s:48 + 16 * s], T.IN2[:, 32 + 16 * s:48 + 16 * s], T.O[:, 256 * s + 15:256 * s + 256:16], T.UU[:, 75 + 16 * s:76 + 16 * s],
-                 A.add, A.max, "IN2 O%d CU" % s, "", "O2")
-        tt(T.PK[:, 0:128], T.O2[:].indirect(PI), T.EM[:, 128:256], A.mult, "O2 LS EM", "PK")
-        scan(T.PK[:, 128:256], T.RST[:], T.PK[:, 0:128], 0.0, A.mult, A.add, "RST PK", "PS")
-        tt(T.YT[:, 0:32], T.PK[:, 128:256].indirect(LS[:, 36 + 2 * t:38 + 2 * t]), T.YT[:, 64:96], A.min, "PS LS KM", "YT")
-        turn(T.YT[:, 32:64], T.YT[:, 0:32], "YT", "TR")
-        LB, lb = T["LB%d" % t], "LB%d" % t
+        weave([P(raised, 1), P(summed, 1), P(strides, 1), P(borders, 1), P(runs, 1), P(ends, 1), P(picked, 1),
+               lambda: tt(T.YT[:, 0:32], T.PK[:, 128:256].indirect(LS[:, 36 + 2 * t:38 + 2 * t]), T.YT[:, 64:96], A.min, "PS0 PS1 LS KM", "YT"),
+               lambda: turn(T.YT[:, 32:64], T.YT[:, 0:32], "YT", "TR")],
+              [P(kept, 2),
+               lambda: ts(T.YT[:, 64:96], T.KK[:, 16:32].indirect(LS[:, 30 + 2 * t:32 + 2 * t]), -1048832.0, 1048576.0, A.mult, A.add, "K2 LS", "KM"),
+               flags, P(runs, 0), P(ends, 0), P(picked, 0)])
         for q in range(8):
-            dma("Y" if q % 2 == 0 else "A", LB[16 * q:16 * q + 16, :], T.YT[q::16, 32:64], "dl%d" % t, "TR", "", lb)
+            dma("Y" if q % 2 == 0 else "A", LB[16 * q:16 * q + 16, 0:16], T.YT[q::16, 32:64], "dl%d" % t, "TR", "", lb)
+        window()
         if t == 0:
             late()
-            cp(T.URQ[:, 128:384].bitcast(dt.uint32), T.UQ[:].bitcast(dt.uint32).indirect(T.UL[:, 8:24]), "UQ UL", "URQ1")
-            act(T.URS[:, 128:384], T.US[:].indirect(T.UL[:, 8:24]), "US UL", "URS1")
-        if t == 1:
-            quant(T.VQ[:], T.VS[:], T.VT[:], "VT", "VQ VS")
         L, JL, D = T.LF, T.JL[:, 0:16], T.DL[:, 32:48]
+        C, DN = T.WC[:, 64:80], T.WC[:, 80:81]
+
+        def within():
+            for i in range(2):
+                scan(T.WC[:, 32 + 16 * i:48 + 16 * i], T.NEG[:, 0:16], T.DL[:, 96 + 16 * i:112 + 16 * i], T.WC[:, 16 * i + 15:16 * i + 16],
+                     A.max, A.add, "NEG dt sa", "", "cb")
+
+        def firsts():
+            cp(T.AU[:], T.AI[:, 0:16], "ai", "AU")
+            for b in range(4):
+                act(T.GW[:, 256 * b:256 * b + 256], T.FW[:, 256 * b:256 * b + 256].indirect(T.AU[:]), "FW%d AU" % b, "GW%d" % b)
 
         def mean(b):
             tt(T.XW[:, 352 * b:352 * b + 256], T.GW[:, 256 * b:256 * b + 256], B(DB[b])[:, 0:256], A.add, "GW%d B%d" % (b, DB[b]), "XZ%d" % b)
-        ts(D, LB[:], 0.0, None, A.is_ge, None, lb, "dl")
-        tt(T.AI[:, 16:32], T.JL[:, 32:48], LB[:], A.subtract, lb + " JB", "ai0")
-        scan(T.DL[:, 1:17], T.NEG[:, 0:16], D, sc(14), A.max, A.add, "dl NEG s14", "pm")
-        ts(T.AI[:, 0:16], T.AI[:, 16:32], 255, None, A.bitwise_and, None, "ai0", "ai")
-        turn(T.DL[:, 64:128], T.DL[:, 0:64], "dl pm", "dt")
-        cp(T.AU[:], T.AI[:, 0:16], "ai", "AU")
-        for b in range(4):
-            act(T.GW[:, 256 * b:256 * b + 256], T.FW[:, 256 * b:256 * b + 256].indirect(T.AU[:]), "FW%d AU" % b, "GW%d" % b)
-        scan(T.WC[:, 0:32], H1, T.DL[:, 64:96], 0.0, A.mult, A.add, "H1 dt", "sa")
-        ts(L[:, 0:16], D, -1024.0, None, A.mult, None, "dl", "l1")
-        for i in range(2):
-            scan(T.WC[:, 32 + 16 * i:48 + 16 * i], T.NEG[:, 0:16], T.DL[:, 96 + 16 * i:112 + 16 * i], T.WC[:, 16 * i + 15:16 * i + 16],
-                 A.max, A.add, "NEG dt sa", "", "cb")
-        tt(L[:, 16:32], L[:, 0:16], JL, A.add, "l1 JL", "l2")
-        turn(T.WC[:, 64:96], T.WC[:, 32:64], "cb", "ct")
-        C, DN = T.WC[:, 64:80], T.WC[:, 80:81]
-        ts(L[:, 32:48], C, DN, None, A.subtract, None, "ct", "l5")
-        tt(L[:, 48:64], L[:, 16:32], C, A.subtract, "l2 ct", "l6")
-        tt(L[:, 64:80], L[:, 32:48], L[:, 48:64], A.max, "l5 l6", "l7")
-        mean(0)
-        ts(T.PU[:], L[:, 64:80], DN, None, A.add, None, "l7 ct", "PU")
-        ts(L[:, 80:96], L[:, 64:80], DN, 256.0, A.add, A.add, "l7 ct", "pos")
-        op("V", lambda: v.tensor_copy(T.LR[:].indirect(T.PU[:]), T.ICOL[:]), "PU ICOL", "LR")
-        mean(1)
-        scan(T.LM[:], T.MK[:, 0:96], T.LR[:, 0:96], 0.0, A.add, A.max, "MK mk1 LR", "ln")
-        mean(2)
-        ts(T.LU[:, 0:6], T.LM[:, 15::16], T.MK[:, 127:128], None, A.subtract, None, "ln mk0", "LU")
-        mean(3)
-        for b in (0, 2, 1, 3):
+
+        def mosaic(b):
             o, i = T.ET[:, b:384:4], T.XW[:, 352 * b:352 * b + 256].indirect(T.LU[:, 0:6])
             if b < 2:
                 act(o, i, "XZ%d LU" % b, "", "ET", scale=2.0 ** -6)
             else:
                 ts(o, i, 2.0 ** -6, None, A.mult, None, "XZ%d LU" % b, "", "ET")
+        weave([lambda: ts(D, LB[:, 16:32], 0.0, None, A.is_ge, None, lk, "dl"),
+               lambda: scan(T.DL[:, 1:17], T.NEG[:, 0:16], D, sc(14), A.max, A.add, "dl NEG s14", "pm"),
+               lambda: turn(T.DL[:, 64:128], T.DL[:, 0:64], "dl pm", "dt"),
+               lambda: scan(T.WC[:, 0:32], H1, T.DL[:, 64:96], 0.0, A.mult, A.add, "H1 dt", "sa"),
+               within,
+               lambda: turn(T.WC[:, 64:96], T.WC[:, 32:64], "cb", "ct"),
+               lambda: (ts(L[:, 32:48], C, DN, None, A.subtract, None, "ct", "l5"), tt(L[:, 48:64], L[:, 16:32], C, A.subtract, "l2 ct", "l6")),
+               lambda: tt(L[:, 64:80], L[:, 32:48], L[:, 48:64], A.max, "l5 l6", "l7"),
+               lambda: ts(T.PU[:], L[:, 64:80], DN, None, A.add, None, "l7 ct", "PU"),
+               lambda: op("V", lambda: v.tensor_copy(T.LR[:].indirect(T.PU[:]), T.ICOL[:]), "PU ICOL", "LR"),
+               lambda: scan(T.LM[:], T.MK[:, 0:96], T.LR[:, 0:96], 0.0, A.add, A.max, "MK mk1 LR", "ln"),
+               lambda: ts(T.LU[:, 0:6], T.LM[:, 15::16], T.MK[:, 143:144], None, A.subtract, None, "ln mk0", "LU")],
+              [None, lambda: ts(L[:, 0:16], D, -1024.0, None, A.mult, None, "dl", "l1"), None,
+               lambda: tt(L[:, 16:32], L[:, 0:16], JL, A.add, "l1 JL", "l2"), None,
+               lambda: tt(T.AI[:, 16:32], T.JL[:, 32:48], LB[:, 0:16], A.subtract, lb + " JB", "ai0"),
+               lambda: ts(T.AI[:, 0:16], T.AI[:, 16:32], 255, None, A.bitwise_and, None, "ai0", "ai"),
+               firsts,
+               lambda: ts(L[:, 80:96], L[:, 64:80], DN, 256.0, A.add, A.add, "l7 ct", "pos"),
+               P(mean, 0), P(mean, 1), P(mean, 2)])
+        mosaic(0)
+        mosaic(1)
+        mean(3)
+        mosaic(2)
+        mosaic(3)
         quant(T.EQ[:], T.ES[:], T.ET[:], "ET ET4", "EQ ES")
         remote(T["AC%d" % t][:, 0:96].bitcast(dt.uint8), T.EQ[:, 0:96].bitcast(dt.uint8), "ca%d" % t, "lc%d" % t, "EQ", "AC%d" % t)
         remote(T["AS%d" % t][:, 0:96], T.ES[:, 0:96], "ca%d" % t, "lc%d" % t, "ES", "AS%d" % t)
         ts(L[:, 96:112], L[:, 80:96], 352.0, 4096.0, A.is_lt, A.mult, "pos", "m0")
+        if t == 0:
+            steps(1)
+        if t == 1:
+            quant(T.VQ[:], T.VS[:], T.VT[:], "VT", "VQ VS")
         tt(L[:, 112:128], L[:, 96:112], L[:, 80:96], A.min, "m0 pos", "m1")
+        if t == 0:
+            steps(2)
+        if t == 1:
+            fill(T.AF[:], 0.0, "AF")
         tt(L[:, 128:144], L[:, 112:128], JL, A.max, "m1 JL", "m2")
         cp(T.SU[:], L[:, 128:144], "m2", "SU")
         if last:
@@ -547,19 +641,27 @@ def rank_program(g, core, T, topo):
             mm(B(DB[b])[:, 0:128], T.ELQ[:, 128 * b:128 * b + 128], T.ELS[:, 128 * b:128 * b + 128], AC[:], AS[:], False, True, "ELQ ELS AC%d AS%d" % (t, t), "", kb)
         for b in range(4):
             kb, o, i = "B%d" % DB[b], T.XW[:, 352 * b + 256:352 * b + 352], B(DB[b])[:, 0:96]
-            o2, i2 = T.XT[:, b::4], T.XW[:, 352 * b:352 * b + 352].indirect(T.SU[:])
+            win, r = T.XW[:, 352 * b:352 * b + 352], "XZ%d XT%d SU" % (b, b)
             if b % 2 == 0:
                 act(o, i, kb, "XT%d" % b, scale=2.0)
-                act(o2, i2, "XZ%d XT%d SU" % (b, b), "", "XT", scale=2.0 ** -6)
+                act(T.XT[:, b::4], win.indirect(T.SU[:]), r, "", "XT", scale=2.0 ** -6)
             else:
                 ts(o, i, 2.0, None, A.mult, None, kb, "XT%d" % b)
-                ts(o2, i2, 2.0 ** -6, None, A.mult, None, "XZ%d XT%d SU" % (b, b), "", "XT")
-    quant(T.XQ[:], T.XS[:], T.XT[:], "XT", "XQ0 XQ1")
-    dma("Y", T.oc[:], T.XQ[:].bitcast(dt.uint8), "dout", "XQ0 XQ1")
+            if b == 1:
+                ts(T.XT[:, b::4], win.indirect(T.SU[:]), 2.0 ** -6, None, A.mult, None, r, "", "XT")
+            if b == 3:
+                ts(T.XT[:, 3:512:4], win.indirect(T.SU[:, 0:8]), 2.0 ** -6, None, A.mult, None, r, "X30")
+                act(T.XT[:, 515::4], win.indirect(T.SU[:, 8:16]), r, "X31", scale=2.0 ** -6)
+    for h in range(2):
+        a, b = 128 * h, 128 * h + 128
+        quant(T.XQ[:, a:b], T.XS[:, a:b], T.XT[:, 4 * a:4 * b], "XT X3%d" % h, "XQ%d" % h)
+        dma("Y", T.oc[:, 4 * a:4 * b], T.XQ[:, a:b].bitcast(dt.uint8), "dout", "XQ%d" % h)
+        mm(B(2 + h)[:, 0:128], T.VQ[:], T.VS[:], T.XQ[:, a:b], T.XS[:, a:b], True, True, "VQ VS XQ%d" % h, "B%d" % (2 + h))
+    cp(T.YO[:, 0:128], B(2)[:, 0:128], "B2", "YO0")
+    dma("Y", T.y[:, 0:128], T.YO[:, 0:128], "dout", "YO0")
     for k in range(4):
         dma("A", T.osc[4 * k:4 * k + 4, :], T.XS[32 * k:32 * k + 4, :], "dout", "XQ0 XQ1")
-    mm(B(3)[:, 0:256], T.VQ[:], T.VS[:], T.XQ[:], T.XS[:], True, True, "VQ VS XQ0 XQ1", "B3")
-    cp(T.YO[:], B(3)[:, 0:256], "B3", "YO")
-    dma("Y", T.y[:], T.YO[:], "dout", "YO")
+    cp(T.YO[:, 128:256], B(3)[:, 0:128], "B3", "YO1")
+    dma("Y", T.y[:, 128:256], T.YO[:, 128:256], "dout", "YO1")
     for s in sorted(tot):
         need("G", [(s, tot[s])])

@@ -9,34 +9,35 @@ for _n, _w, _d in [
         ("HMT", 1024, BF), ("HMQ", 256, F8), ("HMS", 256, U8), ("MTT", 2048, BF), ("MTQ", 512, F8), ("MTS", 512, U8),
         ("ICOL", 256, F32), ("VB", 256, BF), ("I8", 144, BF), ("I16", 256, BF), ("JP", 128, BF), ("TH", 144, F32),
         ("IP", 16, I32), ("SC", 24, F32), ("UI", 30, I32), ("UL", 30, U16), ("PLF", 16, F32), ("PL", 16, U16),
-        ("RW", 32, F32), ("FR", 152, F32), ("FS", 136, F32), ("LS", 80, U16), ("KC", 768, BF),
+        ("RW", 32, F32), ("FR", 160, F32), ("FS", 136, F32), ("LS", 80, U16), ("KC", 768, BF),
         ("CB", 64, F32), ("CE", 128, F32), ("RST", 64, F32), ("TK", 16, F32), ("H4", 128, F32), ("HS", 96, F32),
-        ("NEG", 256, BF), ("JL", 48, F32), ("MK", 256, F32),
+        ("NEG", 256, BF), ("JL", 32, F32), ("MK", 256, F32),
         ("XQ", 256, F8), ("XS", 256, U8), ("XT", 1024, BF), ("BT", 608, BF), ("BQ", 152, F8), ("BS", 152, U8),
         ("W4", 128, F32), ("W2", 32, F32), ("WN", 72, F32), ("SG", 64, F32),
         ("OT", 1024, BF), ("OQ", 256, F8), ("OS", 256, U8), ("HB", 512, BF), ("DS", 1024, BF), ("DG", 512, BF), ("DH", 512, BF),
         ("DT", 1024, BF), ("DQ", 256, F8), ("DP", 256, U8), ("MH", 512, BF), ("HH", 512, F32), ("H16", 34, F32),
-        ("BD", 128, F32), ("EM", 256, F32), ("YY", 64, I32), ("EK", 224, I32), ("HL", 64, F32), ("RR", 256, F32),
-        ("KK", 32, F32), ("UU", 80, F32), ("AL", 64, F32), ("INC", 512, F32), ("IN2", 64, F32), ("O", 512, F32), ("O2", 64, F32),
-        ("PK", 256, F32), ("YT", 128, F32), ("AI", 32, I32), ("LF", 160, F32), ("DL", 128, F32), ("WC", 96, F32), ("AF", 64, F32),
-        ("AU", 16, U16), ("PU", 16, U16), ("LU", 8, U16), ("SU", 16, U16), ("LR", 256, F32), ("LM", 96, F32),
-        ("FW", 1024, BF), ("GW", 1024, BF), ("XW", 1408, BF), ("ET", 512, BF), ("EQ", 128, F8), ("ES", 128, U8), ("YO", 256, F32)]:
+        ("BD", 128, F32), ("EM", 256, F32), ("YY", 96, I32), ("EK", 256, I32), ("HL", 64, F32), ("RR", 256, F32),
+        ("KK", 48, F32), ("UU", 80, F32), ("AL", 64, F32), ("INC", 512, F32), ("IN2", 64, F32), ("O", 512, F32), ("O2", 64, F32),
+        ("PK", 256, F32), ("YT", 128, F32), ("AI", 96, I32), ("TU", 32, U16), ("LF", 160, F32), ("DL", 128, F32), ("WC", 96, F32),
+        ("AF", 64, F32), ("AU", 16, U16), ("PU", 16, U16), ("LU", 8, U16), ("SU", 16, U16), ("LR", 256, F32), ("LM", 96, F32),
+        ("FW", 1280, BF), ("GW", 768, BF), ("XW", 1408, BF), ("ET", 512, BF), ("EQ", 128, F8), ("ES", 128, U8), ("YO", 256, F32)]:
     SCRATCH[_n] = ("sbuf", [128, _w], _d)
 for _t in range(3):
     SCRATCH["MS%d" % _t] = ("sbuf", [128, 16], F32)
     SCRATCH["WL%d" % _t] = ("sbuf", [128, 16], F32)
-    SCRATCH["LB%d" % _t] = ("sbuf", [128, 32], F32)
     SCRATCH["AC%d" % _t] = ("sbuf", [128, 128], F8)
     SCRATCH["AS%d" % _t] = ("sbuf", [128, 128], U8)
 for _b in range(8):
     SCRATCH["B%d" % _b] = ("psum", [128, 512], F32)
-SEMAPHORES = ["cV", "cA", "cP", "cG", "dx", "du", "dv", "dw", "dfill", "dout"]
+SEMAPHORES = ["cV", "cA", "cP", "cG", "dx", "dy", "du", "dv", "dw", "dfill", "dout"]
 for _t in range(3):
     SEMAPHORES += ["wa%d" % _t, "ca%d" % _t, "lw%d" % _t, "lc%d" % _t, "dl%d" % _t, "dk%d" % _t]
 
 RAISE = 2.0 ** -6
 UNIT = 2.0 ** -17
 TOP = 0x15555
+CYCLE, WAKE, ISSUE, LOCAL, REMOTE, TURNS = 0.001, 0.12, 0.05, 1.5, 2.0, 6
+PATIENCE = {"V": 16.0, "A": 30.0, "P": 1.0, "G": 2.0, "Y": 1.0}
 
 
 def rank_program(g, core, T, topo):
@@ -46,67 +47,8 @@ def rank_program(g, core, T, topo):
     mate = T.cores[rank + 1 if rank % 2 == 0 else rank - 1]
     A, AF = AluOpType, ActivationFunctionType
     Q = {"V": g.vector, "A": g.scalar, "P": g.tensor, "G": g, "Y": g.sync}
-    own = {"V": "cV", "A": "cA", "P": "cP", "G": "cG", "Y": None}
-    tot, lastw, readers, epoch, known = {}, {}, {}, {}, {e: {} for e in Q}
-
-    def need(e, toks):
-        for s, v in sorted(toks):
-            n = tot[s] if v is None else v
-            if known[e].get(s, 0) < n:
-                Q[e].wait_ge(T.sem[s], n)
-                known[e][s] = n
-
-    def deps(e, r, w, add, compute):
-        toks = {}
-
-        def put(tk, war=False):
-            s, v = tk
-            if war and compute and s == own[e]:
-                return
-            n = tot[s] if v is None else v
-            toks[s] = max(toks.get(s, 0), n)
-        for k in r:
-            for tk in lastw[k]:
-                put(tk)
-            if k[0] == "B" and k[1:].isdigit():
-                for tk in readers.get(k, []):
-                    put(tk, True)
-        for k in w:
-            for tk in lastw.get(k, []):
-                put(tk)
-            for tk in readers.get(k, []):
-                put(tk, True)
-        for k in add:
-            if readers.get(k):
-                epoch[k] = [(tk, False) for tk in lastw.get(k, [])] + [(tk, True) for tk in readers[k]]
-                lastw[k], readers[k] = [], []
-            for tk, war in epoch.get(k, []):
-                put(tk, war or e == "P")
-        need(e, list(toks.items()))
-
-    def note(tk, r, w, add):
-        for k in r:
-            readers.setdefault(k, []).append(tk)
-        for k in w:
-            lastw[k], readers[k], epoch[k] = [tk], [], [(tk, False)]
-        for k in add:
-            lastw.setdefault(k, []).append(tk)
-
-    def op(e, f, r, w="", add=""):
-        r, w, add = r.split(), w.split(), add.split()
-        deps(e, r, w, add, True)
-        s = own[e]
-        f().then_inc(T.sem[s], 1)
-        tot[s] = tot.get(s, 0) + 1
-        note((s, tot[s]), r, w, add)
-
-    def dma(e, out, in_, s, r, w="", add=""):
-        r, w, add = r.split(), w.split(), add.split()
-        deps(e, r, w, add, False)
-        Q[e].dma_start(out, in_).then_inc(T.sem[s], 16)
-        tot[s] = tot.get(s, 0) + 16
-        note((s, None), r, w, add)
-
+    own = {"V": "cV", "A": "cA", "P": "cP", "G": "cG"}
+    v, ac, pe = g.vector, g.scalar, g.tensor
     eng = topo.engines(core, mate)
     ne = 1
     while ne * 2 <= len(eng):
@@ -116,552 +58,525 @@ def rank_program(g, core, T, topo):
         msk |= 1 << _e
     rid, pid = topo.addr(mate)[:2]
 
-    def remote(out, in_, rs, ls, r, w):
-        deps("G", r.split(), [], [], False)
-        g.remote_dma(out_ap=out, in_ap=in_, remote_sem=T.sem[rs], local_sem=T.sem[ls], pid=pid, routing_id=rid, dma_engine_mask=msk)
-        tot[ls] = tot.get(ls, 0) + ne
-        tot[rs] = tot.get(rs, 0) + ne
-        note((ls, None), r.split(), [], [])
-        for k in w.split():
-            lastw.setdefault(k, []).append((rs, None))
+    calls = []
 
-    v, ac, pe = g.vector, g.scalar, g.tensor
+    def call(e, f, sems, r, w, add, busy, late=0.0):
+        calls.append({"e": e, "f": f, "sems": sems, "r": r.split(), "w": w.split(), "add": add.split(), "busy": busy, "late": late})
+
+    def op(e, f, r, w, add, cycles):
+        call(e, lambda: f().then_inc(T.sem[own[e]], 1), [(own[e], 1)], r, w, add, cycles * CYCLE)
+
+    def dma(e, out, in_, s, r, w="", add=""):
+        call(e, lambda: Q[e].dma_start(out, in_).then_inc(T.sem[s], 16), [(s, 16)], r, w, add, ISSUE, LOCAL)
+
+    def remote(out, in_, rs, ls, r, w):
+        call("G", lambda: g.remote_dma(out_ap=out, in_ap=in_, remote_sem=T.sem[rs], local_sem=T.sem[ls], pid=pid, routing_id=rid, dma_engine_mask=msk),
+             [(ls, ne), (rs, ne)], r, "", w, 3 * ISSUE, REMOTE)
+
+    def track(seq, meet):
+        lastw, readers, epoch, raised = {}, {}, {}, {}
+        for i in seq:
+            c = calls[i]
+
+            def after(j, war, landed):
+                d = calls[j]
+                s = d["sems"][-1 if landed else 0][0]
+                if s == own.get(d["e"]):
+                    meet(i, j, s, not (war and c["e"] == d["e"] and c["sems"][0][0] == s))
+                else:
+                    for k in raised[s]:
+                        meet(i, k, s, True)
+            for k in c["r"]:
+                for j in lastw[k]:
+                    after(j, False, True)
+                if k[0] == "B" and k[1:].isdigit():
+                    for j in readers.get(k, []):
+                        if calls[j]["e"] != c["e"]:
+                            after(j, True, False)
+            for k in c["w"]:
+                for j in lastw.get(k, []):
+                    after(j, False, True)
+                for j in readers.get(k, []):
+                    after(j, True, False)
+            for k in c["add"]:
+                if readers.get(k):
+                    epoch[k] = [(j, False) for j in lastw.get(k, [])] + [(j, True) for j in readers[k]]
+                    lastw[k], readers[k] = [], []
+                for j, war in epoch.get(k, []):
+                    after(j, war or c["e"] == "P", not war)
+            meet(i, None, None, None)
+            for s, n in c["sems"]:
+                raised.setdefault(s, []).append(i)
+            for k in c["r"]:
+                readers.setdefault(k, []).append(i)
+            for k in c["w"]:
+                lastw[k], readers[k], epoch[k] = [i], [], [(i, False)]
+            for k in c["add"]:
+                lastw.setdefault(k, []).append(i)
+
+    def arrange():
+        n = len(calls)
+        pre, post = [{} for c in calls], [{} for c in calls]
+        busy = [c["busy"] for c in calls]
+
+        def meet(i, j, s, wait):
+            if j is not None:
+                pre[i][j] = post[j][i] = max(pre[i].get(j, 0.0), calls[j]["late"] + WAKE if wait else 0.0)
+        track(range(n), meet)
+
+        def lay(before, behind, rank, first):
+            left, ready, free, seq, end = [len(p) for p in before], list(first), {e: 0.0 for e in Q}, [], [0.0] * n
+            pool = {e: [i for i in range(n) if calls[i]["e"] == e and not before[i]] for e in Q}
+            while len(seq) < n:
+                t0, e = min((max(free[e], min(ready[i] for i in pool[e])), e) for e in Q if pool[e])
+                i = max(pool[e], key=lambda i: (rank[i] - PATIENCE[e] * max(0.0, ready[i] - t0), -i))
+                pool[e].remove(i)
+                seq.append(i)
+                free[e] = end[i] = max(t0, ready[i]) + busy[i]
+                for k, d in behind[i].items():
+                    ready[k] = max(ready[k], end[i] + d)
+                    left[k] -= 1
+                    if not left[k]:
+                        pool[calls[k]["e"]].append(k)
+            return seq, end
+        products = [i for i in range(n) if calls[i]["e"] == "P"]
+        for j, i in zip(products, products[1:]):
+            meet(i, j, None, False)
+        late, tail = [c["late"] for c in calls], [0.0] * n
+        for i in reversed(range(n)):
+            tail[i] = busy[i] + max([late[i]] + [d + tail[k] for k, d in post[i].items()])
+        best = None
+        for turns in range(TURNS):
+            seq, end = lay(pre, post, tail, [0.0] * n)
+            span = max(end[i] + late[i] for i in range(n))
+            if best is None or span < best[0]:
+                best = (span, seq)
+            tail = lay(post, pre, end, late)[1]
+        return best[1]
+
+    def issue(seq):
+        tot, count, known, want = {}, {}, {e: {} for e in Q}, {}
+
+        def meet(i, j, s, wait):
+            c = calls[i]
+            if j is None:
+                for s in sorted(want):
+                    if known[c["e"]].get(s, 0) < want[s]:
+                        Q[c["e"]].wait_ge(T.sem[s], want[s])
+                        known[c["e"]][s] = want[s]
+                want.clear()
+                c["f"]()
+                for s, n in c["sems"]:
+                    tot[s] = tot.get(s, 0) + n
+                    count[i, s] = tot[s]
+            elif wait:
+                want[s] = max(want.get(s, 0), count[j, s])
+        track(seq, meet)
+        for s in sorted(tot):
+            if known["G"].get(s, 0) < tot[s]:
+                g.wait_ge(T.sem[s], tot[s])
+
+    def ind(win, off):
+        return (win.indirect(off), 16 * off.shape[1])
+
+    def bare(a):
+        return a[0] if isinstance(a, tuple) else a
+
+    def cycles(out, *ins, least=64, each=1.0, fast=False):
+        if isinstance(out, tuple):
+            return 50 + 3.8 * out[1]
+        if isinstance(ins[0], tuple):
+            return 50 + 1.6 * ins[0][1]
+        if fast and all(SCRATCH[a.name][2] in (BF, U16) for a in (out,) + ins):
+            each = 0.5
+        return max(least, each * out.shape[1])
 
     def ts(out, in0, s1, s2, o0, o1, r, w="", add=""):
         if o1 is None:
-            op("V", lambda: v.tensor_scalar(out, in0, s1, None, o0), r, w, add)
+            op("V", lambda: v.tensor_scalar(out, bare(in0), s1, None, o0), r, w, add, cycles(out, in0, fast=True))
         else:
-            op("V", lambda: v.tensor_scalar(out, in0, s1, s2, o0, o1), r, w, add)
+            op("V", lambda: v.tensor_scalar(out, bare(in0), s1, s2, o0, o1), r, w, add, cycles(out, in0, fast=True))
 
     def tt(out, a, b, o, r, w="", add=""):
-        op("V", lambda: v.tensor_tensor(out, a, b, o), r, w, add)
+        both = isinstance(a, tuple) or all(SCRATCH[x.name][0] == "sbuf" for x in (a, b))
+        op("V", lambda: v.tensor_tensor(out, bare(a), b, o), r, w, add, cycles(out, a, each=2.0 if both else 1.0))
 
     def cp(out, a, r, w="", add=""):
-        op("V", lambda: v.tensor_copy(out, a), r, w, add)
+        op("V", lambda: v.tensor_copy(bare(out), bare(a)), r, w, add, cycles(out, a, fast=True))
 
     def scan(out, d0, d1, ini, o0, o1, r, w="", add=""):
-        op("V", lambda: v.tensor_tensor_scan(out, d0, d1, ini, o0, o1), r, w, add)
+        op("V", lambda: v.tensor_tensor_scan(out, d0, d1, ini, o0, o1), r, w, add, cycles(out, d0, d1, fast=True))
 
     def turn(out, a, r, w):
-        op("V", lambda: v.transpose(out, a), r, w)
+        op("V", lambda: v.transpose(out, a), r, w, "", cycles(out, a))
 
     def fill(ap, c, w="", add=""):
-        op("V", lambda: v.memset(ap, c), "", w, add)
+        op("V", lambda: v.memset(ap, c), "", w, add, cycles(ap, ap, fast=True))
 
     def quant(c, s, t, r, w):
-        op("V", lambda: v.quantize_mx(c, s, t), r, w)
+        op("V", lambda: v.quantize_mx(c, s, t), r, w, "", 15 + 0.28 * t.shape[1])
 
     def act(out, in_, r, w="", add="", scale=1.0, bias=None):
+        n = cycles(out, in_, least=100)
         if bias is not None:
-            op("A", lambda: ac.activation(out, in_, AF.Identity, bias=bias, scale=scale), r, w, add)
+            op("A", lambda: ac.activation(out, bare(in_), AF.Identity, bias=bias, scale=scale), r, w, add, n)
         elif scale == 1.0:
-            op("A", lambda: ac.activation(out, in_, AF.Copy), r, w, add)
+            op("A", lambda: ac.activation(out, bare(in_), AF.Copy), r, w, add, n)
         else:
-            op("A", lambda: ac.activation(out, in_, AF.Copy, scale=scale), r, w, add)
+            op("A", lambda: ac.activation(out, bare(in_), AF.Copy, scale=scale), r, w, add, n)
 
     def row(out, n, a, b, w="", add=""):
         act(out, T.ICOL[:, 0:n], "ICOL", w, add, scale=float(a), bias=float(b))
 
     def mm(out, l, ls, rr, rs, a, z, r, w="", add=""):
-        op("P", lambda: pe.matmul_mx(out, l, ls, rr, rs, a, z), r, w, add)
+        op("P", lambda: pe.matmul_mx(out, l, ls, rr, rs, a, z), r, w, add, 1.25 * (out.shape[1] + 16))
 
-    def iota(out, pat, base, ch, w, flag=True):
+    def iota(out, pat, base, ch, w, add="", flag=True):
         if flag:
-            op("G", lambda: g.iota(out, pat, base, ch, allow_small_or_imprecise_dtypes=True), "", w)
+            op("G", lambda: g.iota(out, pat, base, ch, allow_small_or_imprecise_dtypes=True), "", w, add, 130 + 2 * out.shape[1])
         else:
-            op("G", lambda: g.iota(out, pat, base, ch), "", w)
+            op("G", lambda: g.iota(out, pat, base, ch), "", w, add, 130 + 2 * out.shape[1])
 
-    def where0(out, in_, pat, base, r, add):
-        op("G", lambda: g.affine_select(out, in_, pat, A.is_equal, 0.0, base, 1), r, "", add)
-
-    def weave(chain, fillers):
-        fillers = list(fillers)
-        for c in chain:
-            c()
-            if fillers:
-                f = fillers.pop(0)
-                if f:
-                    f()
-        for f in fillers:
-            if f:
-                f()
+    def where0(out, in_, pat, base, r, w="", add=""):
+        op("G", lambda: g.affine_select(out, in_, pat, A.is_equal, 0.0, base, 1), r, w, add, 170 + 2 * out.shape[1])
 
     def B(b):
         return T["B%d" % b]
 
-    IP, SC, LS = T.IP, T.SC, T.LS
+    IP, SC, LS, RW, FR, FS, MK = T.IP, T.SC, T.LS, T.RW, T.FR, T.FS, T.MK
 
     def sc(c):
         return SC[:, c:c + 1]
-    KL, BL, BI, AI2, EI, PI = LS[:, 0:4], LS[:, 26:30], LS[:, 6:10], LS[:, 10:14], LS[:, 14:22], LS[:, 22:26]
     H1, H2, HN = T.HS[:, 0:32], T.HS[:, 32:48], T.HS[:, 48:64]
 
     dma("A", T.UT[:], T.u[:], "du", "", "UT")
-    dma("Y", T.X0[:], T.x[:], "dx", "", "X0")
-    dma("Y", T.WQ[:].bitcast(dt.uint8), T.wc[:], "dw", "", "WQ")
-    dma("Y", T.WS[:], T.ws[:], "dw", "", "WS")
-    dma("Y", T.VT[:], T.v[:], "dv", "", "VT")
+    dma("Y", T.X0[:, 0:512], T.x[:, 0:512], "dx", "", "X00")
+    dma("Y", T.X0[:, 512:1024], T.x[:, 512:1024], "dy", "", "X01")
 
-    iota(IP[:, 0:1], [[0, 1]], 0, 1, "ip0", False)
-    iota(T.UI[:], [[3, 3], [0, 10]], 7 + 128, -1, "UI", False)
+    iota(IP[:, 0:1], [[0, 1]], 0, 1, "ip0", flag=False)
+    iota(T.UI[:], [[3, 3], [0, 10]], 7 + 128, -1, "UI", flag=False)
     iota(T.I16[:], [[0, 16], [1, 16]], 0, 0, "I16")
     iota(T.I8[:], [[1, 18], [0, 8]], 0, 0, "I8")
-    iota(SC[:, 4:8], [[-2, 2], [128, 2]], 0, 1, "s4")
-    iota(T.JP[:], [[4, 4], [1, 2], [16, 16]], 0, 0, "JP")
+    iota(SC[:, 4:8], [[-8, 2], [128, 2]], 0, 1, "s4")
+    iota(T.JP[:], [[1, 4], [4, 2], [16, 16]], 0, 0, "JP")
     iota(T.ICOL[:], [[1, 256]], 0, 0, "ICOL")
-    fill(T.CT[:], 0.0, "CT")
+    iota(T.VB[:], [[1, 256]], 0, 0, "VB")
+    for z in range(4):
+        iota(FR[:, 128 + 2 * z::8], [[0, 2], [64, 2]], 31 - (16 >> z), 0, "", "EA")
+    iota(T.PLF[:], [[-8, 2], [-1, 4], [-4, 2]], 255, 0, "PLF")
+    iota(FR[:, 0:16], [[1, 2], [0, 2], [2, 4]], 0, 0, "", "FR")
+    iota(FR[:, 112:128], [[8, 2], [-40, 2], [-1, 4]], 47, 0, "", "FR")
+    for c, pat, base in ((0, [[8, 2], [0, 2]], 0), (4, [[-4, 2], [16, 2]], 0), (8, [[-4, 2], [8, 2]], 20), (12, [[0, 2], [8, 2]], 0),
+                         (16, [[7, 2], [0, 2]], 12), (20, [[16, 4]], 0)):
+        iota(RW[:, c:c + 4], pat, base, 0, "rw%d" % c)
+    iota(IP[:, 8:14], [[-6, 3], [0, 2]], 48, 1, "ip8", flag=False)
+    iota(T.JL[:, 16:32], [[16, 16]], 0, 0, "JLF")
+    fill(T.KC[:, 256:768], 32.0, "KC1")
+    fill(T.KC[:, 0:256], UNIT, "KC0")
+    fill(T.CT[:, 0:512], 0.0, "CT0")
     fill(T.BT[:], 0.0, "BT")
+    for nm, a, k in (("CT", 512, "CT1"), ("CT", 1024, "CT2"), ("HMT", 0, "hz0"), ("HMT", 512, "hz1"), ("OT", 0, "oz0"), ("OT", 512, "oz1")):
+        act(T[nm][:, a:a + 512], T.KC[:, 256:768], "KC1", k, scale=0.0)
+    fill(T.H4[:], 4.0, "H4")
+    fill(T.H4[:, 0::8], 0.0, "H4")
+    row(T.HS[:, 32:64], 32, 0, 2, "HS2")
+    row(T.HS[:, 32:48:8], 2, 0, 0, "", "HS2")
+    row(T.HS[:, 48:64:4], 4, 0, 0, "", "HS2")
+    row(T.HS[:, 0:32], 32, 0, 1, "H1")
+    row(T.HS[:, 0:32:16], 2, 0, 0, "H1")
+    row(T.HS[:, 64:96], 32, 0, 1, "HC")
+    row(T.HS[:, 64:80:8], 2, 0, 0, "", "HC")
+    row(T.HS[:, 80:96:4], 4, 0, 0, "", "HC")
+    row(T.NEG[:], 256, 0, -1, "NEG")
+    for o, n, z in ((17, 2, 0), (18, 4, 1), (20, 8, 2), (24, 16, 3), (16, 16, 4)):
+        row(FR[:, o:32:n], 16 // n, 0, z, "", "FR")
+    for o, n, z in ((0, 8, 1), (8, 4, 2), (12, 2, 3), (14, 2, 3)):
+        row(FR[:, 48 + o:48 + o + n], n, 1 << z, (1 << z) - 1, "", "FR")
+        if o < 14:
+            row(FR[:, 32 + o:32 + o + max(n, 4)], max(n, 4), 0, z, "", "FR")
+    act(FR[:, 129::2], FR[:, 128::2], "EA", "EB", bias=32.0)
+    for i in range(3):
+        o = -6 * i % 16
+        act(FR[:, 64 + 16 * i:80 + 16 * i], FR[:, 128 + o:144 + o], "EA EB", "", "FR")
+    for o, n in ((1, 2), (2, 4), (4, 8)):
+        act(T.CB[:, o::n], T.I16[:, o:64:n], "I16", "", "CB", scale=1.0 / n, bias=-o / n)
+    act(T.CB[:, 0::8], T.I16[:, 0:64:8], "I16", "", "CB", scale=-0.125, bias=1.0)
+    for o, n in ((0, 16), (16, 8), (24, 4), (28, 2)):
+        row(T.CE[:, o:o + n:2], n // 2, 2, 1, "", "CE0")
+        row(T.CE[:, o + 1:o + n:2], n // 2, 2, 0, "", "CE0")
+    row(T.CE[:, 30:32], 2, 0, -1, "", "CE0")
+    act(T.CE[:, 32:64], T.CE[:, 0:32], "CE0", "CE1")
+    act(T.CE[:, 64:128], T.CE[:, 0:64], "CE0 CE1", "CE")
+    row(T.WN[:, 32:40], 8, 0, 0, "wn0")
+    row(T.AL[:, 16:32], 16, 0, 0, "al2")
+    row(T.KK[:, 0:16], 16, 0, 0, "K0 K1")
+    row(T.DL[:, 0:64], 64, 0, 0, "dl pm p0")
+    row(T.ET[:, 384:512], 128, 0, 0, "ET4")
+    row(T.AF[:], 64, 0, 0, "af")
     ts(IP[:, 1:2], IP[:, 0:1], 15, None, A.bitwise_and, None, "ip0", "ip1")
     ts(IP[:, 2:3], IP[:, 0:1], 4, None, A.arith_shift_right, None, "ip0", "ip2")
-    ts(T.UI[:], T.UI[:], 7, None, A.bitwise_and, None, "UI", "UI")
-    fill(T.H4[:], 4.0, "H4")
-    for c, i, a in ((1, 1, 0.0), (2, 2, 0.0), (3, 2, 8.0)):
-        ts(sc(c), IP[:, i:i + 1], a, None, A.add, None, "ip%d" % i, "s%d" % c)
-    ts(T.UL[:], T.UI[:], 16, None, A.mult, None, "UI", "UL")
-    fill(T.H4[:, 0::8], 0.0, "H4")
     ts(IP[:, 3:4], IP[:, 0:1], 5, None, A.arith_shift_right, None, "ip0", "ip3")
     ts(IP[:, 4:5], IP[:, 2:3], 1, None, A.bitwise_and, None, "ip2", "ip4")
+    for c, i, a in ((1, 1, 0.0), (2, 2, 0.0), (3, 2, 8.0)):
+        ts(sc(c), IP[:, i:i + 1], a, None, A.add, None, "ip%d" % i, "s%d" % c)
     ts(sc(8), IP[:, 1:2], -16.0, 255.0, A.mult, A.add, "ip1", "s8")
-    for s in range(2):
-        ts(T.CT[:, s:512:4], T.I16[:, 0:128], sc(2 + s), None, A.is_equal, None, "I16 s%d" % (2 + s), "", "CT")
-    ts(sc(9), IP[:, 3:4], -4.0, sc(8), A.mult, A.add, "ip3 s8", "s9")
+    ts(sc(9), IP[:, 3:4], -1.0, sc(8), A.mult, A.add, "ip3 s8", "s9")
+    ts(sc(10), IP[:, 4:5], -4.0, sc(9), A.mult, A.add, "ip4 s9", "s10")
+    act(sc(11), sc(10), "s10", "s11", bias=-8.0)
+    ts(sc(12), IP[:, 1:2], 0.0, None, A.is_equal, None, "ip1", "s12")
+    act(sc(16), sc(1), "s1", "s16", scale=16.0)
+    act(SC[:, 17:19], SC[:, 10:12], "s10 s11", "s17", scale=-1.0, bias=131072.0 + 255.0)
+    row(T.RST[:], 64, 0, -1e9, "RST")
+    for o in (0, 16, 24, 28, 30):
+        act(T.RST[:, o::32], SC[:, 17:19], "s17", "", "RST")
+    act(T.JL[:, 0:16], T.JL[:, 16:32], "JLF s1", "JL", bias=sc(1))
+    act(T.DL[:, 0:1], sc(12), "s12", "p0", scale=-1.0)
     ts(T.TH[:], T.I8[:], sc(1), 1e29, A.not_equal, A.mult, "I8 s1", "TH")
-    ts(sc(10), IP[:, 4:5], -1.0, sc(9), A.mult, A.add, "ip4 s9", "s10")
-    for s in range(2):
-        for h in range(2):
-            ts(T.CT[:, 512 * s + 512 + h:512 * s + 1024:4], T.JP[:], sc(4 + 2 * s + h), None, A.is_equal, None, "JP s4", "", "CT")
     fill(T.TH[:, 136:144], 0.0, "TH")
-    for a in range(0, 1024, 256):
-        act(T.HMT[:, a:a + 256], T.I16[:], "I16", "", "HMT", scale=0.0)
-    epoch["HMT"] = [(tk, False) for tk in lastw["HMT"]]
-    quant(T.UQ[:], T.US[:], T.UT[:], "UT", "UQ US")
-    ts(sc(11), sc(10), -2.0, None, A.add, None, "s10", "s11")
+    scan(T.RR[:, 0:8], T.H4[:, 1:65:8], T.NEG[:, 0:8], 0.25, A.mult, A.max, "H4 NEG", "rr0")
+    for s in range(2):
+        act(T.TK[:, s::2], T.RR[:, 0:8], "rr0", "", "TK", scale=-2.0, bias=float(TOP))
+    for s in range(2):
+        ts(T.CT[:, s:512:4], T.I16[:, 0:128], sc(2 + s), None, A.is_equal, None, "I16 s%d" % (2 + s), "", "CT0")
+        for h in range(2):
+            ts(T.CT[:, 512 * s + 512 + h:512 * s + 1024:4], T.JP[:], sc(4 + 2 * s + h), None, A.is_equal, None, "JP s4", "", "CT%d" % (1 + s))
+        ts(T.HMT[:, s::4], T.VB[:], sc(10 + s), 256.0, A.is_equal, A.mult, "VB s%d hz0 hz1" % (10 + s), "", "HMT")
+    for i in range(3):
+        quant(T.CQ[:, 128 * i:128 * i + 128], T.CS[:, 128 * i:128 * i + 128], T.CT[:, 512 * i:512 * i + 512], "CT%d" % i, "CQ%d" % i)
+    quant(T.HMQ[:], T.HMS[:], T.HMT[:], "HMT", "HMQ")
+    for i in range(4):
+        where0(T.MTT[:, i:1024:4], T.KC[:, 0:256], [[-1, 256]], 128 * (i // 2), "KC0", "", "MT0")
+        where0(T.MTT[:, 1024 + i::4], T.KC[:, 0:256], [[-1, 16], [-16, 16]], 128 * (i // 2), "KC0", "", "MT1")
+        where0(T.ELT[:, 512 * i:512 * i + 512], T.KC[:, 256:768], [[-1, 128], [128, 4]], -128 * i, "KC1", "ET%d" % (5 + i))
+        quant(T.ELQ[:, 128 * i:128 * i + 128], T.ELS[:, 128 * i:128 * i + 128], T.ELT[:, 512 * i:512 * i + 512], "ET%d" % (5 + i), "EL%d" % i)
+    for i in range(2):
+        quant(T.MTQ[:, 256 * i:256 * i + 256], T.MTS[:, 256 * i:256 * i + 256], T.MTT[:, 1024 * i:1024 * i + 1024], "MT%d" % i, "MQ%d" % i)
+    ts(T.UI[:], T.UI[:], 7, None, A.bitwise_and, None, "UI", "UI")
+    ts(T.UL[:], T.UI[:], 16, None, A.mult, None, "UI", "UL")
+    quant(T.UQ[:], T.US[:], T.UT[:], "UT", "UQ")
+    for i in range(3):
+        cp(T.URQ[:, 144 * i:144 * i + 144].bitcast(dt.uint32), ind(T.UQ[:].bitcast(dt.uint32), T.UL[:, 10 * i:10 * i + 9]), "UQ UL", "URQ%d" % i)
+        act(T.URS[:, 144 * i:144 * i + 144], ind(T.US[:], T.UL[:, 10 * i:10 * i + 9]), "UQ UL", "URS%d" % i)
+    ts(MK[:, 128:256], T.I16[:, 0:128], sc(1), 8000.0, A.not_equal, A.mult, "I16 s1", "mk0")
+    tt(MK[:, 1:128], MK[:, 129:256], MK[:, 128:255], A.subtract, "mk0", "MK")
+    act(MK[:, 0:1], MK[:, 128:129], "mk0", "mk1")
+    act(MK[:, 16:128:16], MK[:, 16:128:16], "MK", "MK", bias=-3000.0)
+    scan(FS[:, 0:128], MK[:, 0:128], FR[:, 0:128], 0.0, A.add, A.max, "MK mk1 FR", "fs0")
+    ts(FS[:, 128:136], FS[:, 15:128:16], MK[:, 143:144], None, A.subtract, None, "fs0 mk0", "FS")
+    ks, tz, z1, p1, bs = [FS[:, 128 + i:129 + i] for i in (0, 1, 2, 3, 7)]
+    ts(T.PL[:], T.PLF[:], sc(16), None, A.subtract, None, "PLF s16", "PL")
+    ts(LS[:, 0:4], RW[:, 0:4], ks, None, A.add, None, "rw0 FS", "Lk")
+    ts(sc(13), tz, 2.0, None, A.is_le, None, "FS", "s13")
+    ts(RW[:, 28:32], RW[:, 8:12], tz, 30.0, A.subtract, A.subtract, "rw8 FS", "rw28")
+    ts(LS[:, 6:10], RW[:, 28:32], sc(13), 32.0, A.mult, A.add, "rw28 s13", "Li")
+    ts(RW[:, 24:28], RW[:, 16:20], sc(12), tz, A.mult, A.add, "rw16 s12 FS", "rw24")
+    tt(RW[:, 24:28], RW[:, 24:28], RW[:, 12:16], A.add, "rw24 rw12", "rw24")
+    cp(LS[:, 10:14], RW[:, 24:28], "rw24", "La")
+    ts(LS[:, 14:22:2], RW[:, 8:12], 3.0, None, A.add, None, "rw8", "", "Le")
+    ts(LS[:, 15:22:2], RW[:, 8:12], z1, 3.0, A.subtract, A.add, "rw8 FS", "", "Le")
+    ts(LS[:, 22:26:2], RW[:, 20:22], sc(1), None, A.add, None, "rw20 s1", "", "Lp")
+    ts(LS[:, 23:26:2], RW[:, 20:22], p1, None, A.add, None, "rw20 FS", "", "Lp")
+    ts(LS[:, 26:30], RW[:, 4:8], bs, None, A.add, None, "rw4 FS", "Lb")
+    ts(IP[:, 8:14], IP[:, 8:14], 15, None, A.bitwise_and, None, "ip8", "ip8")
+    cp(LS[:, 30:36], IP[:, 8:14], "ip8", "Lg")
+    ts(LS[:, 42:48], IP[:, 8:14], 16.0, 15.0, A.mult, A.add, "ip8", "Lr")
+    for s in range(2):
+        cp(LS[:, 36 + s:42:2], FS[:, 132:135], "FS", "", "Ls")
+        ts(LS[:, 48 + 16 * s:64 + 16 * s], T.PLF[:], 0.0, RW[:, 24 + s:25 + s], A.mult, A.add, "PLF rw24", "Ln%d" % s)
 
-    def steps(i):
-        cp(T.URQ[:, 144 * i:144 * i + 144].bitcast(dt.uint32), T.UQ[:].bitcast(dt.uint32).indirect(T.UL[:, 10 * i:10 * i + 9]), "UQ UL", "URQ%d" % i)
-        act(T.URS[:, 144 * i:144 * i + 144], T.US[:].indirect(T.UL[:, 10 * i:10 * i + 9]), "US UL", "URS%d" % i)
-    steps(0)
-
-    def rows():
-        row(T.HS[:, 32:64], 32, 0, 2, "HS2")
-        row(T.NEG[:], 256, 0, -1, "NEG")
-        row(T.HS[:, 32:48:8], 2, 0, 0, "HS2")
-        row(T.HS[:, 48:64:4], 4, 0, 0, "", "HS2")
-        for o, n, z in ((17, 2, 0), (18, 4, 1), (20, 8, 2), (24, 16, 3), (16, 16, 4)):
-            row(T.FR[:, o:32:n], 16 // n, 0, z, "", "FR")
-        for o, n, z in ((0, 8, 1), (8, 4, 2), (12, 2, 3), (14, 2, 3)):
-            row(T.FR[:, 48 + o:48 + o + n], n, 1 << z, (1 << z) - 1, "", "FR")
-            if o < 14:
-                row(T.FR[:, 32 + o:32 + o + max(n, 4)], max(n, 4), 0, z, "", "FR")
-        row(T.HS[:, 0:32], 32, 0, 1, "H1")
-        for i in range(3):
-            o = -3 * i % 8
-            act(T.FR[:, 64 + 16 * i:80 + 16 * i], T.FR[:, 128 + o:144 + o], "EB", "", "FR")
-        row(T.HS[:, 0:32:16], 2, 0, 0, "H1")
-        row(T.WN[:, 32:40], 8, 0, 0, "wn0")
-
-    def rows_b():
-        for o, n in ((1, 2), (2, 4), (4, 8)):
-            act(T.CB[:, o::n], T.I16[:, o:64:n], "I16", "", "CB", scale=1.0 / n, bias=-o / n)
-        act(T.CB[:, 0::8], T.I16[:, 0:64:8], "I16", "", "CB", scale=-0.125, bias=1.0)
-        for o, n in ((0, 16), (16, 8), (24, 4), (28, 2)):
-            row(T.CE[:, o:o + n:2], n // 2, 2, 1, "", "CE0")
-            row(T.CE[:, o + 1:o + n:2], n // 2, 2, 0, "", "CE0")
-        row(T.CE[:, 30:32], 2, 0, -1, "", "CE0")
-
-    def rows_c():
-        act(T.CE[:, 32:64], T.CE[:, 0:32], "CE0", "CE1")
-        row(T.HS[:, 64:96], 32, 0, 1, "HC")
-        act(T.CE[:, 64:128], T.CE[:, 0:64], "CE0 CE1", "CE")
-        row(T.RST[:], 64, 0, 1, "RST")
-        row(T.HS[:, 64:80:8], 2, 0, 0, "", "HC")
-        row(T.HS[:, 80:96:4], 4, 0, 0, "", "HC")
-        for o in (0, 16, 24, 28, 30):
-            row(T.RST[:, o::32], 2, 0, 0, "", "RST")
-        row(T.AL[:, 16:32], 16, 0, 0, "al2")
-        row(T.KK[:, 0:16], 16, 0, 0, "K0 K1")
-
-    def number_rows():
-        for z in range(4):
-            op("G", lambda: g.iota(T.FR[:, 128 + z::4], [[0, 3], [64, 2]], 31 - (16 >> z), 0, allow_small_or_imprecise_dtypes=True), "", "", "EB")
-        iota(T.PLF[:], [[-2, 2], [-4, 4], [-1, 2]], 255, 0, "PLF")
-        iota(T.FR[:, 0:16], [[1, 2], [0, 2], [2, 4]], 0, 0, "FR0")
-        iota(T.FR[:, 112:128], [[8, 2], [-40, 2], [-1, 4]], 47, 0, "FR7")
-        for c, pat, base in ((0, [[8, 2], [0, 2]], 0), (4, [[-4, 2], [16, 2]], 0), (8, [[-4, 2], [8, 2]], 20), (12, [[0, 2], [8, 2]], 0),
-                             (16, [[7, 2], [0, 2]], 12), (20, [[16, 4]], 0)):
-            iota(T.RW[:, c:c + 4], pat, base, 0, "rw%d" % c)
-        iota(IP[:, 8:11], [[-3, 3]], 24, 1, "ip8", False)
-        iota(T.JL[:, 16:32], [[16, 16]], 0, 0, "JLF")
-
-    def falling_order():
-        for s in range(2):
-            ts(T.HMT[:, s::4], T.VB[:], sc(10 + s), 256.0, A.is_equal, A.mult, "VB s%d" % (10 + s), "", "HMT")
-        quant(T.HMQ[:], T.HMS[:], T.HMT[:], "HMT", "HMQ HMS")
-
-    def word_order():
-        for i in range(4):
-            where0(T.MTT[:, i:1024:4], T.KC[:, 0:256], [[-1, 256]], 128 * (i // 2), "KC0", "MT0")
-        for i in range(4):
-            where0(T.MTT[:, 1024 + i::4], T.KC[:, 0:256], [[-1, 16], [-16, 16]], 128 * (i // 2), "KC0", "MT1")
-        for b in range(4):
-            where0(T.ELT[:, 512 * b:512 * b + 512], T.KC[:, 256:768], [[-1, 128], [128, 4]], -128 * b, "KC1", "ELT")
-
-    def lists():
-        ts(T.MK[:, 128:256], T.I16[:, 0:128], sc(1), 8000.0, A.not_equal, A.mult, "I16 s1", "mk0")
-        ts(sc(16), IP[:, 1:2], 16.0, None, A.mult, None, "ip1", "s16")
-        tt(T.MK[:, 1:128], T.MK[:, 129:256], T.MK[:, 128:255], A.subtract, "mk0", "MK")
-        cp(T.MK[:, 0:1], T.MK[:, 128:129], "mk0", "mk1")
-        ts(T.MK[:, 16:128:16], T.MK[:, 16:128:16], 3000.0, None, A.subtract, None, "MK", "MK")
-        ts(T.PL[:], T.PLF[:], sc(16), None, A.subtract, None, "PLF s16", "PL")
-        ts(IP[:, 12:15], IP[:, 8:11], 7, None, A.bitwise_and, None, "ip8", "ip12")
-        scan(T.FS[:, 0:128], T.MK[:, 0:128], T.FR[:, 0:128], 0.0, A.add, A.max, "MK mk1 FR FR0 FR7", "fs0")
-        for s in range(2):
-            ts(LS[:, 30 + s:36:2], IP[:, 12:15], 2.0, float(s), A.mult, A.add, "ip12", "", "LS")
-        ts(T.FS[:, 128:136], T.FS[:, 15:128:16], T.MK[:, 143:144], None, A.subtract, None, "fs0 mk0", "FS")
-        ts(sc(12), IP[:, 1:2], 0.0, None, A.is_equal, None, "ip1", "s12")
-        scan(T.RR[:, 0:8], T.H4[:, 1:65:8], T.NEG[:, 0:8], 0.25, A.mult, A.max, "H4 NEG", "rr0")
-        for s in range(2):
-            ts(T.TK[:, s::2], T.RR[:, 0:8], -2.0, float(TOP), A.mult, A.add, "rr0", "", "TK")
-
-    def lists_b():
-        ks, tz, z1, p1, bs = [T.FS[:, 128 + i:129 + i] for i in (0, 1, 2, 3, 7)]
-        ts(LS[:, 14:22:2], T.RW[:, 8:12], 3.0, None, A.add, None, "rw8", "", "LS")
-        ts(sc(13), tz, 2.0, None, A.is_le, None, "FS", "s13")
-        ts(T.RW[:, 24:28], T.RW[:, 16:20], sc(12), tz, A.mult, A.add, "rw16 s12 FS", "rw24")
-        ts(T.RW[:, 28:32], T.RW[:, 8:12], tz, 30.0, A.subtract, A.subtract, "rw8 FS", "rw28")
-        ts(LS[:, 15:22:2], T.RW[:, 8:12], z1, 3.0, A.subtract, A.add, "rw8 FS", "", "LS")
-        ts(BL, T.RW[:, 4:8], bs, None, A.add, None, "rw4 FS", "", "LS")
-        tt(T.RW[:, 24:28], T.RW[:, 24:28], T.RW[:, 12:16], A.add, "rw24 rw12", "rw24")
-        ts(BI, T.RW[:, 28:32], sc(13), 32.0, A.mult, A.add, "rw28 s13", "", "LS")
-        ts(KL, T.RW[:, 0:4], ks, None, A.add, None, "rw0 FS", "", "LS")
-        ts(LS[:, 22:26:2], T.RW[:, 20:22], sc(1), None, A.add, None, "rw20 s1", "", "LS")
-        ts(LS[:, 23:26:2], T.RW[:, 20:22], p1, None, A.add, None, "rw20 FS", "", "LS")
-        cp(AI2, T.RW[:, 24:28], "rw24", "", "LS")
-        for s in range(2):
-            ts(LS[:, 36 + s:42:2], T.FS[:, 132:135], 32.0 * s, None, A.add, None, "FS", "", "LS")
-            ts(LS[:, 48 + 16 * s:64 + 16 * s], T.PLF[:], 0.0, T.RW[:, 24 + s:25 + s], A.mult, A.add, "PLF rw24", "", "LS")
-
-    def late():
-        fill(T.DL[:, 0:64], 0.0, "dl pm")
-        ts(sc(14), sc(12), -1.0, None, A.mult, None, "s12", "s14")
-        ts(T.JL[:, 0:16], T.JL[:, 16:32], sc(1), None, A.add, None, "JLF s1", "JL")
-        ts(T.JL[:, 32:48], T.JL[:, 16:32], sc(1), 131072.0, A.add, A.add, "JLF s1", "JB")
-        cp(T.DL[:, 0:1], sc(14), "s14 pm", "pm")
-        fill(T.ET[:, 384:512], 0.0, "ET4")
-
-    quant(T.CQ[:], T.CS[:], T.CT[:], "CT", "CQ CS")
-    number_rows()
-    iota(T.VB[:], [[1, 256]], 0, 0, "VB")
-    rows()
     DB = (4, 5, 6, 7)
     for t in range(3):
-        last = t == 2
         src = T.X0 if t == 0 else T.XT
         for h in range(2):
-            quant(T.XQ[:, 128 * h:128 * h + 128], T.XS[:, 128 * h:128 * h + 128], src[:, 512 * h:512 * h + 512], "X0" if t == 0 else "XT X3%d" % h, "XQ%d" % h)
+            quant(T.XQ[:, 128 * h:128 * h + 128], T.XS[:, 128 * h:128 * h + 128], src[:, 512 * h:512 * h + 512], ("X0%d" if t == 0 else "XT X3%d") % h, "XQ%d" % h)
         if t == 0:
             for i in range(3):
-                dma("Y", T["AC%d" % i][:, 96:128].bitcast(dt.uint8), T.XQ[:, 0:32].bitcast(dt.uint8), "dfill", "XQ0", "", "AC%d" % i)
-                dma("Y", T["AS%d" % i][:, 96:128], T.XS[:, 0:32], "dfill", "XQ0", "", "AS%d" % i)
+                dma("Y", T["AC%d" % i][:, 96:128].bitcast(dt.uint8), T.XQ[:, 0:32].bitcast(dt.uint8), "dfill", "XQ0", "pc%d" % i)
+                dma("Y", T["AS%d" % i][:, 96:128], T.XS[:, 0:32], "dfill", "XQ0", "ps%d" % i)
+            dma("Y", T.WQ[:].bitcast(dt.uint8), T.wc[:], "dw", "X01", "WQ")
+            dma("Y", T.WS[:], T.ws[:], "dw", "X01", "WS")
+            dma("Y", T.VT[:], T.v[:], "dv", "X01", "VT")
+            quant(T.VQ[:], T.VS[:], T.VT[:], "VT", "VQ")
         for s in range(2):
             mm(B(s)[:, 0:144], T.XQ[:, 128 * s:128 * s + 128], T.XS[:, 128 * s:128 * s + 128], T.URQ[:, 144 * t:144 * t + 144], T.URS[:, 144 * t:144 * t + 144],
                True, True, "XQ%d URQ%d URS%d" % (s, t, t), "B%d" % s)
-        if t == 0:
-            fill(T.KC[:, 0:256], UNIT, "KC0")
-            fill(T.KC[:, 256:768], 32.0, "KC1")
-        for s in range(2):
             tt(T.BT[:, s:576:4], B(s)[:, 0:144], T.TH[:], A.is_gt, "B%d TH" % s, "", "BT")
-        quant(T.BQ[:], T.BS[:], T.BT[:], "BT", "BQ BS")
-        mm(B(2)[:, 0:128], T.CQ[:, 0:128], T.CS[:, 0:128], T.BQ[:, 0:128], T.BS[:, 0:128], True, True, "CQ CS BQ BS", "B2")
-        mm(B(3)[:, 0:128], T.CQ[:, 128:256], T.CS[:, 128:256], T.BQ[:, 24:152], T.BS[:, 24:152], True, False, "CQ CS BQ BS", "B3")
-        mm(B(3)[:, 0:128], T.CQ[:, 256:384], T.CS[:, 256:384], T.BQ[:, 16:144], T.BS[:, 16:144], False, True, "CQ CS BQ BS", "", "B3")
-        if t == 0:
-            fill(T.OT[:], 0.0, "OT")
+        quant(T.BQ[:], T.BS[:], T.BT[:], "BT", "BQ")
+        mm(B(2)[:, 0:128], T.CQ[:, 0:128], T.CS[:, 0:128], T.BQ[:, 0:128], T.BS[:, 0:128], True, True, "CQ0 BQ", "B2")
+        mm(B(3)[:, 0:128], T.CQ[:, 128:256], T.CS[:, 128:256], T.BQ[:, 24:152], T.BS[:, 24:152], True, False, "CQ1 BQ", "B3")
+        mm(B(3)[:, 0:128], T.CQ[:, 256:384], T.CS[:, 256:384], T.BQ[:, 16:144], T.BS[:, 16:144], False, True, "CQ2 BQ", "", "B3")
         scan(T.W4[:], T.H4[:], B(2)[:, 0:128], 0.0, A.mult, A.add, "H4 B2", "W4")
         cp(T["MS%d" % t][:], T.W4[:, 7::8], "W4", "MS%d" % t)
         remote(T["WL%d" % t][:], T["MS%d" % t][:], "wa%d" % t, "lw%d" % t, "MS%d" % t, "WL%d" % t)
         bits = B(3)[:, 112:128]
         scan(T.W2[:, 0:16], H2, bits, 0.0, A.mult, A.add, "HS2 B3", "W2")
         scan(T.WN[:, 16:32], HN, bits, 0.0, A.mult, A.add, "HS2 B3", "P4")
-        for s in range(2):
-            ts(T.OT[:, s::4], T.VB[:], T.W2[:, 8 * s + 7:8 * s + 8], None, A.is_equal, None, "VB W2", "", "OT")
         scan(T.W2[:, 16:32], T.H4[:, 0:16], bits, 0.0, A.mult, A.add, "H4 B3", "W3")
         act(T.WN[:, 0:16], bits, "B3", "bits")
-        quant(T.OQ[:], T.OS[:], T.OT[:], "OT", "OQ OS")
-        if t == 0:
-            falling_order()
+        for s in range(2):
+            ts(T.OT[:, s::4], T.VB[:], T.W2[:, 8 * s + 7:8 * s + 8], None, A.is_equal, None, "VB W2 oz0 oz1", "", "OT")
+        quant(T.OQ[:], T.OS[:], T.OT[:], "OT", "OQ")
         for h in range(2):
-            mm(B(h)[:, 0:256], T.OQ[:, 128 * h:128 * h + 128], T.OS[:, 128 * h:128 * h + 128], T.HMQ[:], T.HMS[:], True, True, "OQ OS HMQ HMS", "B%d" % h)
+            a, b, c = 256 * h, 256 * h + 256, 512 * h + 256
+            mm(B(h)[:, 0:256], T.OQ[:, 128 * h:128 * h + 128], T.OS[:, 128 * h:128 * h + 128], T.HMQ[:], T.HMS[:], True, True, "OQ HMQ", "B%d" % h)
+            act(T.HB[:, a:b], B(h)[:, 0:256], "B%d" % h, "HB%d" % h)
+            scan(T.DS[:, c - 256:c], T.NEG[:], T.HB[:, a:b], 0.0, A.add, A.max, "NEG HB%d" % h, "DR%d" % h)
+            scan(T.DS[:, c:c + 256], T.NEG[:], T.HB[:, a:b], T.DS[:, c - 1:c], A.add, A.max, "NEG DR%d HB%d" % (h, h), "DS%d" % h)
+            act(T.DG[:, a:b], ind(T.DS[:, c:c + 256], T.PL[:]), "DS%d PL" % h, "DG%d" % h)
+            if h == 0:
+                act(T.DH[:, a:b], T.DG[:, a:b], "DG%d" % h, "DH%d" % h, bias=2055.5)
+            else:
+                ts(T.DH[:, a:b], T.DG[:, a:b], 2055.5, None, A.add, None, "DG%d" % h, "DH%d" % h)
+            ts(T.DT[:, 2 * h::4], T.DH[:, a:b], 2048.0, None, A.subtract, None, "DH%d" % h, "dh%d" % h)
+            scan(T.DT[:, 2 * h + 1::4], T.DG[:, a:b], T.DT[:, 2 * h::4], 0.0, A.max, A.subtract, "DG%d dh%d" % (h, h), "dw%d" % h)
+        quant(T.DQ[:], T.DP[:], T.DT[:], "dh0 dw0 dh1 dw1", "DQ")
 
         def unpack():
             for b in range(4):
                 mm(B(DB[b])[:, 0:256], T.ELQ[:, 128 * b:128 * b + 128], T.ELS[:, 128 * b:128 * b + 128], T.XQ[:], T.XS[:], True, True,
-                   "ELQ ELS XQ0 XQ1", "B%d" % DB[b])
-
-        def window():
-            for b in range(4):
+                   "EL%d XQ0 XQ1" % b, "B%d" % DB[b])
                 act(T.FW[:, 256 * b:256 * b + 256], B(DB[b])[:, 0:256], "B%d" % DB[b], "FW%d" % b)
-
-        def signs():
-            act(T.SG[:], T.WN[:].indirect(BL), "P4 bits pm1 pm2 wn0 LS", "SG", scale=RAISE)
-            act(T.H16[:, 32:34], T.WN[:, 19:32:8], "P4", "HO", scale=RAISE, bias=-15 * RAISE)
-
-        def holds():
-            for s in range(2):
-                ts(T.MH[:, 256 * s:256 * s + 256], T.I16[:], T.WN[:, 19 + 8 * s:20 + 8 * s], 1.0 - RAISE, A.is_gt, A.subtract, "I16 P4", "MH%d" % s)
-
-        def marks():
-            tt(T.BD[:, 0:64], T.WN[:, 0:40].indirect(BI), T.CB[:], A.is_equal, "P4 bits wn0 LS CB", "bd0")
-            tt(T.EM[:, 0:128], T.WN[:, 0:40].indirect(EI), T.CE[:], A.is_equal, "P4 bits wn0 LS CE0 CE1 CE", "em0")
+            act(T.FW[:, 1024:1280], B(DB[3])[:, 0:256], "B%d" % DB[3], "FW4")
+        if t > 0:
+            unpack()
+        for b in (2, 3, 0, 1):
+            s, o = b % 2, 256 * (b // 2)
+            mm(B(b)[:, 0:256], T.DQ[:, 128 * s:128 * s + 128], T.DP[:, 128 * s:128 * s + 128], T.MTQ[:, o:o + 256], T.MTS[:, o:o + 256], True, True,
+               "DQ MQ%d" % (b // 2), "B%d" % b)
+        act(T.H16[:, 32:34], T.WN[:, 19:32:8], "P4", "HO", scale=RAISE, bias=-15 * RAISE)
+        for s in range(2):
+            a, b = 256 * s, 256 * s + 256
+            ts(T.MH[:, a:b], T.I16[:], T.WN[:, 19 + 8 * s:20 + 8 * s], 1.0 - RAISE, A.is_gt, A.subtract, "I16 P4", "MH%d" % s)
+            scan(T.HH[:, a:b], T.MH[:, a:b], B(2 + s)[:, 0:256], 0.0, A.add, A.max, "MH%d B%d" % (s, 2 + s), "HH%d" % s)
+            act(T.H16[:, 16 * s:16 * s + 16], T.HH[:, a + 15:b:16], "HH%d HO" % s, "H16%d" % s, bias=T.H16[:, 32 + s:33 + s])
         for i in (1, 2):
             act(T.WN[:, 24 + 16 * i:40 + 16 * i], T.WN[:, 0:16], "bits", "pm%d" % i, scale=-2.0 * i, bias=1.0 * i)
+        act(T.SG[:], ind(T.WN[:], LS[:, 26:30]), "P4 bits pm1 pm2 wn0 Lb", "SG", scale=RAISE)
+        tt(T.BD[:, 0:64], ind(T.WN[:, 0:40], LS[:, 6:10]), T.CB[:], A.is_equal, "P4 bits wn0 Li CB", "bd0")
+        tt(T.EM[:, 0:128], ind(T.WN[:, 0:40], LS[:, 14:22]), T.CE[:], A.is_equal, "P4 bits wn0 Le CE0 CE1 CE", "em0")
+        act(T.BD[:, 64:128], T.BD[:, 0:64], "bd0", "BD", scale=-256 * UNIT)
+        act(T.EM[:, 128:256], T.EM[:, 0:128], "em0", "EM", scale=-1 / UNIT)
+        act(T.KK[:, 16:48], ind(T.TK[:], LS[:, 30 + 2 * t:32 + 2 * t]), "TK Lg", "TG")
         if t == 0:
-            word_order()
-            rows_b()
-        else:
             unpack()
-        for h in range(2):
-            act(T.HB[:, 256 * h:256 * h + 256], B(h)[:, 0:256], "B%d" % h, "HB%d" % h)
-        if t == 0:
-            rows_c()
-            lists()
-        else:
-            holds()
-            marks()
-
-        def turn1(h):
-            scan(T.DS[:, 512 * h:512 * h + 256], T.NEG[:], T.HB[:, 256 * h:256 * h + 256], 0.0, A.add, A.max, "NEG HB%d" % h, "DR%d" % h)
-
-        def turn2(h):
-            scan(T.DS[:, 512 * h + 256:512 * h + 512], T.NEG[:], T.HB[:, 256 * h:256 * h + 256], T.DS[:, 512 * h + 255:512 * h + 256], A.add, A.max,
-                 "NEG DR%d HB%d" % (h, h), "DS%d" % h)
-            act(T.DG[:, 256 * h:256 * h + 256], T.DS[:, 512 * h + 256:512 * h + 512].indirect(T.PL[:]), "DS%d PL" % h, "DG%d" % h)
-            act(T.DH[:, 256 * h:256 * h + 256], T.DG[:, 256 * h:256 * h + 256], "DG%d" % h, "DH%d" % h, bias=2055.5)
-
-        def high(h):
-            ts(T.DT[:, 2 * h::4], T.DH[:, 256 * h:256 * h + 256], 2048.0, None, A.subtract, None, "DH%d" % h, "dh%d" % h)
-
-        def low(h):
-            scan(T.DT[:, 2 * h + 1::4], T.DG[:, 256 * h:256 * h + 256], T.DT[:, 2 * h::4], 0.0, A.max, A.subtract, "DG%d dh%d" % (h, h), "dw%d" % h)
-
-        def table():
-            quant(T.DQ[:], T.DP[:], T.DT[:], "dh0 dw0 dh1 dw1", "DQ DP")
-            for b in range(4):
-                s, o = b % 2, 256 * (b // 2)
-                if t == 0 and b == 2:
-                    order(1)
-                mm(B(b)[:, 0:256], T.DQ[:, 128 * s:128 * s + 128], T.DP[:, 128 * s:128 * s + 128], T.MTQ[:, o:o + 256], T.MTS[:, o:o + 256], True, True,
-                   "DQ DP MQ%d" % (b // 2), "B%d" % b)
-
-        def order(i):
-            if t == 0:
-                quant(T.MTQ[:, 256 * i:256 * i + 256], T.MTS[:, 256 * i:256 * i + 256], T.MTT[:, 1024 * i:1024 * i + 1024], "MT%d" % i, "MQ%d" % i)
-
-        def block(s):
-            scan(T.HH[:, 256 * s:256 * s + 256], T.MH[:, 256 * s:256 * s + 256], B(2 + s)[:, 0:256], 0.0, A.add, A.max, "MH%d B%d" % (s, 2 + s), "HH%d" % s)
-            act(T.H16[:, 16 * s:16 * s + 16], T.HH[:, 256 * s + 15:256 * s + 256:16], "HH%d HO" % s, "H16%d" % s, bias=T.H16[:, 32 + s:33 + s])
-
         WL, H, NK = T["WL%d" % t], T.HL[:, 0:32], T.HL[:, 32:64]
-
-        def same(k):
-            ts(T.EK[:, 32 * k:32 * k + 32], T.YY[:, 0:32], 4 ** k, None, A.bitwise_and, None, "YY", "ek%d" % k)
-
-        def sums():
-            for s in range(2):
-                ts(T.YY[:, 16 * s:16 * s + 16], WL[:], T.W2[:, 23 + 8 * s:24 + 8 * s], float(TOP), A.subtract, A.add, "WL%d W3" % t, "", "YY")
-
-        def best(k):
-            scan(T.RR[:, 32 * k:32 * k + 32], H1, H, 0.0, A.mult, A.max, "H1 H", "rr%d" % k)
-
-        def live(k):
-            for s in range(2):
-                ts(T.HL[:, 32 + 16 * s:48 + 16 * s], T.EK[:, 32 * k + 16 * s:32 * k + 16 * s + 16], T.RR[:, 32 * k + 16 * s + 15:32 * k + 16 * s + 16],
-                   1.5 * 4 ** k - TOP, A.subtract, A.is_ge, "ek%d rr%d" % (k, k), "nk%d" % s)
-        chain = [sums,
-                 lambda: ts(T.YY[:, 32:64], T.YY[:, 0:32], TOP, None, A.bitwise_and, None, "YY", "y1"),
-                 lambda: ts(NK, T.YY[:, 32:64], float(TOP), 2.0 * TOP, A.not_equal, A.mult, "y1", "nk0 nk1"),
-                 lambda: tt(H, T.YY[:, 32:64], NK, A.min, "y1 nk0 nk1", "H")]
+        for s in range(2):
+            ts(T.YY[:, 32 + 16 * s:48 + 16 * s], WL[:], T.W2[:, 23 + 8 * s:24 + 8 * s], float(TOP), A.subtract, A.add, "WL%d W3" % t, "", "YY")
+        ts(T.YY[:, 64:96], T.YY[:, 32:64], TOP, None, A.bitwise_and, None, "YY", "y1")
+        ts(T.YY[:, 0:32], T.YY[:, 32:64], 4.0, None, A.mult, None, "YY", "Y4")
+        ts(NK, T.YY[:, 64:96], float(TOP), 2.0 * TOP, A.not_equal, A.mult, "y1", "nk0 nk1")
+        tt(H, T.YY[:, 64:96], NK, A.min, "y1 nk0 nk1", "H")
+        for k in range(0, 8, 2):
+            ts(T.EK[:, 32 * k:32 * k + 64], T.YY[:, 0:64], 4 ** (k + 1), None, A.bitwise_and, None, "YY Y4", "ek%d ek%d" % (k, k + 1))
         for k in range(8):
-            chain.append(lambda k=k: best(k))
+            scan(T.RR[:, 32 * k:32 * k + 32], H1, H, 0.0, A.mult, A.max, "H1 H", "rr%d" % k)
             if k < 7:
-                chain += [lambda k=k: live(k), lambda: tt(H, H, NK, A.mult, "H nk0 nk1", "H")]
-
-        K = T.KK[:, 0:16]
-
-        def kept(i):
-            a, b, o = ((0, 4, 0), (4, 7, 0), (0, 8, 16))[i]
-            tt(T.KK[:, o + 2 * a:o + 2 * b], T.RR[:, 32 * a + 15:32 * b:16], T.TK[:, 2 * a:2 * b], A.is_gt, "TK " + " ".join("rr%d" % k for k in range(a, b)), "K%d" % i)
-
-        def raised(n):
-            tt(T.UU[:, 32 * n:32 * n + 32], K.indirect(LS[:, 2 * n:2 * n + 2]), T.SG[:, 32 * n:32 * n + 32], A.mult, "K0 K1 LS SG", "UU%d" % n)
-        CU = (T.UU[:, 64:80], T.AL[:, 48:64])
-
-        def summed(n):
-            scan(CU[n], T.HS[:, 64 + 16 * n:80 + 16 * n], T.UU[:, 32 * n:32 * n + 16], 0.0, A.mult, A.add, "HC UU%d" % n, "CU%d" % n)
-
-        def strides(n):
-            tt(T.AL[:, 32 * n:32 * n + 16], T.UU[:, 32 * n + 16:32 * n + 32], CU[n], A.subtract, "UU%d CU%d" % (n, n), "al%d" % n)
-            if n == 0:
-                ts(T.AL[:, 16:32:8], T.UU[:, 67:80:8], -1.0, -256 * UNIT, A.mult, A.add, "CU0", "al2")
                 for s in range(2):
-                    act(T.INC[:, 256 * s:256 * s + 256], T.AL[:, 0:32].indirect(LS[:, 48 + 16 * s:64 + 16 * s]), "al0 al2 LS", "INC%d" % s)
-
-        def borders(n):
-            tt(T.IN2[:, 32 * n:32 * n + 32], T.AL[:, 32 * n:32 * n + 32].indirect(LS[:, 10 + 2 * n:12 + 2 * n]), T.BD[:, 64 + 32 * n:96 + 32 * n], A.add,
-               ("al0 al2", "al1 CU1")[n] + " LS BD", "IN2%d" % n)
-
-        def start(s):
-            return T.UU[:, 71 + 8 * s:72 + 8 * s]
-
-        def blocks(s):
-            scan(T.O[:, 256 * s:256 * s + 256], T.INC[:, 256 * s:256 * s + 256], B(s)[:, 0:256], start(s), A.add, A.max, "INC%d B%d CU0" % (s, s), "O%d" % s)
-
-        def runs(n):
+                    o = 32 * k + 16 * s
+                    ts(T.HL[:, 32 + 16 * s:48 + 16 * s], T.EK[:, o:o + 16], T.RR[:, o + 15:o + 16], 1.5 * 4 ** k - TOP, A.subtract, A.is_ge,
+                       "ek%d rr%d" % (k, k), "nk%d" % s)
+                tt(H, H, NK, A.mult, "H nk0 nk1", "H")
+        CU = (T.UU[:, 64:80], T.AL[:, 48:64])
+        for n, a, b in ((0, 0, 4), (1, 4, 7)):
+            o = 32 * n
+            tt(T.KK[:, 2 * a:2 * b], T.RR[:, 32 * a + 15:32 * b:16], T.TK[:, 2 * a:2 * b], A.is_gt, "TK " + " ".join("rr%d" % k for k in range(a, b)), "K%d" % n)
+            tt(T.UU[:, o:o + 32], ind(T.KK[:, 0:16], LS[:, 2 * n:2 * n + 2]), T.SG[:, o:o + 32], A.mult, "K0 K1 Lk SG", "UU%d" % n)
+            scan(CU[n], T.HS[:, 64 + 16 * n:80 + 16 * n], T.UU[:, o:o + 16], 0.0, A.mult, A.add, "HC UU%d" % n, "CU%d" % n)
+            tt(T.AL[:, o:o + 16], T.UU[:, o + 16:o + 32], CU[n], A.subtract, "UU%d CU%d" % (n, n), "al%d" % n)
+            if n == 0:
+                act(T.AL[:, 16:32:8], T.UU[:, 67:80:8], "CU0", "al2", scale=-1.0, bias=-256 * UNIT)
+            tt(T.IN2[:, o:o + 32], ind(T.AL[:, o:o + 32], LS[:, 10 + 2 * n:12 + 2 * n]), T.BD[:, 64 + o:96 + o], A.add, ("al0 al2", "al1 CU1")[n] + " La BD", "IN2%d" % n)
             for s in range(2):
-                o, d = 32 * n + 16 * s, (T.H16[:, 16 * s:16 * s + 16], T.O[:, 256 * s + 15:256 * s + 256:16])[n]
-                scan(T.O2[:, o:o + 16], T.IN2[:, o:o + 16], d, start(s), A.add, A.max, "IN2%d CU0 %s%d" % (n, ("H16", "O")[n], s), "", "O2%d" % n)
-
-        def ends(n):
-            tt(T.PK[:, 64 * n:64 * n + 64], T.O2[:, 32 * n:32 * n + 32].indirect(PI), T.EM[:, 128 + 64 * n:192 + 64 * n], A.mult, "O2%d LS EM" % n, "PK%d" % n)
-
-        def picked(n):
-            scan(T.PK[:, 128 + 64 * n:192 + 64 * n], T.RST[:], T.PK[:, 64 * n:64 * n + 64], 0.0, A.mult, A.add, "RST PK%d" % n, "PS%d" % n)
-
-        def scaled():
-            signs()
-            act(T.BD[:, 64:128], T.BD[:, 0:64], "bd0", "BD", scale=-256 * UNIT)
-            act(T.EM[:, 128:256], T.EM[:, 0:128], "em0", "EM", scale=1 / UNIT)
-        LB, lb, lk = T["LB%d" % t], "LB%d" % t, "LK%d" % t
-
-        def flags():
-            turn(T.YT[:, 96:128], T.YT[:, 64:96], "KM", "TK2")
-            for q in range(8):
-                dma("Y" if q % 2 == 0 else "A", LB[16 * q:16 * q + 16, 16:32], T.YT[q::16, 96:128], "dk%d" % t, "TK2", "", lk)
-
-        def P(f, *a):
-            return lambda: f(*a)
-        for f in (turn1, turn2):
-            for h in range(2):
-                f(h)
-        if t == 0:
-            lists_b()
-            marks()
-            holds()
-        scaled()
-        weave(chain, [None, P(same, 0), P(same, 1), P(same, 2), None, P(order, 0), P(same, 3),
-                      P(high, 0), P(low, 0), P(same, 4), P(high, 1), P(low, 1), P(same, 5), table,
-                      P(kept, 0), P(raised, 0), P(summed, 0), P(strides, 0), P(same, 6), P(borders, 0), P(block, 0), P(block, 1),
-                      P(blocks, 0), P(kept, 1), P(blocks, 1)])
-        if t == 0:
-            quant(T.ELQ[:], T.ELS[:], T.ELT[:], "ELT", "ELQ ELS")
-            unpack()
-        weave([P(raised, 1), P(summed, 1), P(strides, 1), P(borders, 1), P(runs, 1), P(ends, 1), P(picked, 1),
-               lambda: tt(T.YT[:, 0:32], T.PK[:, 128:256].indirect(LS[:, 36 + 2 * t:38 + 2 * t]), T.YT[:, 64:96], A.min, "PS0 PS1 LS KM", "YT"),
-               lambda: turn(T.YT[:, 32:64], T.YT[:, 0:32], "YT", "TR")],
-              [P(kept, 2),
-               lambda: ts(T.YT[:, 64:96], T.KK[:, 16:32].indirect(LS[:, 30 + 2 * t:32 + 2 * t]), -1048832.0, 1048576.0, A.mult, A.add, "K2 LS", "KM"),
-               flags, P(runs, 0), P(ends, 0), P(picked, 0)])
-        for q in range(8):
-            dma("Y" if q % 2 == 0 else "A", LB[16 * q:16 * q + 16, 0:16], T.YT[q::16, 32:64], "dl%d" % t, "TR", "", lb)
-        window()
-        if t == 0:
-            late()
-        L, JL, D = T.LF, T.JL[:, 0:16], T.DL[:, 32:48]
-        C, DN = T.WC[:, 64:80], T.WC[:, 80:81]
-
-        def within():
-            for i in range(2):
-                scan(T.WC[:, 32 + 16 * i:48 + 16 * i], T.NEG[:, 0:16], T.DL[:, 96 + 16 * i:112 + 16 * i], T.WC[:, 16 * i + 15:16 * i + 16],
-                     A.max, A.add, "NEG dt sa", "", "cb")
-
-        def firsts():
-            cp(T.AU[:], T.AI[:, 0:16], "ai", "AU")
-            for b in range(4):
-                act(T.GW[:, 256 * b:256 * b + 256], T.FW[:, 256 * b:256 * b + 256].indirect(T.AU[:]), "FW%d AU" % b, "GW%d" % b)
-
-        def mean(b):
-            tt(T.XW[:, 352 * b:352 * b + 256], T.GW[:, 256 * b:256 * b + 256], B(DB[b])[:, 0:256], A.add, "GW%d B%d" % (b, DB[b]), "XZ%d" % b)
-
-        def mosaic(b):
-            o, i = T.ET[:, b:384:4], T.XW[:, 352 * b:352 * b + 256].indirect(T.LU[:, 0:6])
-            if b < 2:
+                start = T.UU[:, 71 + 8 * s:72 + 8 * s]
+                if n == 0:
+                    a, b = 256 * s, 256 * s + 256
+                    act(T.INC[:, a:b], ind(T.AL[:, 0:32], LS[:, 48 + 16 * s:64 + 16 * s]), "al0 al2 Ln%d" % s, "INC%d" % s)
+                    scan(T.O[:, a:b], T.INC[:, a:b], B(s)[:, 0:256], start, A.add, A.max, "INC%d B%d CU0" % (s, s), "O%d" % s)
+                d = (T.H16[:, 16 * s:16 * s + 16], T.O[:, 256 * s + 15:256 * s + 256:16])[n]
+                scan(T.O2[:, o + 16 * s:o + 16 * s + 16], T.IN2[:, o + 16 * s:o + 16 * s + 16], d, start, A.add, A.max,
+                     "IN2%d CU0 %s%d" % (n, ("H16", "O")[n], s), "", "O2%d" % n)
+            tt(T.PK[:, 2 * o:2 * o + 64], ind(T.O2[:, o:o + 32], LS[:, 22:26]), T.EM[:, 128 + 2 * o:192 + 2 * o], A.mult, "O2%d Lp EM" % n, "PK%d" % n)
+            scan(T.PK[:, 128 + 2 * o:192 + 2 * o], T.RST[:], T.PK[:, 2 * o:2 * o + 64], -1e9, A.max, A.add, "RST PK%d" % n, "PS%d" % n)
+        tt(T.YT[:, 64:96], ind(T.RR[:], LS[:, 42 + 2 * t:44 + 2 * t]), T.KK[:, 16:48], A.is_le, "Lr TG " + " ".join("rr%d" % k for k in range(8)), "DF")
+        turn(T.YT[:, 96:128], T.YT[:, 64:96], "DF", "TF")
+        for q in range(4):
+            dma("YA"[q % 2], T.DL[q::4, 32:48], T.YT[32 * q:32 * q + 16, 96:128], "dk%d" % t, "TF", "", "dl")
+        for s in range(2):
+            act(T.YT[:, s:32:2], T.YT[:, 64 + s:96:2], "DF s17", "", "KM", scale=-1048576.0, bias=sc(17 + s))
+        tt(T.AI[:, 0:32], ind(T.PK[:, 128:256], LS[:, 36 + 2 * t:38 + 2 * t]), T.YT[:, 0:32], A.max, "PS0 PS1 Ls KM", "YT")
+        turn(T.AI[:, 32:64], T.AI[:, 0:32], "YT", "TR")
+        ts(T.AI[:, 64:96], T.AI[:, 32:64], 255, None, A.bitwise_and, None, "TR", "ai")
+        cp(T.TU[:], T.AI[:, 64:96], "ai", "TU")
+        for q in range(4):
+            dma("YA"[q % 2], T.AU[q::4, :], T.TU[32 * q:32 * q + 16, :], "dl%d" % t, "TU", "", "AU")
+        L, JL, D, C, DN = T.LF, T.JL[:, 0:16], T.DL[:, 32:48], T.WC[:, 64:80], T.WC[:, 80:81]
+        scan(T.DL[:, 1:17], T.NEG[:, 0:16], D, T.DL[:, 0:1], A.max, A.add, "dl NEG p0", "pm")
+        turn(T.DL[:, 64:128], T.DL[:, 0:64], "dl pm p0", "dt")
+        scan(T.WC[:, 0:32], H1, T.DL[:, 64:96], 0.0, A.mult, A.add, "H1 dt", "sa")
+        for i in range(2):
+            scan(T.WC[:, 32 + 16 * i:48 + 16 * i], T.NEG[:, 0:16], T.DL[:, 96 + 16 * i:112 + 16 * i], T.WC[:, 16 * i + 15:16 * i + 16], A.max, A.add,
+                 "NEG dt sa", "", "cb")
+        turn(T.WC[:, 64:96], T.WC[:, 32:64], "cb", "ct")
+        act(L[:, 0:16], D, "dl", "l1", scale=-1024.0)
+        tt(L[:, 16:32], L[:, 0:16], JL, A.add, "l1 JL", "l2")
+        ts(L[:, 32:48], C, DN, None, A.subtract, None, "ct", "l5")
+        tt(L[:, 48:64], L[:, 16:32], C, A.subtract, "l2 ct", "l6")
+        tt(L[:, 64:80], L[:, 32:48], L[:, 48:64], A.max, "l5 l6", "l7")
+        ts(T.PU[:], L[:, 64:80], DN, None, A.add, None, "l7 ct", "PU")
+        cp(ind(T.LR[:], T.PU[:]), T.ICOL[:], "PU ICOL", "LR")
+        scan(T.LM[:], MK[:, 0:96], T.LR[:, 0:96], 0.0, A.add, A.max, "MK mk1 LR", "ln")
+        ts(T.LU[:, 0:6], T.LM[:, 15::16], MK[:, 143:144], None, A.subtract, None, "ln mk0", "LU")
+        for b in range(4):
+            z, f = T.XW[:, 352 * b:352 * b + 256], ind(T.FW[:, 256 * b:256 * b + 256], T.AU[:])
+            if b == 3:
+                tt(z, f, T.FW[:, 1024:1280], A.add, "FW3 FW4 AU", "XZ3")
+            else:
+                act(T.GW[:, 256 * b:256 * b + 256], f, "FW%d AU" % b, "GW%d" % b)
+                tt(z, T.GW[:, 256 * b:256 * b + 256], B(DB[b])[:, 0:256], A.add, "GW%d B%d" % (b, DB[b]), "XZ%d" % b)
+        for b in range(4):
+            o, i = T.ET[:, b:384:4], ind(T.XW[:, 352 * b:352 * b + 256], T.LU[:, 0:6])
+            if b != 2:
                 act(o, i, "XZ%d LU" % b, "", "ET", scale=2.0 ** -6)
             else:
                 ts(o, i, 2.0 ** -6, None, A.mult, None, "XZ%d LU" % b, "", "ET")
-        weave([lambda: ts(D, LB[:, 16:32], 0.0, None, A.is_ge, None, lk, "dl"),
-               lambda: scan(T.DL[:, 1:17], T.NEG[:, 0:16], D, sc(14), A.max, A.add, "dl NEG s14", "pm"),
-               lambda: turn(T.DL[:, 64:128], T.DL[:, 0:64], "dl pm", "dt"),
-               lambda: scan(T.WC[:, 0:32], H1, T.DL[:, 64:96], 0.0, A.mult, A.add, "H1 dt", "sa"),
-               within,
-               lambda: turn(T.WC[:, 64:96], T.WC[:, 32:64], "cb", "ct"),
-               lambda: (ts(L[:, 32:48], C, DN, None, A.subtract, None, "ct", "l5"), tt(L[:, 48:64], L[:, 16:32], C, A.subtract, "l2 ct", "l6")),
-               lambda: tt(L[:, 64:80], L[:, 32:48], L[:, 48:64], A.max, "l5 l6", "l7"),
-               lambda: ts(T.PU[:], L[:, 64:80], DN, None, A.add, None, "l7 ct", "PU"),
-               lambda: op("V", lambda: v.tensor_copy(T.LR[:].indirect(T.PU[:]), T.ICOL[:]), "PU ICOL", "LR"),
-               lambda: scan(T.LM[:], T.MK[:, 0:96], T.LR[:, 0:96], 0.0, A.add, A.max, "MK mk1 LR", "ln"),
-               lambda: ts(T.LU[:, 0:6], T.LM[:, 15::16], T.MK[:, 143:144], None, A.subtract, None, "ln mk0", "LU")],
-              [None, lambda: ts(L[:, 0:16], D, -1024.0, None, A.mult, None, "dl", "l1"), None,
-               lambda: tt(L[:, 16:32], L[:, 0:16], JL, A.add, "l1 JL", "l2"), None,
-               lambda: tt(T.AI[:, 16:32], T.JL[:, 32:48], LB[:, 0:16], A.subtract, lb + " JB", "ai0"),
-               lambda: ts(T.AI[:, 0:16], T.AI[:, 16:32], 255, None, A.bitwise_and, None, "ai0", "ai"),
-               firsts,
-               lambda: ts(L[:, 80:96], L[:, 64:80], DN, 256.0, A.add, A.add, "l7 ct", "pos"),
-               P(mean, 0), P(mean, 1), P(mean, 2)])
-        mosaic(0)
-        mosaic(1)
-        mean(3)
-        mosaic(2)
-        mosaic(3)
-        quant(T.EQ[:], T.ES[:], T.ET[:], "ET ET4", "EQ ES")
+        quant(T.EQ[:], T.ES[:], T.ET[:], "ET ET4", "EQ")
         remote(T["AC%d" % t][:, 0:96].bitcast(dt.uint8), T.EQ[:, 0:96].bitcast(dt.uint8), "ca%d" % t, "lc%d" % t, "EQ", "AC%d" % t)
-        remote(T["AS%d" % t][:, 0:96], T.ES[:, 0:96], "ca%d" % t, "lc%d" % t, "ES", "AS%d" % t)
+        remote(T["AS%d" % t][:, 0:96], T.ES[:, 0:96], "ca%d" % t, "lc%d" % t, "EQ", "AC%d" % t)
+        ts(L[:, 80:96], L[:, 64:80], DN, 256.0, A.add, A.add, "l7 ct", "pos")
         ts(L[:, 96:112], L[:, 80:96], 352.0, 4096.0, A.is_lt, A.mult, "pos", "m0")
-        if t == 0:
-            steps(1)
-        if t == 1:
-            quant(T.VQ[:], T.VS[:], T.VT[:], "VT", "VQ VS")
         tt(L[:, 112:128], L[:, 96:112], L[:, 80:96], A.min, "m0 pos", "m1")
-        if t == 0:
-            steps(2)
-        if t == 1:
-            fill(T.AF[:], 0.0, "AF")
         tt(L[:, 128:144], L[:, 112:128], JL, A.max, "m1 JL", "m2")
         cp(T.SU[:], L[:, 128:144], "m2", "SU")
-        if last:
-            cp(T.AF[:, 0:16], T.AI[:, 0:16], "ai AF", "af")
+        if t == 2:
+            cp(T.AF[:, 0:16], T.AU[:], "AU", "af")
             turn(T.AF[:, 32:64], T.AF[:, 0:32], "af", "at")
             for q in range(8):
                 p = 32 * (q // 2)
                 dma("Y", T.al[q:q + 1, 0:256], T.AF[p:p + 16, 32 + 16 * (q % 2):48 + 16 * (q % 2)], "dout", "at")
             dma("Y", T.al[:, 256:352], T.LR[0::16, 0:96], "dout", "LR")
-        AC, AS = T["AC%d" % t], T["AS%d" % t]
-        for b in range(4):
-            kb = "B%d" % DB[b]
-            mm(B(DB[b])[:, 0:128], T.WQ[:, 128 * b:128 * b + 128], T.WS[:, 128 * b:128 * b + 128], AC[:], AS[:], True, False, "WQ WS AC%d AS%d" % (t, t), kb)
-            mm(B(DB[b])[:, 0:128], T.ELQ[:, 128 * b:128 * b + 128], T.ELS[:, 128 * b:128 * b + 128], AC[:], AS[:], False, True, "ELQ ELS AC%d AS%d" % (t, t), "", kb)
+        AC, AS, ka = T["AC%d" % t], T["AS%d" % t], " AC%d pc%d ps%d" % (t, t, t)
         for b in range(4):
             kb, o, i = "B%d" % DB[b], T.XW[:, 352 * b + 256:352 * b + 352], B(DB[b])[:, 0:96]
+            mm(B(DB[b])[:, 0:128], T.WQ[:, 128 * b:128 * b + 128], T.WS[:, 128 * b:128 * b + 128], AC[:], AS[:], True, False, "WQ WS" + ka, kb)
+            mm(B(DB[b])[:, 0:128], T.ELQ[:, 128 * b:128 * b + 128], T.ELS[:, 128 * b:128 * b + 128], AC[:], AS[:], False, True, "EL%d" % b + ka, "", kb)
             win, r = T.XW[:, 352 * b:352 * b + 352], "XZ%d XT%d SU" % (b, b)
             if b % 2 == 0:
                 act(o, i, kb, "XT%d" % b, scale=2.0)
-                act(T.XT[:, b::4], win.indirect(T.SU[:]), r, "", "XT", scale=2.0 ** -6)
+                act(T.XT[:, b::4], ind(win, T.SU[:]), r, "", "XT", scale=2.0 ** -6)
             else:
                 ts(o, i, 2.0, None, A.mult, None, kb, "XT%d" % b)
             if b == 1:
-                ts(T.XT[:, b::4], win.indirect(T.SU[:]), 2.0 ** -6, None, A.mult, None, r, "", "XT")
+                ts(T.XT[:, b::4], ind(win, T.SU[:]), 2.0 ** -6, None, A.mult, None, r, "", "XT")
             if b == 3:
-                ts(T.XT[:, 3:512:4], win.indirect(T.SU[:, 0:8]), 2.0 ** -6, None, A.mult, None, r, "X30")
-                act(T.XT[:, 515::4], win.indirect(T.SU[:, 8:16]), r, "X31", scale=2.0 ** -6)
+                ts(T.XT[:, 3:512:4], ind(win, T.SU[:, 0:8]), 2.0 ** -6, None, A.mult, None, r, "X30")
+                act(T.XT[:, 515::4], ind(win, T.SU[:, 8:16]), r, "X31", scale=2.0 ** -6)
     for h in range(2):
         a, b = 128 * h, 128 * h + 128
         quant(T.XQ[:, a:b], T.XS[:, a:b], T.XT[:, 4 * a:4 * b], "XT X3%d" % h, "XQ%d" % h)
         dma("Y", T.oc[:, 4 * a:4 * b], T.XQ[:, a:b].bitcast(dt.uint8), "dout", "XQ%d" % h)
-        mm(B(2 + h)[:, 0:128], T.VQ[:], T.VS[:], T.XQ[:, a:b], T.XS[:, a:b], True, True, "VQ VS XQ%d" % h, "B%d" % (2 + h))
-    cp(T.YO[:, 0:128], B(2)[:, 0:128], "B2", "YO0")
-    dma("Y", T.y[:, 0:128], T.YO[:, 0:128], "dout", "YO0")
+        mm(B(2 + h)[:, 0:128], T.VQ[:], T.VS[:], T.XQ[:, a:b], T.XS[:, a:b], True, True, "VQ XQ%d" % h, "B%d" % (2 + h))
+        cp(T.YO[:, a:b], B(2 + h)[:, 0:128], "B%d" % (2 + h), "YO%d" % h)
+        dma("YA"[h], T.y[:, a:b], T.YO[:, a:b], "dout", "YO%d" % h)
     for k in range(4):
         dma("A", T.osc[4 * k:4 * k + 4, :], T.XS[32 * k:32 * k + 4, :], "dout", "XQ0 XQ1")
-    cp(T.YO[:, 128:256], B(3)[:, 0:128], "B3", "YO1")
-    dma("Y", T.y[:, 128:256], T.YO[:, 128:256], "dout", "YO1")
-    for s in sorted(tot):
-        need("G", [(s, tot[s])])
+    issue(arrange())

@@ -10,14 +10,14 @@ for _n, _w, _d in [
         ("ICOL", 256, F32), ("VB", 256, BF), ("I8", 144, BF), ("I16", 256, BF), ("JP", 128, BF), ("TH", 144, F32),
         ("IP", 16, I32), ("SC", 24, F32), ("UI", 30, I32), ("UL", 30, U16), ("PLF", 16, F32), ("PL", 16, U16),
         ("RW", 32, F32), ("FR", 160, F32), ("FS", 136, F32), ("LS", 80, U16), ("KC", 768, BF),
-        ("CB", 64, F32), ("CE", 128, F32), ("RST", 64, F32), ("TK", 16, F32), ("H4", 128, F32), ("HS", 96, F32),
+        ("CB", 64, F32), ("CE", 128, F32), ("RST", 64, F32), ("H4", 128, F32), ("HS", 96, F32),
         ("NEG", 256, BF), ("JL", 32, F32), ("MK", 256, F32),
         ("XQ", 256, F8), ("XS", 256, U8), ("XT", 1024, BF), ("BT", 608, BF), ("BQ", 152, F8), ("BS", 152, U8),
-        ("W4", 128, F32), ("W2", 32, F32), ("WN", 72, F32), ("SG", 64, F32),
+        ("W4", 128, F32), ("W2", 48, F32), ("WN", 72, F32), ("SG", 64, F32),
         ("OT", 1024, BF), ("OQ", 256, F8), ("OS", 256, U8), ("HB", 512, BF), ("DS", 1024, BF), ("DG", 512, BF), ("DH", 512, BF),
         ("DT", 1024, BF), ("DQ", 256, F8), ("DP", 256, U8), ("MH", 512, BF), ("HH", 512, F32), ("H16", 34, F32),
-        ("BD", 128, F32), ("EM", 256, F32), ("YY", 96, I32), ("EK", 256, I32), ("HL", 64, F32), ("RR", 256, F32),
-        ("KK", 48, F32), ("UU", 80, F32), ("AL", 64, F32), ("INC", 512, F32), ("IN2", 64, F32), ("O", 512, F32), ("O2", 64, F32),
+        ("BD", 128, F32), ("EM", 256, F32), ("YY", 102, I32), ("EK", 272, I32), ("HL", 102, F32), ("RR", 272, F32),
+        ("KK", 16, F32), ("PN", 272, F32), ("UU", 80, F32), ("AL", 64, F32), ("INC", 512, F32), ("IN2", 64, F32), ("O", 512, F32), ("O2", 64, F32),
         ("PK", 256, F32), ("YT", 128, F32), ("AI", 96, I32), ("TU", 32, U16), ("LF", 160, F32), ("DL", 128, F32), ("WC", 96, F32),
         ("AF", 64, F32), ("AU", 16, U16), ("PU", 16, U16), ("LU", 8, U16), ("SU", 16, U16), ("LR", 256, F32), ("LM", 96, F32),
         ("FW", 1280, BF), ("GW", 768, BF), ("XW", 1408, BF), ("ET", 512, BF), ("EQ", 128, F8), ("ES", 128, U8), ("YO", 256, F32)]:
@@ -36,8 +36,13 @@ for _t in range(3):
 RAISE = 2.0 ** -6
 UNIT = 2.0 ** -17
 TOP = 0x15555
-CYCLE, WAKE, ISSUE, LOCAL, REMOTE, TURNS = 0.001, 0.12, 0.05, 1.5, 2.0, 6
-PATIENCE = {"V": 16.0, "A": 30.0, "P": 1.0, "G": 2.0, "Y": 1.0}
+HALF = 1 << 17
+END = 1 << 20
+MARK = 1 << 21
+CYCLE, WAKE, ISSUE, LOCAL, REMOTE, TURNS = 0.00104, (0.11, 0.13), 0.05, 1.4, 1.9, 5
+WEIGHTS = [(p, h) for p in (12.0, 24.0, 48.0) for h in (2.0, 4.0, 8.0)]
+OPT = {"up": "AA", "hi": "AA"}
+ORDER = []
 
 
 def rank_program(g, core, T, topo):
@@ -67,11 +72,11 @@ def rank_program(g, core, T, topo):
         call(e, lambda: f().then_inc(T.sem[own[e]], 1), [(own[e], 1)], r, w, add, cycles * CYCLE)
 
     def dma(e, out, in_, s, r, w="", add=""):
-        call(e, lambda: Q[e].dma_start(out, in_).then_inc(T.sem[s], 16), [(s, 16)], r, w, add, ISSUE, LOCAL)
+        call(e, lambda: Q[e].dma_start(out, in_).then_inc(T.sem[s], 16), [(s, 16)], r, w, add, ISSUE, LOCAL + 0.0018 * out.shape[1])
 
     def remote(out, in_, rs, ls, r, w):
         call("G", lambda: g.remote_dma(out_ap=out, in_ap=in_, remote_sem=T.sem[rs], local_sem=T.sem[ls], pid=pid, routing_id=rid, dma_engine_mask=msk),
-             [(ls, ne), (rs, ne)], r, "", w, 3 * ISSUE, REMOTE)
+             [(ls, ne), (rs, ne)], r, "", w, 3 * ISSUE, REMOTE + (rs == "wa0"))
 
     def track(seq, meet):
         lastw, readers, epoch, raised = {}, {}, {}, {}
@@ -121,15 +126,17 @@ def rank_program(g, core, T, topo):
 
         def meet(i, j, s, wait):
             if j is not None:
-                pre[i][j] = post[j][i] = max(pre[i].get(j, 0.0), calls[j]["late"] + WAKE if wait else 0.0)
+                pre[i][j] = post[j][i] = max(pre[i].get(j, 0.0), calls[j]["late"] + WAKE[calls[i]["e"] != calls[j]["e"]] if wait else 0.0)
         track(range(n), meet)
 
-        def lay(before, behind, rank, first):
+        def lay(before, behind, rank, first, patience, hurry):
             left, ready, free, seq, end = [len(p) for p in before], list(first), {e: 0.0 for e in Q}, [], [0.0] * n
             pool = {e: [i for i in range(n) if calls[i]["e"] == e and not before[i]] for e in Q}
             while len(seq) < n:
                 t0, e = min((max(free[e], min(ready[i] for i in pool[e])), e) for e in Q if pool[e])
-                i = max(pool[e], key=lambda i: (rank[i] - PATIENCE[e] * max(0.0, ready[i] - t0), -i))
+                j = max(pool[e], key=lambda i: rank[i])
+                i = max(pool[e], key=lambda i: (rank[i] - (patience if e in "VA" else 2.0) * max(0.0, ready[i] - t0)
+                                                - (hurry * max(0.0, max(t0, ready[i]) + busy[i] - max(t0, ready[j])) if i != j else 0.0), -i))
                 pool[e].remove(i)
                 seq.append(i)
                 free[e] = end[i] = max(t0, ready[i]) + busy[i]
@@ -146,12 +153,14 @@ def rank_program(g, core, T, topo):
         for i in reversed(range(n)):
             tail[i] = busy[i] + max([late[i]] + [d + tail[k] for k, d in post[i].items()])
         best = None
-        for turns in range(TURNS):
-            seq, end = lay(pre, post, tail, [0.0] * n)
-            span = max(end[i] + late[i] for i in range(n))
-            if best is None or span < best[0]:
-                best = (span, seq)
-            tail = lay(post, pre, end, late)[1]
+        for patience, hurry in WEIGHTS:
+            rank = tail
+            for turns in range(TURNS):
+                seq, end = lay(pre, post, rank, [0.0] * n, patience, hurry)
+                span = max(end[i] + late[i] for i in range(n))
+                if best is None or span < best[0]:
+                    best = (span, seq)
+                rank = lay(post, pre, end, late, patience, hurry)[1]
         return best[1]
 
     def issue(seq):
@@ -225,6 +234,14 @@ def rank_program(g, core, T, topo):
         else:
             op("A", lambda: ac.activation(out, bare(in_), AF.Copy, scale=scale), r, w, add, n)
 
+    def aff(e, out, in_, m, c, r, w="", add=""):
+        if e == "A":
+            act(out, in_, r, w, add, scale=m, bias=c)
+        elif c is None:
+            ts(out, in_, m, None, A.mult, None, r, w, add)
+        else:
+            ts(out, in_, m, c, A.mult, A.add, r, w, add)
+
     def row(out, n, a, b, w="", add=""):
         act(out, T.ICOL[:, 0:n], "ICOL", w, add, scale=float(a), bias=float(b))
 
@@ -258,6 +275,7 @@ def rank_program(g, core, T, topo):
     iota(T.I16[:], [[0, 16], [1, 16]], 0, 0, "I16")
     iota(T.I8[:], [[1, 18], [0, 8]], 0, 0, "I8")
     iota(SC[:, 4:8], [[-8, 2], [128, 2]], 0, 1, "s4")
+    iota(SC[:, 14:16], [[-128, 2]], 255, -1, "s14")
     iota(T.JP[:], [[1, 4], [4, 2], [16, 16]], 0, 0, "JP")
     iota(T.ICOL[:], [[1, 256]], 0, 0, "ICOL")
     iota(T.VB[:], [[1, 256]], 0, 0, "VB")
@@ -333,17 +351,17 @@ def rank_program(g, core, T, topo):
     act(T.DL[:, 0:1], sc(12), "s12", "p0", scale=-1.0)
     ts(T.TH[:], T.I8[:], sc(1), 1e29, A.not_equal, A.mult, "I8 s1", "TH")
     fill(T.TH[:, 136:144], 0.0, "TH")
-    scan(T.RR[:, 0:8], T.H4[:, 1:65:8], T.NEG[:, 0:8], 0.25, A.mult, A.max, "H4 NEG", "rr0")
+    row(T.PN[:, 16::17], 16, 0, 1, "pd")
     for s in range(2):
-        act(T.TK[:, s::2], T.RR[:, 0:8], "rr0", "", "TK", scale=-2.0, bias=float(TOP))
+        fill(T.YY[:, 50 + 17 * s:51 + 17 * s], TOP + s * HALF + END, "", "yd")
+    row(T.HL[:, 0:1], 1, 0, 0, "d0")
     for s in range(2):
         ts(T.CT[:, s:512:4], T.I16[:, 0:128], sc(2 + s), None, A.is_equal, None, "I16 s%d" % (2 + s), "", "CT0")
         for h in range(2):
             ts(T.CT[:, 512 * s + 512 + h:512 * s + 1024:4], T.JP[:], sc(4 + 2 * s + h), None, A.is_equal, None, "JP s4", "", "CT%d" % (1 + s))
-        ts(T.HMT[:, s::4], T.VB[:], sc(10 + s), 256.0, A.is_equal, A.mult, "VB s%d hz0 hz1" % (10 + s), "", "HMT")
+        ts(T.HMT[:, s::4], T.VB[:], sc(14 + s), 256.0, A.is_equal, A.mult, "VB s14 hz0 hz1", "", "HMT")
     for i in range(3):
         quant(T.CQ[:, 128 * i:128 * i + 128], T.CS[:, 128 * i:128 * i + 128], T.CT[:, 512 * i:512 * i + 512], "CT%d" % i, "CQ%d" % i)
-    quant(T.HMQ[:], T.HMS[:], T.HMT[:], "HMT", "HMQ")
     for i in range(4):
         where0(T.MTT[:, i:1024:4], T.KC[:, 0:256], [[-1, 256]], 128 * (i // 2), "KC0", "", "MT0")
         where0(T.MTT[:, 1024 + i::4], T.KC[:, 0:256], [[-1, 16], [-16, 16]], 128 * (i // 2), "KC0", "", "MT1")
@@ -378,8 +396,7 @@ def rank_program(g, core, T, topo):
     ts(LS[:, 23:26:2], RW[:, 20:22], p1, None, A.add, None, "rw20 FS", "", "Lp")
     ts(LS[:, 26:30], RW[:, 4:8], bs, None, A.add, None, "rw4 FS", "Lb")
     ts(IP[:, 8:14], IP[:, 8:14], 15, None, A.bitwise_and, None, "ip8", "ip8")
-    cp(LS[:, 30:36], IP[:, 8:14], "ip8", "Lg")
-    ts(LS[:, 42:48], IP[:, 8:14], 16.0, 15.0, A.mult, A.add, "ip8", "Lr")
+    ts(LS[:, 42:48], IP[:, 8:14], 17.0, 16.0, A.mult, A.add, "ip8", "Lr")
     for s in range(2):
         cp(LS[:, 36 + s:42:2], FS[:, 132:135], "FS", "", "Ls")
         ts(LS[:, 48 + 16 * s:64 + 16 * s], T.PLF[:], 0.0, RW[:, 24 + s:25 + s], A.mult, A.add, "PLF rw24", "Ln%d" % s)
@@ -401,6 +418,7 @@ def rank_program(g, core, T, topo):
             mm(B(s)[:, 0:144], T.XQ[:, 128 * s:128 * s + 128], T.XS[:, 128 * s:128 * s + 128], T.URQ[:, 144 * t:144 * t + 144], T.URS[:, 144 * t:144 * t + 144],
                True, True, "XQ%d URQ%d URS%d" % (s, t, t), "B%d" % s)
             tt(T.BT[:, s:576:4], B(s)[:, 0:144], T.TH[:], A.is_gt, "B%d TH" % s, "", "BT")
+            ts(T.W2[:, 32 + 8 * s:40 + 8 * s], B(s)[:, 0:8], 0.0, None, A.is_gt, None, "B%d" % s, "", "W1")
         quant(T.BQ[:], T.BS[:], T.BT[:], "BT", "BQ")
         mm(B(2)[:, 0:128], T.CQ[:, 0:128], T.CS[:, 0:128], T.BQ[:, 0:128], T.BS[:, 0:128], True, True, "CQ0 BQ", "B2")
         mm(B(3)[:, 0:128], T.CQ[:, 128:256], T.CS[:, 128:256], T.BQ[:, 24:152], T.BS[:, 24:152], True, False, "CQ1 BQ", "B3")
@@ -409,13 +427,15 @@ def rank_program(g, core, T, topo):
         cp(T["MS%d" % t][:], T.W4[:, 7::8], "W4", "MS%d" % t)
         remote(T["WL%d" % t][:], T["MS%d" % t][:], "wa%d" % t, "lw%d" % t, "MS%d" % t, "WL%d" % t)
         bits = B(3)[:, 112:128]
-        scan(T.W2[:, 0:16], H2, bits, 0.0, A.mult, A.add, "HS2 B3", "W2")
+        scan(T.W2[:, 0:16], H2, T.W2[:, 32:48], 0.0, A.mult, A.add, "HS2 W1", "W2")
         scan(T.WN[:, 16:32], HN, bits, 0.0, A.mult, A.add, "HS2 B3", "P4")
         scan(T.W2[:, 16:32], T.H4[:, 0:16], bits, 0.0, A.mult, A.add, "H4 B3", "W3")
         act(T.WN[:, 0:16], bits, "B3", "bits")
         for s in range(2):
             ts(T.OT[:, s::4], T.VB[:], T.W2[:, 8 * s + 7:8 * s + 8], None, A.is_equal, None, "VB W2 oz0 oz1", "", "OT")
-        quant(T.OQ[:], T.OS[:], T.OT[:], "OT", "OQ")
+        quant(T.OQ[:], T.OS[:], T.OT[:], "OT MS%d" % t, "OQ")
+        if t == 0:
+            quant(T.HMQ[:], T.HMS[:], T.HMT[:], "HMT MS0", "HMQ")
         for h in range(2):
             a, b, c = 256 * h, 256 * h + 256, 512 * h + 256
             mm(B(h)[:, 0:256], T.OQ[:, 128 * h:128 * h + 128], T.OS[:, 128 * h:128 * h + 128], T.HMQ[:], T.HMS[:], True, True, "OQ HMQ", "B%d" % h)
@@ -423,11 +443,8 @@ def rank_program(g, core, T, topo):
             scan(T.DS[:, c - 256:c], T.NEG[:], T.HB[:, a:b], 0.0, A.add, A.max, "NEG HB%d" % h, "DR%d" % h)
             scan(T.DS[:, c:c + 256], T.NEG[:], T.HB[:, a:b], T.DS[:, c - 1:c], A.add, A.max, "NEG DR%d HB%d" % (h, h), "DS%d" % h)
             act(T.DG[:, a:b], ind(T.DS[:, c:c + 256], T.PL[:]), "DS%d PL" % h, "DG%d" % h)
-            if h == 0:
-                act(T.DH[:, a:b], T.DG[:, a:b], "DG%d" % h, "DH%d" % h, bias=2055.5)
-            else:
-                ts(T.DH[:, a:b], T.DG[:, a:b], 2055.5, None, A.add, None, "DG%d" % h, "DH%d" % h)
-            ts(T.DT[:, 2 * h::4], T.DH[:, a:b], 2048.0, None, A.subtract, None, "DH%d" % h, "dh%d" % h)
+            aff(OPT["up"][h], T.DH[:, a:b], T.DG[:, a:b], 1.0, 2055.5, "DG%d" % h, "DH%d" % h)
+            aff(OPT["hi"][h], T.DT[:, 2 * h::4], T.DH[:, a:b], 1.0, -2048.0, "DH%d" % h, "dh%d" % h)
             scan(T.DT[:, 2 * h + 1::4], T.DG[:, a:b], T.DT[:, 2 * h::4], 0.0, A.max, A.subtract, "DG%d dh%d" % (h, h), "dw%d" % h)
         quant(T.DQ[:], T.DP[:], T.DT[:], "dh0 dw0 dh1 dw1", "DQ")
 
@@ -456,30 +473,31 @@ def rank_program(g, core, T, topo):
         tt(T.EM[:, 0:128], ind(T.WN[:, 0:40], LS[:, 14:22]), T.CE[:], A.is_equal, "P4 bits wn0 Le CE0 CE1 CE", "em0")
         act(T.BD[:, 64:128], T.BD[:, 0:64], "bd0", "BD", scale=-256 * UNIT)
         act(T.EM[:, 128:256], T.EM[:, 0:128], "em0", "EM", scale=-1 / UNIT)
-        act(T.KK[:, 16:48], ind(T.TK[:], LS[:, 30 + 2 * t:32 + 2 * t]), "TK Lg", "TG")
         if t == 0:
             unpack()
-        WL, H, NK = T["WL%d" % t], T.HL[:, 0:32], T.HL[:, 32:64]
         for s in range(2):
-            ts(T.YY[:, 32 + 16 * s:48 + 16 * s], WL[:], T.W2[:, 23 + 8 * s:24 + 8 * s], float(TOP), A.subtract, A.add, "WL%d W3" % t, "", "YY")
-        ts(T.YY[:, 64:96], T.YY[:, 32:64], TOP, None, A.bitwise_and, None, "YY", "y1")
-        ts(T.YY[:, 0:32], T.YY[:, 32:64], 4.0, None, A.mult, None, "YY", "Y4")
-        ts(NK, T.YY[:, 64:96], float(TOP), 2.0 * TOP, A.not_equal, A.mult, "y1", "nk0 nk1")
-        tt(H, T.YY[:, 64:96], NK, A.min, "y1 nk0 nk1", "H")
+            ts(T.YY[:, 34 + 17 * s:50 + 17 * s], T["WL%d" % t][:], T.W2[:, 23 + 8 * s:24 + 8 * s], float(TOP + s * HALF + MARK), A.subtract, A.add,
+               "WL%d W3" % t, "y%d" % s)
+        ts(T.YY[:, 68:102], T.YY[:, 34:68], TOP + HALF + END, None, A.bitwise_and, None, "y0 y1 yd", "h")
+        for s in range(2):
+            ts(T.PN[:, 17 * s:17 * s + 16], T.YY[:, 68 + 17 * s:84 + 17 * s], float(TOP + s * HALF), END + MARK + 2.0, A.not_equal, A.mult, "h", "pn0%d" % s)
+        tt(T.HL[:, 1:34], T.YY[:, 68:101], T.YY[:, 69:102], A.subtract, "h", "df")
+        ts(T.YY[:, 0:34], T.YY[:, 34:68], 4.0, -3.0 * MARK, A.mult, A.add, "y0 y1 yd", "Y4")
         for k in range(0, 8, 2):
-            ts(T.EK[:, 32 * k:32 * k + 64], T.YY[:, 0:64], 4 ** (k + 1), None, A.bitwise_and, None, "YY Y4", "ek%d ek%d" % (k, k + 1))
+            ts(T.EK[:, 34 * k:34 * k + 68], T.YY[:, 0:68], MARK + 4 ** (k + 1), None, A.bitwise_and, None, "y0 y1 yd Y4", "ek%d ek%d" % (k, k + 1))
         for k in range(8):
-            scan(T.RR[:, 32 * k:32 * k + 32], H1, H, 0.0, A.mult, A.max, "H1 H", "rr%d" % k)
+            pn, kp, o = T.PN[:, 34 * k:34 * k + 34], " pd pn%d0 pn%d1" % (k, k), 34 + 34 * (k % 2)
+            scan(T.RR[:, 34 * k:34 * k + 34], T.HL[:, 0:34], pn, -1e9, A.add, A.max, "d0 df" + kp, "rr%d" % k)
             if k < 7:
+                tt(T.HL[:, o:o + 34], T.EK[:, 34 * k:34 * k + 34], pn, A.min, "ek%d" % k + kp, "ev%d" % (k % 2))
                 for s in range(2):
-                    o = 32 * k + 16 * s
-                    ts(T.HL[:, 32 + 16 * s:48 + 16 * s], T.EK[:, o:o + 16], T.RR[:, o + 15:o + 16], 1.5 * 4 ** k - TOP, A.subtract, A.is_ge,
-                       "ek%d rr%d" % (k, k), "nk%d" % s)
-                tt(H, H, NK, A.mult, "H nk0 nk1", "H")
+                    b = 34 * k + 17 * s
+                    ts(T.PN[:, b + 34:b + 50], T.HL[:, o + 17 * s:o + 17 * s + 16], T.RR[:, b + 16:b + 17], END + MARK + 2.0 * 4 ** (k + 1), A.is_ge, A.mult,
+                       "ev%d rr%d" % (k % 2, k), "pn%d%d" % (k + 1, s))
         CU = (T.UU[:, 64:80], T.AL[:, 48:64])
         for n, a, b in ((0, 0, 4), (1, 4, 7)):
             o = 32 * n
-            tt(T.KK[:, 2 * a:2 * b], T.RR[:, 32 * a + 15:32 * b:16], T.TK[:, 2 * a:2 * b], A.is_gt, "TK " + " ".join("rr%d" % k for k in range(a, b)), "K%d" % n)
+            ts(T.KK[:, 2 * a:2 * b], T.RR[:, 34 * a + 16:34 * b:17], float(MARK), None, A.is_gt, None, " ".join("rr%d" % k for k in range(a, b)), "K%d" % n)
             tt(T.UU[:, o:o + 32], ind(T.KK[:, 0:16], LS[:, 2 * n:2 * n + 2]), T.SG[:, o:o + 32], A.mult, "K0 K1 Lk SG", "UU%d" % n)
             scan(CU[n], T.HS[:, 64 + 16 * n:80 + 16 * n], T.UU[:, o:o + 16], 0.0, A.mult, A.add, "HC UU%d" % n, "CU%d" % n)
             tt(T.AL[:, o:o + 16], T.UU[:, o + 16:o + 32], CU[n], A.subtract, "UU%d CU%d" % (n, n), "al%d" % n)
@@ -497,7 +515,7 @@ def rank_program(g, core, T, topo):
                      "IN2%d CU0 %s%d" % (n, ("H16", "O")[n], s), "", "O2%d" % n)
             tt(T.PK[:, 2 * o:2 * o + 64], ind(T.O2[:, o:o + 32], LS[:, 22:26]), T.EM[:, 128 + 2 * o:192 + 2 * o], A.mult, "O2%d Lp EM" % n, "PK%d" % n)
             scan(T.PK[:, 128 + 2 * o:192 + 2 * o], T.RST[:], T.PK[:, 2 * o:2 * o + 64], -1e9, A.max, A.add, "RST PK%d" % n, "PS%d" % n)
-        tt(T.YT[:, 64:96], ind(T.RR[:], LS[:, 42 + 2 * t:44 + 2 * t]), T.KK[:, 16:48], A.is_le, "Lr TG " + " ".join("rr%d" % k for k in range(8)), "DF")
+        ts(T.YT[:, 64:96], ind(T.RR[:], LS[:, 42 + 2 * t:44 + 2 * t]), float(MARK), None, A.is_le, None, "Lr " + " ".join("rr%d" % k for k in range(8)), "DF")
         turn(T.YT[:, 96:128], T.YT[:, 64:96], "DF", "TF")
         for q in range(4):
             dma("YA"[q % 2], T.DL[q::4, 32:48], T.YT[32 * q:32 * q + 16, 96:128], "dk%d" % t, "TF", "", "dl")
@@ -579,4 +597,6 @@ def rank_program(g, core, T, topo):
         dma("YA"[h], T.y[:, a:b], T.YO[:, a:b], "dout", "YO%d" % h)
     for k in range(4):
         dma("A", T.osc[4 * k:4 * k + 4, :], T.XS[32 * k:32 * k + 4, :], "dout", "XQ0 XQ1")
-    issue(arrange())
+    if not ORDER:
+        ORDER.extend(arrange())
+    issue(ORDER)

@@ -1,4 +1,4 @@
-from concourse.mybir import dt, AluOpType, ActivationFunctionType
+from concourse.mybir import dt, AluOpType, AxisListType, ActivationFunctionType
 
 F32, BF, I32, U16, F8, U8 = "float32", "bfloat16", "int32", "uint16", "float8_e4m3fn_x4", "uint8"
 SCRATCH = {}
@@ -16,7 +16,7 @@ for _n, _w, _d in [
         ("W4", 128, F32), ("W2", 48, F32), ("WN", 72, F32), ("SG", 64, F32),
         ("OT", 1024, BF), ("OQ", 256, F8), ("OS", 256, U8), ("HB", 512, BF), ("DS", 1024, BF), ("DG", 512, BF), ("DH", 512, BF),
         ("DT", 1024, BF), ("DQ", 256, F8), ("DP", 256, U8), ("MH", 512, BF), ("HH", 512, F32), ("H16", 34, F32),
-        ("BD", 128, F32), ("EM", 256, F32), ("YY", 102, I32), ("EK", 272, I32), ("HL", 102, F32), ("RR", 272, F32),
+        ("BD", 128, F32), ("EM", 256, F32), ("YY", 102, I32), ("EK", 272, I32), ("HL", 168, F32), ("RR", 272, F32),
         ("KK", 16, F32), ("PN", 272, F32), ("UU", 80, F32), ("AL", 64, F32), ("INC", 512, F32), ("IN2", 64, F32), ("O", 512, F32), ("O2", 64, F32),
         ("PK", 256, F32), ("YT", 128, F32), ("AI", 96, I32), ("TU", 32, U16), ("LF", 160, F32), ("DL", 128, F32), ("WC", 96, F32),
         ("AF", 64, F32), ("AU", 16, U16), ("PU", 16, U16), ("LU", 8, U16), ("SU", 16, U16), ("LR", 256, F32), ("LM", 96, F32),
@@ -36,12 +36,11 @@ for _t in range(3):
 RAISE = 2.0 ** -6
 UNIT = 2.0 ** -17
 TOP = 0x15555
-HALF = 1 << 17
-END = 1 << 20
-MARK = 1 << 21
-CYCLE, WAKE, ISSUE, LOCAL, REMOTE, TURNS = 0.00104, (0.11, 0.13), 0.05, 1.4, 1.9, 5
-WEIGHTS = [(p, h) for p in (12.0, 24.0, 48.0) for h in (2.0, 4.0, 8.0)]
-OPT = {"up": "AA", "hi": "AA"}
+HALF = 1 << 18
+DEAD = -2.0 ** 19
+CYCLE, WAKE, ISSUE, LOCAL, REMOTE, TURNS = 0.00104, (0.19, 0.19), 0.05, 1.2, 1.7, 5
+WEIGHTS = [(p, h) for p in (8.0, 12.0, 20.0, 40.0) for h in (1.0, 2.0, 4.0, 8.0)]
+OPT = {"inc": "AA", "wr": "A", "no": (0, 2, 1, 3), "z": "AVAA", "up": "AA", "hi": "AA"}
 ORDER = []
 
 
@@ -87,7 +86,7 @@ def rank_program(g, core, T, topo):
                 d = calls[j]
                 s = d["sems"][-1 if landed else 0][0]
                 if s == own.get(d["e"]):
-                    meet(i, j, s, not (war and c["e"] == d["e"] and c["sems"][0][0] == s))
+                    meet(i, j, s, not (war and c["e"] == d["e"] == "P"))
                 else:
                     for k in raised[s]:
                         meet(i, k, s, True)
@@ -216,6 +215,9 @@ def rank_program(g, core, T, topo):
     def scan(out, d0, d1, ini, o0, o1, r, w="", add=""):
         op("V", lambda: v.tensor_tensor_scan(out, d0, d1, ini, o0, o1), r, w, add, cycles(out, d0, d1, fast=True))
 
+    def least(out, a, r, w, add):
+        op("V", lambda: v.tensor_reduce(out, a, AxisListType.X, A.min), r, w, add, cycles(a, a))
+
     def turn(out, a, r, w):
         op("V", lambda: v.transpose(out, a), r, w, "", cycles(out, a))
 
@@ -278,7 +280,7 @@ def rank_program(g, core, T, topo):
     iota(SC[:, 14:16], [[-128, 2]], 255, -1, "s14")
     iota(T.JP[:], [[1, 4], [4, 2], [16, 16]], 0, 0, "JP")
     iota(T.ICOL[:], [[1, 256]], 0, 0, "ICOL")
-    iota(T.VB[:], [[1, 256]], 0, 0, "VB")
+    row(T.VB[:], 256, 1, 0, "VB")
     for z in range(4):
         iota(FR[:, 128 + 2 * z::8], [[0, 2], [64, 2]], 31 - (16 >> z), 0, "", "EA")
     iota(T.PLF[:], [[-8, 2], [-1, 4], [-4, 2]], 255, 0, "PLF")
@@ -291,10 +293,14 @@ def rank_program(g, core, T, topo):
     iota(T.JL[:, 16:32], [[16, 16]], 0, 0, "JLF")
     fill(T.KC[:, 256:768], 32.0, "KC1")
     fill(T.KC[:, 0:256], UNIT, "KC0")
-    fill(T.CT[:, 0:512], 0.0, "CT0")
-    fill(T.BT[:], 0.0, "BT")
-    for nm, a, k in (("CT", 512, "CT1"), ("CT", 1024, "CT2"), ("HMT", 0, "hz0"), ("HMT", 512, "hz1"), ("OT", 0, "oz0"), ("OT", 512, "oz1")):
-        act(T[nm][:, a:a + 512], T.KC[:, 256:768], "KC1", k, scale=0.0)
+    for nm in ("CT", "BT", "HMT", "OT"):
+        for i in (2, 3):
+            if OPT["z"][("CT", "BT", "HMT", "OT").index(nm)] == "V":
+                fill(T[nm][:, i::4], 0.0, "", "z" + nm)
+            else:
+                act(T[nm][:, i::4], T.KC[:, 256:256 + SCRATCH[nm][1][1] // 4], "KC1", "", "z" + nm, scale=0.0)
+    for i in (0, 1):
+        fill(T.BT[:, 576 + i::4], 0.0, "", "zBT")
     fill(T.H4[:], 4.0, "H4")
     fill(T.H4[:, 0::8], 0.0, "H4")
     row(T.HS[:, 32:64], 32, 0, 2, "HS2")
@@ -351,20 +357,26 @@ def rank_program(g, core, T, topo):
     act(T.DL[:, 0:1], sc(12), "s12", "p0", scale=-1.0)
     ts(T.TH[:], T.I8[:], sc(1), 1e29, A.not_equal, A.mult, "I8 s1", "TH")
     fill(T.TH[:, 136:144], 0.0, "TH")
-    row(T.PN[:, 16::17], 16, 0, 1, "pd")
+    scan(T.RR[:, 0:8], T.H4[:, 1:65:8], T.NEG[:, 0:8], 0.25, A.mult, A.max, "H4 NEG", "rr0")
     for s in range(2):
-        fill(T.YY[:, 50 + 17 * s:51 + 17 * s], TOP + s * HALF + END, "", "yd")
-    row(T.HL[:, 0:1], 1, 0, 0, "d0")
+        act(T.PN[:, 16 + 17 * s::34], T.RR[:, 0:8], "rr0", "", "pd", scale=-6.0)
+        fill(T.YY[:, 80 + 17 * s:81 + 17 * s], TOP + s * HALF - 2, "", "yd")
+    row(T.HL[:, 34:102:34], 2, 0, 0, "d0")
+    row(T.RR[:, 238:272], 34, 0, 0, "rr7")
     for s in range(2):
         ts(T.CT[:, s:512:4], T.I16[:, 0:128], sc(2 + s), None, A.is_equal, None, "I16 s%d" % (2 + s), "", "CT0")
         for h in range(2):
             ts(T.CT[:, 512 * s + 512 + h:512 * s + 1024:4], T.JP[:], sc(4 + 2 * s + h), None, A.is_equal, None, "JP s4", "", "CT%d" % (1 + s))
-        ts(T.HMT[:, s::4], T.VB[:], sc(14 + s), 256.0, A.is_equal, A.mult, "VB s14 hz0 hz1", "", "HMT")
+        ts(T.HMT[:, s::4], T.VB[:], sc(14 + s), 256.0, A.is_equal, A.mult, "VB s14", "", "HMT")
     for i in range(3):
-        quant(T.CQ[:, 128 * i:128 * i + 128], T.CS[:, 128 * i:128 * i + 128], T.CT[:, 512 * i:512 * i + 512], "CT%d" % i, "CQ%d" % i)
+        quant(T.CQ[:, 128 * i:128 * i + 128], T.CS[:, 128 * i:128 * i + 128], T.CT[:, 512 * i:512 * i + 512], "zCT CT%d" % i, "CQ%d" % i)
     for i in range(4):
-        where0(T.MTT[:, i:1024:4], T.KC[:, 0:256], [[-1, 256]], 128 * (i // 2), "KC0", "", "MT0")
-        where0(T.MTT[:, 1024 + i::4], T.KC[:, 0:256], [[-1, 16], [-16, 16]], 128 * (i // 2), "KC0", "", "MT1")
+        for n, pat in ((0, [[-1, 256]]), (1, [[-1, 16], [-16, 16]])):
+            o = 1024 * n + i
+            if i % 2 == 0:
+                where0(T.MTT[:, o:1024 * n + 1024:4], T.KC[:, 0:256], pat, 64 * i, "KC0", "mt%d%d" % (n, i))
+            else:
+                act(T.MTT[:, o:1024 * n + 1024:4], T.MTT[:, o - 1:1024 * n + 1024:4], "mt%d%d" % (n, i - 1), "", "MT%d" % n)
         where0(T.ELT[:, 512 * i:512 * i + 512], T.KC[:, 256:768], [[-1, 128], [128, 4]], -128 * i, "KC1", "ET%d" % (5 + i))
         quant(T.ELQ[:, 128 * i:128 * i + 128], T.ELS[:, 128 * i:128 * i + 128], T.ELT[:, 512 * i:512 * i + 512], "ET%d" % (5 + i), "EL%d" % i)
     for i in range(2):
@@ -399,7 +411,6 @@ def rank_program(g, core, T, topo):
     ts(LS[:, 42:48], IP[:, 8:14], 17.0, 16.0, A.mult, A.add, "ip8", "Lr")
     for s in range(2):
         cp(LS[:, 36 + s:42:2], FS[:, 132:135], "FS", "", "Ls")
-        ts(LS[:, 48 + 16 * s:64 + 16 * s], T.PLF[:], 0.0, RW[:, 24 + s:25 + s], A.mult, A.add, "PLF rw24", "Ln%d" % s)
 
     DB = (4, 5, 6, 7)
     for t in range(3):
@@ -408,8 +419,8 @@ def rank_program(g, core, T, topo):
             quant(T.XQ[:, 128 * h:128 * h + 128], T.XS[:, 128 * h:128 * h + 128], src[:, 512 * h:512 * h + 512], ("X0%d" if t == 0 else "XT X3%d") % h, "XQ%d" % h)
         if t == 0:
             for i in range(3):
-                dma("Y", T["AC%d" % i][:, 96:128].bitcast(dt.uint8), T.XQ[:, 0:32].bitcast(dt.uint8), "dfill", "XQ0", "pc%d" % i)
-                dma("Y", T["AS%d" % i][:, 96:128], T.XS[:, 0:32], "dfill", "XQ0", "ps%d" % i)
+                dma("Y", T["AC%d" % i][:, 0:32].bitcast(dt.uint8), T.XQ[:, 0:32].bitcast(dt.uint8), "dfill", "XQ0", "pc%d" % i)
+                dma("Y", T["AS%d" % i][:, 0:32], T.XS[:, 0:32], "dfill", "XQ0", "ps%d" % i)
             dma("Y", T.WQ[:].bitcast(dt.uint8), T.wc[:], "dw", "X01", "WQ")
             dma("Y", T.WS[:], T.ws[:], "dw", "X01", "WS")
             dma("Y", T.VT[:], T.v[:], "dv", "X01", "VT")
@@ -419,7 +430,7 @@ def rank_program(g, core, T, topo):
                True, True, "XQ%d URQ%d URS%d" % (s, t, t), "B%d" % s)
             tt(T.BT[:, s:576:4], B(s)[:, 0:144], T.TH[:], A.is_gt, "B%d TH" % s, "", "BT")
             ts(T.W2[:, 32 + 8 * s:40 + 8 * s], B(s)[:, 0:8], 0.0, None, A.is_gt, None, "B%d" % s, "", "W1")
-        quant(T.BQ[:], T.BS[:], T.BT[:], "BT", "BQ")
+        quant(T.BQ[:], T.BS[:], T.BT[:], "zBT BT", "BQ")
         mm(B(2)[:, 0:128], T.CQ[:, 0:128], T.CS[:, 0:128], T.BQ[:, 0:128], T.BS[:, 0:128], True, True, "CQ0 BQ", "B2")
         mm(B(3)[:, 0:128], T.CQ[:, 128:256], T.CS[:, 128:256], T.BQ[:, 24:152], T.BS[:, 24:152], True, False, "CQ1 BQ", "B3")
         mm(B(3)[:, 0:128], T.CQ[:, 256:384], T.CS[:, 256:384], T.BQ[:, 16:144], T.BS[:, 16:144], False, True, "CQ2 BQ", "", "B3")
@@ -432,10 +443,10 @@ def rank_program(g, core, T, topo):
         scan(T.W2[:, 16:32], T.H4[:, 0:16], bits, 0.0, A.mult, A.add, "H4 B3", "W3")
         act(T.WN[:, 0:16], bits, "B3", "bits")
         for s in range(2):
-            ts(T.OT[:, s::4], T.VB[:], T.W2[:, 8 * s + 7:8 * s + 8], None, A.is_equal, None, "VB W2 oz0 oz1", "", "OT")
-        quant(T.OQ[:], T.OS[:], T.OT[:], "OT MS%d" % t, "OQ")
+            ts(T.OT[:, s::4], T.VB[:], T.W2[:, 8 * s + 7:8 * s + 8], None, A.is_equal, None, "VB W2", "", "OT")
+        quant(T.OQ[:], T.OS[:], T.OT[:], "zOT OT MS%d" % t, "OQ")
         if t == 0:
-            quant(T.HMQ[:], T.HMS[:], T.HMT[:], "HMT MS0", "HMQ")
+            quant(T.HMQ[:], T.HMS[:], T.HMT[:], "zHMT HMT", "HMQ")
         for h in range(2):
             a, b, c = 256 * h, 256 * h + 256, 512 * h + 256
             mm(B(h)[:, 0:256], T.OQ[:, 128 * h:128 * h + 128], T.OS[:, 128 * h:128 * h + 128], T.HMQ[:], T.HMS[:], True, True, "OQ HMQ", "B%d" % h)
@@ -456,7 +467,7 @@ def rank_program(g, core, T, topo):
             act(T.FW[:, 1024:1280], B(DB[3])[:, 0:256], "B%d" % DB[3], "FW4")
         if t > 0:
             unpack()
-        for b in (2, 3, 0, 1):
+        for b in OPT["no"]:
             s, o = b % 2, 256 * (b // 2)
             mm(B(b)[:, 0:256], T.DQ[:, 128 * s:128 * s + 128], T.DP[:, 128 * s:128 * s + 128], T.MTQ[:, o:o + 256], T.MTS[:, o:o + 256], True, True,
                "DQ MQ%d" % (b // 2), "B%d" % b)
@@ -476,46 +487,56 @@ def rank_program(g, core, T, topo):
         if t == 0:
             unpack()
         for s in range(2):
-            ts(T.YY[:, 34 + 17 * s:50 + 17 * s], T["WL%d" % t][:], T.W2[:, 23 + 8 * s:24 + 8 * s], float(TOP + s * HALF + MARK), A.subtract, A.add,
-               "WL%d W3" % t, "y%d" % s)
-        ts(T.YY[:, 68:102], T.YY[:, 34:68], TOP + HALF + END, None, A.bitwise_and, None, "y0 y1 yd", "h")
-        for s in range(2):
-            ts(T.PN[:, 17 * s:17 * s + 16], T.YY[:, 68 + 17 * s:84 + 17 * s], float(TOP + s * HALF), END + MARK + 2.0, A.not_equal, A.mult, "h", "pn0%d" % s)
-        tt(T.HL[:, 1:34], T.YY[:, 68:101], T.YY[:, 69:102], A.subtract, "h", "df")
-        ts(T.YY[:, 0:34], T.YY[:, 34:68], 4.0, -3.0 * MARK, A.mult, A.add, "y0 y1 yd", "Y4")
+            top, y, h = TOP + s * HALF, T.YY[:, 32 + 16 * s:48 + 16 * s], T.YY[:, 64 + 17 * s:80 + 17 * s]
+            ts(y, T["WL%d" % t][:], T.W2[:, 23 + 8 * s:24 + 8 * s], float(top), A.subtract, A.add, "WL%d W3" % t, "y%d" % s)
+            ts(h, y, top, None, A.bitwise_and, None, "y%d" % s, "h%d" % s)
+            ts(T.PN[:, 17 * s:17 * s + 16], h, float(top), DEAD, A.is_equal, A.mult, "h%d" % s, "pn0%d" % s)
+        ts(T.YY[:, 0:32], T.YY[:, 32:64], 4.0, None, A.mult, None, "y0 y1", "Y4")
         for k in range(0, 8, 2):
-            ts(T.EK[:, 34 * k:34 * k + 68], T.YY[:, 0:68], MARK + 4 ** (k + 1), None, A.bitwise_and, None, "y0 y1 yd Y4", "ek%d ek%d" % (k, k + 1))
-        for k in range(8):
-            pn, kp, o = T.PN[:, 34 * k:34 * k + 34], " pd pn%d0 pn%d1" % (k, k), 34 + 34 * (k % 2)
-            scan(T.RR[:, 34 * k:34 * k + 34], T.HL[:, 0:34], pn, -1e9, A.add, A.max, "d0 df" + kp, "rr%d" % k)
-            if k < 7:
-                tt(T.HL[:, o:o + 34], T.EK[:, 34 * k:34 * k + 34], pn, A.min, "ek%d" % k + kp, "ev%d" % (k % 2))
-                for s in range(2):
-                    b = 34 * k + 17 * s
-                    ts(T.PN[:, b + 34:b + 50], T.HL[:, o + 17 * s:o + 17 * s + 16], T.RR[:, b + 16:b + 17], END + MARK + 2.0 * 4 ** (k + 1), A.is_ge, A.mult,
-                       "ev%d rr%d" % (k % 2, k), "pn%d%d" % (k + 1, s))
+            ts(T.EK[:, 32 * k:32 * k + 64], T.YY[:, 0:64], 4 ** (k + 1), None, A.bitwise_and, None, "y0 y1 Y4", "ek%d ek%d" % (k, k + 1))
+        for k in range(7):
+            pn, kp, d = T.PN[:, 34 * k:34 * k + 34], " pd pn%d0 pn%d1" % (k, k), 34 + 34 * (k % 2)
+            lv, o, kl = (T.YY, 64, "h0 h1 yd") if k == 0 else (T.HL, 134 * (k % 2), "H%d" % (k % 2))
+            tt(T.HL[:, d + 1:d + 34], lv[:, o:o + 33], lv[:, o + 1:o + 34], A.subtract, kl, "df%d" % (k % 2))
+            scan(T.RR[:, 34 * k:34 * k + 34], T.HL[:, d:d + 34], pn, -1e9, A.add, A.max, "d0 df%d" % (k % 2) + kp, "rr%d" % k)
+            if k < 6:
+                tt(T.HL[:, 134 * (1 - k % 2):134 * (1 - k % 2) + 34], lv[:, o:o + 34], pn, A.add, kl + kp, "H%d" % (1 - k % 2))
+            for s in range(2):
+                a, b = 32 * k + 16 * s, 34 * k + 17 * s
+                if k < 6:
+                    ts(T.PN[:, b + 34:b + 50], T.EK[:, a:a + 16], T.RR[:, b + 16:b + 17], DEAD, A.is_lt, A.mult, "ek%d rr%d" % (k, k), "pn%d%d" % (k + 1, s))
+                else:
+                    e = T.HL[:, 102 + 16 * s:118 + 16 * s]
+                    tt(e, T.EK[:, a:a + 16], T.HL[:, 17 * s:17 * s + 16], A.min, "ek6 H0", "e%d" % s)
+                    tt(e, e, T.PN[:, b:b + 16], A.add, "e%d pn6%d" % (s, s), "e%d" % s)
+                    ts(T.PN[:, b + 34:b + 50], e, T.RR[:, b + 16:b + 17], None, A.is_lt, None, "e%d rr6" % s, "pn7%d" % s)
         CU = (T.UU[:, 64:80], T.AL[:, 48:64])
         for n, a, b in ((0, 0, 4), (1, 4, 7)):
             o = 32 * n
-            ts(T.KK[:, 2 * a:2 * b], T.RR[:, 34 * a + 16:34 * b:17], float(MARK), None, A.is_gt, None, " ".join("rr%d" % k for k in range(a, b)), "K%d" % n)
+            ts(T.KK[:, 2 * a:2 * b], T.RR[:, 34 * a + 16:34 * b:17], 0.0, None, A.is_gt, None, " ".join("rr%d" % k for k in range(a, b)), "K%d" % n)
             tt(T.UU[:, o:o + 32], ind(T.KK[:, 0:16], LS[:, 2 * n:2 * n + 2]), T.SG[:, o:o + 32], A.mult, "K0 K1 Lk SG", "UU%d" % n)
             scan(CU[n], T.HS[:, 64 + 16 * n:80 + 16 * n], T.UU[:, o:o + 16], 0.0, A.mult, A.add, "HC UU%d" % n, "CU%d" % n)
             tt(T.AL[:, o:o + 16], T.UU[:, o + 16:o + 32], CU[n], A.subtract, "UU%d CU%d" % (n, n), "al%d" % n)
             if n == 0:
-                act(T.AL[:, 16:32:8], T.UU[:, 67:80:8], "CU0", "al2", scale=-1.0, bias=-256 * UNIT)
+                aff(OPT["wr"], T.AL[:, 16:32:8], T.UU[:, 67:80:8], -1.0, -256 * UNIT, "CU0", "al2")
             tt(T.IN2[:, o:o + 32], ind(T.AL[:, o:o + 32], LS[:, 10 + 2 * n:12 + 2 * n]), T.BD[:, 64 + o:96 + o], A.add, ("al0 al2", "al1 CU1")[n] + " La BD", "IN2%d" % n)
             for s in range(2):
                 start = T.UU[:, 71 + 8 * s:72 + 8 * s]
                 if n == 0:
                     a, b = 256 * s, 256 * s + 256
-                    act(T.INC[:, a:b], ind(T.AL[:, 0:32], LS[:, 48 + 16 * s:64 + 16 * s]), "al0 al2 Ln%d" % s, "INC%d" % s)
+                    for o1, n1, c in ((1, 2, 8 * s), (2, 4, 8 * s + 1), (4, 8, 8 * s + 2), (8, 16, 8 * s + 3), (0, 16, 16 + 8 * s)):
+                        aff(OPT["inc"][s] if n1 > 2 else "A", T.INC[:, a + o1:b:n1], T.ICOL[:, 0:256 // n1], 0.0, T.AL[:, c:c + 1],
+                            "ICOL al2" if o1 == 0 else "ICOL al0", "", "INC%d" % s)
                     scan(T.O[:, a:b], T.INC[:, a:b], B(s)[:, 0:256], start, A.add, A.max, "INC%d B%d CU0" % (s, s), "O%d" % s)
                 d = (T.H16[:, 16 * s:16 * s + 16], T.O[:, 256 * s + 15:256 * s + 256:16])[n]
                 scan(T.O2[:, o + 16 * s:o + 16 * s + 16], T.IN2[:, o + 16 * s:o + 16 * s + 16], d, start, A.add, A.max,
                      "IN2%d CU0 %s%d" % (n, ("H16", "O")[n], s), "", "O2%d" % n)
             tt(T.PK[:, 2 * o:2 * o + 64], ind(T.O2[:, o:o + 32], LS[:, 22:26]), T.EM[:, 128 + 2 * o:192 + 2 * o], A.mult, "O2%d Lp EM" % n, "PK%d" % n)
             scan(T.PK[:, 128 + 2 * o:192 + 2 * o], T.RST[:], T.PK[:, 2 * o:2 * o + 64], -1e9, A.max, A.add, "RST PK%d" % n, "PS%d" % n)
-        ts(T.YT[:, 64:96], ind(T.RR[:], LS[:, 42 + 2 * t:44 + 2 * t]), float(MARK), None, A.is_le, None, "Lr " + " ".join("rr%d" % k for k in range(8)), "DF")
+        ts(T.YT[:, 64:96], ind(T.RR[:], LS[:, 42 + 2 * t:44 + 2 * t]), 0.0, None, A.is_le, None, "Lr " + " ".join("rr%d" % k for k in range(8)), "DF")
+        for s in range(2):
+            c = 64 + 2 * ((3 * t + 7) % 8) + s
+            least(T.YT[:, c:c + 1], T.PN[:, 238 + 17 * s:254 + 17 * s], "pn7%d" % s, "", "DF")
         turn(T.YT[:, 96:128], T.YT[:, 64:96], "DF", "TF")
         for q in range(4):
             dma("YA"[q % 2], T.DL[q::4, 32:48], T.YT[32 * q:32 * q + 16, 96:128], "dk%d" % t, "TF", "", "dl")
@@ -558,25 +579,25 @@ def rank_program(g, core, T, topo):
             else:
                 ts(o, i, 2.0 ** -6, None, A.mult, None, "XZ%d LU" % b, "", "ET")
         quant(T.EQ[:], T.ES[:], T.ET[:], "ET ET4", "EQ")
-        remote(T["AC%d" % t][:, 0:96].bitcast(dt.uint8), T.EQ[:, 0:96].bitcast(dt.uint8), "ca%d" % t, "lc%d" % t, "EQ", "AC%d" % t)
-        remote(T["AS%d" % t][:, 0:96], T.ES[:, 0:96], "ca%d" % t, "lc%d" % t, "EQ", "AC%d" % t)
-        ts(L[:, 80:96], L[:, 64:80], DN, 256.0, A.add, A.add, "l7 ct", "pos")
+        remote(T["AC%d" % t][:, 32:128].bitcast(dt.uint8), T.EQ[:, 0:96].bitcast(dt.uint8), "ca%d" % t, "lc%d" % t, "EQ", "AC%d" % t)
+        remote(T["AS%d" % t][:, 32:128], T.ES[:, 0:96], "ca%d" % t, "lc%d" % t, "EQ", "AC%d" % t)
+        ts(L[:, 80:96], L[:, 64:80], DN, 256.0, A.add, A.add, "l7 ct EQ", "pos")
         ts(L[:, 96:112], L[:, 80:96], 352.0, 4096.0, A.is_lt, A.mult, "pos", "m0")
         tt(L[:, 112:128], L[:, 96:112], L[:, 80:96], A.min, "m0 pos", "m1")
         tt(L[:, 128:144], L[:, 112:128], JL, A.max, "m1 JL", "m2")
         cp(T.SU[:], L[:, 128:144], "m2", "SU")
         if t == 2:
-            cp(T.AF[:, 0:16], T.AU[:], "AU", "af")
+            cp(T.AF[:, 0:16], T.AU[:], "AU EQ", "af")
             turn(T.AF[:, 32:64], T.AF[:, 0:32], "af", "at")
             for q in range(8):
                 p = 32 * (q // 2)
                 dma("Y", T.al[q:q + 1, 0:256], T.AF[p:p + 16, 32 + 16 * (q % 2):48 + 16 * (q % 2)], "dout", "at")
             dma("Y", T.al[:, 256:352], T.LR[0::16, 0:96], "dout", "LR")
-        AC, AS, ka = T["AC%d" % t], T["AS%d" % t], " AC%d pc%d ps%d" % (t, t, t)
+        AC, AS, ka = T["AC%d" % t][:], T["AS%d" % t][:, 0:128], " AC%d pc%d ps%d" % (t, t, t)
         for b in range(4):
-            kb, o, i = "B%d" % DB[b], T.XW[:, 352 * b + 256:352 * b + 352], B(DB[b])[:, 0:96]
-            mm(B(DB[b])[:, 0:128], T.WQ[:, 128 * b:128 * b + 128], T.WS[:, 128 * b:128 * b + 128], AC[:], AS[:], True, False, "WQ WS" + ka, kb)
-            mm(B(DB[b])[:, 0:128], T.ELQ[:, 128 * b:128 * b + 128], T.ELS[:, 128 * b:128 * b + 128], AC[:], AS[:], False, True, "EL%d" % b + ka, "", kb)
+            kb, o, i = "B%d" % DB[b], T.XW[:, 352 * b + 256:352 * b + 352], B(DB[b])[:, 32:128]
+            mm(B(DB[b])[:, 0:128], T.WQ[:, 128 * b:128 * b + 128], T.WS[:, 128 * b:128 * b + 128], AC, AS, True, False, "WQ WS" + ka, kb)
+            mm(B(DB[b])[:, 0:128], T.ELQ[:, 128 * b:128 * b + 128], T.ELS[:, 128 * b:128 * b + 128], AC, AS, False, True, "EL%d" % b + ka, "", kb)
             win, r = T.XW[:, 352 * b:352 * b + 352], "XZ%d XT%d SU" % (b, b)
             if b % 2 == 0:
                 act(o, i, kb, "XT%d" % b, scale=2.0)

@@ -1,46 +1,46 @@
-from concourse.mybir import dt, AluOpType, AxisListType, ActivationFunctionType
+from concourse.mybir import dt, AluOpType, ActivationFunctionType
 
 F32, BF, I32, U16, F8, U8 = "float32", "bfloat16", "int32", "uint16", "float8_e4m3fn_x4", "uint8"
 SCRATCH = {}
 for _n, _w, _d in [
-        ("X0", 1024, BF), ("UT", 512, BF), ("VT", 512, BF), ("WQ", 512, F8), ("WS", 512, U8),
-        ("UQ", 128, F8), ("US", 128, U8), ("VQ", 128, F8), ("VS", 128, U8), ("URQ", 432, F8), ("URS", 432, U8),
-        ("ELT", 2048, BF), ("ELQ", 512, F8), ("ELS", 512, U8), ("CT", 1536, BF), ("CQ", 384, F8), ("CS", 384, U8),
-        ("HMT", 1024, BF), ("HMQ", 256, F8), ("HMS", 256, U8), ("MTT", 2048, BF), ("MTQ", 512, F8), ("MTS", 512, U8),
-        ("ICOL", 256, F32), ("VB", 256, BF), ("I8", 144, BF), ("I16", 256, BF), ("JP", 128, BF), ("TH", 144, F32),
-        ("IP", 16, I32), ("SC", 24, F32), ("UI", 30, I32), ("UL", 30, U16), ("PLF", 16, F32), ("PL", 16, U16),
-        ("RW", 32, F32), ("FR", 160, F32), ("FS", 136, F32), ("LS", 80, U16), ("KC", 768, BF),
-        ("CB", 64, F32), ("CE", 128, F32), ("RST", 64, F32), ("H4", 128, F32), ("HS", 96, F32),
-        ("NEG", 256, BF), ("JL", 32, F32), ("MK", 256, F32),
-        ("XQ", 256, F8), ("XS", 256, U8), ("XT", 1024, BF), ("BT", 608, BF), ("BQ", 152, F8), ("BS", 152, U8),
-        ("W4", 128, F32), ("W2", 48, F32), ("WN", 72, F32), ("SG", 64, F32),
-        ("OT", 1024, BF), ("OQ", 256, F8), ("OS", 256, U8), ("HB", 512, BF), ("DS", 1024, BF), ("DG", 512, BF), ("DH", 512, BF),
-        ("DT", 1024, BF), ("DQ", 256, F8), ("DP", 256, U8), ("MH", 512, BF), ("HH", 512, F32), ("H16", 34, F32),
-        ("BD", 128, F32), ("EM", 256, F32), ("YY", 102, I32), ("EK", 272, I32), ("HL", 168, F32), ("RR", 272, F32),
-        ("KK", 16, F32), ("PN", 272, F32), ("UU", 80, F32), ("AL", 64, F32), ("INC", 512, F32), ("IN2", 64, F32), ("O", 512, F32), ("O2", 64, F32),
-        ("PK", 256, F32), ("YT", 128, F32), ("AI", 96, I32), ("TU", 32, U16), ("LF", 160, F32), ("DL", 128, F32), ("WC", 96, F32),
-        ("AF", 64, F32), ("AU", 16, U16), ("PU", 16, U16), ("LU", 8, U16), ("SU", 16, U16), ("LR", 256, F32), ("LM", 96, F32),
-        ("FW", 1280, BF), ("GW", 768, BF), ("XW", 1408, BF), ("ET", 512, BF), ("EQ", 128, F8), ("ES", 128, U8), ("YO", 256, F32)]:
+        ("X0", 1024, BF), ("UT", 1024, BF), ("VT", 512, BF), ("WQ", 512, F8), ("WS", 512, U8),
+        ("UQ", 256, F8), ("US", 256, U8), ("VQ", 128, F8), ("VS", 128, U8),
+        ("ELT", 516, BF), ("ELQ", 512, F8), ("ELS", 512, U8), ("MTT", 2048, BF), ("MTQ", 512, F8), ("MTS", 512, U8),
+        ("ICOL", 256, F32), ("VB", 256, BF), ("I16", 256, BF), ("TAB", 256, F32), ("IP", 40, I32), ("SC", 32, F32),
+        ("RW", 64, F32), ("LS", 56, U16), ("CE", 272, F32), ("LW", 544, F32), ("WX", 64, F32), ("LX", 18, U16), ("HS", 112, F32),
+        ("NEG", 256, BF), ("JL", 16, F32), ("MK", 256, F32), ("ICT", 256, F32), ("LT", 16, U16),
+        ("XQ", 256, F8), ("XS", 256, U8), ("XT", 1024, BF), ("W1", 16, F32), ("W2", 32, F32), ("WN", 16, F32), ("MS", 24, U16),
+        ("OT", 512, BF), ("OQ", 128, F8), ("OS", 128, U8), ("HB", 512, BF), ("DS", 1024, BF), ("DH", 512, BF),
+        ("DT", 1024, BF), ("DQ", 256, F8), ("DP", 256, U8), ("MH", 512, BF), ("HH", 512, F32), ("H16", 40, F32),
+        ("DM", 272, F32), ("YY", 68, I32), ("NB", 68, I32), ("N2", 136, I32), ("EK", 476, I32), ("DF", 68, F32), ("TH", 96, F32),
+        ("RR", 272, F32), ("PN", 544, F32), ("DI", 40, F32), ("INC", 128, F32), ("O", 512, F32), ("VH", 34, F32),
+        ("CL", 102, F32), ("PS", 272, F32), ("YT", 96, F32), ("YA", 64, F32), ("TU", 32, U16),
+        ("IN", 36, F32), ("RB", 96, F32), ("RT", 128, F32), ("CC", 20, F32), ("LF", 128, F32), ("AI", 32, I32), ("AF", 16, F32), ("LO", 96, F32),
+        ("AU", 16, U16), ("PU", 16, U16), ("LU", 8, U16), ("SU", 16, U16), ("LR", 256, F32), ("LM", 96, F32),
+        ("FW", 2048, BF), ("FT", 1024, BF), ("FL", 384, BF), ("GW", 1024, BF), ("XW", 1408, BF),
+        ("ET", 512, BF), ("EQ", 128, F8), ("ES", 128, U8), ("YO", 256, F32)]:
     SCRATCH[_n] = ("sbuf", [128, _w], _d)
 for _t in range(3):
-    SCRATCH["MS%d" % _t] = ("sbuf", [128, 16], F32)
-    SCRATCH["WL%d" % _t] = ("sbuf", [128, 16], F32)
+    SCRATCH["WL%d" % _t] = ("sbuf", [128, 4], U16)
     SCRATCH["AC%d" % _t] = ("sbuf", [128, 128], F8)
     SCRATCH["AS%d" % _t] = ("sbuf", [128, 128], U8)
 for _b in range(8):
     SCRATCH["B%d" % _b] = ("psum", [128, 512], F32)
-SEMAPHORES = ["cV", "cA", "cP", "cG", "dx", "dy", "du", "dv", "dw", "dfill", "dout"]
+SEMAPHORES = ["cV", "cA", "cP", "cG", "dx", "dy", "du", "du2", "dv", "dw", "dfill", "dout"]
 for _t in range(3):
-    SEMAPHORES += ["wa%d" % _t, "ca%d" % _t, "lw%d" % _t, "lc%d" % _t, "dl%d" % _t, "dk%d" % _t]
+    SEMAPHORES += ["wa%d" % _t, "ca%d" % _t, "lw%d" % _t, "lc%d" % _t, "dl%d" % _t, "dk%d" % _t, "dc%d" % _t]
 
 RAISE = 2.0 ** -6
 UNIT = 2.0 ** -17
-TOP = 0x15555
+LOW = 0x5555
 HALF = 1 << 18
-DEAD = -2.0 ** 19
-CYCLE, WAKE, ISSUE, LOCAL, REMOTE, TURNS = 0.00104, (0.19, 0.19), 0.05, 1.2, 1.7, 5
+DEAD = 2.0 ** 19
+CEIL = 2.0 ** 17
+STEP = 1024.0
+RL = 68
+CYCLE, WAKE, ISSUE, LOCAL, REMOTE, TURNS, MOVES = 0.00104, (0.19, 0.19), 0.05, 1.2, 1.7, 5, 60000
 WEIGHTS = [(p, h) for p in (8.0, 12.0, 20.0, 40.0) for h in (1.0, 2.0, 4.0, 8.0)]
-OPT = {"inc": "AA", "wr": "A", "no": (0, 2, 1, 3), "z": "AVAA", "up": "AA", "hi": "AA"}
+OPT = {"no": (2, 0, 3, 1), "dq": "YAYAYAYA", "et": "VAAA", "xz": "AAVV"}
 ORDER = []
 
 
@@ -160,6 +160,43 @@ def rank_program(g, core, T, topo):
                 if best is None or span < best[0]:
                     best = (span, seq)
                 rank = lay(post, pre, end, late, patience, hurry)[1]
+        gaps = [list(p.items()) for p in pre]
+        queue = [c["e"] for c in calls]
+
+        def times(seq, a, end):
+            free = {}
+            for i in reversed(seq[:a]):
+                if queue[i] not in free:
+                    free[queue[i]] = end[i]
+                    if len(free) == len(Q):
+                        break
+            for i in seq[a:]:
+                t0 = free.get(queue[i], 0.0)
+                for j, d in gaps[i]:
+                    if end[j] + d > t0:
+                        t0 = end[j] + d
+                free[queue[i]] = end[i] = t0 + busy[i]
+            return max(end[i] + late[i] for i in seq[-40:]) + 0.02 * sum(end) / n
+        seq, end, x = best[1], [0.0] * n, 1
+        span = times(seq, 0, end)
+        for turns in range(MOVES):
+            if turns % 500 == 0:
+                seq.sort(key=lambda i: end[i] - busy[i])
+            x = (x * 1103515245 + 12345) % (1 << 31)
+            p, step, far = (x >> 8) % n, (1, -1)[x >> 4 & 1], 1 + (x >> 5 & 7) % 5
+            i, q = seq[p], p
+            while far and 0 <= q + step < n and seq[q + step] not in (post[i] if step > 0 else pre[i]):
+                q += step
+                far -= queue[seq[q]] == queue[i]
+            if far:
+                continue
+            new = list(seq)
+            new.insert(q, new.pop(p))
+            trial = list(end)
+            s = times(new, min(p, q), trial)
+            if s <= span:
+                seq, end, span = new, trial, s
+        best = (max(end[i] + late[i] for i in range(n)), seq)
         return best[1]
 
     def issue(seq):
@@ -215,9 +252,6 @@ def rank_program(g, core, T, topo):
     def scan(out, d0, d1, ini, o0, o1, r, w="", add=""):
         op("V", lambda: v.tensor_tensor_scan(out, d0, d1, ini, o0, o1), r, w, add, cycles(out, d0, d1, fast=True))
 
-    def least(out, a, r, w, add):
-        op("V", lambda: v.tensor_reduce(out, a, AxisListType.X, A.min), r, w, add, cycles(a, a))
-
     def turn(out, a, r, w):
         op("V", lambda: v.transpose(out, a), r, w, "", cycles(out, a))
 
@@ -227,22 +261,14 @@ def rank_program(g, core, T, topo):
     def quant(c, s, t, r, w):
         op("V", lambda: v.quantize_mx(c, s, t), r, w, "", 15 + 0.28 * t.shape[1])
 
-    def act(out, in_, r, w="", add="", scale=1.0, bias=None):
+    def act(out, in_, r, w="", add="", scale=1.0, bias=None, func=None):
         n = cycles(out, in_, least=100)
         if bias is not None:
-            op("A", lambda: ac.activation(out, bare(in_), AF.Identity, bias=bias, scale=scale), r, w, add, n)
+            op("A", lambda: ac.activation(out, bare(in_), func or AF.Identity, bias=bias, scale=scale), r, w, add, n)
         elif scale == 1.0:
             op("A", lambda: ac.activation(out, bare(in_), AF.Copy), r, w, add, n)
         else:
             op("A", lambda: ac.activation(out, bare(in_), AF.Copy, scale=scale), r, w, add, n)
-
-    def aff(e, out, in_, m, c, r, w="", add=""):
-        if e == "A":
-            act(out, in_, r, w, add, scale=m, bias=c)
-        elif c is None:
-            ts(out, in_, m, None, A.mult, None, r, w, add)
-        else:
-            ts(out, in_, m, c, A.mult, A.add, r, w, add)
 
     def row(out, n, a, b, w="", add=""):
         act(out, T.ICOL[:, 0:n], "ICOL", w, add, scale=float(a), bias=float(b))
@@ -256,163 +282,128 @@ def rank_program(g, core, T, topo):
         else:
             op("G", lambda: g.iota(out, pat, base, ch), "", w, add, 130 + 2 * out.shape[1])
 
-    def where0(out, in_, pat, base, r, w="", add=""):
-        op("G", lambda: g.affine_select(out, in_, pat, A.is_equal, 0.0, base, 1), r, w, add, 170 + 2 * out.shape[1])
-
     def B(b):
         return T["B%d" % b]
 
-    IP, SC, LS, RW, FR, FS, MK = T.IP, T.SC, T.LS, T.RW, T.FR, T.FS, T.MK
+    def back(buf, a, n):
+        return buf[:, a:a - n:-1] if a >= n else buf[:, a::-1]
+
+    IP, SC, LS, RW, MK, PN, EK, RR = T.IP, T.SC, T.LS, T.RW, T.MK, T.PN, T.EK, T.RR
 
     def sc(c):
         return SC[:, c:c + 1]
-    H1, H2, HN = T.HS[:, 0:32], T.HS[:, 32:48], T.HS[:, 48:64]
+    H1, H2, H4, HN, THR = T.HS[:, 0:32], T.HS[:, 32:48], T.HS[:, 48:64], T.HS[:, 64:80], T.HS[:, 96:112]
+    JL = T.JL[:, 0:16]
 
-    dma("A", T.UT[:], T.u[:], "du", "", "UT")
+    dma("A", T.UT[:, 0:512], T.u[:], "du", "", "UT0")
     dma("Y", T.X0[:, 0:512], T.x[:, 0:512], "dx", "", "X00")
     dma("Y", T.X0[:, 512:1024], T.x[:, 512:1024], "dy", "", "X01")
 
-    iota(IP[:, 0:1], [[0, 1]], 0, 1, "ip0", flag=False)
-    iota(T.UI[:], [[3, 3], [0, 10]], 7 + 128, -1, "UI", flag=False)
-    iota(T.I16[:], [[0, 16], [1, 16]], 0, 0, "I16")
-    iota(T.I8[:], [[1, 18], [0, 8]], 0, 0, "I8")
-    iota(SC[:, 4:8], [[-8, 2], [128, 2]], 0, 1, "s4")
-    iota(SC[:, 14:16], [[-128, 2]], 255, -1, "s14")
-    iota(T.JP[:], [[1, 4], [4, 2], [16, 16]], 0, 0, "JP")
     iota(T.ICOL[:], [[1, 256]], 0, 0, "ICOL")
+    iota(IP[:, 0:1], [[0, 1]], 0, 1, "ip0", flag=False)
+    iota(T.I16[:], [[0, 16], [1, 16]], 0, 0, "I16")
+    iota(T.TAB[:, 0:8], [[16, 2], [4, 2], [1, 2]], 0, 0, "TAB")
+    for i in range(3, 8):
+        act(T.TAB[:, 1 << i:2 << i], T.TAB[:, 0:1 << i], "TAB", "TAB", bias=float(4 ** i))
+    iota(SC[:, 0:4], [[15 * 2048, 2], [128, 2]], 256, 1, "J")
+    iota(RW[:, 16:24], [[17, 2], [0, 4]], 0, 0, "rw16")
+    iota(RW[:, 36:42], [[-3, 3], [4, 2]], 8, 0, "rw36")
+    iota(RW[:, 42:48], [[-3, 3], [0, 2]], 8, 0, "rw42")
+    iota(RW[:, 48:52], [[2, 2], [0, 2]], 0, 0, "rw48")
+    iota(T.LW[:, 0:136], [[-1, 4], [8, 2], [0, 17]], 48 + 7, 0, "LW")
+    iota(T.LW[:, 16:136:17], [[-1, 4], [8, 2]], 32 + 7, 0, "LW")
+    row(T.CE[:, 0:136], 136, 0, 0, "CE")
+    row(T.CE[:, 0:136:17], 8, 0, 2 ** 20, "CE")
+    for k in range(4):
+        o, z = 34 * k, 1 << k
+        for a, n, c, b, m in ((z, 8 >> k, 0, 1, 4), (2 * z, (8 >> k) - 1, 16, -9, -12)):
+            if n:
+                iota(T.LW[:, o + a:o + 16:2 * z], [[0, n]], c + 7 - k, 0, "", "LW lw%d" % k)
+                iota(T.CE[:, o + a:o + 16:2 * z], [[m * int(STEP), n]], b * int(STEP), 0, "", "CE ce%d" % k)
+        act(T.LW[:, o + 17:o + 33], T.LW[:, o:o + 16], "lw%d" % k, "", "LV", bias=8.0)
+        act(T.CE[:, o + 17:o + 33], T.CE[:, o:o + 16], "ce%d" % k, "", "CF")
+    act(T.LW[:, 136:272], T.LW[:, 0:136], "LW LV", "LV", bias=-4.0)
+    act(T.CE[:, 136:272], T.CE[:, 0:136], "CE CF", "CF")
+    row(T.WX[:, 48:64], 16, 0, 0, "wx0")
     row(T.VB[:], 256, 1, 0, "VB")
-    for z in range(4):
-        iota(FR[:, 128 + 2 * z::8], [[0, 2], [64, 2]], 31 - (16 >> z), 0, "", "EA")
-    iota(T.PLF[:], [[-8, 2], [-1, 4], [-4, 2]], 255, 0, "PLF")
-    iota(FR[:, 0:16], [[1, 2], [0, 2], [2, 4]], 0, 0, "", "FR")
-    iota(FR[:, 112:128], [[8, 2], [-40, 2], [-1, 4]], 47, 0, "", "FR")
-    for c, pat, base in ((0, [[8, 2], [0, 2]], 0), (4, [[-4, 2], [16, 2]], 0), (8, [[-4, 2], [8, 2]], 20), (12, [[0, 2], [8, 2]], 0),
-                         (16, [[7, 2], [0, 2]], 12), (20, [[16, 4]], 0)):
-        iota(RW[:, c:c + 4], pat, base, 0, "rw%d" % c)
-    iota(IP[:, 8:14], [[-6, 3], [0, 2]], 48, 1, "ip8", flag=False)
-    iota(T.JL[:, 16:32], [[16, 16]], 0, 0, "JLF")
-    fill(T.KC[:, 256:768], 32.0, "KC1")
-    fill(T.KC[:, 0:256], UNIT, "KC0")
-    for nm in ("CT", "BT", "HMT", "OT"):
-        for i in (2, 3):
-            if OPT["z"][("CT", "BT", "HMT", "OT").index(nm)] == "V":
-                fill(T[nm][:, i::4], 0.0, "", "z" + nm)
-            else:
-                act(T[nm][:, i::4], T.KC[:, 256:256 + SCRATCH[nm][1][1] // 4], "KC1", "", "z" + nm, scale=0.0)
-    for i in (0, 1):
-        fill(T.BT[:, 576 + i::4], 0.0, "", "zBT")
-    fill(T.H4[:], 4.0, "H4")
-    fill(T.H4[:, 0::8], 0.0, "H4")
-    row(T.HS[:, 32:64], 32, 0, 2, "HS2")
-    row(T.HS[:, 32:48:8], 2, 0, 0, "", "HS2")
-    row(T.HS[:, 48:64:4], 4, 0, 0, "", "HS2")
-    row(T.HS[:, 0:32], 32, 0, 1, "H1")
-    row(T.HS[:, 0:32:16], 2, 0, 0, "H1")
-    row(T.HS[:, 64:96], 32, 0, 1, "HC")
-    row(T.HS[:, 64:80:8], 2, 0, 0, "", "HC")
-    row(T.HS[:, 80:96:4], 4, 0, 0, "", "HC")
+    fill(T.MS[:], 0, "MS0 MS1 MS2")
+    fill(H2, 2.0, "H2")
+    fill(T.HS[:, 32:48:8], 0.0, "H2")
+    for key, o, n, c, a, z in (("H1", 0, 32, 1, 0, 16), ("H4", 48, 16, 4, 8, 8), ("HN", 64, 16, 2, 0, 4)):
+        row(T.HS[:, o:o + n], n, 0, c, key)
+        row(T.HS[:, o + a:o + n:z], len(range(a, n, z)), 0, 0, key)
     row(T.NEG[:], 256, 0, -1, "NEG")
-    for o, n, z in ((17, 2, 0), (18, 4, 1), (20, 8, 2), (24, 16, 3), (16, 16, 4)):
-        row(FR[:, o:32:n], 16 // n, 0, z, "", "FR")
-    for o, n, z in ((0, 8, 1), (8, 4, 2), (12, 2, 3), (14, 2, 3)):
-        row(FR[:, 48 + o:48 + o + n], n, 1 << z, (1 << z) - 1, "", "FR")
-        if o < 14:
-            row(FR[:, 32 + o:32 + o + max(n, 4)], max(n, 4), 0, z, "", "FR")
-    act(FR[:, 129::2], FR[:, 128::2], "EA", "EB", bias=32.0)
-    for i in range(3):
-        o = -6 * i % 16
-        act(FR[:, 64 + 16 * i:80 + 16 * i], FR[:, 128 + o:144 + o], "EA EB", "", "FR")
-    for o, n in ((1, 2), (2, 4), (4, 8)):
-        act(T.CB[:, o::n], T.I16[:, o:64:n], "I16", "", "CB", scale=1.0 / n, bias=-o / n)
-    act(T.CB[:, 0::8], T.I16[:, 0:64:8], "I16", "", "CB", scale=-0.125, bias=1.0)
-    for o, n in ((0, 16), (16, 8), (24, 4), (28, 2)):
-        row(T.CE[:, o:o + n:2], n // 2, 2, 1, "", "CE0")
-        row(T.CE[:, o + 1:o + n:2], n // 2, 2, 0, "", "CE0")
-    row(T.CE[:, 30:32], 2, 0, -1, "", "CE0")
-    act(T.CE[:, 32:64], T.CE[:, 0:32], "CE0", "CE1")
-    act(T.CE[:, 64:128], T.CE[:, 0:64], "CE0 CE1", "CE")
-    row(T.WN[:, 32:40], 8, 0, 0, "wn0")
-    row(T.AL[:, 16:32], 16, 0, 0, "al2")
-    row(T.KK[:, 0:16], 16, 0, 0, "K0 K1")
-    row(T.DL[:, 0:64], 64, 0, 0, "dl pm p0")
+    row(THR, 16, 0, 1e9, "THR")
+    scan(T.HS[:, 96:104], T.HS[:, 48:56], T.NEG[:, 0:8], 0.5, A.mult, A.max, "H4 NEG", "THR")
+    row(PN[:, 0:256], 256, 0, 0, "", "p0")
+    row(PN[:, 256:512], 256, 0, 0, "", "p0")
+    row(PN[:, 512:544], 32, 0, 0, "", "p0")
+    act(PN[:, RL + 32:7 * RL:34], T.ICOL[:, 0:12], "ICOL p0", "pd", scale=0.0, bias=CEIL)
+    fill(T.YY[:], 0, "yd")
+    fill(T.YY[:, 32:33], 4 * HALF, "yd")
+    row(T.DF[:, 0::34], 2, 0, 0, "d0")
+    row(T.DI[:, 0:1], 1, 0, 0, "", "di0")
+    row(T.DI[:, 34:40], 6, 0, 4 * DEAD, "", "di0")
+    row(T.IN[:, 32:36], 4, 0, 0, "in0")
+    row(T.RT[:, 31:32], 1, 0, -1, "rt0")
     row(T.ET[:, 384:512], 128, 0, 0, "ET4")
-    row(T.AF[:], 64, 0, 0, "af")
-    ts(IP[:, 1:2], IP[:, 0:1], 15, None, A.bitwise_and, None, "ip0", "ip1")
-    ts(IP[:, 2:3], IP[:, 0:1], 4, None, A.arith_shift_right, None, "ip0", "ip2")
-    ts(IP[:, 3:4], IP[:, 0:1], 5, None, A.arith_shift_right, None, "ip0", "ip3")
-    ts(IP[:, 4:5], IP[:, 2:3], 1, None, A.bitwise_and, None, "ip2", "ip4")
-    for c, i, a in ((1, 1, 0.0), (2, 2, 0.0), (3, 2, 8.0)):
-        ts(sc(c), IP[:, i:i + 1], a, None, A.add, None, "ip%d" % i, "s%d" % c)
-    ts(sc(8), IP[:, 1:2], -16.0, 255.0, A.mult, A.add, "ip1", "s8")
-    ts(sc(9), IP[:, 3:4], -1.0, sc(8), A.mult, A.add, "ip3 s8", "s9")
-    ts(sc(10), IP[:, 4:5], -4.0, sc(9), A.mult, A.add, "ip4 s9", "s10")
-    act(sc(11), sc(10), "s10", "s11", bias=-8.0)
-    ts(sc(12), IP[:, 1:2], 0.0, None, A.is_equal, None, "ip1", "s12")
-    act(sc(16), sc(1), "s1", "s16", scale=16.0)
-    act(SC[:, 17:19], SC[:, 10:12], "s10 s11", "s17", scale=-1.0, bias=131072.0 + 255.0)
-    row(T.RST[:], 64, 0, -1e9, "RST")
-    for o in (0, 16, 24, 28, 30):
-        act(T.RST[:, o::32], SC[:, 17:19], "s17", "", "RST")
-    act(T.JL[:, 0:16], T.JL[:, 16:32], "JLF s1", "JL", bias=sc(1))
-    act(T.DL[:, 0:1], sc(12), "s12", "p0", scale=-1.0)
-    ts(T.TH[:], T.I8[:], sc(1), 1e29, A.not_equal, A.mult, "I8 s1", "TH")
-    fill(T.TH[:, 136:144], 0.0, "TH")
-    scan(T.RR[:, 0:8], T.H4[:, 1:65:8], T.NEG[:, 0:8], 0.25, A.mult, A.max, "H4 NEG", "rr0")
-    for s in range(2):
-        act(T.PN[:, 16 + 17 * s::34], T.RR[:, 0:8], "rr0", "", "pd", scale=-6.0)
-        fill(T.YY[:, 80 + 17 * s:81 + 17 * s], TOP + s * HALF - 2, "", "yd")
-    row(T.HL[:, 34:102:34], 2, 0, 0, "d0")
-    row(T.RR[:, 238:272], 34, 0, 0, "rr7")
-    for s in range(2):
-        ts(T.CT[:, s:512:4], T.I16[:, 0:128], sc(2 + s), None, A.is_equal, None, "I16 s%d" % (2 + s), "", "CT0")
-        for h in range(2):
-            ts(T.CT[:, 512 * s + 512 + h:512 * s + 1024:4], T.JP[:], sc(4 + 2 * s + h), None, A.is_equal, None, "JP s4", "", "CT%d" % (1 + s))
-        ts(T.HMT[:, s::4], T.VB[:], sc(14 + s), 256.0, A.is_equal, A.mult, "VB s14", "", "HMT")
-    for i in range(3):
-        quant(T.CQ[:, 128 * i:128 * i + 128], T.CS[:, 128 * i:128 * i + 128], T.CT[:, 512 * i:512 * i + 512], "zCT CT%d" % i, "CQ%d" % i)
+    act(T.H16[:, 16:34:17], SC[:, 0:2], "J", "h0")
+    act(T.VH[:, 16:34:17], SC[:, 0:2], "J", "v0")
+    for c, sh, m in ((1, 0, 15), (2, 2, 2), (3, 0, 1), (4, 1, 1), (5, 2, 1), (6, 1, 7), (7, 0, 6)):
+        ts(IP[:, c:c + 1], IP[:, 0:1], sh, m, A.arith_shift_right, A.bitwise_and, "ip0", "", "ip")
+    cp(SC[:, 4:9], IP[:, 1:6], "ip", "s4")
+    cp(SC[:, 24:26], IP[:, 6:8], "ip", "s24")
+    for c, i, m, a in ((11, 4, 16, 0), (9, 7, 17, 16), (12, 6, 17, 16), (10, 8, 8, 0)):
+        act(sc(c), sc(i), "s4", "s%d" % c, scale=float(m), bias=float(a))
+    ts(sc(16), sc(4), 0.0, 34.0, A.is_equal, A.mult, "s4", "s16")
+    act(JL, T.ICOL[:, 0:16], "ICOL s11", "JL", bias=sc(11))
+    cp(T.LT[:], JL, "JL", "LT")
+    act(T.ICT[:], ind(T.ICOL[:], T.LT[:]), "ICOL LT", "ICT")
+    ts(LS[:, 36:44], RW[:, 16:24], sc(4), sc(16), A.add, A.max, "rw16 s4 s16", "Li")
+    ts(IP[:, 8:14], RW[:, 36:42], sc(5), sc(6), A.add, A.add, "rw36 s4", "k0")
+    ts(IP[:, 16:22], IP[:, 8:14], 7, None, A.bitwise_and, None, "k0", "k1")
+    ts(RW[:, 0:6], IP[:, 16:22], 5.0, 34.0, A.min, A.mult, "k1", "k5")
+    ts(LS[:, 44:50], RW[:, 0:6], sc(9), None, A.add, None, "k5 s9", "Lr")
+    ts(LS[:, 30:36], IP[:, 16:22], sc(10), None, A.max, None, "k1 s10", "Lt")
+    act(T.TH[:], ind(THR, LS[:, 30:36]), "THR Lt", "TH")
+    ts(IP[:, 24:30], RW[:, 42:48], sc(24), None, A.add, None, "rw42 s24", "k2")
+    ts(IP[:, 32:38], IP[:, 24:30], 7, None, A.bitwise_and, None, "k2", "k3")
+    ts(LS[:, 50:56], IP[:, 32:38], 34.0, sc(12), A.mult, A.add, "k3 s12", "Ly")
+    act(sc(13), sc(25), "s24 s4", "s13", scale=4.0, bias=sc(6))
+    ts(LS[:, 0:4], RW[:, 48:52], sc(13), None, A.add, None, "rw48 s13", "Lk")
+    ts(MK[:, 128:256], T.I16[:, 0:128], sc(4), 8000.0, A.not_equal, A.mult, "I16 s4", "mk0")
+    tt(MK[:, 1:96], MK[:, 129:224], MK[:, 128:223], A.subtract, "mk0", "MK")
+    act(MK[:, 0:1], MK[:, 128:129], "mk0", "mk1")
+    act(MK[:, 16:96:16], MK[:, 16:96:16], "MK", "MK", bias=-3000.0)
+    for a, b in ((0, 96), (96, 192), (192, 272)):
+        scan(T.LW[:, 272 + a:272 + b], MK[:, 0:b - a], T.LW[:, a:b], 0.0, A.add, A.max, "MK mk1 LW LV", "", "LY")
+    ts(T.LX[:, 0:17], T.LW[:, 287::16], MK[:, 143:144], None, A.subtract, None, "LY mk0", "Lm")
+    iota(SC[:, 20:22], [[128, 2]], 0, 1, "s20")
+    fill(T.ELT[:], 0.0, "ELT")
+    ts(T.ELT[:, 3:515:4], T.VB[:, 0:128], sc(20), 32.0, A.is_equal, A.mult, "VB s20", "ELT")
+    ts(IP[:, 38:39], IP[:, 0:1], 4, None, A.arith_shift_right, None, "ip0", "ip6")
+    ts(sc(22), IP[:, 38:39], sc(11), None, A.add, None, "ip6 s11", "s22")
+    act(sc(23), sc(22), "s22", "s23", bias=8.0)
     for i in range(4):
-        for n, pat in ((0, [[-1, 256]]), (1, [[-1, 16], [-16, 16]])):
+        quant(T.ELQ[:, 128 * i:128 * i + 128], T.ELS[:, 128 * i:128 * i + 128], T.ELT[:, 3 - i:515 - i], "ELT", "EL%d" % i)
+        for n, c, key in ((0, -1.0, "s20"), (1, UNIT, "s22 s23")):
             o = 1024 * n + i
             if i % 2 == 0:
-                where0(T.MTT[:, o:1024 * n + 1024:4], T.KC[:, 0:256], pat, 64 * i, "KC0", "mt%d%d" % (n, i))
+                ts(T.MTT[:, o:1024 * n + 1024:4], T.VB[:], sc(20 + 2 * n + i // 2), c, A.is_equal, A.mult, "VB " + key, "mt%d%d" % (n, i))
             else:
                 act(T.MTT[:, o:1024 * n + 1024:4], T.MTT[:, o - 1:1024 * n + 1024:4], "mt%d%d" % (n, i - 1), "", "MT%d" % n)
-        where0(T.ELT[:, 512 * i:512 * i + 512], T.KC[:, 256:768], [[-1, 128], [128, 4]], -128 * i, "KC1", "ET%d" % (5 + i))
-        quant(T.ELQ[:, 128 * i:128 * i + 128], T.ELS[:, 128 * i:128 * i + 128], T.ELT[:, 512 * i:512 * i + 512], "ET%d" % (5 + i), "EL%d" % i)
     for i in range(2):
         quant(T.MTQ[:, 256 * i:256 * i + 256], T.MTS[:, 256 * i:256 * i + 256], T.MTT[:, 1024 * i:1024 * i + 1024], "MT%d" % i, "MQ%d" % i)
-    ts(T.UI[:], T.UI[:], 7, None, A.bitwise_and, None, "UI", "UI")
-    ts(T.UL[:], T.UI[:], 16, None, A.mult, None, "UI", "UL")
-    quant(T.UQ[:], T.US[:], T.UT[:], "UT", "UQ")
-    for i in range(3):
-        cp(T.URQ[:, 144 * i:144 * i + 144].bitcast(dt.uint32), ind(T.UQ[:].bitcast(dt.uint32), T.UL[:, 10 * i:10 * i + 9]), "UQ UL", "URQ%d" % i)
-        act(T.URS[:, 144 * i:144 * i + 144], ind(T.US[:], T.UL[:, 10 * i:10 * i + 9]), "UQ UL", "URS%d" % i)
-    ts(MK[:, 128:256], T.I16[:, 0:128], sc(1), 8000.0, A.not_equal, A.mult, "I16 s1", "mk0")
-    tt(MK[:, 1:128], MK[:, 129:256], MK[:, 128:255], A.subtract, "mk0", "MK")
-    act(MK[:, 0:1], MK[:, 128:129], "mk0", "mk1")
-    act(MK[:, 16:128:16], MK[:, 16:128:16], "MK", "MK", bias=-3000.0)
-    scan(FS[:, 0:128], MK[:, 0:128], FR[:, 0:128], 0.0, A.add, A.max, "MK mk1 FR", "fs0")
-    ts(FS[:, 128:136], FS[:, 15:128:16], MK[:, 143:144], None, A.subtract, None, "fs0 mk0", "FS")
-    ks, tz, z1, p1, bs = [FS[:, 128 + i:129 + i] for i in (0, 1, 2, 3, 7)]
-    ts(T.PL[:], T.PLF[:], sc(16), None, A.subtract, None, "PLF s16", "PL")
-    ts(LS[:, 0:4], RW[:, 0:4], ks, None, A.add, None, "rw0 FS", "Lk")
-    ts(sc(13), tz, 2.0, None, A.is_le, None, "FS", "s13")
-    ts(RW[:, 28:32], RW[:, 8:12], tz, 30.0, A.subtract, A.subtract, "rw8 FS", "rw28")
-    ts(LS[:, 6:10], RW[:, 28:32], sc(13), 32.0, A.mult, A.add, "rw28 s13", "Li")
-    ts(RW[:, 24:28], RW[:, 16:20], sc(12), tz, A.mult, A.add, "rw16 s12 FS", "rw24")
-    tt(RW[:, 24:28], RW[:, 24:28], RW[:, 12:16], A.add, "rw24 rw12", "rw24")
-    cp(LS[:, 10:14], RW[:, 24:28], "rw24", "La")
-    ts(LS[:, 14:22:2], RW[:, 8:12], 3.0, None, A.add, None, "rw8", "", "Le")
-    ts(LS[:, 15:22:2], RW[:, 8:12], z1, 3.0, A.subtract, A.add, "rw8 FS", "", "Le")
-    ts(LS[:, 22:26:2], RW[:, 20:22], sc(1), None, A.add, None, "rw20 s1", "", "Lp")
-    ts(LS[:, 23:26:2], RW[:, 20:22], p1, None, A.add, None, "rw20 FS", "", "Lp")
-    ts(LS[:, 26:30], RW[:, 4:8], bs, None, A.add, None, "rw4 FS", "Lb")
-    ts(IP[:, 8:14], IP[:, 8:14], 15, None, A.bitwise_and, None, "ip8", "ip8")
-    ts(LS[:, 42:48], IP[:, 8:14], 17.0, 16.0, A.mult, A.add, "ip8", "Lr")
-    for s in range(2):
-        cp(LS[:, 36 + s:42:2], FS[:, 132:135], "FS", "", "Ls")
+    quant(T.UQ[:, 0:128], T.US[:, 0:128], T.UT[:, 0:512], "UT0", "UQ0")
 
     DB = (4, 5, 6, 7)
+    pairs = [slice(0, 32, 2), slice(34, 66, 2)]
+    words = [slice(1, 33, 2), slice(35, 67, 2)]
+    both = [slice(0, 32), slice(34, 66)]
+    even, odd = slice(0, RL, 2), slice(1, RL, 2)
+
+    def at(buf, k, s):
+        return buf[:, RL * k + s.start:RL * k + s.stop:s.step]
     for t in range(3):
         src = T.X0 if t == 0 else T.XT
         for h in range(2):
@@ -424,175 +415,159 @@ def rank_program(g, core, T, topo):
             dma("Y", T.WQ[:].bitcast(dt.uint8), T.wc[:], "dw", "X01", "WQ")
             dma("Y", T.WS[:], T.ws[:], "dw", "X01", "WS")
             dma("Y", T.VT[:], T.v[:], "dv", "X01", "VT")
+            dma("Y", T.UT[:, 512:1024], T.u[:], "du2", "X01", "UT1")
             quant(T.VQ[:], T.VS[:], T.VT[:], "VT", "VQ")
+            quant(T.UQ[:, 128:256], T.US[:, 128:256], T.UT[:, 512:1024], "UT1", "UQ1")
         for s in range(2):
-            mm(B(s)[:, 0:144], T.XQ[:, 128 * s:128 * s + 128], T.XS[:, 128 * s:128 * s + 128], T.URQ[:, 144 * t:144 * t + 144], T.URS[:, 144 * t:144 * t + 144],
-               True, True, "XQ%d URQ%d URS%d" % (s, t, t), "B%d" % s)
-            tt(T.BT[:, s:576:4], B(s)[:, 0:144], T.TH[:], A.is_gt, "B%d TH" % s, "", "BT")
-            ts(T.W2[:, 32 + 8 * s:40 + 8 * s], B(s)[:, 0:8], 0.0, None, A.is_gt, None, "B%d" % s, "", "W1")
-        quant(T.BQ[:], T.BS[:], T.BT[:], "zBT BT", "BQ")
-        mm(B(2)[:, 0:128], T.CQ[:, 0:128], T.CS[:, 0:128], T.BQ[:, 0:128], T.BS[:, 0:128], True, True, "CQ0 BQ", "B2")
-        mm(B(3)[:, 0:128], T.CQ[:, 128:256], T.CS[:, 128:256], T.BQ[:, 24:152], T.BS[:, 24:152], True, False, "CQ1 BQ", "B3")
-        mm(B(3)[:, 0:128], T.CQ[:, 256:384], T.CS[:, 256:384], T.BQ[:, 16:144], T.BS[:, 16:144], False, True, "CQ2 BQ", "", "B3")
-        scan(T.W4[:], T.H4[:], B(2)[:, 0:128], 0.0, A.mult, A.add, "H4 B2", "W4")
-        cp(T["MS%d" % t][:], T.W4[:, 7::8], "W4", "MS%d" % t)
-        remote(T["WL%d" % t][:], T["MS%d" % t][:], "wa%d" % t, "lw%d" % t, "MS%d" % t, "WL%d" % t)
-        bits = B(3)[:, 112:128]
-        scan(T.W2[:, 0:16], H2, T.W2[:, 32:48], 0.0, A.mult, A.add, "HS2 W1", "W2")
-        scan(T.WN[:, 16:32], HN, bits, 0.0, A.mult, A.add, "HS2 B3", "P4")
-        scan(T.W2[:, 16:32], T.H4[:, 0:16], bits, 0.0, A.mult, A.add, "H4 B3", "W3")
-        act(T.WN[:, 0:16], bits, "B3", "bits")
-        for s in range(2):
-            ts(T.OT[:, s::4], T.VB[:], T.W2[:, 8 * s + 7:8 * s + 8], None, A.is_equal, None, "VB W2", "", "OT")
-        quant(T.OQ[:], T.OS[:], T.OT[:], "zOT OT MS%d" % t, "OQ")
-        if t == 0:
-            quant(T.HMQ[:], T.HMS[:], T.HMT[:], "zHMT HMT", "HMQ")
+            mm(B(s)[:, 0:128], T.XQ[:, 128 * s:128 * s + 128], T.XS[:, 128 * s:128 * s + 128], T.UQ[:, 48 * t:48 * t + 128], T.US[:, 48 * t:48 * t + 128],
+               True, True, "XQ%d UQ0" % s + " UQ1" * (t > 0), "B%d" % s)
+            ts(T.W1[:, 8 * s:8 * s + 8], B(s)[:, 112::-16], 0.0, None, A.is_gt, None, "B%d" % s, "", "W1")
+        scan(T.W2[:, 0:16], H2, T.W1[:], 0.0, A.mult, A.add, "H2 W1", "W2")
+        cp(T.MS[:, 8 * t:8 * t + 4:2], T.W2[:, 7:16:8], "W2", "MS%d" % t)
+        WL = T["WL%d" % t]
+        remote(WL[:], T.MS[:, 8 * t:8 * t + 4], "wa%d" % t, "lw%d" % t, "MS%d" % t, "WL%d" % t)
+        scan(T.W2[:, 16:32], H4, T.W1[:], 4.0, A.mult, A.add, "H4 W1", "W3")
+        scan(T.WN[:], HN, T.W1[:], 0.0, A.mult, A.add, "HN W1", "P4")
+        for i in range(4):
+            h, s = i // 2, i % 2
+            ts(T.OT[:, i::4], T.VB[:, 128 * h:128 * h + 128], T.W2[:, 8 * s + 7:8 * s + 8], None, A.is_equal, None, "VB W2", "", "OT")
+        quant(T.OQ[:], T.OS[:], T.OT[:], "OT MS%d" % t, "OQ")
         for h in range(2):
-            a, b, c = 256 * h, 256 * h + 256, 512 * h + 256
-            mm(B(h)[:, 0:256], T.OQ[:, 128 * h:128 * h + 128], T.OS[:, 128 * h:128 * h + 128], T.HMQ[:], T.HMS[:], True, True, "OQ HMQ", "B%d" % h)
-            act(T.HB[:, a:b], B(h)[:, 0:256], "B%d" % h, "HB%d" % h)
-            scan(T.DS[:, c - 256:c], T.NEG[:], T.HB[:, a:b], 0.0, A.add, A.max, "NEG HB%d" % h, "DR%d" % h)
-            scan(T.DS[:, c:c + 256], T.NEG[:], T.HB[:, a:b], T.DS[:, c - 1:c], A.add, A.max, "NEG DR%d HB%d" % (h, h), "DS%d" % h)
-            act(T.DG[:, a:b], ind(T.DS[:, c:c + 256], T.PL[:]), "DS%d PL" % h, "DG%d" % h)
-            aff(OPT["up"][h], T.DH[:, a:b], T.DG[:, a:b], 1.0, 2055.5, "DG%d" % h, "DH%d" % h)
-            aff(OPT["hi"][h], T.DT[:, 2 * h::4], T.DH[:, a:b], 1.0, -2048.0, "DH%d" % h, "dh%d" % h)
-            scan(T.DT[:, 2 * h + 1::4], T.DG[:, a:b], T.DT[:, 2 * h::4], 0.0, A.max, A.subtract, "DG%d dh%d" % (h, h), "dw%d" % h)
+            a, b, o = 256 * h, 256 * h + 256, 512 * h
+            mm(B(2 + h)[:, 0:256], T.OQ[:], T.OS[:], T.ELQ[:, a:b], T.ELS[:, a:b], True, True, "OQ EL%d EL%d" % (2 * h, 2 * h + 1), "B%d" % (2 + h))
+            act(T.HB[:, a:b], B(2 + h)[:, 0:256], "B%d" % (2 + h), "HB%d" % h, scale=255 / 32)
+            scan(back(T.DS, o + 511, 256), T.NEG[:], back(T.HB, b - 1, 256), 0.0, A.add, A.max, "NEG HB%d" % h, "DR%d" % h)
+            scan(back(T.DS, o + 255, 256), T.NEG[:], back(T.HB, b - 1, 256), T.DS[:, o + 256:o + 257], A.add, A.max, "NEG DR%d HB%d" % (h, h), "DS%d" % h)
+            ds = T.DS[:, o + 1:o + 257]
+            act(T.DH[:, a:b], ds, "DR%d DS%d" % (h, h), "DH%d" % h, bias=2055.5)
+            act(T.DT[:, 2 * h::4], T.DH[:, a:b], "DH%d" % h, "dh%d" % h, bias=-2048.0)
+            scan(T.DT[:, 2 * h + 1::4], ds, T.DT[:, 2 * h::4], 0.0, A.max, A.subtract, "DR%d DS%d dh%d" % (h, h, h), "dw%d" % h)
         quant(T.DQ[:], T.DP[:], T.DT[:], "dh0 dw0 dh1 dw1", "DQ")
-
-        def unpack():
-            for b in range(4):
-                mm(B(DB[b])[:, 0:256], T.ELQ[:, 128 * b:128 * b + 128], T.ELS[:, 128 * b:128 * b + 128], T.XQ[:], T.XS[:], True, True,
-                   "EL%d XQ0 XQ1" % b, "B%d" % DB[b])
-                act(T.FW[:, 256 * b:256 * b + 256], B(DB[b])[:, 0:256], "B%d" % DB[b], "FW%d" % b)
-            act(T.FW[:, 1024:1280], B(DB[3])[:, 0:256], "B%d" % DB[3], "FW4")
-        if t > 0:
-            unpack()
+        for b in range(4):
+            mm(B(DB[b])[:, 0:256], T.ELQ[:, 128 * b:128 * b + 128], T.ELS[:, 128 * b:128 * b + 128], T.XQ[:], T.XS[:], True, True,
+               "EL%d XQ0 XQ1" % b, "B%d" % DB[b])
+            f = T.FW[:, 512 * b:512 * b + 256]
+            act(f, B(DB[b])[:, 0:256], "B%d" % DB[b], "FW%d" % b, scale=2.0 ** -6)
+            dma("Y", T.FW[:, 512 * b + 256:512 * b + 512], f, "dc%d" % t, "FW%d" % b, "FX%d" % b)
+            act(T.FT[:, 256 * b:256 * b + 256], ind(f, T.LT[:]), "FW%d LT" % b, "FT%d" % b)
         for b in OPT["no"]:
             s, o = b % 2, 256 * (b // 2)
             mm(B(b)[:, 0:256], T.DQ[:, 128 * s:128 * s + 128], T.DP[:, 128 * s:128 * s + 128], T.MTQ[:, o:o + 256], T.MTS[:, o:o + 256], True, True,
                "DQ MQ%d" % (b // 2), "B%d" % b)
-        act(T.H16[:, 32:34], T.WN[:, 19:32:8], "P4", "HO", scale=RAISE, bias=-15 * RAISE)
         for s in range(2):
-            a, b = 256 * s, 256 * s + 256
-            ts(T.MH[:, a:b], T.I16[:], T.WN[:, 19 + 8 * s:20 + 8 * s], 1.0 - RAISE, A.is_gt, A.subtract, "I16 P4", "MH%d" % s)
+            a, b, hi = 256 * s, 256 * s + 256, T.WN[:, 8 * s + 3:8 * s + 4]
+            act(T.H16[:, 36 + s:37 + s], hi, "P4 J", "HO%d" % s, scale=-RAISE / UNIT, bias=sc(2 + s))
+            ts(T.MH[:, a:b], T.I16[:], hi, 1.0 - RAISE, A.is_gt, A.subtract, "I16 P4", "MH%d" % s)
             scan(T.HH[:, a:b], T.MH[:, a:b], B(2 + s)[:, 0:256], 0.0, A.add, A.max, "MH%d B%d" % (s, 2 + s), "HH%d" % s)
-            act(T.H16[:, 16 * s:16 * s + 16], T.HH[:, a + 15:b:16], "HH%d HO" % s, "H16%d" % s, bias=T.H16[:, 32 + s:33 + s])
-        for i in (1, 2):
-            act(T.WN[:, 24 + 16 * i:40 + 16 * i], T.WN[:, 0:16], "bits", "pm%d" % i, scale=-2.0 * i, bias=1.0 * i)
-        act(T.SG[:], ind(T.WN[:], LS[:, 26:30]), "P4 bits pm1 pm2 wn0 Lb", "SG", scale=RAISE)
-        tt(T.BD[:, 0:64], ind(T.WN[:, 0:40], LS[:, 6:10]), T.CB[:], A.is_equal, "P4 bits wn0 Li CB", "bd0")
-        tt(T.EM[:, 0:128], ind(T.WN[:, 0:40], LS[:, 14:22]), T.CE[:], A.is_equal, "P4 bits wn0 Le CE0 CE1 CE", "em0")
-        act(T.BD[:, 64:128], T.BD[:, 0:64], "bd0", "BD", scale=-256 * UNIT)
-        act(T.EM[:, 128:256], T.EM[:, 0:128], "em0", "EM", scale=-1 / UNIT)
-        if t == 0:
-            unpack()
+            act(T.H16[:, 17 * s:17 * s + 16], T.HH[:, a + 15:b:16], "HH%d HO%d" % (s, s), "H16%d" % s, scale=-1 / UNIT, bias=T.H16[:, 36 + s:37 + s])
+        act(T.WX[:, 0:16], T.WN[:], "P4", "", "WX", scale=-2 * STEP)
+        act(T.WX[:, 16:32], T.WN[:], "P4", "", "WX", scale=6 * STEP)
+        for k in range(4):
+            act(T.WX[:, 35 - k:48:4], T.WN[:, 3 - k::4], "P4", "", "WX", scale=32.0, bias=-32.0 * ((15 >> k) ^ 1), func=AF.Square)
+        tt(T.DM[:], ind(T.WX[:], T.LX[:, 0:17]), T.CE[:], A.add, "WX wx0 Lm CE CF", "DM")
         for s in range(2):
-            top, y, h = TOP + s * HALF, T.YY[:, 32 + 16 * s:48 + 16 * s], T.YY[:, 64 + 17 * s:80 + 17 * s]
-            ts(y, T["WL%d" % t][:], T.W2[:, 23 + 8 * s:24 + 8 * s], float(top), A.subtract, A.add, "WL%d W3" % t, "y%d" % s)
-            ts(h, y, top, None, A.bitwise_and, None, "y%d" % s, "h%d" % s)
-            ts(T.PN[:, 17 * s:17 * s + 16], h, float(top), DEAD, A.is_equal, A.mult, "h%d" % s, "pn0%d" % s)
-        ts(T.YY[:, 0:32], T.YY[:, 32:64], 4.0, None, A.mult, None, "y0 y1", "Y4")
-        for k in range(0, 8, 2):
-            ts(T.EK[:, 32 * k:32 * k + 64], T.YY[:, 0:64], 4 ** (k + 1), None, A.bitwise_and, None, "y0 y1 Y4", "ek%d ek%d" % (k, k + 1))
+            w4, theirs = T.W2[:, 23 + 8 * s:24 + 8 * s], ind(T.TAB[:], WL[:, 2 * s:2 * s + 1])
+            ts(at(T.YY, 0, words[s]), T.TAB[:, 0::17], w4, 4.0, A.add, A.mult, "TAB W3 yd", "x%d" % s)
+            ts(at(T.YY, 0, pairs[s]), theirs, w4, 4.0, A.add, A.mult, "TAB W3 yd WL%d" % t, "y%d" % s)
+        ts(T.NB[:, 0:34], T.YY[:, even], 4 * (LOW + HALF), 2, A.bitwise_and, A.arith_shift_right, "y0 y1 yd", "NB")
+        ts(T.NB[:, 34:68], T.YY[:, even], 4 * (4 ** 6 + HALF), 1, A.bitwise_and, A.arith_shift_right, "y0 y1 yd", "N6")
+        tt(T.DF[:, 35:68], T.NB[:, 34:67], T.NB[:, 35:68], A.subtract, "N6", "d6")
+        for o, ys, c in ((1, "x0 x1 yd", "s"), (0, "y0 y1 yd", "p")):
+            ts(T.N2[:, RL + o:2 * RL:2], T.YY[:, o::2], 4 * LOW, None, A.bitwise_and, None, ys, "n4" + c)
+            ts(T.N2[:, o:RL:2], T.YY[:, o::2], 4 * LOW, 1, A.bitwise_and, A.arith_shift_right, ys, "n2" + c)
+            for k in range(0, 6, 2):
+                ts(EK[:, RL * k + o:RL * k + 2 * RL:2], T.N2[:, o::2], 2 * 4 ** k + 4 ** (k + 2), None, A.bitwise_and, None,
+                   "n2%s n4%s" % (c, c), "", "ek%d ek%d" % (k, k + 1))
+        ts(PN[:, even], T.N2[:, RL:2 * RL:2], 0.0, DEAD, A.is_equal, A.mult, "n4p p0", "pn00 pn01")
+        tt(T.DF[:, 1:34], T.NB[:, 0:33], T.NB[:, 1:34], A.subtract, "NB", "df")
+        ts(at(EK, 6, odd), T.N2[:, odd], 2 * 4 ** 6, None, A.bitwise_and, None, "n2s", "ek6")
         for k in range(7):
-            pn, kp, d = T.PN[:, 34 * k:34 * k + 34], " pd pn%d0 pn%d1" % (k, k), 34 + 34 * (k % 2)
-            lv, o, kl = (T.YY, 64, "h0 h1 yd") if k == 0 else (T.HL, 134 * (k % 2), "H%d" % (k % 2))
-            tt(T.HL[:, d + 1:d + 34], lv[:, o:o + 33], lv[:, o + 1:o + 34], A.subtract, kl, "df%d" % (k % 2))
-            scan(T.RR[:, 34 * k:34 * k + 34], T.HL[:, d:d + 34], pn, -1e9, A.add, A.max, "d0 df%d" % (k % 2) + kp, "rr%d" % k)
+            kp = " pd pn%d0 pn%d1" % (k, k)
             if k < 6:
-                tt(T.HL[:, 134 * (1 - k % 2):134 * (1 - k % 2) + 34], lv[:, o:o + 34], pn, A.add, kl + kp, "H%d" % (1 - k % 2))
+                for s in range(2):
+                    c = (both if k % 4 else pairs)[s]
+                    tt(at(EK, k, c), at(EK, k, c), at(PN, k, c), A.add, "ek%d pn%d%d" % (k, k, s), "ec%d%d" % (k, s))
+            else:
+                tt(at(EK, 6, odd), at(EK, 6, odd), at(PN, 6, odd), A.add, "ek6 pn60 pn61", "ec60 ec61")
+            scan(RR[:, 34 * k:34 * k + 34], T.DF[:, 0:34], at(PN, k, even), 1e9, A.add, A.min, "d0 df" + kp, "rr%d" % k)
             for s in range(2):
-                a, b = 32 * k + 16 * s, 34 * k + 17 * s
-                if k < 6:
-                    ts(T.PN[:, b + 34:b + 50], T.EK[:, a:a + 16], T.RR[:, b + 16:b + 17], DEAD, A.is_lt, A.mult, "ek%d rr%d" % (k, k), "pn%d%d" % (k + 1, s))
-                else:
-                    e = T.HL[:, 102 + 16 * s:118 + 16 * s]
-                    tt(e, T.EK[:, a:a + 16], T.HL[:, 17 * s:17 * s + 16], A.min, "ek6 H0", "e%d" % s)
-                    tt(e, e, T.PN[:, b:b + 16], A.add, "e%d pn6%d" % (s, s), "e%d" % s)
-                    ts(T.PN[:, b + 34:b + 50], e, T.RR[:, b + 16:b + 17], None, A.is_lt, None, "e%d rr6" % s, "pn7%d" % s)
-        CU = (T.UU[:, 64:80], T.AL[:, 48:64])
-        for n, a, b in ((0, 0, 4), (1, 4, 7)):
-            o = 32 * n
-            ts(T.KK[:, 2 * a:2 * b], T.RR[:, 34 * a + 16:34 * b:17], 0.0, None, A.is_gt, None, " ".join("rr%d" % k for k in range(a, b)), "K%d" % n)
-            tt(T.UU[:, o:o + 32], ind(T.KK[:, 0:16], LS[:, 2 * n:2 * n + 2]), T.SG[:, o:o + 32], A.mult, "K0 K1 Lk SG", "UU%d" % n)
-            scan(CU[n], T.HS[:, 64 + 16 * n:80 + 16 * n], T.UU[:, o:o + 16], 0.0, A.mult, A.add, "HC UU%d" % n, "CU%d" % n)
-            tt(T.AL[:, o:o + 16], T.UU[:, o + 16:o + 32], CU[n], A.subtract, "UU%d CU%d" % (n, n), "al%d" % n)
-            if n == 0:
-                aff(OPT["wr"], T.AL[:, 16:32:8], T.UU[:, 67:80:8], -1.0, -256 * UNIT, "CU0", "al2")
-            tt(T.IN2[:, o:o + 32], ind(T.AL[:, o:o + 32], LS[:, 10 + 2 * n:12 + 2 * n]), T.BD[:, 64 + o:96 + o], A.add, ("al0 al2", "al1 CU1")[n] + " La BD", "IN2%d" % n)
-            for s in range(2):
-                start = T.UU[:, 71 + 8 * s:72 + 8 * s]
-                if n == 0:
-                    a, b = 256 * s, 256 * s + 256
-                    for o1, n1, c in ((1, 2, 8 * s), (2, 4, 8 * s + 1), (4, 8, 8 * s + 2), (8, 16, 8 * s + 3), (0, 16, 16 + 8 * s)):
-                        aff(OPT["inc"][s] if n1 > 2 else "A", T.INC[:, a + o1:b:n1], T.ICOL[:, 0:256 // n1], 0.0, T.AL[:, c:c + 1],
-                            "ICOL al2" if o1 == 0 else "ICOL al0", "", "INC%d" % s)
-                    scan(T.O[:, a:b], T.INC[:, a:b], B(s)[:, 0:256], start, A.add, A.max, "INC%d B%d CU0" % (s, s), "O%d" % s)
-                d = (T.H16[:, 16 * s:16 * s + 16], T.O[:, 256 * s + 15:256 * s + 256:16])[n]
-                scan(T.O2[:, o + 16 * s:o + 16 * s + 16], T.IN2[:, o + 16 * s:o + 16 * s + 16], d, start, A.add, A.max,
-                     "IN2%d CU0 %s%d" % (n, ("H16", "O")[n], s), "", "O2%d" % n)
-            tt(T.PK[:, 2 * o:2 * o + 64], ind(T.O2[:, o:o + 32], LS[:, 22:26]), T.EM[:, 128 + 2 * o:192 + 2 * o], A.mult, "O2%d Lp EM" % n, "PK%d" % n)
-            scan(T.PK[:, 128 + 2 * o:192 + 2 * o], T.RST[:], T.PK[:, 2 * o:2 * o + 64], -1e9, A.max, A.add, "RST PK%d" % n, "PS%d" % n)
-        ts(T.YT[:, 64:96], ind(T.RR[:], LS[:, 42 + 2 * t:44 + 2 * t]), 0.0, None, A.is_le, None, "Lr " + " ".join("rr%d" % k for k in range(8)), "DF")
+                r = RR[:, 34 * k + 17 * s + 16:34 * k + 17 * s + 17]
+                c = (both if k < 6 else words)[s]
+                ts(at(PN, k + 1, c), at(EK, k, c), r, DEAD, A.is_gt if k else A.is_ge, A.mult, "p0 ek%d ec%d%d rr%d" % (k, k, s, k), "pn%d%d" % (k + 1, s))
+        scan(RR[:, 238:272], T.DF[:, 34:68], at(PN, 6, even), 1e9, A.add, A.min, "d0 d6 pd pn60 pn61", "rr7")
+        tt(T.YT[:, 0:32], ind(RR[:, 0:204], LS[:, 44 + 2 * t:46 + 2 * t]), T.TH[:, 32 * t:32 * t + 32], A.is_ge, "Lr TH " + " ".join("rr%d" % k for k in range(6)), "DF")
+        c6, c7 = [8 * (q // 2) + q % 2 for q in ((3 * t + 6) % 8, (3 * t + 7) % 8)]
+        ts(T.YT[:, c6:c6 + 3:2], RR[:, 220:238:17], 2.0 * 4 ** 6, None, A.is_ge, None, "rr6", "", "DF")
+        tt(T.YT[:, c7:c7 + 3:2], RR[:, 254::17], RR[:, 220:238:17], A.is_ge, "rr6 rr7", "", "DF")
+        turn(T.YT[:, 32:64], T.YT[:, 0:32], "DF", "TF")
+        for q in range(8):
+            p, c = 32 * (q // 2), 16 * (q % 2)
+            dma(OPT["dq"][q], T.IN[q::8, 0:32], T.YT[p:p + 32, 32 + c:48 + c], "dk%d" % t, "TF", "", "IN")
+        lo = RL * 4 + 1
+        tt(T.DI[:, 1:34], PN[:, lo:lo + 66:2], PN[:, lo + 2:lo + 68:2], A.subtract, "pn40 pn41", "DI")
         for s in range(2):
-            c = 64 + 2 * ((3 * t + 7) % 8) + s
-            least(T.YT[:, c:c + 1], T.PN[:, 238 + 17 * s:254 + 17 * s], "pn7%d" % s, "", "DF")
-        turn(T.YT[:, 96:128], T.YT[:, 64:96], "DF", "TF")
-        for q in range(4):
-            dma("YA"[q % 2], T.DL[q::4, 32:48], T.YT[32 * q:32 * q + 16, 96:128], "dk%d" % t, "TF", "", "dl")
+            act(T.INC[:, 64 * s:64 * s + 64], ind(T.DI[:], LS[:, 36 + 4 * s:40 + 4 * s]), "DI di0 Li", "INC%d" % s, scale=STEP / DEAD)
+            for q in range(4):
+                a = 256 * s + 64 * q
+                scan(T.O[:, a:a + 64], T.INC[:, 64 * s:64 * s + 64], B(s)[:, 64 * q:64 * q + 64], 0.0, A.add, A.min, "INC%d B%d" % (s, s), "", "O%d" % s)
+            act(T.H16[:, 38 + s:39 + s], PN[:, lo + 30 + 34 * s:lo + 31 + 34 * s], "pn4%d J" % s, "vb%d" % s, scale=STEP / DEAD, bias=sc(s))
+            act(T.VH[:, 17 * s:17 * s + 16], T.O[:, 256 * s + 15:256 * s + 256:16], "O%d vb%d" % (s, s), "", "VH", bias=T.H16[:, 38 + s:39 + s])
+        for n, vals, kv, k, steps in ((0, T.H16[:, 0:34], "h0 H160 H161", 4, range(4)), (1, T.VH[:], "v0 VH", 6, range(4, 7)), (2, T.VH[:], "v0 VH", 7, (7,))):
+            c = T.CL[:, 34 * n:34 * n + 34]
+            tt(c, vals, at(PN, k, odd), A.add, kv + " p0 pn%d0 pn%d1" % (k, k), "CL%d" % n)
+            for q in steps:
+                scan(T.PS[:, 34 * q:34 * q + 34], T.DM[:, 34 * q:34 * q + 34], c, 0.0, A.add, A.min, "DM CL%d" % n, "", "PS")
         for s in range(2):
-            act(T.YT[:, s:32:2], T.YT[:, 64 + s:96:2], "DF s17", "", "KM", scale=-1048576.0, bias=sc(17 + s))
-        tt(T.AI[:, 0:32], ind(T.PK[:, 128:256], LS[:, 36 + 2 * t:38 + 2 * t]), T.YT[:, 0:32], A.max, "PS0 PS1 Ls KM", "YT")
-        turn(T.AI[:, 32:64], T.AI[:, 0:32], "YT", "TR")
-        ts(T.AI[:, 64:96], T.AI[:, 32:64], 255, None, A.bitwise_and, None, "TR", "ai")
-        cp(T.TU[:], T.AI[:, 64:96], "ai", "TU")
-        for q in range(4):
-            dma("YA"[q % 2], T.AU[q::4, :], T.TU[32 * q:32 * q + 16, :], "dl%d" % t, "TU", "", "AU")
-        L, JL, D, C, DN = T.LF, T.JL[:, 0:16], T.DL[:, 32:48], T.WC[:, 64:80], T.WC[:, 80:81]
-        scan(T.DL[:, 1:17], T.NEG[:, 0:16], D, T.DL[:, 0:1], A.max, A.add, "dl NEG p0", "pm")
-        turn(T.DL[:, 64:128], T.DL[:, 0:64], "dl pm p0", "dt")
-        scan(T.WC[:, 0:32], H1, T.DL[:, 64:96], 0.0, A.mult, A.add, "H1 dt", "sa")
-        for i in range(2):
-            scan(T.WC[:, 32 + 16 * i:48 + 16 * i], T.NEG[:, 0:16], T.DL[:, 96 + 16 * i:112 + 16 * i], T.WC[:, 16 * i + 15:16 * i + 16], A.max, A.add,
-                 "NEG dt sa", "", "cb")
-        turn(T.WC[:, 64:96], T.WC[:, 32:64], "cb", "ct")
-        act(L[:, 0:16], D, "dl", "l1", scale=-1024.0)
-        tt(L[:, 16:32], L[:, 0:16], JL, A.add, "l1 JL", "l2")
-        ts(L[:, 32:48], C, DN, None, A.subtract, None, "ct", "l5")
-        tt(L[:, 48:64], L[:, 16:32], C, A.subtract, "l2 ct", "l6")
-        tt(L[:, 64:80], L[:, 32:48], L[:, 48:64], A.max, "l5 l6", "l7")
-        ts(T.PU[:], L[:, 64:80], DN, None, A.add, None, "l7 ct", "PU")
-        cp(ind(T.LR[:], T.PU[:]), T.ICOL[:], "PU ICOL", "LR")
+            act(T.YT[:, 64 + s:96:2], ind(T.YT[:, 0:32], LS[:, 2 * s:2 * s + 1]), "DF Lk J", "", "KM", scale=-STEP, bias=sc(s))
+        tt(T.YA[:, 0:32], ind(T.PS[:], LS[:, 50 + 2 * t:52 + 2 * t]), T.YT[:, 64:96], A.max, "PS Ly KM", "YA")
+        turn(T.YA[:, 32:64], T.YA[:, 0:32], "YA", "TR")
+        cp(T.TU[:], T.YA[:, 32:64], "TR", "TU")
+        for q in range(8):
+            p, c = 32 * (q // 2), 16 * (q % 2)
+            dma(OPT["dq"][q], T.AU[q::8, :], T.TU[p:p + 16, c:c + 16], "dl%d" % t, "TU", "", "AU")
+        L, C, ND, NY = T.LF, T.CC[:, 0:16], T.CC[:, 16:17], T.CC[:, 18:19]
+        scan(T.RB[:, 32:64], H1, T.IN[:, 0:32], 0.0, A.mult, A.add, "H1 IN", "", "RB")
+        scan(back(T.RB, 31, 32), back(T.IN, 32, 32), H1, 0.0, A.add, A.mult, "H1 IN in0", "", "RB")
+        act(T.RB[:, 64:96], T.IN[:, 0:32], "IN s11", "", "RB", scale=-STEP, bias=sc(11))
+        turn(T.RT[:, 32:128], T.RB[:], "RB", "RT")
+        scan(T.CC[:, 0:17], T.RT[:, 31:48], T.RT[:, 64:81], 0.0, A.add, A.add, "RT rt0", "ct")
+        ts(L[:, 0:16], C, ND, sc(4), A.subtract, A.subtract, "ct s4", "l5")
+        tt(L[:, 16:32], T.RT[:, 96:112], C, A.subtract, "RT ct", "l6")
+        act(NY, ND, "ct s4", "ny", bias=sc(4))
+        tt(L[:, 32:48], L[:, 0:16], L[:, 16:32], A.max, "l5 l6", "l7")
+        ts(T.PU[:], L[:, 32:48], NY, None, A.add, None, "l7 ny", "PU")
+        cp(ind(T.LR[:], T.PU[:]), T.ICT[:], "PU ICT", "LR")
         scan(T.LM[:], MK[:, 0:96], T.LR[:, 0:96], 0.0, A.add, A.max, "MK mk1 LR", "ln")
         ts(T.LU[:, 0:6], T.LM[:, 15::16], MK[:, 143:144], None, A.subtract, None, "ln mk0", "LU")
         for b in range(4):
-            z, f = T.XW[:, 352 * b:352 * b + 256], ind(T.FW[:, 256 * b:256 * b + 256], T.AU[:])
-            if b == 3:
-                tt(z, f, T.FW[:, 1024:1280], A.add, "FW3 FW4 AU", "XZ3")
+            z, f = T.XW[:, 352 * b:352 * b + 256], ind(T.FW[:, 512 * b:512 * b + 512], T.AU[:])
+            ft, gw, fl, o = T.FT[:, 256 * b:256 * b + 256], T.GW[:, 256 * b:256 * b + 256], T.FL[:, 96 * b:96 * b + 96], T.ET[:, b:384:4]
+            move = {"A": act, "V": cp}[OPT["et"][b]]
+            if OPT["xz"][b] == "V":
+                tt(z, f, ft, A.add, "FW%d FX%d FT%d AU" % (b, b, b), "XZ%d" % b)
+                move(o, ind(z, T.LU[:, 0:6]), "XZ%d LU" % b, "", "ET")
             else:
-                act(T.GW[:, 256 * b:256 * b + 256], f, "FW%d AU" % b, "GW%d" % b)
-                tt(z, T.GW[:, 256 * b:256 * b + 256], B(DB[b])[:, 0:256], A.add, "GW%d B%d" % (b, DB[b]), "XZ%d" % b)
-        for b in range(4):
-            o, i = T.ET[:, b:384:4], ind(T.XW[:, 352 * b:352 * b + 256], T.LU[:, 0:6])
-            if b != 2:
-                act(o, i, "XZ%d LU" % b, "", "ET", scale=2.0 ** -6)
-            else:
-                ts(o, i, 2.0 ** -6, None, A.mult, None, "XZ%d LU" % b, "", "ET")
+                act(gw, f, "FW%d FX%d AU" % (b, b), "GW%d" % b)
+                move(fl, ind(ft, T.LU[:, 0:6]), "FT%d LU" % b, "FL%d" % b)
+                tt(o, ind(gw, T.LU[:, 0:6]), fl, A.add, "GW%d FL%d LU" % (b, b), "", "ET")
         quant(T.EQ[:], T.ES[:], T.ET[:], "ET ET4", "EQ")
         remote(T["AC%d" % t][:, 32:128].bitcast(dt.uint8), T.EQ[:, 0:96].bitcast(dt.uint8), "ca%d" % t, "lc%d" % t, "EQ", "AC%d" % t)
         remote(T["AS%d" % t][:, 32:128], T.ES[:, 0:96], "ca%d" % t, "lc%d" % t, "EQ", "AC%d" % t)
-        ts(L[:, 80:96], L[:, 64:80], DN, 256.0, A.add, A.add, "l7 ct EQ", "pos")
-        ts(L[:, 96:112], L[:, 80:96], 352.0, 4096.0, A.is_lt, A.mult, "pos", "m0")
-        tt(L[:, 112:128], L[:, 96:112], L[:, 80:96], A.min, "m0 pos", "m1")
-        tt(L[:, 128:144], L[:, 112:128], JL, A.max, "m1 JL", "m2")
-        cp(T.SU[:], L[:, 128:144], "m2", "SU")
+        for b in range(4):
+            if OPT["xz"][b] == "A":
+                tt(T.XW[:, 352 * b:352 * b + 256], T.GW[:, 256 * b:256 * b + 256], T.FT[:, 256 * b:256 * b + 256], A.add, "GW%d FT%d EQ" % (b, b), "XZ%d" % b)
+        ts(L[:, 48:64], T.PU[:], 256.0, None, A.add, None, "PU EQ", "pos")
+        ts(L[:, 64:80], T.PU[:], 96.0, 4096.0, A.is_lt, A.mult, "PU EQ", "m0")
+        tt(L[:, 80:96], L[:, 64:80], L[:, 48:64], A.min, "m0 pos", "m1")
+        tt(L[:, 96:112], L[:, 80:96], JL, A.max, "m1 JL", "m2")
+        cp(T.SU[:], L[:, 96:112], "m2", "SU")
         if t == 2:
-            cp(T.AF[:, 0:16], T.AU[:], "AU EQ", "af")
-            turn(T.AF[:, 32:64], T.AF[:, 0:32], "af", "at")
-            for q in range(8):
-                p = 32 * (q // 2)
-                dma("Y", T.al[q:q + 1, 0:256], T.AF[p:p + 16, 32 + 16 * (q % 2):48 + 16 * (q % 2)], "dout", "at")
-            dma("Y", T.al[:, 256:352], T.LR[0::16, 0:96], "dout", "LR")
+            cp(T.AI[:, 0:16], T.AU[:], "AU EQ", "a0")
+            ts(T.AI[:, 16:32], T.AI[:, 0:16], 255, None, A.bitwise_and, None, "a0", "ai")
+            cp(T.AF[:], T.AI[:, 16:32], "ai", "af")
+            dma("Y", T.al[:, 0:256], T.AF[:], "dout", "af")
+            act(T.LO[:], ind(T.ICT[:], T.LU[:, 0:6]), "ICT LU EQ", "LO")
+            dma("Y", T.al[:, 256:352], T.LO[0::16, :], "dout", "LO")
         AC, AS, ka = T["AC%d" % t][:], T["AS%d" % t][:, 0:128], " AC%d pc%d ps%d" % (t, t, t)
         for b in range(4):
             kb, o, i = "B%d" % DB[b], T.XW[:, 352 * b + 256:352 * b + 352], B(DB[b])[:, 32:128]
@@ -600,15 +575,15 @@ def rank_program(g, core, T, topo):
             mm(B(DB[b])[:, 0:128], T.ELQ[:, 128 * b:128 * b + 128], T.ELS[:, 128 * b:128 * b + 128], AC, AS, False, True, "EL%d" % b + ka, "", kb)
             win, r = T.XW[:, 352 * b:352 * b + 352], "XZ%d XT%d SU" % (b, b)
             if b % 2 == 0:
-                act(o, i, kb, "XT%d" % b, scale=2.0)
-                act(T.XT[:, b::4], ind(win, T.SU[:]), r, "", "XT", scale=2.0 ** -6)
+                act(o, i, kb, "XT%d" % b, scale=2.0 ** -5)
+                act(T.XT[:, b::4], ind(win, T.SU[:]), r, "", "XT")
             else:
-                ts(o, i, 2.0, None, A.mult, None, kb, "XT%d" % b)
+                ts(o, i, 2.0 ** -5, None, A.mult, None, kb, "XT%d" % b)
             if b == 1:
-                ts(T.XT[:, b::4], ind(win, T.SU[:]), 2.0 ** -6, None, A.mult, None, r, "", "XT")
+                cp(T.XT[:, b::4], ind(win, T.SU[:]), r, "", "XT")
             if b == 3:
-                ts(T.XT[:, 3:512:4], ind(win, T.SU[:, 0:8]), 2.0 ** -6, None, A.mult, None, r, "X30")
-                act(T.XT[:, 515::4], ind(win, T.SU[:, 8:16]), r, "X31", scale=2.0 ** -6)
+                cp(T.XT[:, 3:512:4], ind(win, T.SU[:, 0:8]), r, "X30")
+                act(T.XT[:, 515::4], ind(win, T.SU[:, 8:16]), r, "X31")
     for h in range(2):
         a, b = 128 * h, 128 * h + 128
         quant(T.XQ[:, a:b], T.XS[:, a:b], T.XT[:, 4 * a:4 * b], "XT X3%d" % h, "XQ%d" % h)

from concourse.mybir import dt, AluOpType, ActivationFunctionType

F32, BF, I32, U16, F8, U8 = "float32", "bfloat16", "int32", "uint16", "float8_e4m3fn_x4", "uint8"
SCRATCH = {}
for _n, _w, _d in [
        ("X0", 1024, BF), ("UT", 1024, BF), ("VT", 512, BF), ("WQ", 512, F8), ("WS", 512, U8),
        ("UQ", 256, F8), ("US", 256, U8), ("VQ", 128, F8), ("VS", 128, U8),
        ("ELT", 516, BF), ("ELQ", 512, F8), ("ELS", 512, U8), ("MTT", 2048, BF), ("MTQ", 512, F8), ("MTS", 512, U8),
        ("ICOL", 256, F32), ("VB", 256, BF), ("I16", 256, BF), ("TAB", 256, F32), ("IP", 40, I32), ("SC", 32, F32),
        ("RW", 64, F32), ("LS", 56, U16), ("CE", 272, F32), ("LW", 544, F32), ("WX", 64, F32), ("LX", 18, U16), ("HS", 112, F32),
        ("NEG", 256, BF), ("JL", 16, F32), ("MK", 256, F32), ("ICT", 256, F32), ("LT", 16, U16),
        ("XQ", 256, F8), ("XS", 256, U8), ("XT", 1024, BF), ("W1", 16, F32), ("W2", 32, F32), ("WN", 16, F32), ("MS", 24, U16),
        ("OT", 512, BF), ("OQ", 128, F8), ("OS", 128, U8), ("HB", 512, BF), ("DS", 1024, BF), ("DH", 512, BF),
        ("DT", 1024, BF), ("DQ", 256, F8), ("DP", 256, U8), ("MH", 512, BF), ("HH", 512, F32), ("H16", 40, F32),
        ("DM", 272, F32), ("YY", 68, I32), ("NB", 68, I32), ("N2", 136, I32), ("EK", 476, I32), ("DF", 68, F32), ("TH", 96, F32),
        ("RR", 272, F32), ("PN", 544, F32), ("DI", 40, F32), ("INC", 128, F32), ("O", 512, F32), ("VH", 34, F32),
        ("CL", 102, F32), ("PS", 272, F32), ("YT", 96, F32), ("YA", 64, F32), ("TU", 32, U16),
        ("IN", 36, F32), ("RB", 96, F32), ("RT", 128, F32), ("CC", 20, F32), ("LF", 128, F32), ("AI", 32, I32), ("AF", 16, F32), ("LO", 96, F32),
        ("AU", 16, U16), ("PU", 16, U16), ("LU", 8, U16), ("SU", 16, U16), ("LR", 256, F32), ("LM", 96, F32),
        ("FW", 2048, BF), ("FT", 1024, BF), ("FL", 384, BF), ("GW", 1024, BF), ("XW", 1408, BF),
        ("ET", 512, BF), ("EQ", 128, F8), ("ES", 128, U8), ("YO", 256, F32)]:
    SCRATCH[_n] = ("sbuf", [128, _w], _d)
for _t in range(3):
    SCRATCH["WL%d" % _t] = ("sbuf", [128, 4], U16)
    SCRATCH["AC%d" % _t] = ("sbuf", [128, 128], F8)
    SCRATCH["AS%d" % _t] = ("sbuf", [128, 128], U8)
for _b in range(8):
    SCRATCH["B%d" % _b] = ("psum", [128, 512], F32)
SEMAPHORES = ["cV", "cA", "cP", "cG", "dx", "dy", "du", "du2", "dv", "dw", "dfill", "dout"]
for _t in range(3):
    SEMAPHORES += ["wa%d" % _t, "ca%d" % _t, "lw%d" % _t, "lc%d" % _t, "dl%d" % _t, "dk%d" % _t, "dc%d" % _t]

RAISE = 2.0 ** -6
UNIT = 2.0 ** -17
LOW = 0x5555
HALF = 1 << 18
DEAD = 2.0 ** 19
CEIL = 2.0 ** 17
STEP = 1024.0
RL = 68
CYCLE, WAKE, ISSUE, LOCAL, REMOTE, TURNS, MOVES = 0.00104, (0.19, 0.19), 0.05, 1.2, 1.7, 5, 60000
WEIGHTS = [(p, h) for p in (8.0, 12.0, 20.0, 40.0) for h in (1.0, 2.0, 4.0, 8.0)]
OPT = {"no": (2, 0, 3, 1), "dq": "YAYAYAYA", "et": "VAAA", "xz": "AAVV"}
ORDER = []


def rank_program(g, core, T, topo):
    rank = T.rank_of(core)
    if rank is None:
        return
    mate = T.cores[rank + 1 if rank % 2 == 0 else rank - 1]
    A, AF = AluOpType, ActivationFunctionType
    Q = {"V": g.vector, "A": g.scalar, "P": g.tensor, "G": g, "Y": g.sync}
    own = {"V": "cV", "A": "cA", "P": "cP", "G": "cG"}
    v, ac, pe = g.vector, g.scalar, g.tensor
    eng = topo.engines(core, mate)
    ne = 1
    while ne * 2 <= len(eng):
        ne *= 2
    msk = 0
    for _e in eng[:ne]:
        msk |= 1 << _e
    rid, pid = topo.addr(mate)[:2]

    calls = []

    def call(e, f, sems, r, w, add, busy, late=0.0):
        calls.append({"e": e, "f": f, "sems": sems, "r": r.split(), "w": w.split(), "add": add.split(), "busy": busy, "late": late})

    def op(e, f, r, w, add, cycles):
        call(e, lambda: f().then_inc(T.sem[own[e]], 1), [(own[e], 1)], r, w, add, cycles * CYCLE)

    def dma(e, out, in_, s, r, w="", add=""):
        call(e, lambda: Q[e].dma_start(out, in_).then_inc(T.sem[s], 16), [(s, 16)], r, w, add, ISSUE, LOCAL + 0.0018 * out.shape[1])

    def remote(out, in_, rs, ls, r, w):
        call("G", lambda: g.remote_dma(out_ap=out, in_ap=in_, remote_sem=T.sem[rs], local_sem=T.sem[ls], pid=pid, routing_id=rid, dma_engine_mask=msk),
             [(ls, ne), (rs, ne)], r, "", w, 3 * ISSUE, REMOTE + (rs == "wa0"))

    def track(seq, meet):
        lastw, readers, epoch, raised = {}, {}, {}, {}
        for i in seq:
            c = calls[i]

            def after(j, war, landed):
                d = calls[j]
                s = d["sems"][-1 if landed else 0][0]
                if s == own.get(d["e"]):
                    meet(i, j, s, not (war and c["e"] == d["e"] == "P"))
                else:
                    for k in raised[s]:
                        meet(i, k, s, True)
            for k in c["r"]:
                for j in lastw[k]:
                    after(j, False, True)
                if k[0] == "B" and k[1:].isdigit():
                    for j in readers.get(k, []):
                        if calls[j]["e"] != c["e"]:
                            after(j, True, False)
            for k in c["w"]:
                for j in lastw.get(k, []):
                    after(j, False, True)
                for j in readers.get(k, []):
                    after(j, True, False)
            for k in c["add"]:
                if readers.get(k):
                    epoch[k] = [(j, False) for j in lastw.get(k, [])] + [(j, True) for j in readers[k]]
                    lastw[k], readers[k] = [], []
                for j, war in epoch.get(k, []):
                    after(j, war or c["e"] == "P", not war)
            meet(i, None, None, None)
            for s, n in c["sems"]:
                raised.setdefault(s, []).append(i)
            for k in c["r"]:
                readers.setdefault(k, []).append(i)
            for k in c["w"]:
                lastw[k], readers[k], epoch[k] = [i], [], [(i, False)]
            for k in c["add"]:
                lastw.setdefault(k, []).append(i)

    def arrange():
        n = len(calls)
        pre, post = [{} for c in calls], [{} for c in calls]
        busy = [c["busy"] for c in calls]

        def meet(i, j, s, wait):
            if j is not None:
                pre[i][j] = post[j][i] = max(pre[i].get(j, 0.0), calls[j]["late"] + WAKE[calls[i]["e"] != calls[j]["e"]] if wait else 0.0)
        track(range(n), meet)

        def lay(before, behind, rank, first, patience, hurry):
            left, ready, free, seq, end = [len(p) for p in before], list(first), {e: 0.0 for e in Q}, [], [0.0] * n
            pool = {e: [i for i in range(n) if calls[i]["e"] == e and not before[i]] for e in Q}
            while len(seq) < n:
                t0, e = min((max(free[e], min(ready[i] for i in pool[e])), e) for e in Q if pool[e])
                j = max(pool[e], key=lambda i: rank[i])
                i = max(pool[e], key=lambda i: (rank[i] - (patience if e in "VA" else 2.0) * max(0.0, ready[i] - t0)
                                                - (hurry * max(0.0, max(t0, ready[i]) + busy[i] - max(t0, ready[j])) if i != j else 0.0), -i))
                pool[e].remove(i)
                seq.append(i)
                free[e] = end[i] = max(t0, ready[i]) + busy[i]
                for k, d in behind[i].items():
                    ready[k] = max(ready[k], end[i] + d)
                    left[k] -= 1
                    if not left[k]:
                        pool[calls[k]["e"]].append(k)
            return seq, end
        products = [i for i in range(n) if calls[i]["e"] == "P"]
        for j, i in zip(products, products[1:]):
            meet(i, j, None, False)
        late, tail = [c["late"] for c in calls], [0.0] * n
        for i in reversed(range(n)):
            tail[i] = busy[i] + max([late[i]] + [d + tail[k] for k, d in post[i].items()])
        best = None
        for patience, hurry in WEIGHTS:
            rank = tail
            for turns in range(TURNS):
                seq, end = lay(pre, post, rank, [0.0] * n, patience, hurry)
                span = max(end[i] + late[i] for i in range(n))
                if best is None or span < best[0]:
                    best = (span, seq)
                rank = lay(post, pre, end, late, patience, hurry)[1]
        gaps = [list(p.items()) for p in pre]
        queue = [c["e"] for c in calls]

        def times(seq, a, end):
            free = {}
            for i in reversed(seq[:a]):
                if queue[i] not in free:
                    free[queue[i]] = end[i]
                    if len(free) == len(Q):
                        break
            for i in seq[a:]:
                t0 = free.get(queue[i], 0.0)
                for j, d in gaps[i]:
                    if end[j] + d > t0:
                        t0 = end[j] + d
                free[queue[i]] = end[i] = t0 + busy[i]
            return max(end[i] + late[i] for i in seq[-40:]) + 0.02 * sum(end) / n
        seq, end, x = best[1], [0.0] * n, 1
        span = times(seq, 0, end)
        for turns in range(MOVES):
            if turns % 500 == 0:
                seq.sort(key=lambda i: end[i] - busy[i])
            x = (x * 1103515245 + 12345) % (1 << 31)
            p, step, far = (x >> 8) % n, (1, -1)[x >> 4 & 1], 1 + (x >> 5 & 7) % 5
            i, q = seq[p], p
            while far and 0 <= q + step < n and seq[q + step] not in (post[i] if step > 0 else pre[i]):
                q += step
                far -= queue[seq[q]] == queue[i]
            if far:
                continue
            new = list(seq)
            new.insert(q, new.pop(p))
            trial = list(end)
            s = times(new, min(p, q), trial)
            if s <= span:
                seq, end, span = new, trial, s
        best = (max(end[i] + late[i] for i in range(n)), seq)
        return best[1]

    def issue(seq):
        tot, count, known, want = {}, {}, {e: {} for e in Q}, {}

        def meet(i, j, s, wait):
            c = calls[i]
            if j is None:
                for s in sorted(want):
                    if known[c["e"]].get(s, 0) < want[s]:
                        Q[c["e"]].wait_ge(T.sem[s], want[s])
                        known[c["e"]][s] = want[s]
                want.clear()
                c["f"]()
                for s, n in c["sems"]:
                    tot[s] = tot.get(s, 0) + n
                    count[i, s] = tot[s]
            elif wait:
                want[s] = max(want.get(s, 0), count[j, s])
        track(seq, meet)
        for s in sorted(tot):
            if known["G"].get(s, 0) < tot[s]:
                g.wait_ge(T.sem[s], tot[s])

    def ind(win, off):
        return (win.indirect(off), 16 * off.shape[1])

    def bare(a):
        return a[0] if isinstance(a, tuple) else a

    def cycles(out, *ins, least=64, each=1.0, fast=False):
        if isinstance(out, tuple):
            return 50 + 3.8 * out[1]
        if isinstance(ins[0], tuple):
            return 50 + 1.6 * ins[0][1]
        if fast and all(SCRATCH[a.name][2] in (BF, U16) for a in (out,) + ins):
            each = 0.5
        return max(least, each * out.shape[1])

    def ts(out, in0, s1, s2, o0, o1, r, w="", add=""):
        if o1 is None:
            op("V", lambda: v.tensor_scalar(out, bare(in0), s1, None, o0), r, w, add, cycles(out, in0, fast=True))
        else:
            op("V", lambda: v.tensor_scalar(out, bare(in0), s1, s2, o0, o1), r, w, add, cycles(out, in0, fast=True))

    def tt(out, a, b, o, r, w="", add=""):
        both = isinstance(a, tuple) or all(SCRATCH[x.name][0] == "sbuf" for x in (a, b))
        op("V", lambda: v.tensor_tensor(out, bare(a), b, o), r, w, add, cycles(out, a, each=2.0 if both else 1.0))

    def cp(out, a, r, w="", add=""):
        op("V", lambda: v.tensor_copy(bare(out), bare(a)), r, w, add, cycles(out, a, fast=True))

    def scan(out, d0, d1, ini, o0, o1, r, w="", add=""):
        op("V", lambda: v.tensor_tensor_scan(out, d0, d1, ini, o0, o1), r, w, add, cycles(out, d0, d1, fast=True))

    def turn(out, a, r, w):
        op("V", lambda: v.transpose(out, a), r, w, "", cycles(out, a))

    def fill(ap, c, w="", add=""):
        op("V", lambda: v.memset(ap, c), "", w, add, cycles(ap, ap, fast=True))

    def quant(c, s, t, r, w):
        op("V", lambda: v.quantize_mx(c, s, t), r, w, "", 15 + 0.28 * t.shape[1])

    def act(out, in_, r, w="", add="", scale=1.0, bias=None, func=None):
        n = cycles(out, in_, least=100)
        if bias is not None:
            op("A", lambda: ac.activation(out, bare(in_), func or AF.Identity, bias=bias, scale=scale), r, w, add, n)
        elif scale == 1.0:
            op("A", lambda: ac.activation(out, bare(in_), AF.Copy), r, w, add, n)
        else:
            op("A", lambda: ac.activation(out, bare(in_), AF.Copy, scale=scale), r, w, add, n)

    def row(out, n, a, b, w="", add=""):
        act(out, T.ICOL[:, 0:n], "ICOL", w, add, scale=float(a), bias=float(b))

    def mm(out, l, ls, rr, rs, a, z, r, w="", add=""):
        op("P", lambda: pe.matmul_mx(out, l, ls, rr, rs, a, z), r, w, add, 1.25 * (out.shape[1] + 16))

    def iota(out, pat, base, ch, w, add="", flag=True):
        if flag:
            op("G", lambda: g.iota(out, pat, base, ch, allow_small_or_imprecise_dtypes=True), "", w, add, 130 + 2 * out.shape[1])
        else:
            op("G", lambda: g.iota(out, pat, base, ch), "", w, add, 130 + 2 * out.shape[1])

    def B(b):
        return T["B%d" % b]

    def back(buf, a, n):
        return buf[:, a:a - n:-1] if a >= n else buf[:, a::-1]

    IP, SC, LS, RW, MK, PN, EK, RR = T.IP, T.SC, T.LS, T.RW, T.MK, T.PN, T.EK, T.RR

    def sc(c):
        return SC[:, c:c + 1]
    H1, H2, H4, HN, THR = T.HS[:, 0:32], T.HS[:, 32:48], T.HS[:, 48:64], T.HS[:, 64:80], T.HS[:, 96:112]
    JL = T.JL[:, 0:16]

    dma("A", T.UT[:, 0:512], T.u[:], "du", "", "UT0")
    dma("Y", T.X0[:, 0:512], T.x[:, 0:512], "dx", "", "X00")
    dma("Y", T.X0[:, 512:1024], T.x[:, 512:1024], "dy", "", "X01")

    iota(T.ICOL[:], [[1, 256]], 0, 0, "ICOL")
    iota(IP[:, 0:1], [[0, 1]], 0, 1, "ip0", flag=False)
    iota(T.I16[:], [[0, 16], [1, 16]], 0, 0, "I16")
    iota(T.TAB[:, 0:8], [[16, 2], [4, 2], [1, 2]], 0, 0, "TAB")
    for i in range(3, 8):
        act(T.TAB[:, 1 << i:2 << i], T.TAB[:, 0:1 << i], "TAB", "TAB", bias=float(4 ** i))
    iota(SC[:, 0:4], [[15 * 2048, 2], [128, 2]], 256, 1, "J")
    iota(RW[:, 16:24], [[17, 2], [0, 4]], 0, 0, "rw16")
    iota(RW[:, 36:42], [[-3, 3], [4, 2]], 8, 0, "rw36")
    iota(RW[:, 42:48], [[-3, 3], [0, 2]], 8, 0, "rw42")
    iota(RW[:, 48:52], [[2, 2], [0, 2]], 0, 0, "rw48")
    iota(T.LW[:, 0:136], [[-1, 4], [8, 2], [0, 17]], 48 + 7, 0, "LW")
    iota(T.LW[:, 16:136:17], [[-1, 4], [8, 2]], 32 + 7, 0, "LW")
    row(T.CE[:, 0:136], 136, 0, 0, "CE")
    row(T.CE[:, 0:136:17], 8, 0, 2 ** 20, "CE")
    for k in range(4):
        o, z = 34 * k, 1 << k
        for a, n, c, b, m in ((z, 8 >> k, 0, 1, 4), (2 * z, (8 >> k) - 1, 16, -9, -12)):
            if n:
                iota(T.LW[:, o + a:o + 16:2 * z], [[0, n]], c + 7 - k, 0, "", "LW lw%d" % k)
                iota(T.CE[:, o + a:o + 16:2 * z], [[m * int(STEP), n]], b * int(STEP), 0, "", "CE ce%d" % k)
        act(T.LW[:, o + 17:o + 33], T.LW[:, o:o + 16], "lw%d" % k, "", "LV", bias=8.0)
        act(T.CE[:, o + 17:o + 33], T.CE[:, o:o + 16], "ce%d" % k, "", "CF")
    act(T.LW[:, 136:272], T.LW[:, 0:136], "LW LV", "LV", bias=-4.0)
    act(T.CE[:, 136:272], T.CE[:, 0:136], "CE CF", "CF")
    row(T.WX[:, 48:64], 16, 0, 0, "wx0")
    row(T.VB[:], 256, 1, 0, "VB")
    fill(T.MS[:], 0, "MS0 MS1 MS2")
    fill(H2, 2.0, "H2")
    fill(T.HS[:, 32:48:8], 0.0, "H2")
    for key, o, n, c, a, z in (("H1", 0, 32, 1, 0, 16), ("H4", 48, 16, 4, 8, 8), ("HN", 64, 16, 2, 0, 4)):
        row(T.HS[:, o:o + n], n, 0, c, key)
        row(T.HS[:, o + a:o + n:z], len(range(a, n, z)), 0, 0, key)
    row(T.NEG[:], 256, 0, -1, "NEG")
    row(THR, 16, 0, 1e9, "THR")
    scan(T.HS[:, 96:104], T.HS[:, 48:56], T.NEG[:, 0:8], 0.5, A.mult, A.max, "H4 NEG", "THR")
    row(PN[:, 0:256], 256, 0, 0, "", "p0")
    row(PN[:, 256:512], 256, 0, 0, "", "p0")
    row(PN[:, 512:544], 32, 0, 0, "", "p0")
    act(PN[:, RL + 32:7 * RL:34], T.ICOL[:, 0:12], "ICOL p0", "pd", scale=0.0, bias=CEIL)
    fill(T.YY[:], 0, "yd")
    fill(T.YY[:, 32:33], 4 * HALF, "yd")
    row(T.DF[:, 0::34], 2, 0, 0, "d0")
    row(T.DI[:, 0:1], 1, 0, 0, "", "di0")
    row(T.DI[:, 34:40], 6, 0, 4 * DEAD, "", "di0")
    row(T.IN[:, 32:36], 4, 0, 0, "in0")
    row(T.RT[:, 31:32], 1, 0, -1, "rt0")
    row(T.ET[:, 384:512], 128, 0, 0, "ET4")
    act(T.H16[:, 16:34:17], SC[:, 0:2], "J", "h0")
    act(T.VH[:, 16:34:17], SC[:, 0:2], "J", "v0")
    for c, sh, m in ((1, 0, 15), (2, 2, 2), (3, 0, 1), (4, 1, 1), (5, 2, 1), (6, 1, 7), (7, 0, 6)):
        ts(IP[:, c:c + 1], IP[:, 0:1], sh, m, A.arith_shift_right, A.bitwise_and, "ip0", "", "ip")
    cp(SC[:, 4:9], IP[:, 1:6], "ip", "s4")
    cp(SC[:, 24:26], IP[:, 6:8], "ip", "s24")
    for c, i, m, a in ((11, 4, 16, 0), (9, 7, 17, 16), (12, 6, 17, 16), (10, 8, 8, 0)):
        act(sc(c), sc(i), "s4", "s%d" % c, scale=float(m), bias=float(a))
    ts(sc(16), sc(4), 0.0, 34.0, A.is_equal, A.mult, "s4", "s16")
    act(JL, T.ICOL[:, 0:16], "ICOL s11", "JL", bias=sc(11))
    cp(T.LT[:], JL, "JL", "LT")
    act(T.ICT[:], ind(T.ICOL[:], T.LT[:]), "ICOL LT", "ICT")
    ts(LS[:, 36:44], RW[:, 16:24], sc(4), sc(16), A.add, A.max, "rw16 s4 s16", "Li")
    ts(IP[:, 8:14], RW[:, 36:42], sc(5), sc(6), A.add, A.add, "rw36 s4", "k0")
    ts(IP[:, 16:22], IP[:, 8:14], 7, None, A.bitwise_and, None, "k0", "k1")
    ts(RW[:, 0:6], IP[:, 16:22], 5.0, 34.0, A.min, A.mult, "k1", "k5")
    ts(LS[:, 44:50], RW[:, 0:6], sc(9), None, A.add, None, "k5 s9", "Lr")
    ts(LS[:, 30:36], IP[:, 16:22], sc(10), None, A.max, None, "k1 s10", "Lt")
    act(T.TH[:], ind(THR, LS[:, 30:36]), "THR Lt", "TH")
    ts(IP[:, 24:30], RW[:, 42:48], sc(24), None, A.add, None, "rw42 s24", "k2")
    ts(IP[:, 32:38], IP[:, 24:30], 7, None, A.bitwise_and, None, "k2", "k3")
    ts(LS[:, 50:56], IP[:, 32:38], 34.0, sc(12), A.mult, A.add, "k3 s12", "Ly")
    act(sc(13), sc(25), "s24 s4", "s13", scale=4.0, bias=sc(6))
    ts(LS[:, 0:4], RW[:, 48:52], sc(13), None, A.add, None, "rw48 s13", "Lk")
    ts(MK[:, 128:256], T.I16[:, 0:128], sc(4), 8000.0, A.not_equal, A.mult, "I16 s4", "mk0")
    tt(MK[:, 1:96], MK[:, 129:224], MK[:, 128:223], A.subtract, "mk0", "MK")
    act(MK[:, 0:1], MK[:, 128:129], "mk0", "mk1")
    act(MK[:, 16:96:16], MK[:, 16:96:16], "MK", "MK", bias=-3000.0)
    for a, b in ((0, 96), (96, 192), (192, 272)):
        scan(T.LW[:, 272 + a:272 + b], MK[:, 0:b - a], T.LW[:, a:b], 0.0, A.add, A.max, "MK mk1 LW LV", "", "LY")
    ts(T.LX[:, 0:17], T.LW[:, 287::16], MK[:, 143:144], None, A.subtract, None, "LY mk0", "Lm")
    iota(SC[:, 20:22], [[128, 2]], 0, 1, "s20")
    fill(T.ELT[:], 0.0, "ELT")
    ts(T.ELT[:, 3:515:4], T.VB[:, 0:128], sc(20), 32.0, A.is_equal, A.mult, "VB s20", "ELT")
    ts(IP[:, 38:39], IP[:, 0:1], 4, None, A.arith_shift_right, None, "ip0", "ip6")
    ts(sc(22), IP[:, 38:39], sc(11), None, A.add, None, "ip6 s11", "s22")
    act(sc(23), sc(22), "s22", "s23", bias=8.0)
    for i in range(4):
        quant(T.ELQ[:, 128 * i:128 * i + 128], T.ELS[:, 128 * i:128 * i + 128], T.ELT[:, 3 - i:515 - i], "ELT", "EL%d" % i)
        for n, c, key in ((0, -1.0, "s20"), (1, UNIT, "s22 s23")):
            o = 1024 * n + i
            if i % 2 == 0:
                ts(T.MTT[:, o:1024 * n + 1024:4], T.VB[:], sc(20 + 2 * n + i // 2), c, A.is_equal, A.mult, "VB " + key, "mt%d%d" % (n, i))
            else:
                act(T.MTT[:, o:1024 * n + 1024:4], T.MTT[:, o - 1:1024 * n + 1024:4], "mt%d%d" % (n, i - 1), "", "MT%d" % n)
    for i in range(2):
        quant(T.MTQ[:, 256 * i:256 * i + 256], T.MTS[:, 256 * i:256 * i + 256], T.MTT[:, 1024 * i:1024 * i + 1024], "MT%d" % i, "MQ%d" % i)
    quant(T.UQ[:, 0:128], T.US[:, 0:128], T.UT[:, 0:512], "UT0", "UQ0")

    DB = (4, 5, 6, 7)
    pairs = [slice(0, 32, 2), slice(34, 66, 2)]
    words = [slice(1, 33, 2), slice(35, 67, 2)]
    both = [slice(0, 32), slice(34, 66)]
    even, odd = slice(0, RL, 2), slice(1, RL, 2)

    def at(buf, k, s):
        return buf[:, RL * k + s.start:RL * k + s.stop:s.step]
    for t in range(3):
        src = T.X0 if t == 0 else T.XT
        for h in range(2):
            quant(T.XQ[:, 128 * h:128 * h + 128], T.XS[:, 128 * h:128 * h + 128], src[:, 512 * h:512 * h + 512], ("X0%d" if t == 0 else "XT X3%d") % h, "XQ%d" % h)
        if t == 0:
            for i in range(3):
                dma("Y", T["AC%d" % i][:, 0:32].bitcast(dt.uint8), T.XQ[:, 0:32].bitcast(dt.uint8), "dfill", "XQ0", "pc%d" % i)
                dma("Y", T["AS%d" % i][:, 0:32], T.XS[:, 0:32], "dfill", "XQ0", "ps%d" % i)
            dma("Y", T.WQ[:].bitcast(dt.uint8), T.wc[:], "dw", "X01", "WQ")
            dma("Y", T.WS[:], T.ws[:], "dw", "X01", "WS")
            dma("Y", T.VT[:], T.v[:], "dv", "X01", "VT")
            dma("Y", T.UT[:, 512:1024], T.u[:], "du2", "X01", "UT1")
            quant(T.VQ[:], T.VS[:], T.VT[:], "VT", "VQ")
            quant(T.UQ[:, 128:256], T.US[:, 128:256], T.UT[:, 512:1024], "UT1", "UQ1")
        for s in range(2):
            mm(B(s)[:, 0:128], T.XQ[:, 128 * s:128 * s + 128], T.XS[:, 128 * s:128 * s + 128], T.UQ[:, 48 * t:48 * t + 128], T.US[:, 48 * t:48 * t + 128],
               True, True, "XQ%d UQ0" % s + " UQ1" * (t > 0), "B%d" % s)
            ts(T.W1[:, 8 * s:8 * s + 8], B(s)[:, 112::-16], 0.0, None, A.is_gt, None, "B%d" % s, "", "W1")
        scan(T.W2[:, 0:16], H2, T.W1[:], 0.0, A.mult, A.add, "H2 W1", "W2")
        cp(T.MS[:, 8 * t:8 * t + 4:2], T.W2[:, 7:16:8], "W2", "MS%d" % t)
        WL = T["WL%d" % t]
        remote(WL[:], T.MS[:, 8 * t:8 * t + 4], "wa%d" % t, "lw%d" % t, "MS%d" % t, "WL%d" % t)
        scan(T.W2[:, 16:32], H4, T.W1[:], 4.0, A.mult, A.add, "H4 W1", "W3")
        scan(T.WN[:], HN, T.W1[:], 0.0, A.mult, A.add, "HN W1", "P4")
        for i in range(4):
            h, s = i // 2, i % 2
            ts(T.OT[:, i::4], T.VB[:, 128 * h:128 * h + 128], T.W2[:, 8 * s + 7:8 * s + 8], None, A.is_equal, None, "VB W2", "", "OT")
        quant(T.OQ[:], T.OS[:], T.OT[:], "OT MS%d" % t, "OQ")
        for h in range(2):
            a, b, o = 256 * h, 256 * h + 256, 512 * h
            mm(B(2 + h)[:, 0:256], T.OQ[:], T.OS[:], T.ELQ[:, a:b], T.ELS[:, a:b], True, True, "OQ EL%d EL%d" % (2 * h, 2 * h + 1), "B%d" % (2 + h))
            act(T.HB[:, a:b], B(2 + h)[:, 0:256], "B%d" % (2 + h), "HB%d" % h, scale=255 / 32)
            scan(back(T.DS, o + 511, 256), T.NEG[:], back(T.HB, b - 1, 256), 0.0, A.add, A.max, "NEG HB%d" % h, "DR%d" % h)
            scan(back(T.DS, o + 255, 256), T.NEG[:], back(T.HB, b - 1, 256), T.DS[:, o + 256:o + 257], A.add, A.max, "NEG DR%d HB%d" % (h, h), "DS%d" % h)
            ds = T.DS[:, o + 1:o + 257]
            act(T.DH[:, a:b], ds, "DR%d DS%d" % (h, h), "DH%d" % h, bias=2055.5)
            act(T.DT[:, 2 * h::4], T.DH[:, a:b], "DH%d" % h, "dh%d" % h, bias=-2048.0)
            scan(T.DT[:, 2 * h + 1::4], ds, T.DT[:, 2 * h::4], 0.0, A.max, A.subtract, "DR%d DS%d dh%d" % (h, h, h), "dw%d" % h)
        quant(T.DQ[:], T.DP[:], T.DT[:], "dh0 dw0 dh1 dw1", "DQ")
        for b in range(4):
            mm(B(DB[b])[:, 0:256], T.ELQ[:, 128 * b:128 * b + 128], T.ELS[:, 128 * b:128 * b + 128], T.XQ[:], T.XS[:], True, True,
               "EL%d XQ0 XQ1" % b, "B%d" % DB[b])
            f = T.FW[:, 512 * b:512 * b + 256]
            act(f, B(DB[b])[:, 0:256], "B%d" % DB[b], "FW%d" % b, scale=2.0 ** -6)
            dma("Y", T.FW[:, 512 * b + 256:512 * b + 512], f, "dc%d" % t, "FW%d" % b, "FX%d" % b)
            act(T.FT[:, 256 * b:256 * b + 256], ind(f, T.LT[:]), "FW%d LT" % b, "FT%d" % b)
        for b in OPT["no"]:
            s, o = b % 2, 256 * (b // 2)
            mm(B(b)[:, 0:256], T.DQ[:, 128 * s:128 * s + 128], T.DP[:, 128 * s:128 * s + 128], T.MTQ[:, o:o + 256], T.MTS[:, o:o + 256], True, True,
               "DQ MQ%d" % (b // 2), "B%d" % b)
        for s in range(2):
            a, b, hi = 256 * s, 256 * s + 256, T.WN[:, 8 * s + 3:8 * s + 4]
            act(T.H16[:, 36 + s:37 + s], hi, "P4 J", "HO%d" % s, scale=-RAISE / UNIT, bias=sc(2 + s))
            ts(T.MH[:, a:b], T.I16[:], hi, 1.0 - RAISE, A.is_gt, A.subtract, "I16 P4", "MH%d" % s)
            scan(T.HH[:, a:b], T.MH[:, a:b], B(2 + s)[:, 0:256], 0.0, A.add, A.max, "MH%d B%d" % (s, 2 + s), "HH%d" % s)
            act(T.H16[:, 17 * s:17 * s + 16], T.HH[:, a + 15:b:16], "HH%d HO%d" % (s, s), "H16%d" % s, scale=-1 / UNIT, bias=T.H16[:, 36 + s:37 + s])
        act(T.WX[:, 0:16], T.WN[:], "P4", "", "WX", scale=-2 * STEP)
        act(T.WX[:, 16:32], T.WN[:], "P4", "", "WX", scale=6 * STEP)
        for k in range(4):
            act(T.WX[:, 35 - k:48:4], T.WN[:, 3 - k::4], "P4", "", "WX", scale=32.0, bias=-32.0 * ((15 >> k) ^ 1), func=AF.Square)
        tt(T.DM[:], ind(T.WX[:], T.LX[:, 0:17]), T.CE[:], A.add, "WX wx0 Lm CE CF", "DM")
        for s in range(2):
            w4, theirs = T.W2[:, 23 + 8 * s:24 + 8 * s], ind(T.TAB[:], WL[:, 2 * s:2 * s + 1])
            ts(at(T.YY, 0, words[s]), T.TAB[:, 0::17], w4, 4.0, A.add, A.mult, "TAB W3 yd", "x%d" % s)
            ts(at(T.YY, 0, pairs[s]), theirs, w4, 4.0, A.add, A.mult, "TAB W3 yd WL%d" % t, "y%d" % s)
        ts(T.NB[:, 0:34], T.YY[:, even], 4 * (LOW + HALF), 2, A.bitwise_and, A.arith_shift_right, "y0 y1 yd", "NB")
        ts(T.NB[:, 34:68], T.YY[:, even], 4 * (4 ** 6 + HALF), 1, A.bitwise_and, A.arith_shift_right, "y0 y1 yd", "N6")
        tt(T.DF[:, 35:68], T.NB[:, 34:67], T.NB[:, 35:68], A.subtract, "N6", "d6")
        for o, ys, c in ((1, "x0 x1 yd", "s"), (0, "y0 y1 yd", "p")):
            ts(T.N2[:, RL + o:2 * RL:2], T.YY[:, o::2], 4 * LOW, None, A.bitwise_and, None, ys, "n4" + c)
            ts(T.N2[:, o:RL:2], T.YY[:, o::2], 4 * LOW, 1, A.bitwise_and, A.arith_shift_right, ys, "n2" + c)
            for k in range(0, 6, 2):
                ts(EK[:, RL * k + o:RL * k + 2 * RL:2], T.N2[:, o::2], 2 * 4 ** k + 4 ** (k + 2), None, A.bitwise_and, None,
                   "n2%s n4%s" % (c, c), "", "ek%d ek%d" % (k, k + 1))
        ts(PN[:, even], T.N2[:, RL:2 * RL:2], 0.0, DEAD, A.is_equal, A.mult, "n4p p0", "pn00 pn01")
        tt(T.DF[:, 1:34], T.NB[:, 0:33], T.NB[:, 1:34], A.subtract, "NB", "df")
        ts(at(EK, 6, odd), T.N2[:, odd], 2 * 4 ** 6, None, A.bitwise_and, None, "n2s", "ek6")
        for k in range(7):
            kp = " pd pn%d0 pn%d1" % (k, k)
            if k < 6:
                for s in range(2):
                    c = (both if k % 4 else pairs)[s]
                    tt(at(EK, k, c), at(EK, k, c), at(PN, k, c), A.add, "ek%d pn%d%d" % (k, k, s), "ec%d%d" % (k, s))
            else:
                tt(at(EK, 6, odd), at(EK, 6, odd), at(PN, 6, odd), A.add, "ek6 pn60 pn61", "ec60 ec61")
            scan(RR[:, 34 * k:34 * k + 34], T.DF[:, 0:34], at(PN, k, even), 1e9, A.add, A.min, "d0 df" + kp, "rr%d" % k)
            for s in range(2):
                r = RR[:, 34 * k + 17 * s + 16:34 * k + 17 * s + 17]
                c = (both if k < 6 else words)[s]
                ts(at(PN, k + 1, c), at(EK, k, c), r, DEAD, A.is_gt if k else A.is_ge, A.mult, "p0 ek%d ec%d%d rr%d" % (k, k, s, k), "pn%d%d" % (k + 1, s))
        scan(RR[:, 238:272], T.DF[:, 34:68], at(PN, 6, even), 1e9, A.add, A.min, "d0 d6 pd pn60 pn61", "rr7")
        tt(T.YT[:, 0:32], ind(RR[:, 0:204], LS[:, 44 + 2 * t:46 + 2 * t]), T.TH[:, 32 * t:32 * t + 32], A.is_ge, "Lr TH " + " ".join("rr%d" % k for k in range(6)), "DF")
        c6, c7 = [8 * (q // 2) + q % 2 for q in ((3 * t + 6) % 8, (3 * t + 7) % 8)]
        ts(T.YT[:, c6:c6 + 3:2], RR[:, 220:238:17], 2.0 * 4 ** 6, None, A.is_ge, None, "rr6", "", "DF")
        tt(T.YT[:, c7:c7 + 3:2], RR[:, 254::17], RR[:, 220:238:17], A.is_ge, "rr6 rr7", "", "DF")
        turn(T.YT[:, 32:64], T.YT[:, 0:32], "DF", "TF")
        for q in range(8):
            p, c = 32 * (q // 2), 16 * (q % 2)
            dma(OPT["dq"][q], T.IN[q::8, 0:32], T.YT[p:p + 32, 32 + c:48 + c], "dk%d" % t, "TF", "", "IN")
        lo = RL * 4 + 1
        tt(T.DI[:, 1:34], PN[:, lo:lo + 66:2], PN[:, lo + 2:lo + 68:2], A.subtract, "pn40 pn41", "DI")
        for s in range(2):
            act(T.INC[:, 64 * s:64 * s + 64], ind(T.DI[:], LS[:, 36 + 4 * s:40 + 4 * s]), "DI di0 Li", "INC%d" % s, scale=STEP / DEAD)
            for q in range(4):
                a = 256 * s + 64 * q
                scan(T.O[:, a:a + 64], T.INC[:, 64 * s:64 * s + 64], B(s)[:, 64 * q:64 * q + 64], 0.0, A.add, A.min, "INC%d B%d" % (s, s), "", "O%d" % s)
            act(T.H16[:, 38 + s:39 + s], PN[:, lo + 30 + 34 * s:lo + 31 + 34 * s], "pn4%d J" % s, "vb%d" % s, scale=STEP / DEAD, bias=sc(s))
            act(T.VH[:, 17 * s:17 * s + 16], T.O[:, 256 * s + 15:256 * s + 256:16], "O%d vb%d" % (s, s), "", "VH", bias=T.H16[:, 38 + s:39 + s])
        for n, vals, kv, k, steps in ((0, T.H16[:, 0:34], "h0 H160 H161", 4, range(4)), (1, T.VH[:], "v0 VH", 6, range(4, 7)), (2, T.VH[:], "v0 VH", 7, (7,))):
            c = T.CL[:, 34 * n:34 * n + 34]
            tt(c, vals, at(PN, k, odd), A.add, kv + " p0 pn%d0 pn%d1" % (k, k), "CL%d" % n)
            for q in steps:
                scan(T.PS[:, 34 * q:34 * q + 34], T.DM[:, 34 * q:34 * q + 34], c, 0.0, A.add, A.min, "DM CL%d" % n, "", "PS")
        for s in range(2):
            act(T.YT[:, 64 + s:96:2], ind(T.YT[:, 0:32], LS[:, 2 * s:2 * s + 1]), "DF Lk J", "", "KM", scale=-STEP, bias=sc(s))
        tt(T.YA[:, 0:32], ind(T.PS[:], LS[:, 50 + 2 * t:52 + 2 * t]), T.YT[:, 64:96], A.max, "PS Ly KM", "YA")
        turn(T.YA[:, 32:64], T.YA[:, 0:32], "YA", "TR")
        cp(T.TU[:], T.YA[:, 32:64], "TR", "TU")
        for q in range(8):
            p, c = 32 * (q // 2), 16 * (q % 2)
            dma(OPT["dq"][q], T.AU[q::8, :], T.TU[p:p + 16, c:c + 16], "dl%d" % t, "TU", "", "AU")
        L, C, ND, NY = T.LF, T.CC[:, 0:16], T.CC[:, 16:17], T.CC[:, 18:19]
        scan(T.RB[:, 32:64], H1, T.IN[:, 0:32], 0.0, A.mult, A.add, "H1 IN", "", "RB")
        scan(back(T.RB, 31, 32), back(T.IN, 32, 32), H1, 0.0, A.add, A.mult, "H1 IN in0", "", "RB")
        act(T.RB[:, 64:96], T.IN[:, 0:32], "IN s11", "", "RB", scale=-STEP, bias=sc(11))
        turn(T.RT[:, 32:128], T.RB[:], "RB", "RT")
        scan(T.CC[:, 0:17], T.RT[:, 31:48], T.RT[:, 64:81], 0.0, A.add, A.add, "RT rt0", "ct")
        ts(L[:, 0:16], C, ND, sc(4), A.subtract, A.subtract, "ct s4", "l5")
        tt(L[:, 16:32], T.RT[:, 96:112], C, A.subtract, "RT ct", "l6")
        act(NY, ND, "ct s4", "ny", bias=sc(4))
        tt(L[:, 32:48], L[:, 0:16], L[:, 16:32], A.max, "l5 l6", "l7")
        ts(T.PU[:], L[:, 32:48], NY, None, A.add, None, "l7 ny", "PU")
        cp(ind(T.LR[:], T.PU[:]), T.ICT[:], "PU ICT", "LR")
        scan(T.LM[:], MK[:, 0:96], T.LR[:, 0:96], 0.0, A.add, A.max, "MK mk1 LR", "ln")
        ts(T.LU[:, 0:6], T.LM[:, 15::16], MK[:, 143:144], None, A.subtract, None, "ln mk0", "LU")
        for b in range(4):
            z, f = T.XW[:, 352 * b:352 * b + 256], ind(T.FW[:, 512 * b:512 * b + 512], T.AU[:])
            ft, gw, fl, o = T.FT[:, 256 * b:256 * b + 256], T.GW[:, 256 * b:256 * b + 256], T.FL[:, 96 * b:96 * b + 96], T.ET[:, b:384:4]
            move = {"A": act, "V": cp}[OPT["et"][b]]
            if OPT["xz"][b] == "V":
                tt(z, f, ft, A.add, "FW%d FX%d FT%d AU" % (b, b, b), "XZ%d" % b)
                move(o, ind(z, T.LU[:, 0:6]), "XZ%d LU" % b, "", "ET")
            else:
                act(gw, f, "FW%d FX%d AU" % (b, b), "GW%d" % b)
                move(fl, ind(ft, T.LU[:, 0:6]), "FT%d LU" % b, "FL%d" % b)
                tt(o, ind(gw, T.LU[:, 0:6]), fl, A.add, "GW%d FL%d LU" % (b, b), "", "ET")
        quant(T.EQ[:], T.ES[:], T.ET[:], "ET ET4", "EQ")
        remote(T["AC%d" % t][:, 32:128].bitcast(dt.uint8), T.EQ[:, 0:96].bitcast(dt.uint8), "ca%d" % t, "lc%d" % t, "EQ", "AC%d" % t)
        remote(T["AS%d" % t][:, 32:128], T.ES[:, 0:96], "ca%d" % t, "lc%d" % t, "EQ", "AC%d" % t)
        for b in range(4):
            if OPT["xz"][b] == "A":
                tt(T.XW[:, 352 * b:352 * b + 256], T.GW[:, 256 * b:256 * b + 256], T.FT[:, 256 * b:256 * b + 256], A.add, "GW%d FT%d EQ" % (b, b), "XZ%d" % b)
        ts(L[:, 48:64], T.PU[:], 256.0, None, A.add, None, "PU EQ", "pos")
        ts(L[:, 64:80], T.PU[:], 96.0, 4096.0, A.is_lt, A.mult, "PU EQ", "m0")
        tt(L[:, 80:96], L[:, 64:80], L[:, 48:64], A.min, "m0 pos", "m1")
        tt(L[:, 96:112], L[:, 80:96], JL, A.max, "m1 JL", "m2")
        cp(T.SU[:], L[:, 96:112], "m2", "SU")
        if t == 2:
            cp(T.AI[:, 0:16], T.AU[:], "AU EQ", "a0")
            ts(T.AI[:, 16:32], T.AI[:, 0:16], 255, None, A.bitwise_and, None, "a0", "ai")
            cp(T.AF[:], T.AI[:, 16:32], "ai", "af")
            dma("Y", T.al[:, 0:256], T.AF[:], "dout", "af")
            act(T.LO[:], ind(T.ICT[:], T.LU[:, 0:6]), "ICT LU EQ", "LO")
            dma("Y", T.al[:, 256:352], T.LO[0::16, :], "dout", "LO")
        AC, AS, ka = T["AC%d" % t][:], T["AS%d" % t][:, 0:128], " AC%d pc%d ps%d" % (t, t, t)
        for b in range(4):
            kb, o, i = "B%d" % DB[b], T.XW[:, 352 * b + 256:352 * b + 352], B(DB[b])[:, 32:128]
            mm(B(DB[b])[:, 0:128], T.WQ[:, 128 * b:128 * b + 128], T.WS[:, 128 * b:128 * b + 128], AC, AS, True, False, "WQ WS" + ka, kb)
            mm(B(DB[b])[:, 0:128], T.ELQ[:, 128 * b:128 * b + 128], T.ELS[:, 128 * b:128 * b + 128], AC, AS, False, True, "EL%d" % b + ka, "", kb)
            win, r = T.XW[:, 352 * b:352 * b + 352], "XZ%d XT%d SU" % (b, b)
            if b % 2 == 0:
                act(o, i, kb, "XT%d" % b, scale=2.0 ** -5)
                act(T.XT[:, b::4], ind(win, T.SU[:]), r, "", "XT")
            else:
                ts(o, i, 2.0 ** -5, None, A.mult, None, kb, "XT%d" % b)
            if b == 1:
                cp(T.XT[:, b::4], ind(win, T.SU[:]), r, "", "XT")
            if b == 3:
                cp(T.XT[:, 3:512:4], ind(win, T.SU[:, 0:8]), r, "X30")
                act(T.XT[:, 515::4], ind(win, T.SU[:, 8:16]), r, "X31")
    for h in range(2):
        a, b = 128 * h, 128 * h + 128
        quant(T.XQ[:, a:b], T.XS[:, a:b], T.XT[:, 4 * a:4 * b], "XT X3%d" % h, "XQ%d" % h)
        dma("Y", T.oc[:, 4 * a:4 * b], T.XQ[:, a:b].bitcast(dt.uint8), "dout", "XQ%d" % h)
        mm(B(2 + h)[:, 0:128], T.VQ[:], T.VS[:], T.XQ[:, a:b], T.XS[:, a:b], True, True, "VQ XQ%d" % h, "B%d" % (2 + h))
        cp(T.YO[:, a:b], B(2 + h)[:, 0:128], "B%d" % (2 + h), "YO%d" % h)
        dma("YA"[h], T.y[:, a:b], T.YO[:, a:b], "dout", "YO%d" % h)
    for k in range(4):
        dma("A", T.osc[4 * k:4 * k + 4, :], T.XS[32 * k:32 * k + 4, :], "dout", "XQ0 XQ1")
    if not ORDER:
        ORDER.extend(arrange())
    issue(ORDER)
